import numpy as np, ml_dtypes
CORES = [35,38,43,46]
N = 4
BF = ml_dtypes.bfloat16
def gentries(a):
    return np.ascontiguousarray(a.reshape(8, 16, -1).transpose(0, 2, 1)).reshape(8, -1)
def gtable(e):
    e = np.asarray(e); return np.ascontiguousarray(e.reshape(8, -1, 16).transpose(0, 2, 1)).reshape(128, -1).astype(np.int32)
def f(rng, *shape):
    return (rng.standard_normal(shape, dtype=np.float32) * np.exp2(rng.integers(-2, 3, shape[:-1] + (1,)))).astype(BF)
def wide(rng, *shape):
    v = f(rng, *shape).astype(np.float32); k = shape[:-2] + (1, shape[-1])
    return (v * np.exp2(rng.integers(-6, 7, k)) * (rng.random(k) > 0.0625)).astype(BF)
V, D, C, R = 2048, 2, 96, 3
def ranks(t):
    return t.reshape(8, D, N, V).transpose(2, 0, 1, 3)
def globe(a, bl):
    out = np.zeros((N, 8, D * V), np.int64)
    for r in range(N):
        own = np.broadcast_to(r * V + np.arange(V), (8, V))
        ghosts = (np.arange(N)[:, None, None] * V + bl[:, :, r]).transpose(1, 0, 2).reshape(8, N * C)
        out[r] = np.take_along_axis(np.concatenate([own, ghosts], 1), a[r].reshape(8, D * V).astype(np.int64), 1)
    return out.reshape(N, 8, D, V).transpose(1, 2, 0, 3).reshape(8, D, N * V)
def unpack(nb, bl):
    return np.stack([gentries(t) for t in nb]).reshape(N, 8, D, V), np.stack([gentries(t) for t in bl]).reshape(N, 8, N, C)
def pack(rng, a, bl, v):
    o = np.argsort(rng.random(a.shape), 2); a = np.take_along_axis(a, o, 2); v = np.take_along_axis(v, o, 2)
    return {"nb": np.stack([gtable(t.reshape(8, D * V)) for t in a]), "bl": np.stack([gtable(t.reshape(8, N * C)) for t in bl]),
            "w": np.ascontiguousarray(v).reshape(N, 8, D * V).astype(np.float32).astype(BF), "x": f(rng, N, 128, V)}
def graphs(rng, p):
    bl = np.argsort(rng.random((N, 8, N, V)), axis=-1)[..., :C]
    a = np.full((N, 8, D, V), -1, np.int64)
    for g in range(8):
        for d in range(D):
            for r in range(N):
                for q in range(r):
                    o = rng.permutation(C); u = bl[r, g, q]; t = bl[q, g, r][o]
                    k = (a[r, g, d, u] < 0) & (a[q, g, d, t] < 0) & (rng.random(C) < p)
                    a[r, g, d, u[k]] = V + q * C + o[k]; a[q, g, d, t[k]] = V + r * C + np.flatnonzero(k)
            for r in range(N):
                e = rng.permutation(np.flatnonzero(a[r, g, d] < 0)); h = len(e) // 2
                a[r, g, d, e[:h]] = e[h:2 * h]; a[r, g, d, e[h:2 * h]] = e[:h]
                if len(e) > 2 * h: a[r, g, d, e[-1]] = (e[-1] + 1) % V
        for r in range(N):
            alias = np.full(V, -1, np.int64); alias[bl[r, g, r]] = V + r * C + np.arange(C)
            b = a[r, g]; n = np.where(b < V, alias[np.minimum(b, V - 1)], -1)
            a[r, g] = np.where((n >= 0) & (rng.random((D, V)) < 0.5), n, b)
    return a, bl
def both(a, bl, z):
    return np.array(ranks(np.take_along_axis(z, np.minimum(globe(a, bl), np.arange(N * V)), 2)))
def setup_inputs(rng):
    a, bl = graphs(rng, 0.6)
    return pack(rng, a, bl, both(a, bl, np.exp2(4 * rng.random((8, D, N * V)))))
def setup_inputs_ties(rng):
    a, bl = graphs(rng, 0.6); z = rng.integers(1, 4, (8, D, N * V)).astype(np.float64); z[rng.integers(0, 8)] = 1
    z *= np.exp2(rng.integers(-20, 21, (8, 1, 1)))
    return pack(rng, a, bl, both(a, bl, z))
def setup_inputs_borders(rng):
    a, bl = graphs(rng, 1.0); v = both(a, bl, np.exp2(3 * rng.random((8, D, N * V))))
    far = ranks(globe(a, bl) // V != np.arange(N * V) // V)
    return pack(rng, a, bl, v * np.where(far, 8, 1))
def setup_inputs_hubs(rng):
    a, bl = graphs(rng, 0.6); v = both(a, bl, np.exp2(4 * rng.random((8, D, N * V))))
    for r in range(N):
        for g in range(8):
            e = rng.permutation(V); h = e[:16]; leaves = e[16:V // 2]; b = a[r, g]; c = v[r, g]
            b[:, leaves] = h[rng.integers(0, 16, (D, len(leaves)))]
            b[0, h] = h[np.arange(16) ^ 1]; c[0, h] = 256
    return pack(rng, a, bl, v)
def setup_inputs_any(rng):
    bl = rng.integers(0, V, (N, 8, N, C)); bl[..., C // 2:] = bl[..., :1]; bl[..., 1] = 0; bl[..., 2] = V - 1
    a = rng.integers(0, V + N * C, (N, 8, D, V)); j = np.arange(V)
    a = np.where(ranks(globe(a, bl) == np.arange(N * V)), (j + 1) % V, a)
    o = rng.permutation(8); a[:, o[0]] = (j + 1) % V; a[:, o[1]] = j ^ 1
    for r in range(N):
        for g in o[2:5]:
            q = r ^ 1
            a[r, g, :, bl[r, g, q, 0]] = V + q * C + rng.choice(np.r_[0, C // 2:C], D)
    return pack(rng, a, bl, np.exp2(4 * rng.random((N, 8, D, V))))
def setup_inputs_spread(rng):
    a, bl = graphs(rng, 0.6); z = np.exp2(rng.integers(-3, 4, (8, D, N * V)) + rng.random((8, D, N * V)))
    d = pack(rng, a, bl, both(a, bl, z)); d["x"] = wide(rng, N, 128, V); return d
def check_inputs(d):
    bad = []
    if d["bl"].min() < 0 or d["bl"].max() >= V: bad.append("bl")
    if d["nb"].min() < 0 or d["nb"].max() >= V + N * C: bad.append("nb")
    if not bad and (globe(*unpack(d["nb"], d["bl"])) == np.arange(N * V)).any(): bad.append("own neighbour")
    u = d["w"].astype(np.float32)
    if not (np.isfinite(u).all() and (u > 0).all()): bad.append("w")
    v = np.abs(d["x"].astype(np.float32))
    if not np.isfinite(v).all(): bad.append("x")
    if not 4.0 * D * float(u.max()) * float(v.max()) < 2.0 ** 127: bad.append("range")
    return bad
def reference(nb, bl, w, x):
    i = np.arange(N * V); A = globe(*unpack(nb, bl))
    u = w.astype(np.float64).reshape(N, 8, D, V).transpose(1, 2, 0, 3).reshape(8, D, N * V)
    mate = np.tile(i, (8, 1)); free = np.ones((8, N * V), bool)
    for t in range(R):
        k = np.where(np.take_along_axis(free[:, None], A, 2), u, 0.0)
        P = np.take_along_axis(A, np.argmax(k, 1)[:, None], 1)[:, 0]
        P = np.where(free & (np.max(k, 1) > 0), P, -1)
        hit = (P >= 0) & (np.take_along_axis(P, np.maximum(P, 0), 1) == i)
        mate = np.where(hit, P, mate); free = free & ~hit
    two = mate != i; first = np.minimum(mate, i); rep = first == i
    num = (np.add.accumulate(rep.reshape(8, N, V).astype(np.int64), 2) - 1 + V * np.arange(N)[:, None]).reshape(8, N * V)
    cm = np.take_along_axis(num, first, 1).reshape(8, N, V)
    xx = np.ascontiguousarray(x.astype(np.float64).reshape(N, 8, 16, V).transpose(1, 2, 0, 3)).reshape(8, 16, N * V)
    X = xx + np.where(two[:, None], np.take_along_axis(xx, mate[:, None], 2), 0.0)
    s = np.zeros((8, 16, N * V))
    for d in range(D):
        s += u[:, d, None] * np.take_along_axis(X, A[:, d, None], 2)
    s = s + np.where(two[:, None], np.take_along_axis(s, mate[:, None], 2), 0.0)
    y = np.zeros((8, 16, N * V))
    for g in range(8):
        y[g][:, num[g, rep[g]]] = s[g][:, rep[g]]
    y = np.ascontiguousarray(y.reshape(8, 16, N, V).transpose(2, 0, 1, 3)).reshape(N, 128, V)
    return {"y": y.astype(np.float32), "cm": np.stack([gtable(cm[:, r]) for r in range(N)]).astype(np.float32)}

@@ -1,0 +1,583 @@
+import math
+from concourse.bass import DstId, RemoteDMATransfer
+from concourse.mybir import AluOpType, ActivationFunctionType
+
+OP = AluOpType
+AF = ActivationFunctionType
+V, C, Z = 2048, 96, 2432
+F32, BF, I32, U16 = "float32", "bfloat16", "int32", "uint16"
+WIDTHS = {
+    F32: dict(nbf=256, col=128, jr=8, jb=8, ir=128, rg=128, rgam=128, aw=128, ownt=256, ownp=128, iff=128, g8=8, sel1f=8, vl=128,
+              vz=128, w0s=128, dn=128, bd=128, hlf=256, h4=256, l4=256, beta=256, alph=256, stf=512, pif=256, t1=256, xf=2432,
+              num=128, cn=128, off=128, ms=128, sp=2432, sb=384, g1=2048, p0=2048, sw=2448, sst=384, id64=2048, inv=4096,
+              ivt=128, cmt=128, cmv=128, tw=2064, xb=384, gA=384, pB=384, bq=768, bqt=256),
+    BF: dict(wsb=4096, xw=2448, ia=256, ic=256, nwa=256, nwb=256, ib=128, i128=64, blk=128, lt=128, tri=128, samg=128, pack=1024,
+             src=512, lst=64, selg=24, sel4=16, sel1=8, nw=2432, bst=384, xst=384, xc=2048, wtb=2, bt=128, gb=8192, rh=256,
+             wr=4096, sq=512, wm=8192, mq=512, zt=128, zl=128, np=256, np9=256, mlh=128, ml10=128, ww=1024, ar=256,
+             mcode=128, tc=128, rep=128, rt=128, up=128, kc=128, one=128, thr=256, tq=128),
+    I32: dict(bli=24, nbi=256, coli=16, li=256, sti=512, lj=256, yi=512, zi=512, ivi=128, bwi=48, nbw=4096, nbl=48),
+    U16: dict(bl16=24, hl16=256, pl16=256, idx=512, mate=128, ms16=128, off16=128, iv16=128, nb16=256, bw16=24, nbb16=48),
+}
+PSUM = {"psw": 2048, "pa": 512, "pb": 512, "pc": 512, "pd": 512}
+SCRATCH = {"snd": ("sbuf", [128, 4, 128], BF), "tg": ("sbuf", [128, 4, 128], BF)}
+for _d in WIDTHS:
+    for _n in WIDTHS[_d]:
+        SCRATCH[_n] = ("sbuf", [128, WIDTHS[_d][_n]], _d)
+for _n in PSUM:
+    SCRATCH[_n] = ("psum", [128, PSUM[_n]], F32)
+EXCH = ["name", "x", "gid", "code", "xs", "num", "s"]
+LOADS = ["bl", "nb", "w", "x", "xc", "nbw", "wr", "y0", "y1", "y2", "y3", "cm"]
+SEMAPHORES = ["cV", "cS", "cP", "cG"] + ["d_" + k for k in LOADS] + ["a_" + k for k in EXCH] + ["l_" + k for k in EXCH]
+SHARE = {"gid": (1024, 1024), "names": (1024, 512), "r0": (1024, 768, 896, 640), "r1": (1024, 1024, 896, 832), "x": 1408}
+
+
+def engine_plan(topo, src, cores):
+    away = [d for d in cores if d != src and topo.chip(d) != topo.chip(src)]
+    near = [d for d in cores if d != src and topo.chip(d) == topo.chip(src)]
+    used, out = [], {}
+    for group in (away, near):
+        for i, d in enumerate(group):
+            free = [e for e in topo.engines(src, d) if e not in used]
+            n = 1
+            while n * 2 <= len(free) // (len(group) - i) and n < 8:
+                n *= 2
+            out[d] = free[:n]
+            used = used + out[d]
+    return out
+
+
+def rank_program(g, core, T, topo):
+    r = T.rank_of(core)
+    if r is None:
+        return
+    cores = [int(c) for c in T.cores]
+    others = [d for d in range(len(cores)) if d != r]
+    queue = {"V": g.vector, "S": g.scalar, "P": g.tensor, "G": g, "Y": g.sync}
+    total, known, hist = {}, {q: {} for q in queue}, {}
+
+    def deps(q, tag, regs, kind, need):
+        for name, p0, p1, c0, c1 in regs:
+            ps = name in PSUM
+            for o, k, a0, a1, b0, b1 in hist.get(name, ()):
+                cross = ps and o["q"] != q
+                if kind == "r" and k == "r" and not cross:
+                    continue
+                if tag is not None and o["tag"] == tag and o["q"] == q:
+                    continue
+                if cross:
+                    hit = c0 // 512 <= (b1 - 1) // 512 and b0 // 512 <= (c1 - 1) // 512
+                else:
+                    hit = c0 < b1 and b0 < c1 and p0 < a1 and a0 < p1
+                if hit and (o["sem"] not in need or need[o["sem"]]["val"] < o["val"]):
+                    need[o["sem"]] = o
+
+    def note(o, outs, ins):
+        for kind, regs in (("w", outs), ("r", ins)):
+            for name, p0, p1, c0, c1 in regs:
+                hist.setdefault(name, []).append((o, kind, p0, p1, c0, c1))
+
+    def add(q, fn, outs, ins, sem=None, inc=1, tag=None, chain=True):
+        need, kq = {}, known[q]
+        deps(q, tag, ins, "r", need)
+        deps(q, tag, outs, "w", need)
+        for s, o in need.items():
+            if kq.get(s, 0) >= o["val"] or any(p is not o and p["know"].get(s, 0) >= o["val"] for p in need.values()):
+                continue
+            queue[q].wait_ge(T.sem[s], o["val"])
+            for k, v in o["know"].items():
+                kq[k] = max(kq.get(k, 0), v)
+        sem = sem or "c" + q
+        total[sem] = total.get(sem, 0) + inc
+        o = {"q": q if sem == "c" + q else q + sem, "tag": tag, "sem": sem, "val": total[sem], "know": dict(kq)}
+        o["know"][sem] = total[sem]
+        made = fn(queue[q])
+        if chain:
+            made.then_inc(T.sem[sem], inc)
+        note(o, outs, ins)
+
+    def X(name, c0, c1, step=1, p0=0, p1=128):
+        ap = T[name][p0:p1, c0:c1] if step == 1 else T[name][p0:p1, c0:c1:step]
+        return ap, [(name, p0, p1, c0, c1)]
+
+    def X3(name, i0, i1, j0, j1):
+        ap = T[name][:, i0:i1, j0:j1] if i1 - i0 > 1 else T[name][:, i0, j0:j1]
+        return ap, [(name, 0, 128, i0 * 128 + j0, (i1 - 1) * 128 + j1)]
+
+    def IX(win, b, offs, c, d, a=0):
+        return T[win][:, a:b].indirect(T[offs][:, c:d]), [(win, 0, 128, a, b), (offs, 0, 128, c, d)]
+
+    def col(j, p1=128):
+        return X("col", j, j + 1, 1, 0, p1)
+
+    def sc(s):
+        return s[0] if isinstance(s, tuple) else s
+
+    def rg(*xs):
+        return [y for x in xs if isinstance(x, tuple) for y in x[1]]
+
+    def tt(out, a, b, op, tag=None):
+        add("V", lambda e: e.tensor_tensor(out=out[0], in0=a[0], in1=b[0], op=op), rg(out), rg(a, b), tag=tag)
+
+    def ts(out, a, s1, op0, s2=None, op1=None, tag=None):
+        if op1 is None:
+            f = lambda e: e.tensor_scalar(out=out[0], in0=a[0], scalar1=sc(s1), scalar2=None, op0=op0)
+        else:
+            f = lambda e: e.tensor_scalar(out=out[0], in0=a[0], scalar1=sc(s1), scalar2=sc(s2), op0=op0, op1=op1)
+        add("V", f, rg(out), rg(a, s1, s2), tag=tag)
+
+    def cp(out, a, tag=None):
+        add("V", lambda e: e.tensor_copy(out=out[0], in_=a[0]), rg(out), rg(a), tag=tag)
+
+    def act(out, a, func=AF.Identity, bias=0.0, scale=1.0, tag=None):
+        if isinstance(bias, float) and isinstance(scale, float) and bias == 0.0 and scale == 1.0:
+            f = lambda e: e.activation(out=out[0], in_=a[0], func=func)
+        else:
+            f = lambda e: e.activation(out=out[0], in_=a[0], func=func, bias=sc(bias), scale=sc(scale))
+        add("S", f, rg(out), rg(a, bias, scale), tag=tag)
+
+    def mm(out, lhsT, rhs, start=True, stop=True, tag=None):
+        add("P", lambda e: e.matmul(out=out[0], lhsT=lhsT[0], rhs=rhs[0], start=start, stop=stop), rg(out), rg(lhsT, rhs), tag=tag)
+
+    def iota(out, pattern, base, cm, whole=False):
+        if whole:
+            f = lambda e: e.iota(out[0], pattern, base, cm)
+        else:
+            f = lambda e: e.iota(out[0], pattern, base, cm, allow_small_or_imprecise_dtypes=True)
+        add("G", f, rg(out), [])
+
+    def keep(out, a):
+        add("G", lambda e: e.affine_select(out[0], a[0], [[1, 512]], OP.is_ge, 0.0, 0, 0), rg(out), rg(a))
+
+    def dma(q, key, out_ap, outs, in_ap, ins):
+        add(q, lambda e: e.dma_start(out=out_ap, in_=in_ap), outs, ins, sem="d_" + key, inc=16)
+
+    plans = {c: engine_plan(topo, c, cores) for c in cores}
+
+    def send(key, src, dst):
+        parts, regs, n = [], [], 0
+        for d in others:
+            eng = plans[core][cores[d]]
+            n += len(eng)
+            a = topo.addr(cores[d])
+            s = src(d)
+            regs += s[1]
+            parts.append(RemoteDMATransfer(dst_ids=[DstId(rid=a[0], pnc=a[1])], dma_engine_mask=sum(1 << e for e in eng),
+                                           remote_sem=T.sem["a_" + key], srcs=[s[0]], dsts=[dst[0]]))
+        add("G", lambda e: e.remote_dma_fused(parts, local_sem=T.sem["l_" + key]), [], regs, sem="l_" + key, inc=n, chain=False)
+
+    def recv(key, regs):
+        n = sum(len(plans[cores[q]][core]) for q in others)
+        total["a_" + key] = n
+        note({"q": "R", "tag": None, "sem": "a_" + key, "val": n, "know": {"a_" + key: n}}, regs, [])
+
+    def ghosts(name):
+        return [(name, 0, 128, V + C * q, V + C * q + C) for q in others]
+
+    def pick(bank, c0, src, s0, sel, w0, w1, tag):
+        n = 16 * (w1 - w0)
+        for b in range(16):
+            mm(X(bank, c0 + b, c0 + n, 16), X(src, s0 + b, s0 + V, 16), X(sel, w0, w1), tag=tag)
+
+    def share(dst, a, win, w, offs, o, n):
+        cp(X(dst, a, a + n), IX(win, w, offs, o, o + n // 16))
+        act(X(dst, a + n, a + V), IX(win, w, offs, o + n // 16, o + 128))
+
+    mine, LN2 = V + C * r, math.log(2.0)
+    R4, KK, QB, QH, GM, WT, NQ, CV = (col(j) for j in (4, 5, 6, 7, 8, 9, 10, 11))
+    MC, CX, CK, CJ = 16, 32, 36, 48
+    dma("Y", "bl", T.bli[:, :], rg(X("bli", 0, 24)), T.bl[:, :], [])
+    dma("S", "nb", T.nbi[:, :], rg(X("nbi", 0, 256)), T.nb[:, :], [])
+    dma("Y", "w", T.wsb[0:8, :], rg(X("wsb", 0, 4096, 1, 0, 8)), T.w[:, :], [])
+    dma("S", "x", T.xw[:, 0:V], rg(X("xw", 0, V)), T.x[:, :], [])
+    dma("Y", "xc", T.xc[:, :], rg(X("xc", 0, V)), T.x[:, :], [])
+
+    iota(X("coli", 0, 1), [[0, 1]], 0, 1, True)
+    iota(X("ir", 0, 128), [[1, 128]], 0, 0)
+    iota(X("jr", 0, 8), [[1, 4], [0, 2]], 4 * r, 0)
+    iota(X("jb", 0, 8), [[0, 4], [1, 2]], 0, 0)
+    iota(X("ia", 0, 256), [[0, 64], [1, 4]], 0, 0)
+    iota(X("ic", 0, 256), [[1, 64], [0, 4]], 0, 0)
+    iota(X("rg", 0, 128), [[1, 8], [0, 16]], 0, 0)
+    for q in range(4):
+        iota(X("rgam", 32 * q, 32 * q + 32), [[2, 2], [0, 8], [1, 2]], 0, 0)
+    for q in range(4):
+        iota(X("aw", 32 * q, 32 * q + 32), [[16, 2], [32, 4], [1, 4]], 0, -1)
+    ts(X("coli", 1, 2), X("coli", 0, 1), 15, OP.bitwise_and)
+    ts(X("coli", 2, 3), X("coli", 0, 1), 4, OP.logical_shift_right)
+    cp(X("col", 0, 3), X("coli", 0, 3))
+    ts(X("col", MC, MC + 16), X("ir", 0, 16), col(1), OP.is_equal)
+    ts(X("ib", 0, 128), X("ir", 0, 128), col(0), OP.is_equal)
+    ts(X("jr", 0, 8), X("jr", 0, 8), col(MC + 2), OP.mult)
+    ts(X("jb", 0, 8), X("jb", 0, 8), col(MC + 3), OP.mult)
+    tt(X("col", CJ, CJ + 8), X("jr", 0, 8), X("jb", 0, 8), OP.add)
+    ts(X("nwa", 0, 256), X("ia", 0, 256), col(MC), OP.mult)
+    ts(X("g8", 0, 8), X("ir", 0, 8), col(2), OP.is_equal)
+    cp(X("bl16", 0, 24), X("bli", 0, 24))
+    ts(X("nwb", 0, 256), X("ic", 0, 256), col(MC + 1), OP.mult)
+    tt(X("nwb", 0, 256), X("nwa", 0, 256), X("nwb", 0, 256), OP.add)
+    for j in range(8):
+        o = X("nw", 256 * j, 256 * j + 256)
+        if j % 3 == 1:
+            act(o, X("nwb", 0, 256), AF.Identity, col(CJ + j))
+        else:
+            ts(o, X("nwb", 0, 256), col(CJ + j), OP.add)
+    cp(X("bst", 0, 384), IX("nw", V, "bl16", 0, 24))
+    send("name", lambda d: X("bst", C * d, C * d + C), X("nw", mine, mine + C))
+    act(X("nw", mine, mine + C), IX("nw", V, "bl16", 6 * r, 6 * r + 6))
+
+    for d in range(2):
+        for b in range(16):
+            mm(X(("pa", "pc")[d], b, 128, 16), X("wsb", d * V + b, d * V + V, 16, 0, 8), X("ib", 0, 8, 1, 0, 8), tag="wt")
+    act(X("w0s", 0, 128), X("pa", 0, 128))
+    act(X("xst", 0, 384), IX("xw", V, "bl16", 0, 24))
+    send("x", lambda d: X("xst", C * d, C * d + C), X("xw", mine, mine + C))
+    act(X("xw", mine, mine + C), IX("xw", V, "bl16", 6 * r, 6 * r + 6))
+    recv("name", ghosts("nw"))
+    recv("x", ghosts("xw"))
+    cp(X("nbf", 0, 256), X("nbi", 0, 256))
+    tt(X("dn", 0, 128), X("nbf", 128, 256), X("nbf", 0, 128), OP.subtract)
+    tt(X("bt", 0, 128), X("pc", 0, 128), X("w0s", 0, 128), OP.is_gt)
+    mm(X("pb", 0, 128), X("bt", 0, 128), X("ib", 0, 128))
+    ts(col(60), col(MC), 16.0, OP.mult, col(MC + 2), OP.add)
+    ts(col(61), col(MC + 3), 64.0, OP.mult, col(MC + 1), OP.add)
+    tt(X("bd", 0, 128), X("pb", 0, 128), X("dn", 0, 128), OP.mult)
+    tt(X("hlf", 0, 128), X("nbf", 0, 128), X("bd", 0, 128), OP.add)
+    cp(X("hl16", 0, 128), X("hlf", 0, 128))
+    tt(X("hlf", 128, 256), X("nbf", 128, 256), X("bd", 0, 128), OP.subtract)
+    cp(X("hl16", 128, 256), X("hlf", 128, 256))
+    for f in range(2):
+        ts(X("selg", 8 * f, 8 * f + 8), X("g8", 0, 8), col(60 + f), OP.mult)
+    ts(col(62), col(MC + 1), 4.0, OP.mult, col(MC), OP.add)
+    ts(col(62), col(MC + 2), 512.0, OP.mult, col(62), OP.add)
+    ts(col(62), col(MC + 3), 256.0, OP.mult, col(62), OP.add)
+    ts(X("selg", 16, 24), X("g8", 0, 8), col(62), OP.mult)
+    ts(X("coli", 3, 4), X("coli", 0, 1), 1, OP.logical_shift_right, 1, OP.bitwise_and)
+    ts(X("coli", 4, 5), X("coli", 0, 1), 3, OP.bitwise_and)
+    ts(X("coli", 5, 6), X("coli", 0, 1), 2, OP.logical_shift_right, 3, OP.bitwise_and)
+    ts(X("coli", 6, 7), X("coli", 0, 1), 5, OP.logical_shift_right, 1, OP.bitwise_and)
+    ts(X("coli", 7, 8), X("coli", 0, 1), 6, OP.logical_shift_right)
+    ts(X("coli", 8, 9), X("coli", 0, 1), 4, OP.logical_shift_right, 1, OP.bitwise_and)
+    cp(X("col", 3, 9), X("coli", 3, 9))
+    ts(CV, R4, 2.0, OP.mult, QH, OP.add)
+    ts(X("col", CX, CX + 4), X("ir", 0, 4), R4, OP.is_equal)
+    ts(X("col", CK, CK + 4), X("ir", 0, 4), KK, OP.is_equal)
+
+    for K in range(2):
+        share("gb", K * V, "nw", Z, "hl16", K * 128, SHARE["gid"][K])
+        pick("pa", K * 256, "gb", K * V, "selg", 0, 16, "gid")
+    for K in range(2):
+        for f in range(2):
+            cp(X3("snd", 0, 4, 64 * f + K * 32, 64 * f + K * 32 + 32), X("pa", K * 256 + f * 128, K * 256 + f * 128 + 128), tag="snd")
+    act(X("wtb", 0, 1), CV, AF.Exp, 0.0, 2 * LN2)
+    send("gid", lambda d: X3("snd", d, d + 1, 0, 128), X3("tg", r, r + 1, 0, 128))
+    for K in range(2):
+        pick("pb", 256 + K * 128, "gb", K * V, "selg", 16, 24, "gid2")
+    cp(X3("tg", r, r + 1, 0, 128), X3("snd", r, r + 1, 0, 128))
+    recv("gid", [("tg", 0, 128, q * 128, q * 128 + 128) for q in others])
+    for K in range(2):
+        iota(X("ownt", 128 * K, 128 * K + 128), [[0, 8], [1, 16]], V * r, 16)
+    for q in range(4):
+        iota(X("ownp", 32 * q, 32 * q + 32), [[0, 2], [1, 4], [2048, 4]], 512 * q, 4)
+    iota(X("kc", 0, 128), [[0, 128]], 8192, 0)
+    iota(X("one", 0, 128), [[0, 128]], 1, 0)
+    iota(X("xw", Z, Z + 16), [[0, 16]], 0, 0)
+    iota(X("sw", Z, Z + 16), [[0, 16]], 0, 0)
+    iota(X("tw", V, V + 16), [[0, 16]], 0, 0)
+    iota(X("vl", 0, 128), [[16, 128]], V, 0)
+    iota(X("nbw", 0, 4096), [[0, 4096]], 0, 0, True)
+    iota(X("inv", 0, V), [[0, V]], V + 64, 0)
+    iota(X("id64", 0, V), [[1, V]], 64, 0)
+    for c in range(16):
+        dma("Y", "wr", T.wr[c:128:16, :], [("wr", 16 * k + c, 16 * k + c + 1, 0, 4096) for k in range(8)], T.w[:, :],
+            [("tg", 0, 128, 0, 512)])
+    for k in range(8):
+        dma("Y", "nbw", T.nbw[16 * k:16 * k + 1, :], [("nbw", 16 * k, 16 * k + 1, 0, 4096)], T.nb[16 * k:16 * k + 16, :], [])
+
+    for x in range(4):
+        ts(X("src", x * 128, x * 128 + 128), X("aw", 0, 128), float(-4 * x), OP.is_equal)
+    act(X("i128", 0, 64), X("ib", 0, 64), AF.Identity, 0.0, 128.0)
+    tt(X("lst", 0, 64), X("i128", 0, 64), X("ib", 64, 128), OP.add)
+    for K in range(2):
+        ts(col(80 + K), col(CK + K), 128.0, OP.mult, col(CK + 2 + K), OP.add)
+        ts(X("sel4", 8 * K, 8 * K + 8), X("g8", 0, 8), col(80 + K), OP.mult)
+    tt(col(63), col(MC), col(MC + 1), OP.add)
+    ts(X("sel1", 0, 8), X("g8", 0, 8), col(63), OP.mult)
+    cp(WT, X("wtb", 0, 1))
+    ts(NQ, QB, 0.0, OP.is_equal)
+    ts(col(64), GM, 2.0, OP.mult, col(3), OP.add)
+    ts(X("iff", 0, 128), X("ir", 0, 128), col(0), OP.is_equal)
+    ts(X("samg", 0, 128), X("rgam", 0, 128), col(64), OP.is_equal)
+    ts(X("col", 84, 88), X("col", CK, CK + 4), WT, OP.mult, NQ, OP.mult)
+    ts(X("col", 88, 92), X("col", CK, CK + 4), WT, OP.mult, QB, OP.mult)
+    for j in range(8):
+        act(X("pack", j * 128, j * 128 + 128), X("samg", 0, 128), AF.Identity, 0.0, col(84 + j))
+    tt(X("rh", 0, 256), X("pb", 256, 512), X("ownt", 0, 256), OP.is_gt)
+    for K in range(2):
+        mm(X("pd", K * 128, K * 128 + 128), X("rh", K * 128, K * 128 + 128), X("ib", 0, 128))
+    for K, n in ((0, "h4"), (1, "l4")):
+        act(X(n, 0, 128), X("hlf", K * 128, K * 128 + 128), AF.Identity, -float(Z))
+        act(X(n, 128, 256), X("pd", K * 128, K * 128 + 128), AF.Identity, -1.0)
+
+    for q in [r] + others:
+        mm(X("pc", q * 128, q * 128 + 128), X3("tg", q, q + 1, 0, 128), X("ib", 0, 128), tag="sq")
+    cp(X("sq", 0, 512), X("pc", 0, 512))
+    for q in range(4):
+        for x in range(4):
+            mm(X("psw", q * 512 + x, q * 512 + 512, 4), X("src", x * 128, x * 128 + 128), X("sq", q * 128, q * 128 + 128), tag="src")
+    for K in range(2):
+        for q in range(4):
+            mm(X("pa", K * 128, K * 128 + 128, 1, 32 * q, 32 * q + 32), X("lst", 32 * K, 32 * K + 32), X("sq", q * 128, q * 128 + 128), tag="lst")
+    cp(X("nb16", 0, 256), X("nbi", 0, 256))
+    ts(X("blk", 0, 128), X("rg", 0, 128), col(2), OP.is_equal)
+    ts(X("tri", 0, 128), X("ir", 0, 128), col(0), OP.is_gt)
+    tt(X("lt", 0, 128), X("tri", 0, 128), X("blk", 0, 128), OP.mult)
+    ts(X("sel1f", 0, 8), X("g8", 0, 8), col(MC), OP.mult)
+    ts(X("bwi", 0, 24), X("bli", 0, 24), 4, OP.logical_shift_right)
+    ts(X("bwi", 24, 48), X("bli", 0, 24), 15, OP.bitwise_and)
+    ts(X("bwi", 24, 48), X("bwi", 24, 48), 256.0, OP.mult)
+    tt(X("bwi", 0, 24), X("bwi", 0, 24), X("bwi", 24, 48), OP.add)
+    cp(X("bw16", 0, 24), X("bwi", 0, 24))
+    for h in range(2):
+        for x in range(4):
+            o, i = X("wm", x * 2048 + h * 1024, x * 2048 + h * 1024 + 1024), X("psw", h * 1024, h * 1024 + 1024)
+            if h == 0:
+                ts(o, i, col(CX + x), OP.mult)
+            else:
+                act(o, i, AF.Identity, 0.0, col(CX + x))
+    cp(X("pl16", 0, 256), X("pa", 0, 256))
+
+    def places(a, b):
+        act(X("mq", a, b), X("stf", a, b), AF.Exp, 0.0, -2 * LN2)
+
+    for K in range(2):
+        share("gb", K * V, "wm", 8192, "pl16", K * 128, SHARE["names"][K])
+        if K == 0:
+            cp(X("li", 0, 256), X("pa", 0, 256))
+            for k in range(2):
+                ts(X("sti", k * 128, k * 128 + 128), X3("tg", 0, 4, k * 32, k * 32 + 32), 0.125, OP.mult, -0.4375, OP.add)
+            cp(X("stf", 0, 256), X("sti", 0, 256))
+            pick("pb", 0, "gb", 0, "sel4", 0, 16, "names")
+    places(0, 256)
+    act(X("vl", 0, 128), X("vl", 0, 128), AF.Identity, col(1))
+    act(X("vz", 0, 128), X("vl", 0, 128), AF.Identity, -float(V + Z))
+    tt(X("zt", 0, 128), X("pb", 0, 128), X("ownp", 0, 128), OP.is_equal)
+
+    def pack_z(parts, before, between):
+        for i, p in enumerate(parts):
+            mm(X("pa", 0, 128), p, X("ib", 0, 128), i == 0, i == len(parts) - 1, tag="zl")
+        before()
+        cp(X("zl", 0, 128), X("pa", 0, 128))
+        for h in range(2):
+            for x in range(4):
+                j = h * 4 + x
+                mm(X("psw", h * 512 + x, h * 512 + 512, 4), X("pack", j * 128, j * 128 + 128), X("zl", 0, 128), tag="pack")
+        between()
+        cp(X("ww", 0, 512), X("psw", 0, 512))
+        act(X("ww", 512, 1024), X("psw", 512, 1024))
+
+    def lists():
+        tt(X("np", 0, 128), X("pb", 128, 256), X("ownp", 0, 128), OP.not_equal)
+        ts(X("li", 0, 256), X("li", 0, 256), 1023, OP.bitwise_and)
+        cp(X("idx", 0, 256), X("li", 0, 256))
+
+    pack_z([X("zt", 0, 128)], lambda: cp(X("pif", 0, 128), X("pb", 0, 128)), lists)
+    pick("pd", 0, "gb", V, "sel4", 0, 16, "names")
+    cp(X("mcode", 0, 128), X("zt", 0, 128))
+
+    def ask(L, n):
+        share("gb", L * V, "ww", 1024, "idx", L * 128, n)
+
+    def answer(L):
+        bank, c0 = ("pc", "pd")[L // 2], (L % 2) * 128
+        if L == 3:
+            mm(X(bank, c0, c0 + 128), X("kc", 0, 128), X("one", 0, 128), True, False, tag="zz")
+        for b in range(16):
+            mm(X(bank, c0 + b, c0 + 128, 16), X("gb", L * V + b, L * V + V, 16), X("sel1", 0, 8), L != 3, L != 3 or b == 15, tag="zz")
+
+    def bits(H):
+        a, bank = H * 256, ("pc", "pd")[H]
+        tt(X("yi", a, a + 256), X(bank, 0, 256), X("mq", a, a + 256), OP.mult)
+        ts(X("zi", a, a + 256), X("yi", a, a + 256), 1, OP.bitwise_and)
+
+    def border_lists(d):
+        for b in range(16):
+            mm(X("pa", d * 128 + b, d * 128 + 128, 16, 0, 24), X("bq", d * 384 + b, d * 384 + 384, 16), X("sel1f", 0, 8), tag="bq")
+
+    ARH, ARL = X("ar", 0, 128), X("ar", 128, 256)
+    for t in range(2):
+        n = SHARE["r%d" % t]
+        if t == 1:
+            border_lists(0)
+        ask(0, n[0])
+        if t == 0:
+            cp(X("pif", 128, 256), X("pd", 0, 128))
+            for K in range(2):
+                mm(X("pb", K * 128, K * 128 + 128), X("pif", K * 128, K * 128 + 128), X("iff", 0, 128))
+            tt(X("np", 128, 256), X("pd", 128, 256), X("ownp", 0, 128), OP.not_equal)
+            tt(X("mlh", 0, 128), X("pd", 0, 128), X("ownp", 0, 128), OP.is_equal)
+        answer(0)
+        ask(1, n[1])
+        if t == 0:
+            cp(X("lj", 0, 256), X("pb", 0, 256))
+            ts(X("lj", 0, 256), X("lj", 0, 256), 1023, OP.bitwise_and)
+            cp(X("idx", 256, 512), X("lj", 0, 256))
+            act(X("np9", 0, 256), X("np", 0, 256), AF.Identity, 0.0, 9.0)
+            act(X("ml10", 0, 128), X("mlh", 0, 128), AF.Identity, 0.0, 10.0)
+            ts(X("sti", 256, 512), X("pif", 0, 256), 1.0 / 1024, OP.mult, -0.5 + 1.0 / 2048, OP.add)
+        answer(1)
+        if t == 0:
+            tt(X("stf", 256, 512), X("sti", 256, 512), X("np9", 0, 256), OP.max)
+            tt(X("stf", 384, 512), X("stf", 384, 512), X("ml10", 0, 128), OP.max)
+        ask(2, n[2])
+        answer(2)
+        if t == 0:
+            places(256, 512)
+        ask(3, n[3])
+        answer(3)
+        bits(0)
+        tt(X("tq", 0, 128), X("zi", 0, 128), X("zt", 0, 128), OP.is_le)
+        tt(X("thr", 0, 128), X("zi", 0, 128), X("zt", 0, 128), OP.max)
+        tt(X("thr", 128, 256), X("zi", 128, 256), X("tq", 0, 128), OP.max)
+        cp(X("bq", 384 * t, 384 * t + 384), IX("nbw", 4096, "bw16", 0, 24, 128 * t))
+        bits(1)
+        tt(X("ar", 0, 256), X("zi", 256, 512), X("thr", 0, 256), OP.is_gt)
+        if t == 0:
+            def more():
+                tt(X("zt", 0, 128), X("zt", 0, 128), ARH, OP.add)
+                tt(X("zt", 0, 128), X("zt", 0, 128), ARL, OP.add)
+            pack_z([X("zt", 0, 128), ARH, ARL], lambda: None, more)
+        tt(X("mcode", 0, 128), X("mcode", 0, 128), ARH, OP.add)
+        tt(X("mcode", 0, 128), X("mcode", 0, 128), ARL, OP.subtract)
+    border_lists(1)
+    act(X("bqt", 0, 256, 1, 0, 24), X("pa", 0, 256, 1, 0, 24), AF.Silu, 64.0)
+    send("code", lambda d: X("mcode", 32 * d, 32 * d + 32), X("tc", 32 * r, 32 * r + 32))
+    cp(X("tc", 32 * r, 32 * r + 32), X("mcode", 32 * r, 32 * r + 32))
+    recv("code", [("tc", 0, 128, 32 * q, 32 * q + 32) for q in others])
+
+    tt(X("beta", 0, 256), X("h4", 0, 256), X("l4", 0, 256), OP.add)
+    ts(X("beta", 0, 256), X("beta", 0, 256), 0.5, OP.mult)
+    tt(X("alph", 0, 256), X("h4", 0, 256), X("beta", 0, 256), OP.subtract)
+    for d in range(2):
+        act(X("gb", V + 384 * d, V + 384 * d + 384), IX("wr", V + V * d, "bl16", 0, 24, V * d))
+    for d in range(2):
+        mm(X("pc", 256 + 24 * d, 280 + 24 * d), X("bqt", d * 128, d * 128 + 128, 1, 0, 24), X("iff", 0, 24, 1, 0, 24))
+
+    mm(X("pc", 0, 128), X("tc", 0, 128), X("ib", 0, 128))
+
+    def quad(a):
+        tt(X("t1", a, a + 128), X("beta", a, a + 128), X("pc", 0, 128), OP.mult)
+        tt(X("t1", a, a + 128), X("t1", a, a + 128), X("alph", a, a + 128), OP.add)
+        tt(X("t1", a, a + 128), X("t1", a, a + 128), X("pc", 0, 128), OP.mult)
+
+    for j in range(4):
+        mm(X("psw", 512 * j, 512 * j + 512), X("ib", 0, 128), X("wr", V + 512 * j, V + 512 * j + 512))
+    quad(0)
+    ts(X("mate", 0, 128), X("t1", 0, 128), float(Z), OP.add)
+    nx = SHARE["x"]
+    tt(X("xf", 0, nx), IX("xw", Z + 16, "mate", 0, nx // 16), X("xc", 0, nx), OP.add)
+    for i, (bank, a, b) in enumerate((("pa", nx, nx + 512), ("pb", nx + 512, V))):
+        act(X("gb", a - nx, b - nx), IX("xw", Z + 16, "mate", a // 16, b // 16))
+        mm(X(bank, 0, b - a), X("ib", 0, 128), X("xc", a, b), True, False, tag="gx")
+        mm(X(bank, 0, b - a), X("ib", 0, 128), X("gb", a - nx, b - nx), False, True, tag="gx")
+    for bank, a, b in (("pa", nx, nx + 512), ("pb", nx + 512, V)):
+        act(X("xf", a, b), X(bank, 0, b - a))
+    mm(X("pb", 0, 384), X("ib", 0, 128), X("gb", V + 384, V + 768))
+    cp(X("xb", 0, 192), IX("xf", V, "bl16", 0, 12))
+    act(X("xb", 192, 384), IX("xf", V, "bl16", 12, 24))
+    send("xs", lambda d: X("xb", C * d, C * d + C), X("xf", mine, mine + C))
+    act(X("xf", mine, mine + C), X("xb", C * r, C * r + C))
+    recv("xs", ghosts("xf"))
+
+    quad(128)
+    ts(X("rep", 0, 128), X("t1", 128, 256), 1.0, OP.add)
+    mm(X("pd", 0, 128), X("rep", 0, 128), X("ib", 0, 128))
+    ts(X("nbl", 0, 48), X("pc", 256, 304), 64.0, OP.subtract)
+    cp(X("nbb16", 0, 48), X("nbl", 0, 48))
+    tt(X("ms", 0, 128), X("vz", 0, 128), X("t1", 0, 128), OP.subtract)
+    tt(X("ms", 0, 128), X("ms", 0, 128), X("rep", 0, 128), OP.mult)
+    tt(X("ms", 0, 128), X("ms", 0, 128), X("t1", 0, 128), OP.add)
+    ts(X("ms16", 0, 128), X("ms", 0, 128), float(Z), OP.add)
+    act(X("rt", 0, 128), X("pd", 0, 128))
+    mm(X("pd", 128, 256), X("rt", 0, 128), X("tri", 0, 128))
+    act(X("up", 0, 128), X("pd", 128, 256))
+    mm(X("pd", 0, 128), X("blk", 0, 128), X("up", 0, 128), True, False, tag="num")
+    mm(X("pd", 0, 128), X("lt", 0, 128), X("rep", 0, 128), False, True, tag="num")
+    act(X("num", 0, 128), X("pd", 0, 128))
+    act(X("cn", 0, 128), X("pd", 0, 128), AF.Identity, float(V * r))
+    tt(X("off", 0, 128), X("num", 0, 128), X("vl", 0, 128), OP.subtract)
+    tt(X("off", 0, 128), X("off", 0, 128), X("rep", 0, 128), OP.mult)
+    tt(X("off", 0, 128), X("off", 0, 128), X("vl", 0, 128), OP.add)
+    cp(X("off16", 0, 128), X("off", 0, 128))
+
+    def SP(c):
+        return X("sp", c, V, 16)[0], [("sp%d" % c, 0, 128, 0, 128)]
+
+    def numbers(offs, c, d, b):
+        ap, regs = IX("sp", b, offs, c, d)
+        return ap, regs + [y for k in range(16) for y in SP(k)[1]]
+
+    for c in range(16):
+        if c < 4:
+            ts(SP(c), X("cn", 0, 128), col(MC + c), OP.mult)
+        else:
+            act(SP(c), X("cn", 0, 128), AF.Identity, 0.0, col(MC + c))
+    act(X("sb", 0, 384), numbers("bl16", 0, 24, V))
+    send("num", lambda d: X("sb", C * d, C * d + C), X("sp", mine, mine + C))
+    act(X("sp", mine, mine + C), X("sb", C * r, C * r + C))
+    recv("num", ghosts("sp"))
+
+    def invert(j):
+        o = IX("inv", 4096, "off16", 32 * j, 32 * j + 32)
+        i = X("id64", 512 * j, 512 * j + 512)
+        add("S", lambda e: e.activation(out=o[0], in_=i[0], func=AF.Silu), [("inv", 0, 128, 0, 4096)],
+            rg(i) + [("off16", 0, 128, 32 * j, 32 * j + 32)])
+
+    def times_w0(a, b):
+        tt(X("p0", a, b), IX("xf", Z, "nb16", a // 16, b // 16), X("wr", a, b), OP.mult)
+
+    act(X("gA", 0, 384), IX("xf", Z, "nbb16", 24, 48))
+    tt(X("pB", 0, 384), IX("xf", Z, "nbb16", 0, 24), X("gb", V, V + 384), OP.mult)
+    times_w0(0, 512)
+    tt(X("pb", 0, 384), X("gA", 0, 384), X("pb", 0, 384), OP.mult)
+    tt(X("sst", 0, 384), X("pB", 0, 384), X("pb", 0, 384), OP.add)
+    send("s", lambda d: X("sst", C * d, C * d + C), X("sw", mine, mine + C))
+    recv("s", ghosts("sw"))
+
+    for j in range(4):
+        a, b = 512 * j, 512 * j + 512
+        act(X("g1", a, b), IX("xf", Z, "nb16", 128 + 32 * j, 160 + 32 * j))
+        if j > 0:
+            invert(j - 1)
+    invert(3)
+    act(X("sw", mine, mine + C), X("sst", C * r, C * r + C))
+    for j in range(4):
+        a, b = 512 * j, 512 * j + 512
+        if j > 0:
+            times_w0(a, b)
+        tt(X("psw", a, b), X("g1", a, b), X("psw", a, b), OP.mult)
+        tt(X("sw", a, b), X("p0", a, b), X("psw", a, b), OP.add)
+        keep(X("p0", a, b), X("sw", a, b))
+    pick("pa", 0, "inv", 0, "sel1f", 0, 8, "inv")
+    act(X("g1", 0, V), numbers("ms16", 0, 128, Z))
+    act(X("ivt", 0, 128), X("pa", 0, 128))
+    mm(X("pb", 0, 128), X("ivt", 0, 128), X("iff", 0, 128))
+    for j in range(2):
+        a, b = 1024 * j, 1024 * j + 1024
+        tt(X("tw", a, b), IX("sw", Z + 16, "mate", 64 * j, 64 * j + 64), X("p0", a, b), OP.add)
+    ts(X("ivi", 0, 128), X("pb", 0, 128), 64.0, OP.subtract)
+    cp(X("iv16", 0, 128), X("ivi", 0, 128))
+    for j in range(4):
+        o, i = X("p0", 512 * j, 512 * j + 512), IX("tw", V + 16, "iv16", 32 * j, 32 * j + 32)
+        if j % 2 == 0:
+            cp(o, i)
+        else:
+            act(o, i)
+        dma("Y", "y%d" % j, T.y[:, 512 * j:512 * j + 512], [], o[0], o[1])
+    pick("pc", 0, "g1", 0, "g8", 0, 8, "cm")
+    act(X("cmt", 0, 128), X("pc", 0, 128))
+    mm(X("pd", 0, 128), X("cmt", 0, 128), X("iff", 0, 128))
+    act(X("cmv", 0, 128), X("pd", 0, 128))
+    dma("Y", "cm", T.cm[:, :], [], T.cmv[:, :], rg(X("cmv", 0, 128)))
+    for s, v in total.items():
+        if known["G"].get(s, 0) < v:
+            g.wait_ge(T.sem[s], v)

@@ -1,34 +1,36 @@
-import math
 from concourse.bass import DstId, RemoteDMATransfer
 from concourse.mybir import AluOpType, ActivationFunctionType
 
 OP = AluOpType
 AF = ActivationFunctionType
 V, C, Z = 2048, 96, 2432
-F32, BF, I32, U16 = "float32", "bfloat16", "int32", "uint16"
+BIG, MID = 16384.0, 1216.0
+OFFG, OFFC = 128 * 517, 128 * 129
+F32, BF, F16, I32, U16 = "float32", "bfloat16", "float16", "int32", "uint16"
 WIDTHS = {
-    F32: dict(nbf=256, col=128, jr=8, jb=8, ir=128, rg=128, rgam=128, aw=128, ownt=256, ownp=128, iff=128, g8=8, sel1f=8, vl=128,
-              vz=128, w0s=128, dn=128, bd=128, hlf=256, h4=256, l4=256, beta=256, alph=256, stf=512, pif=256, t1=256, xf=2432,
-              num=128, cn=128, off=128, ms=128, sp=2432, sb=384, g1=2048, p0=2048, sw=2448, sst=384, id64=2048, inv=4096,
-              ivt=128, cmt=128, cmv=128, tw=2064, xb=384, gA=384, pB=384, bq=768, bqt=256),
-    BF: dict(wsb=4096, xw=2448, ia=256, ic=256, nwa=256, nwb=256, ib=128, i128=64, blk=128, lt=128, tri=128, samg=128, pack=1024,
-             src=512, lst=64, selg=24, sel4=16, sel1=8, nw=2432, bst=384, xst=384, xc=2048, wtb=2, bt=128, gb=8192, rh=256,
-             wr=4096, sq=512, wm=8192, mq=512, zt=128, zl=128, np=256, np9=256, mlh=128, ml10=128, ww=1024, ar=256,
-             mcode=128, tc=128, rep=128, rt=128, up=128, kc=128, one=128, thr=256, tq=128),
-    I32: dict(bli=24, nbi=256, coli=16, li=256, sti=512, lj=256, yi=512, zi=512, ivi=128, bwi=48, nbw=4096, nbl=48),
-    U16: dict(bl16=24, hl16=256, pl16=256, idx=512, mate=128, ms16=128, off16=128, iv16=128, nb16=256, bw16=24, nbb16=48),
+    F32: dict(nbf=256, dn=128, bd=128, hlf=256, col=128, ir=128, dif=128, iff=128, own=256, nth=128, tq=128, dm=256, xf=2432,
+              cn=128, vl=32, off=32, sp=2448, sb=384, g1=2048, p0=2048, sw=2448, sst=384, ivt=128, cmt=128, cmv=128, tw=2056,
+              xb=384, g8=8),
+    BF: dict(wsb=2048, xw=2448, xc=2048, nw=2432, bst=384, hb=2048, hl=2432, hst=384, xst=384, gb=8192, wr=2048, ti=256, nti=256,
+             ibn=128, pm=8, sel=48, selw=8, seli=32, wt=128, e0=272, e1=256, ar=272, ar3=256, m2=256, less=256, nr2=256, nr3=256,
+             ww=1024, wv=1024, one=144, ru=256, mk=512, blk=128, lt=128, ltq=128, b0=144, lt0=144, q0=144, wq=576, km=512,
+             rb=512, inv=2688, selr=128, bt=128, irb=128),
+    F16: dict(hz=256, pz2=256, pz3=256, ih=128),
+    I32: dict(bli=24, nbi=256, ci=64, cj=64, yi=256, zi=256, zj=256),
+    U16: dict(bl16=24, hl16=256, idx=512, mate=128, off16=32, iv16=128, nb16=256),
 }
 PSUM = {"psw": 2048, "pa": 512, "pb": 512, "pc": 512, "pd": 512}
-SCRATCH = {"snd": ("sbuf", [128, 4, 128], BF), "tg": ("sbuf", [128, 4, 128], BF)}
+SCRATCH = {"fld": ("sbuf", [128, 4, 256], F32)}
 for _d in WIDTHS:
     for _n in WIDTHS[_d]:
         SCRATCH[_n] = ("sbuf", [128, WIDTHS[_d][_n]], _d)
 for _n in PSUM:
     SCRATCH[_n] = ("psum", [128, PSUM[_n]], F32)
-EXCH = ["name", "x", "gid", "code", "xs", "num", "s"]
-LOADS = ["bl", "nb", "w", "x", "xc", "nbw", "wr", "y0", "y1", "y2", "y3", "cm"]
+EXCH = ["name", "hl", "w1", "w2", "x", "xs", "num", "s"]
+LOADS = ["bl", "nb", "w", "x", "xc", "wr", "y0", "y1", "y2", "y3", "cm"]
 SEMAPHORES = ["cV", "cS", "cP", "cG"] + ["d_" + k for k in LOADS] + ["a_" + k for k in EXCH] + ["l_" + k for k in EXCH]
-SHARE = {"gid": (1024, 1024), "names": (1024, 512), "r0": (1024, 768, 896, 640), "r1": (1024, 1024, 896, 832), "x": 1408}
+SHARE = {"nh": 1024, "nl": 512, "r2": (1024, 1024, 768, 512), "r3": (768, 768), "x": 1408}
+STEPS = (128, 256, 512, 576, 576)
 
 
 def engine_plan(topo, src, cores):
@@ -99,15 +101,15 @@ def rank_program(g, core, T, topo):
         ap = T[name][p0:p1, c0:c1] if step == 1 else T[name][p0:p1, c0:c1:step]
         return ap, [(name, p0, p1, c0, c1)]
 
-    def X3(name, i0, i1, j0, j1):
-        ap = T[name][:, i0:i1, j0:j1] if i1 - i0 > 1 else T[name][:, i0, j0:j1]
-        return ap, [(name, 0, 128, i0 * 128 + j0, (i1 - 1) * 128 + j1)]
+    def F(i0, i1, j0, j1):
+        ap = T.fld[:, i0:i1, j0:j1] if i1 - i0 > 1 else T.fld[:, i0, j0:j1]
+        return ap, [("fld", 0, 128, i * 256 + j0, i * 256 + j1) for i in range(i0, i1)]
 
     def IX(win, b, offs, c, d, a=0):
         return T[win][:, a:b].indirect(T[offs][:, c:d]), [(win, 0, 128, a, b), (offs, 0, 128, c, d)]
 
-    def col(j, p1=128):
-        return X("col", j, j + 1, 1, 0, p1)
+    def col(j, n=1):
+        return X("col", j, j + n)
 
     def sc(s):
         return s[0] if isinstance(s, tuple) else s
@@ -128,11 +130,11 @@ def rank_program(g, core, T, topo):
     def cp(out, a, tag=None):
         add("V", lambda e: e.tensor_copy(out=out[0], in_=a[0]), rg(out), rg(a), tag=tag)
 
-    def act(out, a, func=AF.Identity, bias=0.0, scale=1.0, tag=None):
+    def act(out, a, bias=0.0, scale=1.0, tag=None):
         if isinstance(bias, float) and isinstance(scale, float) and bias == 0.0 and scale == 1.0:
-            f = lambda e: e.activation(out=out[0], in_=a[0], func=func)
+            f = lambda e: e.activation(out=out[0], in_=a[0], func=AF.Identity)
         else:
-            f = lambda e: e.activation(out=out[0], in_=a[0], func=func, bias=sc(bias), scale=sc(scale))
+            f = lambda e: e.activation(out=out[0], in_=a[0], func=AF.Identity, bias=sc(bias), scale=sc(scale))
         add("S", f, rg(out), rg(a, bias, scale), tag=tag)
 
     def mm(out, lhsT, rhs, start=True, stop=True, tag=None):
@@ -145,8 +147,8 @@ def rank_program(g, core, T, topo):
             f = lambda e: e.iota(out[0], pattern, base, cm, allow_small_or_imprecise_dtypes=True)
         add("G", f, rg(out), [])
 
-    def keep(out, a):
-        add("G", lambda e: e.affine_select(out[0], a[0], [[1, 512]], OP.is_ge, 0.0, 0, 0), rg(out), rg(a))
+    def where(out, a, pattern, base, cm, op=OP.is_ge, fill=0.0):
+        add("G", lambda e: e.affine_select(out[0], a[0], pattern, op, fill, base, cm), rg(out), rg(a))
 
     def dma(q, key, out_ap, outs, in_ap, ins):
         add(q, lambda e: e.dma_start(out=out_ap, in_=in_ap), outs, ins, sem="d_" + key, inc=16)
@@ -170,8 +172,16 @@ def rank_program(g, core, T, topo):
         total["a_" + key] = n
         note({"q": "R", "tag": None, "sem": "a_" + key, "val": n, "know": {"a_" + key: n}}, regs, [])
 
-    def ghosts(name):
-        return [(name, 0, 128, V + C * q, V + C * q + C) for q in others]
+    mine = V + C * r
+
+    def show(key, stage, win):
+        send(key, lambda d: X(stage, C * d, C * d + C), X(win, mine, mine + C))
+        recv(key, [(win, 0, 128, V + C * q, V + C * q + C) for q in others])
+
+    def spread(key, win):
+        own = X(win, 256 * r, 256 * r + 256)
+        send(key, lambda d: own, own)
+        recv(key, [(win, 0, 128, 256 * q, 256 * q + 256) for q in others])
 
     def pick(bank, c0, src, s0, sel, w0, w1, tag):
         n = 16 * (w1 - w0)
@@ -182,332 +192,313 @@ def rank_program(g, core, T, topo):
         cp(X(dst, a, a + n), IX(win, w, offs, o, o + n // 16))
         act(X(dst, a + n, a + V), IX(win, w, offs, o + n // 16, o + 128))
 
-    mine, LN2 = V + C * r, math.log(2.0)
-    R4, KK, QB, QH, GM, WT, NQ, CV = (col(j) for j in (4, 5, 6, 7, 8, 9, 10, 11))
-    MC, CX, CK, CJ = 16, 32, 36, 48
+    IB, TI, IH, IF = X("ti", 0, 128), X("ti", 0, 256), X("ih", 0, 128), X("iff", 0, 128)
+    M8, TX, PW, DC = 0, 8, 12, 16
+    K0, S8, SA, BA, SIDEB, WG, WC, W64, WI, QW = (col(j) for j in range(20, 30))
+    SIDEA, B4, QM = col(56), col(57), 58
+
+    def MC(x):
+        return col(32 + (x - 8) % 16)
+
     dma("Y", "bl", T.bli[:, :], rg(X("bli", 0, 24)), T.bl[:, :], [])
     dma("S", "nb", T.nbi[:, :], rg(X("nbi", 0, 256)), T.nb[:, :], [])
-    dma("Y", "w", T.wsb[0:8, :], rg(X("wsb", 0, 4096, 1, 0, 8)), T.w[:, :], [])
-    dma("S", "x", T.xw[:, 0:V], rg(X("xw", 0, V)), T.x[:, :], [])
-    dma("Y", "xc", T.xc[:, :], rg(X("xc", 0, V)), T.x[:, :], [])
-
-    iota(X("coli", 0, 1), [[0, 1]], 0, 1, True)
-    iota(X("ir", 0, 128), [[1, 128]], 0, 0)
-    iota(X("jr", 0, 8), [[1, 4], [0, 2]], 4 * r, 0)
-    iota(X("jb", 0, 8), [[0, 4], [1, 2]], 0, 0)
-    iota(X("ia", 0, 256), [[0, 64], [1, 4]], 0, 0)
-    iota(X("ic", 0, 256), [[1, 64], [0, 4]], 0, 0)
-    iota(X("rg", 0, 128), [[1, 8], [0, 16]], 0, 0)
-    for q in range(4):
-        iota(X("rgam", 32 * q, 32 * q + 32), [[2, 2], [0, 8], [1, 2]], 0, 0)
-    for q in range(4):
-        iota(X("aw", 32 * q, 32 * q + 32), [[16, 2], [32, 4], [1, 4]], 0, -1)
-    ts(X("coli", 1, 2), X("coli", 0, 1), 15, OP.bitwise_and)
-    ts(X("coli", 2, 3), X("coli", 0, 1), 4, OP.logical_shift_right)
-    cp(X("col", 0, 3), X("coli", 0, 3))
-    ts(X("col", MC, MC + 16), X("ir", 0, 16), col(1), OP.is_equal)
-    ts(X("ib", 0, 128), X("ir", 0, 128), col(0), OP.is_equal)
-    ts(X("jr", 0, 8), X("jr", 0, 8), col(MC + 2), OP.mult)
-    ts(X("jb", 0, 8), X("jb", 0, 8), col(MC + 3), OP.mult)
-    tt(X("col", CJ, CJ + 8), X("jr", 0, 8), X("jb", 0, 8), OP.add)
-    ts(X("nwa", 0, 256), X("ia", 0, 256), col(MC), OP.mult)
-    ts(X("g8", 0, 8), X("ir", 0, 8), col(2), OP.is_equal)
-    cp(X("bl16", 0, 24), X("bli", 0, 24))
-    ts(X("nwb", 0, 256), X("ic", 0, 256), col(MC + 1), OP.mult)
-    tt(X("nwb", 0, 256), X("nwa", 0, 256), X("nwb", 0, 256), OP.add)
-    for j in range(8):
-        o = X("nw", 256 * j, 256 * j + 256)
-        if j % 3 == 1:
-            act(o, X("nwb", 0, 256), AF.Identity, col(CJ + j))
-        else:
-            ts(o, X("nwb", 0, 256), col(CJ + j), OP.add)
-    cp(X("bst", 0, 384), IX("nw", V, "bl16", 0, 24))
-    send("name", lambda d: X("bst", C * d, C * d + C), X("nw", mine, mine + C))
-    act(X("nw", mine, mine + C), IX("nw", V, "bl16", 6 * r, 6 * r + 6))
-
     for d in range(2):
-        for b in range(16):
-            mm(X(("pa", "pc")[d], b, 128, 16), X("wsb", d * V + b, d * V + V, 16, 0, 8), X("ib", 0, 8, 1, 0, 8), tag="wt")
-    act(X("w0s", 0, 128), X("pa", 0, 128))
-    act(X("xst", 0, 384), IX("xw", V, "bl16", 0, 24))
-    send("x", lambda d: X("xst", C * d, C * d + C), X("xw", mine, mine + C))
-    act(X("xw", mine, mine + C), IX("xw", V, "bl16", 6 * r, 6 * r + 6))
-    recv("name", ghosts("nw"))
-    recv("x", ghosts("xw"))
-    cp(X("nbf", 0, 256), X("nbi", 0, 256))
-    tt(X("dn", 0, 128), X("nbf", 128, 256), X("nbf", 0, 128), OP.subtract)
-    tt(X("bt", 0, 128), X("pc", 0, 128), X("w0s", 0, 128), OP.is_gt)
-    mm(X("pb", 0, 128), X("bt", 0, 128), X("ib", 0, 128))
-    ts(col(60), col(MC), 16.0, OP.mult, col(MC + 2), OP.add)
-    ts(col(61), col(MC + 3), 64.0, OP.mult, col(MC + 1), OP.add)
-    tt(X("bd", 0, 128), X("pb", 0, 128), X("dn", 0, 128), OP.mult)
-    tt(X("hlf", 0, 128), X("nbf", 0, 128), X("bd", 0, 128), OP.add)
-    cp(X("hl16", 0, 128), X("hlf", 0, 128))
-    tt(X("hlf", 128, 256), X("nbf", 128, 256), X("bd", 0, 128), OP.subtract)
-    cp(X("hl16", 128, 256), X("hlf", 128, 256))
-    for f in range(2):
-        ts(X("selg", 8 * f, 8 * f + 8), X("g8", 0, 8), col(60 + f), OP.mult)
-    ts(col(62), col(MC + 1), 4.0, OP.mult, col(MC), OP.add)
-    ts(col(62), col(MC + 2), 512.0, OP.mult, col(62), OP.add)
-    ts(col(62), col(MC + 3), 256.0, OP.mult, col(62), OP.add)
-    ts(X("selg", 16, 24), X("g8", 0, 8), col(62), OP.mult)
-    ts(X("coli", 3, 4), X("coli", 0, 1), 1, OP.logical_shift_right, 1, OP.bitwise_and)
-    ts(X("coli", 4, 5), X("coli", 0, 1), 3, OP.bitwise_and)
-    ts(X("coli", 5, 6), X("coli", 0, 1), 2, OP.logical_shift_right, 3, OP.bitwise_and)
-    ts(X("coli", 6, 7), X("coli", 0, 1), 5, OP.logical_shift_right, 1, OP.bitwise_and)
-    ts(X("coli", 7, 8), X("coli", 0, 1), 6, OP.logical_shift_right)
-    ts(X("coli", 8, 9), X("coli", 0, 1), 4, OP.logical_shift_right, 1, OP.bitwise_and)
-    cp(X("col", 3, 9), X("coli", 3, 9))
-    ts(CV, R4, 2.0, OP.mult, QH, OP.add)
-    ts(X("col", CX, CX + 4), X("ir", 0, 4), R4, OP.is_equal)
-    ts(X("col", CK, CK + 4), X("ir", 0, 4), KK, OP.is_equal)
+        dma("Y", "w", T.wsb[8 * d:8 * d + 8, :], rg(X("wsb", 0, V, 1, 8 * d, 8 * d + 8)), T.w[:, V * d:V * d + V], [])
 
+    iota(X("ci", 0, 24), [[-1, 24]], 32, 1, True)
+    iota(X("ir", 0, 128), [[1, 128]], 0, 0)
+    iota(X("ci", 24, 32), [[-16, 8]], 0, 1, True)
+    iota(X("dif", 0, 128), [[1, 128]], 0, -1)
+    iota(X("ci", 32, 36), [[-4, 4]], 16, 1, True)
+    for x in range(4):
+        add("V", lambda e, x=x: e.memset(T.col[:, PW + x:PW + x + 1], 64.0 ** -x), rg(col(PW + x)), [])
+    ts(X("cj", 0, 8), X("ci", 0, 8), 7, OP.bitwise_and)
+    ts(col(M8, 8), X("cj", 0, 8), 0.0, OP.is_equal)
+    cp(X("irb", 0, 128), X("ir", 0, 128))
+    ts(K0, col(M8 + 3), 2.0, OP.mult, col(M8 + 1), OP.add)
+    ts(col(PW, 4), col(PW, 4), col(M8 + 4), OP.mult)
+    ts(col(TX, 4), X("ir", 0, 4), col(M8 + 2), OP.mult)
+    ts(K0, K0, 2.0 * r, OP.mult)
+    tt(col(TX, 4), col(TX, 4), col(PW, 4), OP.add)
+    act(col(DC + 1), col(M8 + 1), col(M8 + 3))
+    act(col(DC + 2), col(M8 + 3), 0.0, 2.0)
+    act(col(DC + 3), col(M8 + 3), col(M8 + 1), 3.0)
+    act(S8, col(M8 + 4), 1.0, -0.875)
+    ts(col(TX, 4), col(TX, 4), K0, OP.add)
+    cp(X("bl16", 0, 24), X("bli", 0, 24))
+    for x in range(4):
+        ts(X("nw", x, 512, 4), X("irb", 0, 128), col(M8), OP.mult, col(TX + x), OP.add, tag="nw")
+    act(X("nw", 512, 1024), X("nw", 0, 512), col(DC + 1))
+    for j in (2, 3):
+        ts(X("nw", 512 * j, 512 * j + 512), X("nw", 0, 512), S8, OP.mult, col(DC + j), OP.add)
+    cp(X("bst", 0, 192), IX("nw", V, "bl16", 0, 12))
+    act(X("bst", 192, 384), IX("nw", V, "bl16", 12, 24))
+    show("name", "bst", "nw")
+    act(X("nw", mine, mine + C), X("bst", C * r, C * r + C))
+
+    ts(IB, X("dif", 0, 128), 0.0, OP.is_equal)
+    tt(X("pm", 0, 8, 1, 0, 16), X("ti", 8, 16, 1, 0, 16), X("ti", 0, 8, 1, 0, 16), OP.subtract)
+    for b in range(16):
+        mm(X("pa", b, 128, 16), X("wsb", b, V, 16, 0, 16), X("pm", 0, 8, 1, 0, 16), tag="wt")
+    cp(X("nbf", 0, 256), X("nbi", 0, 256))
+    ts(X("bt", 0, 128), X("pa", 0, 128), 0.0, OP.is_gt)
+    mm(X("pb", 0, 128), X("bt", 0, 128), IB)
+    tt(X("dn", 0, 128), X("nbf", 128, 256), X("nbf", 0, 128), OP.subtract)
+    ts(X("cj", 8, 24), X("ci", 8, 24), 15, OP.bitwise_and)
+    tt(X("bd", 0, 128), X("pb", 0, 128), X("dn", 0, 128), OP.mult)
+    ts(X("cj", 24, 32), X("ci", 24, 32), 4, OP.arith_shift_right)
+    ts(X("cj", 32, 33), X("ci", 0, 1), 8, OP.bitwise_and)
+    tt(X("hlf", 0, 128), X("nbf", 0, 128), X("bd", 0, 128), OP.add)
+    ts(X("cj", 33, 34), X("ci", 0, 1), 12, OP.bitwise_and)
+    ts(X("cj", 34, 38), X("ci", 32, 36), 12, OP.bitwise_and)
+    cp(X("hl16", 0, 128), X("hlf", 0, 128))
+    ts(col(32, 30), X("cj", 8, 38), 0.0, OP.is_equal)
+    tt(X("hlf", 128, 256), X("nbf", 128, 256), X("bd", 0, 128), OP.subtract)
+    act(SA, MC(4), B4, 2.0 ** 21)
+    act(BA, B4, 0.0, 128.0)
+    act(SIDEB, SIDEA, 1.0, -1.0)
+    act(X("g8", 0, 8), col(48, 8))
+    cp(X("hl16", 128, 256), X("hlf", 128, 256))
+    G8 = X("g8", 0, 8)
+    ts(WG, col(M8 + 3), 512.0, OP.mult, col(M8 + 2), OP.add)
+    ts(WC, col(M8 + 1), 128.0, OP.mult, col(M8), OP.add)
+    ts(WG, col(M8), 4.0, OP.mult, WG, OP.add)
+    ts(X("sel", 16, 24), G8, WC, OP.mult, SIDEA, OP.mult)
+    ts(X("sel", 24, 32), G8, MC(4), OP.mult, 2.0 ** -20, OP.mult)
+    ts(X("sel", 32, 40), G8, WC, OP.mult, SIDEB, OP.mult)
+    ts(X("sel", 40, 48), G8, MC(12), OP.mult, 2.0, OP.mult)
+    ts(X("sel", 0, 8), G8, WG, OP.mult, SIDEA, OP.mult)
+    ts(X("sel", 8, 16), G8, WG, OP.mult, SIDEB, OP.mult)
+    iota(X("own", 0, 128), [[0, 8], [1, 16]], V * r + OFFG, 16)
+    iota(X("own", 128, 256), [[0, 8], [1, 16]], V * r, 16)
+    iota(X("one", 0, 144), [[0, 144]], 1, 0)
+    iota(X("e0", 256, 272), [[0, 16]], 0, 0)
+    iota(X("ar", 256, 272), [[0, 16]], 0, 0)
+    for n in ("b0", "lt0", "q0"):
+        iota(X(n, 0, 144), [[0, 144]], 0, 0)
+    iota(X("wq", 0, 576), [[0, 576]], 0, 0)
+
+    a = 0
+    for n in STEPS:
+        act(X("hb", a, a + n), IX("nw", Z, "hl16", a // 16, (a + n) // 16), BA, SA)
+        tt(X("hl", a, a + n), IX("nw", Z, "hl16", 128 + a // 16, 128 + (a + n) // 16), X("hb", a, a + n), OP.max)
+        a += n
+    cp(X("hst", 0, 192), IX("hl", V, "bl16", 0, 12))
+    act(X("hst", 192, 384), IX("hl", V, "bl16", 12, 24))
+    show("hl", "hst", "hl")
+    act(X("hl", mine, mine + C), X("hst", C * r, C * r + C))
+
+    pick("pa", 0, "hl", 0, "sel", 16, 48, "own")
+    pick("pb", 0, "hl", 0, "sel", 0, 16, "own")
+    ts(IF, X("dif", 0, 128), 0.0, OP.is_equal)
+    ts(IH, X("dif", 0, 128), 0.0, OP.is_equal)
+    ts(X("ti", 128, 256), X("dif", 0, 128), 0.0, OP.is_gt)
     for K in range(2):
-        share("gb", K * V, "nw", Z, "hl16", K * 128, SHARE["gid"][K])
-        pick("pa", K * 256, "gb", K * V, "selg", 0, 16, "gid")
+        mm(X("pc", K * 128, K * 128 + 128), X("hlf", K * 128, K * 128 + 128), IF)
+    act(X("wt", 0, 64), X("ti", 64, 128), 0.0, 8.0)
+    act(F(0, 1, 0, 128), X("pa", 256, 384), float(OFFC))
+    act(F(1, 2, 0, 256), X("pa", 0, 256))
+    act(F(0, 1, 128, 256), X("pa", 384, 512))
+    tt(X("wt", 64, 128), X("wt", 0, 64), X("ti", 0, 64), OP.add)
+    ts(X("wt", 0, 64), X("wt", 64, 128), 2.0, OP.mult)
     for K in range(2):
-        for f in range(2):
-            cp(X3("snd", 0, 4, 64 * f + K * 32, 64 * f + K * 32 + 32), X("pa", K * 256 + f * 128, K * 256 + f * 128 + 128), tag="snd")
-    act(X("wtb", 0, 1), CV, AF.Exp, 0.0, 2 * LN2)
-    send("gid", lambda d: X3("snd", d, d + 1, 0, 128), X3("tg", r, r + 1, 0, 128))
-    for K in range(2):
-        pick("pb", 256 + K * 128, "gb", K * V, "selg", 16, 24, "gid2")
-    cp(X3("tg", r, r + 1, 0, 128), X3("snd", r, r + 1, 0, 128))
-    recv("gid", [("tg", 0, 128, q * 128, q * 128 + 128) for q in others])
-    for K in range(2):
-        iota(X("ownt", 128 * K, 128 * K + 128), [[0, 8], [1, 16]], V * r, 16)
-    for q in range(4):
-        iota(X("ownp", 32 * q, 32 * q + 32), [[0, 2], [1, 4], [2048, 4]], 512 * q, 4)
-    iota(X("kc", 0, 128), [[0, 128]], 8192, 0)
-    iota(X("one", 0, 128), [[0, 128]], 1, 0)
+        mm(X("pd", K * 128, K * 128 + 128), F(K, K + 1, 0, 128), IF)
+    ts(W64, MC(1), 64.0, OP.mult, MC(0), OP.add)
+    tt(X("less", 0, 256), X("pb", 0, 256), X("own", 0, 256), OP.is_lt)
+    ts(W64, MC(2), 64.0 ** 2, OP.mult, W64, OP.add)
+    ts(X("hz", 0, 256), X("pc", 0, 256), MID, OP.subtract)
+    ts(W64, MC(3), 64.0 ** 3, OP.mult, W64, OP.add)
+    ts(X("idx", 0, 256), X("pd", 0, 256), float(OFFC), OP.subtract)
+    ts(X("selw", 0, 8), G8, W64, OP.mult)
+    ONE, GRP = X("one", 0, 128), [[-16, 8], [0, 16]]
+    where(X("blk", 0, 128), ONE, GRP, 0, 1)
+    where(X("blk", 0, 128), X("blk", 0, 128), [[16, 8], [0, 16]], 15, -1)
+
+    def pack(bank, parts, first=True, last=True):
+        for c in range(4):
+            for i, (name, c0, w0) in enumerate(parts):
+                mm(X(bank, c, 256, 4), X(name, c0 + 4 * c, c0 + 4 * c + 128), X("wt", w0, w0 + 64), i == 0, i == len(parts) - 1, tag="pack")
+
+    share("gb", 0, "hl", Z, "hl16", 0, SHARE["nh"])
+    pick("pc", 0, "gb", 0, "sel", 0, 32, "nh")
+    n = SHARE["nl"]
+    act(X("gb", V + n, 2 * V), IX("hl", Z, "hl16", 128 + n // 16, 256))
+    cp(X("gb", V, V + n // 2), IX("hl", Z, "hl16", 128, 128 + n // 32))
+    T1, VI = X("e0", 0, 128), X("e0", 128, 256)
+    tt(X("e0", 0, 256), X("pc", 0, 256), X("own", 0, 256), OP.is_equal)
+    pack("pd", [("e0", 0, 0), ("e0", 128, 64)])
+    cp(X("gb", V + n // 2, V + n), IX("hl", Z, "hl16", 128 + n // 32, 128 + n // 16))
+    cp(X("ww", 256 * r, 256 * r + 256), X("pd", 0, 256))
+    spread("w1", "ww")
+    pick("pa", 0, "gb", V, "sel", 0, 32, "nl")
+    act(F(2, 3, 0, 256), X("pc", 256, 512))
+    mm(X("pb", 0, 128), F(2, 3, 0, 128), IF)
+    UL, LL, LH = X("psw", 1024, 1152), X("psw", 1152, 1280), X("psw", 1280, 1408)
+    tt(X("tq", 0, 128), T1, VI, OP.is_ge)
+    tt(X("dm", 0, 256), X("pc", 256, 512), F(1, 2, 0, 256), OP.subtract)
+    act(LH, X("tq", 0, 128), 0.0, 4.0)
+    tt(X("e1", 0, 256), X("pa", 0, 256), X("own", 0, 256), OP.is_equal)
+    act(F(3, 4, 0, 256), X("pa", 256, 512))
+    mm(X("pb", 128, 256), F(3, 4, 0, 128), IF)
+    act(UL, X("e1", 0, 128), 6.0, -7.0)
+    tt(X("nth", 0, 128), X("e1", 0, 128), X("e1", 128, 256), OP.max)
+    tt(X("nth", 0, 128), X("nth", 0, 128), T1, OP.is_gt)
+    act(LL, X("nth", 0, 128), 4.0, -5.0)
+    ts(X("idx", 256, 512), X("pb", 0, 256), float(OFFC), OP.subtract)
+
+    words = [("ww", 0, 128, 0, 1024)]
+    dma("Y", "x", T.xw[:, 0:V], rg(X("xw", 0, V)), T.x[:, :], words)
+    dma("Y", "xc", T.xc[:, :], rg(X("xc", 0, V)), T.x[:, :], [])
+    for c in range(16):
+        dma("Y", "wr", T.wr[c:128:16, :], [("wr", 16 * k + c, 16 * k + c + 1, 0, V) for k in range(8)], T.w[:, 0:V], [])
+    BLK, QUAD = X("blk", 0, 128), [[-4, 32], [0, 4]]
+    where(X("lt", 0, 128), BLK, [[1, 128]], 0, -1, OP.is_gt)
+    where(X("lt", 0, 128), X("lt", 0, 128), [[1, 128]], 0, -1, OP.not_equal, -BIG)
+    where(X("ltq", 0, 128), ONE, QUAD, 0, 1)
+    where(X("ltq", 0, 128), X("ltq", 0, 128), [[1, 128]], 0, -1)
+    where(X("ltq", 0, 128), X("ltq", 0, 128), [[1, 128]], 0, -1, OP.not_equal, -8.0)
+    B0 = X("b0", 12, 140)
+    where(B0, BLK, [[0, 8], [-1, 16]], 3, 0)
+    where(X("lt0", 12, 140), B0, [[16, 8], [4, 16]], 0, -1, OP.is_gt)
+    where(X("q0", 12, 140), B0, [[-16, 8], [-4, 16]], 0, 1)
+    where(X("q0", 12, 140), X("q0", 12, 140), [[16, 8], [4, 16]], 3, -1)
+    SELR = X("selr", 0, 128, 1, 0, 16)
+    where(SELR, X("one", 0, 128, 1, 0, 16), [[-16, 8], [0, 16]], -128, 16, OP.is_equal)
+    iota(X("km", 0, 512), [[1, 128], [0, 4]], 0, 0)
+    iota(X("vl", 0, 32), [[16, 32]], V - int(BIG), 1)
     iota(X("xw", Z, Z + 16), [[0, 16]], 0, 0)
     iota(X("sw", Z, Z + 16), [[0, 16]], 0, 0)
-    iota(X("tw", V, V + 16), [[0, 16]], 0, 0)
-    iota(X("vl", 0, 128), [[16, 128]], V, 0)
-    iota(X("nbw", 0, 4096), [[0, 4096]], 0, 0, True)
-    iota(X("inv", 0, V), [[0, V]], V + 64, 0)
-    iota(X("id64", 0, V), [[1, V]], 64, 0)
-    for c in range(16):
-        dma("Y", "wr", T.wr[c:128:16, :], [("wr", 16 * k + c, 16 * k + c + 1, 0, 4096) for k in range(8)], T.w[:, :],
-            [("tg", 0, 128, 0, 512)])
-    for k in range(8):
-        dma("Y", "nbw", T.nbw[16 * k:16 * k + 1, :], [("nbw", 16 * k, 16 * k + 1, 0, 4096)], T.nb[16 * k:16 * k + 16, :], [])
+    iota(X("sp", Z, Z + 16), [[0, 16]], int(BIG) // 16, 0)
+    iota(X("tw", 0, 8), [[0, 8]], 0, 0)
 
-    for x in range(4):
-        ts(X("src", x * 128, x * 128 + 128), X("aw", 0, 128), float(-4 * x), OP.is_equal)
-    act(X("i128", 0, 64), X("ib", 0, 64), AF.Identity, 0.0, 128.0)
-    tt(X("lst", 0, 64), X("i128", 0, 64), X("ib", 64, 128), OP.add)
-    for K in range(2):
-        ts(col(80 + K), col(CK + K), 128.0, OP.mult, col(CK + 2 + K), OP.add)
-        ts(X("sel4", 8 * K, 8 * K + 8), X("g8", 0, 8), col(80 + K), OP.mult)
-    tt(col(63), col(MC), col(MC + 1), OP.add)
-    ts(X("sel1", 0, 8), X("g8", 0, 8), col(63), OP.mult)
-    cp(WT, X("wtb", 0, 1))
-    ts(NQ, QB, 0.0, OP.is_equal)
-    ts(col(64), GM, 2.0, OP.mult, col(3), OP.add)
-    ts(X("iff", 0, 128), X("ir", 0, 128), col(0), OP.is_equal)
-    ts(X("samg", 0, 128), X("rgam", 0, 128), col(64), OP.is_equal)
-    ts(X("col", 84, 88), X("col", CK, CK + 4), WT, OP.mult, NQ, OP.mult)
-    ts(X("col", 88, 92), X("col", CK, CK + 4), WT, OP.mult, QB, OP.mult)
-    for j in range(8):
-        act(X("pack", j * 128, j * 128 + 128), X("samg", 0, 128), AF.Identity, 0.0, col(84 + j))
-    tt(X("rh", 0, 256), X("pb", 256, 512), X("ownt", 0, 256), OP.is_gt)
-    for K in range(2):
-        mm(X("pd", K * 128, K * 128 + 128), X("rh", K * 128, K * 128 + 128), X("ib", 0, 128))
-    for K, n in ((0, "h4"), (1, "l4")):
-        act(X(n, 0, 128), X("hlf", K * 128, K * 128 + 128), AF.Identity, -float(Z))
-        act(X(n, 128, 256), X("pd", K * 128, K * 128 + 128), AF.Identity, -1.0)
+    def ask(L, win, n):
+        share("gb", L * V, win, 1024, "idx", L * 128, n)
 
-    for q in [r] + others:
-        mm(X("pc", q * 128, q * 128 + 128), X3("tg", q, q + 1, 0, 128), X("ib", 0, 128), tag="sq")
-    cp(X("sq", 0, 512), X("pc", 0, 512))
-    for q in range(4):
-        for x in range(4):
-            mm(X("psw", q * 512 + x, q * 512 + 512, 4), X("src", x * 128, x * 128 + 128), X("sq", q * 128, q * 128 + 128), tag="src")
-    for K in range(2):
-        for q in range(4):
-            mm(X("pa", K * 128, K * 128 + 128, 1, 32 * q, 32 * q + 32), X("lst", 32 * K, 32 * K + 32), X("sq", q * 128, q * 128 + 128), tag="lst")
-    cp(X("nb16", 0, 256), X("nbi", 0, 256))
-    ts(X("blk", 0, 128), X("rg", 0, 128), col(2), OP.is_equal)
-    ts(X("tri", 0, 128), X("ir", 0, 128), col(0), OP.is_gt)
-    tt(X("lt", 0, 128), X("tri", 0, 128), X("blk", 0, 128), OP.mult)
-    ts(X("sel1f", 0, 8), X("g8", 0, 8), col(MC), OP.mult)
-    ts(X("bwi", 0, 24), X("bli", 0, 24), 4, OP.logical_shift_right)
-    ts(X("bwi", 24, 48), X("bli", 0, 24), 15, OP.bitwise_and)
-    ts(X("bwi", 24, 48), X("bwi", 24, 48), 256.0, OP.mult)
-    tt(X("bwi", 0, 24), X("bwi", 0, 24), X("bwi", 24, 48), OP.add)
-    cp(X("bw16", 0, 24), X("bwi", 0, 24))
-    for h in range(2):
-        for x in range(4):
-            o, i = X("wm", x * 2048 + h * 1024, x * 2048 + h * 1024 + 1024), X("psw", h * 1024, h * 1024 + 1024)
-            if h == 0:
-                ts(o, i, col(CX + x), OP.mult)
-            else:
-                act(o, i, AF.Identity, 0.0, col(CX + x))
-    cp(X("pl16", 0, 256), X("pa", 0, 256))
+    def answer(L, bank, c0):
+        pick(bank, c0, "gb", L * V, "selw", 0, 8, "word")
 
-    def places(a, b):
-        act(X("mq", a, b), X("stf", a, b), AF.Exp, 0.0, -2 * LN2)
-
-    for K in range(2):
-        share("gb", K * V, "wm", 8192, "pl16", K * 128, SHARE["names"][K])
-        if K == 0:
-            cp(X("li", 0, 256), X("pa", 0, 256))
-            for k in range(2):
-                ts(X("sti", k * 128, k * 128 + 128), X3("tg", 0, 4, k * 32, k * 32 + 32), 0.125, OP.mult, -0.4375, OP.add)
-            cp(X("stf", 0, 256), X("sti", 0, 256))
-            pick("pb", 0, "gb", 0, "sel4", 0, 16, "names")
-    places(0, 256)
-    act(X("vl", 0, 128), X("vl", 0, 128), AF.Identity, col(1))
-    act(X("vz", 0, 128), X("vl", 0, 128), AF.Identity, -float(V + Z))
-    tt(X("zt", 0, 128), X("pb", 0, 128), X("ownp", 0, 128), OP.is_equal)
-
-    def pack_z(parts, before, between):
-        for i, p in enumerate(parts):
-            mm(X("pa", 0, 128), p, X("ib", 0, 128), i == 0, i == len(parts) - 1, tag="zl")
-        before()
-        cp(X("zl", 0, 128), X("pa", 0, 128))
-        for h in range(2):
-            for x in range(4):
-                j = h * 4 + x
-                mm(X("psw", h * 512 + x, h * 512 + 512, 4), X("pack", j * 128, j * 128 + 128), X("zl", 0, 128), tag="pack")
-        between()
-        cp(X("ww", 0, 512), X("psw", 0, 512))
-        act(X("ww", 512, 1024), X("psw", 512, 1024))
-
-    def lists():
-        tt(X("np", 0, 128), X("pb", 128, 256), X("ownp", 0, 128), OP.not_equal)
-        ts(X("li", 0, 256), X("li", 0, 256), 1023, OP.bitwise_and)
-        cp(X("idx", 0, 256), X("li", 0, 256))
-
-    pack_z([X("zt", 0, 128)], lambda: cp(X("pif", 0, 128), X("pb", 0, 128)), lists)
-    pick("pd", 0, "gb", V, "sel4", 0, 16, "names")
-    cp(X("mcode", 0, 128), X("zt", 0, 128))
-
-    def ask(L, n):
-        share("gb", L * V, "ww", 1024, "idx", L * 128, n)
-
-    def answer(L):
-        bank, c0 = ("pc", "pd")[L // 2], (L % 2) * 128
-        if L == 3:
-            mm(X(bank, c0, c0 + 128), X("kc", 0, 128), X("one", 0, 128), True, False, tag="zz")
-        for b in range(16):
-            mm(X(bank, c0 + b, c0 + 128, 16), X("gb", L * V + b, L * V + V, 16), X("sel1", 0, 8), L != 3, L != 3 or b == 15, tag="zz")
-
-    def bits(H):
-        a, bank = H * 256, ("pc", "pd")[H]
-        tt(X("yi", a, a + 256), X(bank, 0, 256), X("mq", a, a + 256), OP.mult)
-        ts(X("zi", a, a + 256), X("yi", a, a + 256), 1, OP.bitwise_and)
-
-    def border_lists(d):
-        for b in range(16):
-            mm(X("pa", d * 128 + b, d * 128 + 128, 16, 0, 24), X("bq", d * 384 + b, d * 384 + 384, 16), X("sel1f", 0, 8), tag="bq")
-
-    ARH, ARL = X("ar", 0, 128), X("ar", 128, 256)
-    for t in range(2):
-        n = SHARE["r%d" % t]
-        if t == 1:
-            border_lists(0)
-        ask(0, n[0])
-        if t == 0:
-            cp(X("pif", 128, 256), X("pd", 0, 128))
+    n = SHARE["r2"]
+    TH = 1536
+    for L in range(3):
+        ask(L, "ww", n[L])
+        answer(L, ("pc", "pd")[L // 2], 128 * (L % 2))
+        if L == 0:
             for K in range(2):
-                mm(X("pb", K * 128, K * 128 + 128), X("pif", K * 128, K * 128 + 128), X("iff", 0, 128))
-            tt(X("np", 128, 256), X("pd", 128, 256), X("ownp", 0, 128), OP.not_equal)
-            tt(X("mlh", 0, 128), X("pd", 0, 128), X("ownp", 0, 128), OP.is_equal)
-        answer(0)
-        ask(1, n[1])
-        if t == 0:
-            cp(X("lj", 0, 256), X("pb", 0, 256))
-            ts(X("lj", 0, 256), X("lj", 0, 256), 1023, OP.bitwise_and)
-            cp(X("idx", 256, 512), X("lj", 0, 256))
-            act(X("np9", 0, 256), X("np", 0, 256), AF.Identity, 0.0, 9.0)
-            act(X("ml10", 0, 128), X("mlh", 0, 128), AF.Identity, 0.0, 10.0)
-            ts(X("sti", 256, 512), X("pif", 0, 256), 1.0 / 1024, OP.mult, -0.5 + 1.0 / 2048, OP.add)
-        answer(1)
-        if t == 0:
-            tt(X("stf", 256, 512), X("sti", 256, 512), X("np9", 0, 256), OP.max)
-            tt(X("stf", 384, 512), X("stf", 384, 512), X("ml10", 0, 128), OP.max)
-        ask(2, n[2])
-        answer(2)
-        if t == 0:
-            places(256, 512)
-        ask(3, n[3])
-        answer(3)
-        bits(0)
-        tt(X("tq", 0, 128), X("zi", 0, 128), X("zt", 0, 128), OP.is_le)
-        tt(X("thr", 0, 128), X("zi", 0, 128), X("zt", 0, 128), OP.max)
-        tt(X("thr", 128, 256), X("zi", 128, 256), X("tq", 0, 128), OP.max)
-        cp(X("bq", 384 * t, 384 * t + 384), IX("nbw", 4096, "bw16", 0, 24, 128 * t))
-        bits(1)
-        tt(X("ar", 0, 256), X("zi", 256, 512), X("thr", 0, 256), OP.is_gt)
-        if t == 0:
-            def more():
-                tt(X("zt", 0, 128), X("zt", 0, 128), ARH, OP.add)
-                tt(X("zt", 0, 128), X("zt", 0, 128), ARL, OP.add)
-            pack_z([X("zt", 0, 128), ARH, ARL], lambda: None, more)
-        tt(X("mcode", 0, 128), X("mcode", 0, 128), ARH, OP.add)
-        tt(X("mcode", 0, 128), X("mcode", 0, 128), ARL, OP.subtract)
-    border_lists(1)
-    act(X("bqt", 0, 256, 1, 0, 24), X("pa", 0, 256, 1, 0, 24), AF.Silu, 64.0)
-    send("code", lambda d: X("mcode", 32 * d, 32 * d + 32), X("tc", 32 * r, 32 * r + 32))
-    cp(X("tc", 32 * r, 32 * r + 32), X("mcode", 32 * r, 32 * r + 32))
-    recv("code", [("tc", 0, 128, 32 * q, 32 * q + 32) for q in others])
+                tt(X("dm", 128 * K, 128 * K + 128), X("dm", 128 * K, 128 * K + 128), VI, OP.mult)
+    tt(X("yi", 0, 256), X("pc", 0, 256), F(0, 2, 128, 256), OP.mult)
+    ask(3, "ww", n[3])
+    answer(3, "pd", 128)
+    ts(X("zi", 0, 256), X("yi", 0, 256), 6, OP.bitwise_and)
+    tt(X("zi", 0, 128), X("zi", 0, 128), UL, OP.min)
+    ts(X("nth", 0, 128), X("zi", 128, 256), -2.5, OP.mult, 9.0, OP.add)
+    tt(X("psw", TH, TH + 256), X("zi", 0, 256), X("psw", 1152, 1408), OP.max)
+    tt(X("psw", TH + 256, TH + 384), X("psw", TH, TH + 128), X("nth", 0, 128), OP.max)
+    tt(X("yi", 0, 256), X("pd", 0, 256), F(2, 4, 128, 256), OP.mult)
+    ts(X("zj", 0, 256), X("yi", 0, 256), 4, OP.bitwise_and)
+    tt(X("ar", 0, 256), X("zj", 0, 256), X("psw", TH + 128, TH + 384), OP.is_gt)
+    ARH, ARL = X("ar", 0, 128), X("ar", 128, 256)
+    pack("pa", [("e0", 0, 0), ("ar", 0, 0), ("ar", 128, 64)])
+    tt(F(2, 3, 0, 256), F(1, 2, 0, 256), X("dm", 0, 256), OP.add)
+    cp(X("wv", 256 * r, 256 * r + 256), X("pa", 0, 256))
+    spread("w2", "wv")
 
-    tt(X("beta", 0, 256), X("h4", 0, 256), X("l4", 0, 256), OP.add)
-    ts(X("beta", 0, 256), X("beta", 0, 256), 0.5, OP.mult)
-    tt(X("alph", 0, 256), X("h4", 0, 256), X("beta", 0, 256), OP.subtract)
-    for d in range(2):
-        act(X("gb", V + 384 * d, V + 384 * d + 384), IX("wr", V + V * d, "bl16", 0, 24, V * d))
-    for d in range(2):
-        mm(X("pc", 256 + 24 * d, 280 + 24 * d), X("bqt", d * 128, d * 128 + 128, 1, 0, 24), X("iff", 0, 24, 1, 0, 24))
+    mm(X("pb", 0, 128), F(2, 3, 0, 128), IF)
+    act(X("xst", 0, 384), IX("xc", V, "bl16", 0, 24))
+    show("x", "xst", "xw")
+    act(X("xw", mine, mine + C), X("xst", C * r, C * r + C))
+    act(X("ibn", 0, 128), IB, 0.0, -MID)
+    act(X("nti", 0, 256), TI, 0.0, -1.0)
+    iota(X("inv", 0, 2688), [[0, 2688]], 0, 0)
+    tt(X("tq", 0, 128), ARH, ARL, OP.add)
+    ts(X("idx", 256, 384), X("pb", 0, 128), float(OFFC), OP.subtract)
+    ts(X("nth", 0, 128), X("tq", 0, 128), 5.0, OP.mult, -1.0, OP.add)
+    tt(X("m2", 0, 128), T1, ARH, OP.add)
+    tt(X("psw", 1152, 1280), X("psw", TH, TH + 128), X("nth", 0, 128), OP.max)
+    tt(X("psw", 1024, 1152), X("psw", TH + 128, TH + 256), X("nth", 0, 128), OP.max)
 
-    mm(X("pc", 0, 128), X("tc", 0, 128), X("ib", 0, 128))
+    def mates(h, l, pz, first):
+        for K, m in enumerate((h, l)):
+            tt(X(pz, 128 * K, 128 * K + 128), m, X("hz", 128 * K, 128 * K + 128), OP.mult)
+            mm(X("psw", 0, 128), m, X("ibn", 0, 128), first and K == 0, False, tag="mate")
+            mm(X("psw", 0, 128), X(pz, 128 * K, 128 * K + 128), IH, False, not first and K == 1, tag="mate")
 
-    def quad(a):
-        tt(X("t1", a, a + 128), X("beta", a, a + 128), X("pc", 0, 128), OP.mult)
-        tt(X("t1", a, a + 128), X("t1", a, a + 128), X("alph", a, a + 128), OP.add)
-        tt(X("t1", a, a + 128), X("t1", a, a + 128), X("pc", 0, 128), OP.mult)
+    def lesser(h, l, nr, first):
+        for K, m in enumerate((h, l)):
+            tt(X(nr, 128 * K, 128 * K + 128), m, X("less", 128 * K, 128 * K + 128), OP.mult)
+            mm(X("psw", 512, 768), X(nr, 128 * K, 128 * K + 128), X("nti", 0, 256), False, not first and K == 1, tag="rep")
 
-    for j in range(4):
-        mm(X("psw", 512 * j, 512 * j + 512), X("ib", 0, 128), X("wr", V + 512 * j, V + 512 * j + 512))
-    quad(0)
-    ts(X("mate", 0, 128), X("t1", 0, 128), float(Z), OP.add)
+    mates(X("m2", 0, 128), ARL, "pz2", True)
+
+    n = SHARE["r3"]
+    ask(3, "wv", n[0])
+    answer(3, "pd", 0)
+    mm(X("psw", 512, 768), ONE, TI, True, False, tag="rep")
+    lesser(X("m2", 0, 128), ARL, "nr2", True)
+    ask(2, "wv", n[1])
+    answer(2, "pc", 0)
+    tt(X("yi", 128, 256), X("pd", 0, 128), F(3, 4, 128, 256), OP.mult)
+    ts(X("zj", 128, 256), X("yi", 128, 256), 6, OP.bitwise_and)
+    tt(X("tq", 0, 128), X("zj", 128, 256), X("psw", 1152, 1280), OP.is_gt)
+    cp(X("nb16", 0, 256), X("nbi", 0, 256))
+    tt(X("yi", 0, 128), X("pc", 0, 128), F(2, 3, 128, 256), OP.mult)
+    ts(X("zj", 0, 128), X("yi", 0, 128), 6, OP.bitwise_and)
+    A3, L3 = X("ar3", 0, 128), X("ar3", 128, 256)
+    tt(A3, X("zj", 0, 128), X("psw", 1024, 1152), OP.is_gt)
+    tt(X("tq", 0, 128), X("zj", 0, 128), X("tq", 0, 128), OP.min)
+    tt(X("pz3", 0, 128), A3, X("hz", 0, 128), OP.mult)
+    tt(L3, X("tq", 0, 128), A3, OP.is_gt)
+    mm(X("psw", 0, 128), A3, X("ibn", 0, 128), False, False, tag="mate")
+    mm(X("psw", 0, 128), X("pz3", 0, 128), IH, False, False, tag="mate")
+    tt(X("pz3", 128, 256), L3, X("hz", 128, 256), OP.mult)
+    mm(X("psw", 0, 128), L3, X("ibn", 0, 128), False, False, tag="mate")
+    mm(X("psw", 0, 128), X("pz3", 128, 256), IH, False, True, tag="mate")
+    for c in range(4):
+        act(col(64 + c), MC(4 + c), MC(c), 16.0)
+    act(QW, X("dif", 0, 1), 8.0, -1.0)
+    act(col(72), col(QM + 1), 0.0, -1.0 / BIG)
+    act(col(73), B4, 0.0, -1.0 / BIG)
+    for c in range(4):
+        act(X("seli", 8 * c, 8 * c + 8), G8, 0.0, col(64 + c))
+        act(X("wq", 144 * c + 8, 144 * c + 136, 16), G8, 0.0, col(QM + c))
+    act(X("km", 0, 512), X("km", 0, 512), col(73), col(72))
+
+    ts(X("mate", 0, 128), X("psw", 0, 128), float(Z), OP.add)
     nx = SHARE["x"]
     tt(X("xf", 0, nx), IX("xw", Z + 16, "mate", 0, nx // 16), X("xc", 0, nx), OP.add)
-    for i, (bank, a, b) in enumerate((("pa", nx, nx + 512), ("pb", nx + 512, V))):
+    for bank, a, b in (("pa", nx, nx + 512), ("pb", nx + 512, V)):
         act(X("gb", a - nx, b - nx), IX("xw", Z + 16, "mate", a // 16, b // 16))
-        mm(X(bank, 0, b - a), X("ib", 0, 128), X("xc", a, b), True, False, tag="gx")
-        mm(X(bank, 0, b - a), X("ib", 0, 128), X("gb", a - nx, b - nx), False, True, tag="gx")
+        mm(X(bank, 0, b - a), IB, X("xc", a, b), True, False, tag="gx")
+        mm(X(bank, 0, b - a), IB, X("gb", a - nx, b - nx), False, True, tag="gx")
     for bank, a, b in (("pa", nx, nx + 512), ("pb", nx + 512, V)):
         act(X("xf", a, b), X(bank, 0, b - a))
-    mm(X("pb", 0, 384), X("ib", 0, 128), X("gb", V + 384, V + 768))
+    lesser(A3, L3, "nr3", False)
     cp(X("xb", 0, 192), IX("xf", V, "bl16", 0, 12))
     act(X("xb", 192, 384), IX("xf", V, "bl16", 12, 24))
-    send("xs", lambda d: X("xb", C * d, C * d + C), X("xf", mine, mine + C))
+    show("xs", "xb", "xf")
     act(X("xf", mine, mine + C), X("xb", C * r, C * r + C))
-    recv("xs", ghosts("xf"))
 
-    quad(128)
-    ts(X("rep", 0, 128), X("t1", 128, 256), 1.0, OP.add)
-    mm(X("pd", 0, 128), X("rep", 0, 128), X("ib", 0, 128))
-    ts(X("nbl", 0, 48), X("pc", 256, 304), 64.0, OP.subtract)
-    cp(X("nbb16", 0, 48), X("nbl", 0, 48))
-    tt(X("ms", 0, 128), X("vz", 0, 128), X("t1", 0, 128), OP.subtract)
-    tt(X("ms", 0, 128), X("ms", 0, 128), X("rep", 0, 128), OP.mult)
-    tt(X("ms", 0, 128), X("ms", 0, 128), X("t1", 0, 128), OP.add)
-    ts(X("ms16", 0, 128), X("ms", 0, 128), float(Z), OP.add)
-    act(X("rt", 0, 128), X("pd", 0, 128))
-    mm(X("pd", 128, 256), X("rt", 0, 128), X("tri", 0, 128))
-    act(X("up", 0, 128), X("pd", 128, 256))
-    mm(X("pd", 0, 128), X("blk", 0, 128), X("up", 0, 128), True, False, tag="num")
-    mm(X("pd", 0, 128), X("lt", 0, 128), X("rep", 0, 128), False, True, tag="num")
-    act(X("num", 0, 128), X("pd", 0, 128))
-    act(X("cn", 0, 128), X("pd", 0, 128), AF.Identity, float(V * r))
-    tt(X("off", 0, 128), X("num", 0, 128), X("vl", 0, 128), OP.subtract)
-    tt(X("off", 0, 128), X("off", 0, 128), X("rep", 0, 128), OP.mult)
-    tt(X("off", 0, 128), X("off", 0, 128), X("vl", 0, 128), OP.add)
-    cp(X("off16", 0, 128), X("off", 0, 128))
+    REP, UP = X("ru", 0, 128), X("ru", 128, 256)
+    cp(X("ru", 0, 256), X("psw", 512, 768))
+    mm(X("pd", 0, 128), BLK, UP, True, False, tag="num")
+    mm(X("pd", 0, 128), X("lt", 0, 128), REP, False, True, tag="num")
+    mm(X("pc", 0, 128), X("ltq", 0, 128), REP)
+    for j in range(4):
+        mm(X("psw", 512 * j, 512 * j + 512), SELR, X("wsb", 512 * j, 512 * j + 512, 1, 0, 16))
+    act(X("cn", 0, 128), X("pd", 0, 128), BIG + V * r)
+    ts(col(76, 4), col(QM, 4), QW, OP.mult)
+    ts(col(80, 8), X("ir", 0, 8), -16.0, OP.mult, QW, OP.add)
+    for c in range(4):
+        ts(X("wq", 144 * c + 4, 144 * c + 132, 16), col(80, 8), col(QM + c), OP.mult)
+    for c in range(4):
+        tt(X("wq", 144 * c + 4, 144 * c + 132, 16), X("wq", 144 * c + 4, 144 * c + 132, 16), G8, OP.mult)
+    for i in range(4):
+        ts(X("mk", 128 * i, 128 * i + 128), X("pc", 0, 128), float(i - 8), OP.is_equal, -BIG, OP.mult)
+    for c in range(4):
+        for i in range(4):
+            mm(X("pa", c, 512, 4), X("wq", 144 * c + 4 - i, 144 * c + 132 - i), X("mk", 128 * i, 128 * i + 128), i == 0, i == 3, tag="four")
+    for m in range(4):
+        for i, (lhs, rhs, c0) in enumerate((("b0", "ru", 128), ("lt0", "ru", 0), ("q0", "mk", 0))):
+            mm(X("pb", 0, 32), X(lhs, 12 - 4 * m, 140 - 4 * m), X(rhs, c0 + m, c0 + 128, 4), m + i == 0, m + i == 5, tag="base")
 
     def SP(c):
         return X("sp", c, V, 16)[0], [("sp%d" % c, 0, 128, 0, 128)]
@@ -518,66 +509,56 @@ def rank_program(g, core, T, topo):
 
     for c in range(16):
         if c < 4:
-            ts(SP(c), X("cn", 0, 128), col(MC + c), OP.mult)
+            ts(SP(c), X("cn", 0, 128), MC(c), OP.mult)
         else:
-            act(SP(c), X("cn", 0, 128), AF.Identity, 0.0, col(MC + c))
+            act(SP(c), X("cn", 0, 128), 0.0, MC(c))
+    tt(X("rb", 0, 512), X("pa", 0, 512), X("km", 0, 512), OP.mult)
+    tt(X("off", 0, 32), X("pb", 0, 32), X("vl", 0, 32), OP.min)
+    ts(X("off16", 0, 32), X("off", 0, 32), BIG + 16.0, OP.add)
     act(X("sb", 0, 384), numbers("bl16", 0, 24, V))
-    send("num", lambda d: X("sb", C * d, C * d + C), X("sp", mine, mine + C))
+    show("num", "sb", "sp")
     act(X("sp", mine, mine + C), X("sb", C * r, C * r + C))
-    recv("num", ghosts("sp"))
-
-    def invert(j):
-        o = IX("inv", 4096, "off16", 32 * j, 32 * j + 32)
-        i = X("id64", 512 * j, 512 * j + 512)
-        add("S", lambda e: e.activation(out=o[0], in_=i[0], func=AF.Silu), [("inv", 0, 128, 0, 4096)],
-            rg(i) + [("off16", 0, 128, 32 * j, 32 * j + 32)])
-
-    def times_w0(a, b):
-        tt(X("p0", a, b), IX("xf", Z, "nb16", a // 16, b // 16), X("wr", a, b), OP.mult)
-
-    act(X("gA", 0, 384), IX("xf", Z, "nbb16", 24, 48))
-    tt(X("pB", 0, 384), IX("xf", Z, "nbb16", 0, 24), X("gb", V, V + 384), OP.mult)
-    times_w0(0, 512)
-    tt(X("pb", 0, 384), X("gA", 0, 384), X("pb", 0, 384), OP.mult)
-    tt(X("sst", 0, 384), X("pB", 0, 384), X("pb", 0, 384), OP.add)
-    send("s", lambda d: X("sst", C * d, C * d + C), X("sw", mine, mine + C))
-    recv("s", ghosts("sw"))
 
     for j in range(4):
         a, b = 512 * j, 512 * j + 512
         act(X("g1", a, b), IX("xf", Z, "nb16", 128 + 32 * j, 160 + 32 * j))
-        if j > 0:
-            invert(j - 1)
-    invert(3)
-    act(X("sw", mine, mine + C), X("sst", C * r, C * r + C))
     for j in range(4):
         a, b = 512 * j, 512 * j + 512
-        if j > 0:
-            times_w0(a, b)
+        tt(X("p0", a, b), IX("xf", Z, "nb16", a // 16, b // 16), X("wr", a, b), OP.mult)
         tt(X("psw", a, b), X("g1", a, b), X("psw", a, b), OP.mult)
         tt(X("sw", a, b), X("p0", a, b), X("psw", a, b), OP.add)
-        keep(X("p0", a, b), X("sw", a, b))
-    pick("pa", 0, "inv", 0, "sel1f", 0, 8, "inv")
-    act(X("g1", 0, V), numbers("ms16", 0, 128, Z))
+        if j == 3:
+            cp(X("sst", 0, 192), IX("sw", V, "bl16", 0, 12))
+            act(X("sst", 192, 384), IX("sw", V, "bl16", 12, 24))
+            show("s", "sst", "sw")
+            act(X("sw", mine, mine + C), X("sst", C * r, C * r + C))
+        where(X("p0", a, b), X("sw", a, b), [[1, 512]], 0, 0)
+
+    o = IX("inv", 2688, "off16", 0, 32)
+    add("V", lambda e: e.tensor_copy(out=o[0], in_=T.rb[:, :]), rg(X("inv", 0, 2688)), rg(X("rb", 0, 512), X("off16", 0, 32)))
+    for b in range(16):
+        for i in range(4):
+            mm(X("pa", b, 128, 16), X("inv", 16 + b - i, 16 + b - i + V - 15, 16), X("seli", 8 * i, 8 * i + 8), i == 0, i == 3, tag="inv")
+    act(X("g1", 0, V), numbers("mate", 0, 128, Z + 16))
     act(X("ivt", 0, 128), X("pa", 0, 128))
-    mm(X("pb", 0, 128), X("ivt", 0, 128), X("iff", 0, 128))
+    mm(X("pb", 0, 128), X("ivt", 0, 128), IF)
+    pick("pc", 0, "g1", 0, "g8", 0, 8, "cm")
+    act(X("cmt", 0, 128), X("pc", 0, 128))
+    mm(X("pd", 0, 128), X("cmt", 0, 128), IF)
     for j in range(2):
         a, b = 1024 * j, 1024 * j + 1024
-        tt(X("tw", a, b), IX("sw", Z + 16, "mate", 64 * j, 64 * j + 64), X("p0", a, b), OP.add)
-    ts(X("ivi", 0, 128), X("pb", 0, 128), 64.0, OP.subtract)
-    cp(X("iv16", 0, 128), X("ivi", 0, 128))
+        tt(X("tw", 8 + a, 8 + b), IX("sw", Z + 16, "mate", 64 * j, 64 * j + 64), X("p0", a, b), OP.add)
+    cp(X("iv16", 0, 128), X("pb", 0, 128))
     for j in range(4):
-        o, i = X("p0", 512 * j, 512 * j + 512), IX("tw", V + 16, "iv16", 32 * j, 32 * j + 32)
+        o, i = X("p0", 512 * j, 512 * j + 512), IX("tw", V + 8, "iv16", 32 * j, 32 * j + 32)
         if j % 2 == 0:
             cp(o, i)
         else:
             act(o, i)
         dma("Y", "y%d" % j, T.y[:, 512 * j:512 * j + 512], [], o[0], o[1])
-    pick("pc", 0, "g1", 0, "g8", 0, 8, "cm")
-    act(X("cmt", 0, 128), X("pc", 0, 128))
-    mm(X("pd", 0, 128), X("cmt", 0, 128), X("iff", 0, 128))
-    act(X("cmv", 0, 128), X("pd", 0, 128))
-    dma("Y", "cm", T.cm[:, :], [], T.cmv[:, :], rg(X("cmv", 0, 128)))
+        if j == 0:
+            tt(X("cmv", 0, 128), X("pd", 0, 128), X("cn", 0, 128), OP.min)
+            dma("Y", "cm", T.cm[:, :], [], T.cmv[:, :], rg(X("cmv", 0, 128)))
     for s, v in total.items():
         if known["G"].get(s, 0) < v:
             g.wait_ge(T.sem[s], v)

@@ -10,11 +10,11 @@ F32, BF, F16, I32, U16 = "float32", "bfloat16", "float16", "int32", "uint16"
 WIDTHS = {
     F32: dict(nbf=256, dn=128, bd=128, hlf=256, col=128, ir=128, dif=128, iff=128, own=256, nth=128, tq=128, dm=256, xf=2432,
               cn=128, vl=32, off=32, sp=2448, sb=384, g1=2048, p0=2048, sw=2448, sst=384, ivt=128, cmt=128, cmv=128, tw=2056,
-              xb=384, g8=8),
+              xb=384, g8=8, cmr=2048),
     BF: dict(wsb=2048, xw=2448, xc=2048, nw=2432, bst=384, hb=2048, hl=2432, hst=384, xst=384, gb=8192, wr=2048, ti=256, nti=256,
-             ibn=128, pm=8, sel=48, selw=8, seli=32, wt=128, e0=272, e1=256, ar=272, ar3=256, m2=256, less=256, nr2=256, nr3=256,
+             ibn=128, pm=8, sel=48, selw=8, seli=32, wt=128, e0=272, e1=256, ar=288, ar3=256, m2=256, less=256, nr2=256, nr3=256,
              ww=1024, wv=1024, one=144, ru=256, mk=512, blk=128, lt=128, ltq=128, b0=144, lt0=144, q0=144, wq=576, km=512,
-             rb=512, inv=2688, selr=128, bt=128, irb=128),
+             rb=512, inv=2688, selr=128, selq=128, bt=128, irb=128, zero=144),
     F16: dict(hz=256, pz2=256, pz3=256, ih=128),
     I32: dict(bli=24, nbi=256, ci=64, cj=64, yi=256, zi=256, zj=256),
     U16: dict(bl16=24, hl16=256, idx=512, mate=128, off16=32, iv16=128, nb16=256),
@@ -25,12 +25,15 @@ for _d in WIDTHS:
     for _n in WIDTHS[_d]:
         SCRATCH[_n] = ("sbuf", [128, WIDTHS[_d][_n]], _d)
 for _n in PSUM:
-    SCRATCH[_n] = ("psum", [128, PSUM[_n]], F32)
+    SCRATCH[_n] = ("psum", [128, 8, 64] if _n == "pa" else [128, PSUM[_n]], F32)
 EXCH = ["name", "hl", "w1", "w2", "x", "xs", "num", "s"]
 LOADS = ["bl", "nb", "w", "x", "xc", "wr", "y0", "y1", "y2", "y3", "cm"]
 SEMAPHORES = ["cV", "cS", "cP", "cG"] + ["d_" + k for k in LOADS] + ["a_" + k for k in EXCH] + ["l_" + k for k in EXCH]
-SHARE = {"nh": 1024, "nl": 512, "r2": (1024, 1024, 768, 512), "r3": (768, 768), "x": 1408}
+SHARE = {"nh": 1024, "nl": 512, "r2": (1024, 1024, 768, 768), "r3": (1024, 704), "x": 1408, "sp": 6, "cm": 1536}
 STEPS = (128, 256, 512, 576, 576)
+BOTH = {3: "pc"}
+KEPT = 2
+CUTS = (0, 512, 1024, 1536, 2048)
 
 
 def engine_plan(topo, src, cores):
@@ -98,7 +101,10 @@ def rank_program(g, core, T, topo):
         note(o, outs, ins)
 
     def X(name, c0, c1, step=1, p0=0, p1=128):
-        ap = T[name][p0:p1, c0:c1] if step == 1 else T[name][p0:p1, c0:c1:step]
+        if name == "pa":
+            ap = T.pa[p0:p1, c0 // 64:(c1 + 63) // 64, c0 % 64:64:step]
+        else:
+            ap = T[name][p0:p1, c0:c1] if step == 1 else T[name][p0:p1, c0:c1:step]
         return ap, [(name, p0, p1, c0, c1)]
 
     def F(i0, i1, j0, j1):
@@ -225,12 +231,12 @@ def rank_program(g, core, T, topo):
     act(col(DC + 3), col(M8 + 3), col(M8 + 1), 3.0)
     act(S8, col(M8 + 4), 1.0, -0.875)
     ts(col(TX, 4), col(TX, 4), K0, OP.add)
-    cp(X("bl16", 0, 24), X("bli", 0, 24))
     for x in range(4):
         ts(X("nw", x, 512, 4), X("irb", 0, 128), col(M8), OP.mult, col(TX + x), OP.add, tag="nw")
     act(X("nw", 512, 1024), X("nw", 0, 512), col(DC + 1))
     for j in (2, 3):
         ts(X("nw", 512 * j, 512 * j + 512), X("nw", 0, 512), S8, OP.mult, col(DC + j), OP.add)
+    cp(X("bl16", 0, 24), X("bli", 0, 24))
     cp(X("bst", 0, 192), IX("nw", V, "bl16", 0, 12))
     act(X("bst", 192, 384), IX("nw", V, "bl16", 12, 24))
     show("name", "bst", "nw")
@@ -269,12 +275,16 @@ def rank_program(g, core, T, topo):
     ts(X("sel", 40, 48), G8, MC(12), OP.mult, 2.0, OP.mult)
     ts(X("sel", 0, 8), G8, WG, OP.mult, SIDEA, OP.mult)
     ts(X("sel", 8, 16), G8, WG, OP.mult, SIDEB, OP.mult)
+    ts(X("cj", 38, 39), X("ci", 0, 1), 15, OP.bitwise_and)
+    ts(QW, X("cj", 38, 39), 8.0, OP.add)
+    cp(X("nb16", 0, 256), X("nbi", 0, 256))
     iota(X("own", 0, 128), [[0, 8], [1, 16]], V * r + OFFG, 16)
     iota(X("own", 128, 256), [[0, 8], [1, 16]], V * r, 16)
     iota(X("one", 0, 144), [[0, 144]], 1, 0)
     iota(X("e0", 256, 272), [[0, 16]], 0, 0)
-    iota(X("ar", 256, 272), [[0, 16]], 0, 0)
-    for n in ("b0", "lt0", "q0"):
+    iota(X("ar", 128, 144), [[0, 16]], 0, 0)
+    iota(X("ar", 272, 288), [[0, 16]], 0, 0)
+    for n in ("b0", "lt0", "q0", "zero"):
         iota(X(n, 0, 144), [[0, 144]], 0, 0)
     iota(X("wq", 0, 576), [[0, 576]], 0, 0)
 
@@ -317,7 +327,9 @@ def rank_program(g, core, T, topo):
     def pack(bank, parts, first=True, last=True):
         for c in range(4):
             for i, (name, c0, w0) in enumerate(parts):
-                mm(X(bank, c, 256, 4), X(name, c0 + 4 * c, c0 + 4 * c + 128), X("wt", w0, w0 + 64), i == 0, i == len(parts) - 1, tag="pack")
+                digits = X(name, c0 + 4 * c, c0 + 4 * c + 128)
+                stop = i == len(parts) - 1 if first else last and c == 3
+                mm(X(bank, c, 256, 4), digits, X("wt", w0, w0 + 64), first and i == 0, stop, tag="pack")
 
     share("gb", 0, "hl", Z, "hl16", 0, SHARE["nh"])
     pick("pc", 0, "gb", 0, "sel", 0, 32, "nh")
@@ -344,6 +356,8 @@ def rank_program(g, core, T, topo):
     tt(X("nth", 0, 128), X("e1", 0, 128), X("e1", 128, 256), OP.max)
     tt(X("nth", 0, 128), X("nth", 0, 128), T1, OP.is_gt)
     act(LL, X("nth", 0, 128), 4.0, -5.0)
+    for K in range(2):
+        tt(X("dm", 128 * K, 128 * K + 128), X("dm", 128 * K, 128 * K + 128), VI, OP.mult)
     ts(X("idx", 256, 512), X("pb", 0, 256), float(OFFC), OP.subtract)
 
     words = [("ww", 0, 128, 0, 1024)]
@@ -364,6 +378,7 @@ def rank_program(g, core, T, topo):
     where(X("q0", 12, 140), X("q0", 12, 140), [[16, 8], [4, 16]], 3, -1)
     SELR = X("selr", 0, 128, 1, 0, 16)
     where(SELR, X("one", 0, 128, 1, 0, 16), [[-16, 8], [0, 16]], -128, 16, OP.is_equal)
+    where(X("selq", 0, 128, 1, 0, 16), X("one", 0, 128, 1, 0, 16), [[-16, 8], [0, 16]], 0, 16, OP.is_equal)
     iota(X("km", 0, 512), [[1, 128], [0, 4]], 0, 0)
     iota(X("vl", 0, 32), [[16, 32]], V - int(BIG), 1)
     iota(X("xw", Z, Z + 16), [[0, 16]], 0, 0)
@@ -379,39 +394,55 @@ def rank_program(g, core, T, topo):
 
     n = SHARE["r2"]
     TH = 1536
+    ARH, ARL = X("ar", 0, 128), X("ar", 144, 272)
+
+    def digit(out, K, bank, f, mask):
+        tt(X("yi", 128 * K, 128 * K + 128), X(bank, 0, 128), F(f, f + 1, 128, 256), OP.mult)
+        ts(X(out, 128 * K, 128 * K + 128), X("yi", 128 * K, 128 * K + 128), mask, OP.bitwise_and)
+
     for L in range(3):
         ask(L, "ww", n[L])
-        answer(L, ("pc", "pd")[L // 2], 128 * (L % 2))
-        if L == 0:
-            for K in range(2):
-                tt(X("dm", 128 * K, 128 * K + 128), X("dm", 128 * K, 128 * K + 128), VI, OP.mult)
+        answer(L, ("pc", "pc", "pd")[L], 128 * (L % 2))
+    mm(X("pa", 0, 256), X("zero", 0, 128), TI, True, False, tag="pack")
+    pack("pa", [("e0", 0, 0)], False, False)
     tt(X("yi", 0, 256), X("pc", 0, 256), F(0, 2, 128, 256), OP.mult)
     ask(3, "ww", n[3])
-    answer(3, "pd", 128)
+    answer(3, "pb", 0)
     ts(X("zi", 0, 256), X("yi", 0, 256), 6, OP.bitwise_and)
+    digit("zj", 0, "pd", 2, 4)
     tt(X("zi", 0, 128), X("zi", 0, 128), UL, OP.min)
     ts(X("nth", 0, 128), X("zi", 128, 256), -2.5, OP.mult, 9.0, OP.add)
     tt(X("psw", TH, TH + 256), X("zi", 0, 256), X("psw", 1152, 1408), OP.max)
     tt(X("psw", TH + 256, TH + 384), X("psw", TH, TH + 128), X("nth", 0, 128), OP.max)
-    tt(X("yi", 0, 256), X("pd", 0, 256), F(2, 4, 128, 256), OP.mult)
-    ts(X("zj", 0, 256), X("yi", 0, 256), 4, OP.bitwise_and)
-    tt(X("ar", 0, 256), X("zj", 0, 256), X("psw", TH + 128, TH + 384), OP.is_gt)
-    ARH, ARL = X("ar", 0, 128), X("ar", 128, 256)
-    pack("pa", [("e0", 0, 0), ("ar", 0, 0), ("ar", 128, 64)])
-    tt(F(2, 3, 0, 256), F(1, 2, 0, 256), X("dm", 0, 256), OP.add)
+    tt(ARH, X("zj", 0, 128), X("psw", TH + 128, TH + 256), OP.is_gt)
+    digit("zj", 1, "pb", 3, 4)
+    tt(ARL, X("zj", 128, 256), X("psw", TH + 256, TH + 384), OP.is_gt)
+    pack("pa", [("ar", 0, 0)], False, False)
+    pack("pa", [("ar", 144, 64)], False, True)
+    tt(X("tq", 0, 128), ARH, ARL, OP.add)
     cp(X("wv", 256 * r, 256 * r + 256), X("pa", 0, 256))
     spread("w2", "wv")
 
+    tt(F(2, 3, 0, 256), F(1, 2, 0, 256), X("dm", 0, 256), OP.add)
     mm(X("pb", 0, 128), F(2, 3, 0, 128), IF)
     act(X("xst", 0, 384), IX("xc", V, "bl16", 0, 24))
     show("x", "xst", "xw")
     act(X("xw", mine, mine + C), X("xst", C * r, C * r + C))
+    act(X("nth", 0, 128), X("tq", 0, 128), -1.0, 5.0)
     act(X("ibn", 0, 128), IB, 0.0, -MID)
     act(X("nti", 0, 256), TI, 0.0, -1.0)
     iota(X("inv", 0, 2688), [[0, 2688]], 0, 0)
-    tt(X("tq", 0, 128), ARH, ARL, OP.add)
+    for c in range(4):
+        act(col(64 + c), MC(4 + c), MC(c), 16.0)
+    act(col(76, 4), col(QM, 4), 0.0, QW)
+    act(col(72), col(QM + 1), 0.0, -1.0 / BIG)
+    act(col(73), B4, 0.0, -1.0 / BIG)
+    for c in range(4):
+        act(X("seli", c, 32, 4), G8, 0.0, col(64 + c), tag="wq")
+        act(X("wq", 144 * c + 8, 144 * c + 136, 16), G8, 0.0, col(QM + c), tag="wq")
+        act(X("wq", 144 * c + 4, 144 * c + 132, 16), G8, 0.0, col(76 + c), tag="wq")
+    act(X("km", 0, 512), X("km", 0, 512), col(73), col(72))
     ts(X("idx", 256, 384), X("pb", 0, 128), float(OFFC), OP.subtract)
-    ts(X("nth", 0, 128), X("tq", 0, 128), 5.0, OP.mult, -1.0, OP.add)
     tt(X("m2", 0, 128), T1, ARH, OP.add)
     tt(X("psw", 1152, 1280), X("psw", TH, TH + 128), X("nth", 0, 128), OP.max)
     tt(X("psw", 1024, 1152), X("psw", TH + 128, TH + 256), X("nth", 0, 128), OP.max)
@@ -430,50 +461,50 @@ def rank_program(g, core, T, topo):
     mates(X("m2", 0, 128), ARL, "pz2", True)
 
     n = SHARE["r3"]
-    ask(3, "wv", n[0])
-    answer(3, "pd", 0)
     mm(X("psw", 512, 768), ONE, TI, True, False, tag="rep")
     lesser(X("m2", 0, 128), ARL, "nr2", True)
-    ask(2, "wv", n[1])
+    ask(2, "wv", n[0])
     answer(2, "pc", 0)
-    tt(X("yi", 128, 256), X("pd", 0, 128), F(3, 4, 128, 256), OP.mult)
-    ts(X("zj", 128, 256), X("yi", 128, 256), 6, OP.bitwise_and)
-    tt(X("tq", 0, 128), X("zj", 128, 256), X("psw", 1152, 1280), OP.is_gt)
-    cp(X("nb16", 0, 256), X("nbi", 0, 256))
-    tt(X("yi", 0, 128), X("pc", 0, 128), F(2, 3, 128, 256), OP.mult)
-    ts(X("zj", 0, 128), X("yi", 0, 128), 6, OP.bitwise_and)
+    n1, n2 = n[1] // 2, n[1]
+    act(X("gb", 3 * V + n2, 4 * V), IX("wv", 1024, "idx", 384 + n2 // 16, 512))
+    cp(X("gb", 3 * V, 3 * V + n1), IX("wv", 1024, "idx", 384, 384 + n1 // 16))
+    digit("zj", 0, "pc", 2, 6)
+    cp(X("gb", 3 * V + n1, 3 * V + n2), IX("wv", 1024, "idx", 384 + n1 // 16, 384 + n2 // 16))
+    answer(3, "pd", 0)
     A3, L3 = X("ar3", 0, 128), X("ar3", 128, 256)
     tt(A3, X("zj", 0, 128), X("psw", 1024, 1152), OP.is_gt)
-    tt(X("tq", 0, 128), X("zj", 0, 128), X("tq", 0, 128), OP.min)
+    ts(X("nth", 0, 128), X("zj", 0, 128), -2.5, OP.mult, 4.0, OP.add)
+    ts(X("tq", 0, 128), A3, 5.0, OP.mult, -1.0, OP.add)
+    tt(X("psw", 1152, 1280), X("psw", 1152, 1280), X("nth", 0, 128), OP.max)
     tt(X("pz3", 0, 128), A3, X("hz", 0, 128), OP.mult)
-    tt(L3, X("tq", 0, 128), A3, OP.is_gt)
+    tt(X("psw", 1152, 1280), X("psw", 1152, 1280), X("tq", 0, 128), OP.max)
     mm(X("psw", 0, 128), A3, X("ibn", 0, 128), False, False, tag="mate")
     mm(X("psw", 0, 128), X("pz3", 0, 128), IH, False, False, tag="mate")
+    digit("zj", 1, "pd", 3, 6)
+    tt(L3, X("zj", 128, 256), X("psw", 1152, 1280), OP.is_gt)
     tt(X("pz3", 128, 256), L3, X("hz", 128, 256), OP.mult)
     mm(X("psw", 0, 128), L3, X("ibn", 0, 128), False, False, tag="mate")
     mm(X("psw", 0, 128), X("pz3", 128, 256), IH, False, True, tag="mate")
-    for c in range(4):
-        act(col(64 + c), MC(4 + c), MC(c), 16.0)
-    act(QW, X("dif", 0, 1), 8.0, -1.0)
-    act(col(72), col(QM + 1), 0.0, -1.0 / BIG)
-    act(col(73), B4, 0.0, -1.0 / BIG)
-    for c in range(4):
-        act(X("seli", 8 * c, 8 * c + 8), G8, 0.0, col(64 + c))
-        act(X("wq", 144 * c + 8, 144 * c + 136, 16), G8, 0.0, col(QM + c))
-    act(X("km", 0, 512), X("km", 0, 512), col(73), col(72))
 
     ts(X("mate", 0, 128), X("psw", 0, 128), float(Z), OP.add)
+    def weights(j):
+        mm(X("psw", 512 * j, 512 * j + 512), SELR, X("wsb", 512 * j, 512 * j + 512, 1, 0, 16))
+
     nx = SHARE["x"]
+    hx = (nx + V) // 2
     tt(X("xf", 0, nx), IX("xw", Z + 16, "mate", 0, nx // 16), X("xc", 0, nx), OP.add)
-    for bank, a, b in (("pa", nx, nx + 512), ("pb", nx + 512, V)):
-        act(X("gb", a - nx, b - nx), IX("xw", Z + 16, "mate", a // 16, b // 16))
+    for bank, a, b in (("pa", nx, hx), ("pb", hx, V)):
         mm(X(bank, 0, b - a), IB, X("xc", a, b), True, False, tag="gx")
+    weights(2)
+    for bank, a, b in (("pa", nx, hx), ("pb", hx, V)):
+        act(X("gb", a - nx, b - nx), IX("xw", Z + 16, "mate", a // 16, b // 16))
         mm(X(bank, 0, b - a), IB, X("gb", a - nx, b - nx), False, True, tag="gx")
-    for bank, a, b in (("pa", nx, nx + 512), ("pb", nx + 512, V)):
+    for bank, a, b in (("pa", nx, hx), ("pb", hx, V)):
         act(X("xf", a, b), X(bank, 0, b - a))
+    weights(3)
+    weights(0)
     lesser(A3, L3, "nr3", False)
-    cp(X("xb", 0, 192), IX("xf", V, "bl16", 0, 12))
-    act(X("xb", 192, 384), IX("xf", V, "bl16", 12, 24))
+    act(X("xb", 0, 384), IX("xf", V, "bl16", 0, 24))
     show("xs", "xb", "xf")
     act(X("xf", mine, mine + C), X("xb", C * r, C * r + C))
 
@@ -482,15 +513,7 @@ def rank_program(g, core, T, topo):
     mm(X("pd", 0, 128), BLK, UP, True, False, tag="num")
     mm(X("pd", 0, 128), X("lt", 0, 128), REP, False, True, tag="num")
     mm(X("pc", 0, 128), X("ltq", 0, 128), REP)
-    for j in range(4):
-        mm(X("psw", 512 * j, 512 * j + 512), SELR, X("wsb", 512 * j, 512 * j + 512, 1, 0, 16))
     act(X("cn", 0, 128), X("pd", 0, 128), BIG + V * r)
-    ts(col(76, 4), col(QM, 4), QW, OP.mult)
-    ts(col(80, 8), X("ir", 0, 8), -16.0, OP.mult, QW, OP.add)
-    for c in range(4):
-        ts(X("wq", 144 * c + 4, 144 * c + 132, 16), col(80, 8), col(QM + c), OP.mult)
-    for c in range(4):
-        tt(X("wq", 144 * c + 4, 144 * c + 132, 16), X("wq", 144 * c + 4, 144 * c + 132, 16), G8, OP.mult)
     for i in range(4):
         ts(X("mk", 128 * i, 128 * i + 128), X("pc", 0, 128), float(i - 8), OP.is_equal, -BIG, OP.mult)
     for c in range(4):
@@ -499,6 +522,7 @@ def rank_program(g, core, T, topo):
     for m in range(4):
         for i, (lhs, rhs, c0) in enumerate((("b0", "ru", 128), ("lt0", "ru", 0), ("q0", "mk", 0))):
             mm(X("pb", 0, 32), X(lhs, 12 - 4 * m, 140 - 4 * m), X(rhs, c0 + m, c0 + 128, 4), m + i == 0, m + i == 5, tag="base")
+    weights(1)
 
     def SP(c):
         return X("sp", c, V, 16)[0], [("sp%d" % c, 0, 128, 0, 128)]
@@ -508,54 +532,89 @@ def rank_program(g, core, T, topo):
         return ap, regs + [y for k in range(16) for y in SP(k)[1]]
 
     for c in range(16):
-        if c < 4:
+        if c < SHARE["sp"]:
             ts(SP(c), X("cn", 0, 128), MC(c), OP.mult)
         else:
             act(SP(c), X("cn", 0, 128), 0.0, MC(c))
-    tt(X("rb", 0, 512), X("pa", 0, 512), X("km", 0, 512), OP.mult)
-    tt(X("off", 0, 32), X("pb", 0, 32), X("vl", 0, 32), OP.min)
-    ts(X("off16", 0, 32), X("off", 0, 32), BIG + 16.0, OP.add)
     act(X("sb", 0, 384), numbers("bl16", 0, 24, V))
     show("num", "sb", "sp")
-    act(X("sp", mine, mine + C), X("sb", C * r, C * r + C))
 
     for j in range(4):
         a, b = 512 * j, 512 * j + 512
+        if j in BOTH:
+            mm(X(BOTH[j], 0, 512), X("selq", 0, 128, 1, 0, 16), X("wsb", a, b, 1, 0, 16))
+            act(X("p0", a, b), IX("xf", Z, "nb16", 32 * j, 32 * j + 32))
         act(X("g1", a, b), IX("xf", Z, "nb16", 128 + 32 * j, 160 + 32 * j))
+        if j == 0:
+            act(X("sp", mine, mine + C), X("sb", C * r, C * r + C))
+
+    def first(j):
+        a, b = 512 * j, 512 * j + 512
+        if j in BOTH:
+            tt(X("p0", a, b), X("p0", a, b), X(BOTH[j], 0, 512), OP.mult)
+        else:
+            tt(X("p0", a, b), IX("xf", Z, "nb16", a // 16, b // 16), X("wr", a, b), OP.mult)
+
+    def second(j):
+        a, b = 512 * j, 512 * j + 512
+        tt(X("psw", a, b), X("g1", a, b), X("psw", a, b), OP.mult)
+
+    nc = SHARE["cm"]
+    first(0)
+    first(1)
+    second(0)
     for j in range(4):
         a, b = 512 * j, 512 * j + 512
-        tt(X("p0", a, b), IX("xf", Z, "nb16", a // 16, b // 16), X("wr", a, b), OP.mult)
-        tt(X("psw", a, b), X("g1", a, b), X("psw", a, b), OP.mult)
+        if j < 3:
+            second(j + 1)
+        else:
+            tt(X("off", 0, 32), X("pb", 0, 32), X("vl", 0, 32), OP.min)
         tt(X("sw", a, b), X("p0", a, b), X("psw", a, b), OP.add)
+        if j < 2:
+            first(j + 2)
+        if j == 1:
+            act(X("cmr", 0, nc), numbers("mate", 0, nc // 16, Z + 16))
         if j == 3:
+            ts(X("off16", 0, 32), X("off", 0, 32), BIG + 16.0, OP.add)
             cp(X("sst", 0, 192), IX("sw", V, "bl16", 0, 12))
             act(X("sst", 192, 384), IX("sw", V, "bl16", 12, 24))
             show("s", "sst", "sw")
             act(X("sw", mine, mine + C), X("sst", C * r, C * r + C))
-        where(X("p0", a, b), X("sw", a, b), [[1, 512]], 0, 0)
+        if j >= KEPT:
+            where(X("p0", a, b), X("sw", a, b), [[1, 512]], 0, 0)
+    if nc < V:
+        act(X("cmr", nc, V), numbers("mate", nc // 16, 128, Z + 16))
+    for j in range(KEPT):
+        act(X("psw", 512 * j, 512 * j + 512), X("sw", 512 * j, 512 * j + 512))
 
+    tt(X("rb", 0, 512), X("pa", 0, 512), X("km", 0, 512), OP.mult)
     o = IX("inv", 2688, "off16", 0, 32)
     add("V", lambda e: e.tensor_copy(out=o[0], in_=T.rb[:, :]), rg(X("inv", 0, 2688)), rg(X("rb", 0, 512), X("off16", 0, 32)))
-    for b in range(16):
-        for i in range(4):
-            mm(X("pa", b, 128, 16), X("inv", 16 + b - i, 16 + b - i + V - 15, 16), X("seli", 8 * i, 8 * i + 8), i == 0, i == 3, tag="inv")
-    act(X("g1", 0, V), numbers("mate", 0, 128, Z + 16))
-    act(X("ivt", 0, 128), X("pa", 0, 128))
+    mm(X("pa", 0, 512), X("zero", 0, 128), X("km", 0, 512), True, False, tag="inv")
+    for d in range(-3, 16):
+        o = T.pa[:, :, d + 3:d + 7], rg(X("pa", 0, 512))
+        mm(o, X("inv", 16 + d, 16 + d + V - 15, 16), X("seli", 0, 32), False, d == 15, tag="inv")
+    act(X("ivt", 0, 128), (T.pa[:, :, 3:19], rg(X("pa", 0, 512))))
     mm(X("pb", 0, 128), X("ivt", 0, 128), IF)
-    pick("pc", 0, "g1", 0, "g8", 0, 8, "cm")
+    pick("pc", 0, "cmr", 0, "g8", 0, 8, "cm")
+    for j in range(KEPT):
+        act(X("g1", 512 * j, 512 * j + 512), IX("sw", Z + 16, "mate", 32 * j, 32 * j + 32))
     act(X("cmt", 0, 128), X("pc", 0, 128))
     mm(X("pd", 0, 128), X("cmt", 0, 128), IF)
-    for j in range(2):
-        a, b = 1024 * j, 1024 * j + 1024
-        tt(X("tw", 8 + a, 8 + b), IX("sw", Z + 16, "mate", 64 * j, 64 * j + 64), X("p0", a, b), OP.add)
-    cp(X("iv16", 0, 128), X("pb", 0, 128))
-    for j in range(4):
-        o, i = X("p0", 512 * j, 512 * j + 512), IX("tw", V + 8, "iv16", 32 * j, 32 * j + 32)
+    a = 512 * KEPT
+    tt(X("tw", 8 + a, 8 + V), IX("sw", Z + 16, "mate", a // 16, 128), X("p0", a, V), OP.add)
+    for j in range(KEPT):
+        a, b = 512 * j, 512 * j + 512
+        if j == KEPT - 1:
+            cp(X("iv16", 0, 128), X("pb", 0, 128))
+        tt(X("tw", 8 + a, 8 + b), X("g1", a, b), X("psw", a, b), OP.add)
+    for j, (a, b) in enumerate(zip(CUTS, CUTS[1:])):
+        o, i = X("p0", a, b), IX("tw", V + 8, "iv16", a // 16, b // 16)
         if j % 2 == 0:
             cp(o, i)
         else:
             act(o, i)
-        dma("Y", "y%d" % j, T.y[:, 512 * j:512 * j + 512], [], o[0], o[1])
+        dma("Y", "y%d" % j, T.y[:, a:b], [], o[0], o[1])
         if j == 0:
             tt(X("cmv", 0, 128), X("pd", 0, 128), X("cn", 0, 128), OP.min)
             dma("Y", "cm", T.cm[:, :], [], T.cmv[:, :], rg(X("cmv", 0, 128)))

@@ -8,16 +8,16 @@ BIG, MID = 16384.0, 1216.0
 OFFG, OFFC = 128 * 517, 128 * 129
 F32, BF, F16, I32, U16 = "float32", "bfloat16", "float16", "int32", "uint16"
 WIDTHS = {
-    F32: dict(nbf=256, dn=128, bd=128, hlf=256, col=128, ir=128, dif=128, iff=128, own=256, nth=128, tq=128, dm=256, xf=2432,
-              cn=128, vl=32, off=32, sp=2448, sb=384, g1=2048, p0=2048, sw=2448, sst=384, ivt=128, cmt=128, cmv=128, tw=2056,
-              xb=384, g8=8, cmr=2048),
+    F32: dict(dn=128, hlf=256, hlm=256, mb=384, bq=256, col=128, ir=128, iff=128, own=256, nth=128, tq=128, xf=2432, cn=128,
+              vl=16, off=16, sp=2448, sb=384, g1=2048, p0=2048, sw=2448, sst=384, ivt=128, cmr=2048, cmt=128, cmv=128, tw=2056,
+              xb=384, g8=8),
     BF: dict(wsb=2048, xw=2448, xc=2048, nw=2432, bst=384, hb=2048, hl=2432, hst=384, xst=384, gb=8192, wr=2048, ti=256, nti=256,
-             ibn=128, pm=8, sel=48, selw=8, seli=32, wt=128, e0=272, e1=256, ar=288, ar3=256, m2=256, less=256, nr2=256, nr3=256,
-             ww=1024, wv=1024, one=144, ru=256, mk=512, blk=128, lt=128, ltq=128, b0=144, lt0=144, q0=144, wq=576, km=512,
-             rb=512, inv=2688, selr=128, selq=128, bt=128, irb=128, zero=144),
-    F16: dict(hz=256, pz2=256, pz3=256, ih=128),
-    I32: dict(bli=24, nbi=256, ci=64, cj=64, yi=256, zi=256, zj=256),
-    U16: dict(bl16=24, hl16=256, idx=512, mate=128, off16=32, iv16=128, nb16=256),
+             ibn=128, i8=256, cst=384, pm=8, sel=48, selw=8, seli=64, wt=128, e0=272, e1=256, ar=288, ar3=256, m2=128, nr2=256,
+             nr3=256, ww=1024, wv=1024, one=128, zero=128, ru=256, mk=1024, blk=128, lt=128, lte=128, b0=144, lt0=144, q0=144,
+             wq=288, km=256, rb=256, inv=2448, selr=128, selq=128, bt=128, irb=128, left=128),
+    F16: dict(pz2=256, pz3=256, ih=128, hrow=768, g8h=8),
+    I32: dict(bli=24, nbi=256, ci=64, cj=64, yi=256, zi=256, zj=256, bki=48),
+    U16: dict(bl16=24, hl16=256, idx=512, mate=128, off16=16, iv16=128, nb16=256, bk16=48, hb16=48),
 }
 PSUM = {"psw": 2048, "pa": 512, "pb": 512, "pc": 512, "pd": 512}
 SCRATCH = {"fld": ("sbuf", [128, 4, 256], F32)}
@@ -26,14 +26,14 @@ for _d in WIDTHS:
         SCRATCH[_n] = ("sbuf", [128, WIDTHS[_d][_n]], _d)
 for _n in PSUM:
     SCRATCH[_n] = ("psum", [128, 8, 64] if _n == "pa" else [128, PSUM[_n]], F32)
+SHARE = {"nh": 1024, "nl": (256, 768), "r2": (1024, 1024, 768, 768), "r3": (1024, 448, 832), "x": 1408, "sp": 3, "cm": 1024}
+STEPS = (384, 384, 416, 416, 448)
+BOTH = {1: "pd", 0: "pc"}
+CUTS = (2048, 1792, 1408, 1024, 640, 256, 0)
+CM = 2
 EXCH = ["name", "hl", "w1", "w2", "x", "xs", "num", "s"]
-LOADS = ["bl", "nb", "w", "x", "xc", "wr", "y0", "y1", "y2", "y3", "cm"]
+LOADS = ["bl", "nb", "w", "x", "xc", "wr", "cm"] + ["y%d" % _j for _j in range(len(CUTS) - 1)]
 SEMAPHORES = ["cV", "cS", "cP", "cG"] + ["d_" + k for k in LOADS] + ["a_" + k for k in EXCH] + ["l_" + k for k in EXCH]
-SHARE = {"nh": 1024, "nl": 512, "r2": (1024, 1024, 768, 768), "r3": (1024, 704), "x": 1408, "sp": 6, "cm": 1536}
-STEPS = (128, 256, 512, 576, 576)
-BOTH = {3: "pc"}
-KEPT = 2
-CUTS = (0, 512, 1024, 1536, 2048)
 
 
 def engine_plan(topo, src, cores):
@@ -136,11 +136,11 @@ def rank_program(g, core, T, topo):
     def cp(out, a, tag=None):
         add("V", lambda e: e.tensor_copy(out=out[0], in_=a[0]), rg(out), rg(a), tag=tag)
 
-    def act(out, a, bias=0.0, scale=1.0, tag=None):
+    def act(out, a, bias=0.0, scale=1.0, tag=None, func=AF.Identity):
         if isinstance(bias, float) and isinstance(scale, float) and bias == 0.0 and scale == 1.0:
-            f = lambda e: e.activation(out=out[0], in_=a[0], func=AF.Identity)
+            f = lambda e: e.activation(out=out[0], in_=a[0], func=func)
         else:
-            f = lambda e: e.activation(out=out[0], in_=a[0], func=AF.Identity, bias=sc(bias), scale=sc(scale))
+            f = lambda e: e.activation(out=out[0], in_=a[0], func=func, bias=sc(bias), scale=sc(scale))
         add("S", f, rg(out), rg(a, bias, scale), tag=tag)
 
     def mm(out, lhsT, rhs, start=True, stop=True, tag=None):
@@ -199,130 +199,145 @@ def rank_program(g, core, T, topo):
         act(X(dst, a + n, a + V), IX(win, w, offs, o + n // 16, o + 128))
 
     IB, TI, IH, IF = X("ti", 0, 128), X("ti", 0, 256), X("ih", 0, 128), X("iff", 0, 128)
-    M8, TX, PW, DC = 0, 8, 12, 16
-    K0, S8, SA, BA, SIDEB, WG, WC, W64, WI, QW = (col(j) for j in range(20, 30))
-    SIDEA, B4, QM = col(56), col(57), 58
+    ONE, ZERO, G8, DIAG = X("one", 0, 128), X("zero", 0, 128), X("g8", 0, 8), [[-1, 128]]
+    M8, TX, PW, DC, QM = 0, 8, 12, 16, 48
+    K0, S8, SA, BA, SIDEA, SIDEB, WG, WC, W64, QW = (col(j) for j in range(20, 30))
+    B4 = col(QM)
 
     def MC(x):
-        return col(32 + (x - 8) % 16)
+        return col(32 + x)
+
+    def diagonal(out, value):
+        where(out, ZERO, DIAG, 0, 1, OP.not_equal, value)
 
     dma("Y", "bl", T.bli[:, :], rg(X("bli", 0, 24)), T.bl[:, :], [])
     dma("S", "nb", T.nbi[:, :], rg(X("nbi", 0, 256)), T.nb[:, :], [])
     for d in range(2):
         dma("Y", "w", T.wsb[8 * d:8 * d + 8, :], rg(X("wsb", 0, V, 1, 8 * d, 8 * d + 8)), T.w[:, V * d:V * d + V], [])
 
-    iota(X("ci", 0, 24), [[-1, 24]], 32, 1, True)
+    iota(X("ci", 0, 24), [[-1, 24]], 40, 1, True)
     iota(X("ir", 0, 128), [[1, 128]], 0, 0)
-    iota(X("ci", 24, 32), [[-16, 8]], 0, 1, True)
-    iota(X("dif", 0, 128), [[1, 128]], 0, -1)
-    iota(X("ci", 32, 36), [[-4, 4]], 16, 1, True)
-    for x in range(4):
-        add("V", lambda e, x=x: e.memset(T.col[:, PW + x:PW + x + 1], 64.0 ** -x), rg(col(PW + x)), [])
+    iota(ZERO, [[0, 128]], 0, 0)
+    PM = X("pm", 0, 8, 1, 0, 16)
+    where(PM, X("zero", 0, 8, 1, 0, 16), [[-1, 8]], -8, 1, OP.not_equal, 1.0)
+    where(PM, PM, [[-1, 8]], 0, 1, OP.not_equal, -1.0)
+    iota(X("ci", 24, 28), [[-4, 4]], 16, 1, True)
+    diagonal(IB, 1.0)
+    iota(X("ci", 32, 40), [[-16, 8]], 0, 1, True)
+
+    def fill(x):
+        add("V", lambda e: e.memset(T.col[:, PW + x:PW + x + 1], 64.0 ** -x), rg(col(PW + x)), [])
+
+    fill(0)
+    fill(1)
     ts(X("cj", 0, 8), X("ci", 0, 8), 7, OP.bitwise_and)
+    fill(2)
     ts(col(M8, 8), X("cj", 0, 8), 0.0, OP.is_equal)
-    cp(X("irb", 0, 128), X("ir", 0, 128))
+    fill(3)
+    act(X("irb", 0, 128), X("ir", 0, 128))
     ts(K0, col(M8 + 3), 2.0, OP.mult, col(M8 + 1), OP.add)
     ts(col(PW, 4), col(PW, 4), col(M8 + 4), OP.mult)
-    ts(col(TX, 4), X("ir", 0, 4), col(M8 + 2), OP.mult)
     ts(K0, K0, 2.0 * r, OP.mult)
+    ts(col(TX, 4), X("ir", 0, 4), col(M8 + 2), OP.mult, K0, OP.add)
     tt(col(TX, 4), col(TX, 4), col(PW, 4), OP.add)
-    act(col(DC + 1), col(M8 + 1), col(M8 + 3))
+    act(S8, col(M8 + 4), 1.0, -0.875)
     act(col(DC + 2), col(M8 + 3), 0.0, 2.0)
     act(col(DC + 3), col(M8 + 3), col(M8 + 1), 3.0)
-    act(S8, col(M8 + 4), 1.0, -0.875)
-    ts(col(TX, 4), col(TX, 4), K0, OP.add)
+    act(col(DC + 1), col(M8 + 1), col(M8 + 3))
     for x in range(4):
-        ts(X("nw", x, 512, 4), X("irb", 0, 128), col(M8), OP.mult, col(TX + x), OP.add, tag="nw")
-    act(X("nw", 512, 1024), X("nw", 0, 512), col(DC + 1))
-    for j in (2, 3):
-        ts(X("nw", 512 * j, 512 * j + 512), X("nw", 0, 512), S8, OP.mult, col(DC + j), OP.add)
+        if x < 3:
+            ts(X("nw", x, 512, 4), X("irb", 0, 128), col(M8), OP.mult, col(TX + x), OP.add, tag="nw")
+        else:
+            o = T.nw[:, x:512:4], [("nw3", 0, 128, 0, 512)]
+            act(o, X("irb", 0, 128), col(TX + x), col(M8))
+    NW = T.nw[:, 0:512], rg(X("nw", 0, 512), ("", [("nw3", 0, 128, 0, 512)]))
+    ts(X("nw", 1024, 1536), NW, S8, OP.mult, col(DC + 2), OP.add)
+    act(X("nw", 512, 768), (T.nw[:, 0:256], NW[1]), col(DC + 1))
+    ts(X("nw", 1536, 2048), NW, S8, OP.mult, col(DC + 3), OP.add)
+    ts(X("nw", 768, 1024), (T.nw[:, 256:512], NW[1]), col(DC + 1), OP.add)
     cp(X("bl16", 0, 24), X("bli", 0, 24))
     cp(X("bst", 0, 192), IX("nw", V, "bl16", 0, 12))
     act(X("bst", 192, 384), IX("nw", V, "bl16", 12, 24))
     show("name", "bst", "nw")
     act(X("nw", mine, mine + C), X("bst", C * r, C * r + C))
 
-    ts(IB, X("dif", 0, 128), 0.0, OP.is_equal)
-    tt(X("pm", 0, 8, 1, 0, 16), X("ti", 8, 16, 1, 0, 16), X("ti", 0, 8, 1, 0, 16), OP.subtract)
     for b in range(16):
-        mm(X("pa", b, 128, 16), X("wsb", b, V, 16, 0, 16), X("pm", 0, 8, 1, 0, 16), tag="wt")
-    cp(X("nbf", 0, 256), X("nbi", 0, 256))
+        mm(X("pa", b, 128, 16), X("wsb", b, V, 16, 0, 16), PM, tag="wt")
     ts(X("bt", 0, 128), X("pa", 0, 128), 0.0, OP.is_gt)
     mm(X("pb", 0, 128), X("bt", 0, 128), IB)
-    tt(X("dn", 0, 128), X("nbf", 128, 256), X("nbf", 0, 128), OP.subtract)
-    ts(X("cj", 8, 24), X("ci", 8, 24), 15, OP.bitwise_and)
-    tt(X("bd", 0, 128), X("pb", 0, 128), X("dn", 0, 128), OP.mult)
-    ts(X("cj", 24, 32), X("ci", 24, 32), 4, OP.arith_shift_right)
-    ts(X("cj", 32, 33), X("ci", 0, 1), 8, OP.bitwise_and)
-    tt(X("hlf", 0, 128), X("nbf", 0, 128), X("bd", 0, 128), OP.add)
-    ts(X("cj", 33, 34), X("ci", 0, 1), 12, OP.bitwise_and)
-    ts(X("cj", 34, 38), X("ci", 32, 36), 12, OP.bitwise_and)
-    cp(X("hl16", 0, 128), X("hlf", 0, 128))
-    ts(col(32, 30), X("cj", 8, 38), 0.0, OP.is_equal)
-    tt(X("hlf", 128, 256), X("nbf", 128, 256), X("bd", 0, 128), OP.subtract)
+    ts(X("cj", 32, 48), X("ci", 8, 24), 15, OP.bitwise_and)
+    ts(X("cj", 48, 52), X("ci", 24, 28), 2, OP.logical_shift_right, 3, OP.bitwise_and)
+    ts(X("bki", 24, 48), X("bli", 0, 24), 15, OP.bitwise_and)
+    ts(X("bki", 0, 24), X("bli", 0, 24), 4, OP.logical_shift_right)
+    ts(col(32, 20), X("cj", 32, 52), 0.0, OP.is_equal)
+    cp(X("bk16", 0, 48), X("bki", 0, 48))
+    tt(X("dn", 0, 128), X("nbi", 128, 256), X("nbi", 0, 128), OP.subtract)
+    ts(X("cj", 56, 64), X("ci", 32, 40), 4, OP.arith_shift_right)
+    tt(X("pb", 0, 128), X("pb", 0, 128), X("dn", 0, 128), OP.mult)
+    ts(X("g8h", 0, 8), X("cj", 56, 64), 0.0, OP.is_equal)
+    tt(X("hlf", 0, 128), X("nbi", 0, 128), X("pb", 0, 128), OP.add)
+    tt(X("hlf", 128, 256), X("nbi", 128, 256), X("pb", 0, 128), OP.subtract)
+    ts(G8, X("cj", 56, 64), 0.0, OP.is_equal)
+    act(X("mb", 0, 384), IX("col", 48, "bk16", 24, 48, 32))
+    for K in range(2):
+        act(X("hlm", 128 * K, 128 * K + 128), X("hlf", 128 * K, 128 * K + 128), -MID)
     act(SA, MC(4), B4, 2.0 ** 21)
     act(BA, B4, 0.0, 128.0)
-    act(SIDEB, SIDEA, 1.0, -1.0)
-    act(X("g8", 0, 8), col(48, 8))
-    cp(X("hl16", 128, 256), X("hlf", 128, 256))
-    G8 = X("g8", 0, 8)
-    ts(WG, col(M8 + 3), 512.0, OP.mult, col(M8 + 2), OP.add)
-    ts(WC, col(M8 + 1), 128.0, OP.mult, col(M8), OP.add)
-    ts(WG, col(M8), 4.0, OP.mult, WG, OP.add)
-    ts(X("sel", 16, 24), G8, WC, OP.mult, SIDEA, OP.mult)
-    ts(X("sel", 24, 32), G8, MC(4), OP.mult, 2.0 ** -20, OP.mult)
-    ts(X("sel", 32, 40), G8, WC, OP.mult, SIDEB, OP.mult)
-    ts(X("sel", 40, 48), G8, MC(12), OP.mult, 2.0, OP.mult)
-    ts(X("sel", 0, 8), G8, WG, OP.mult, SIDEA, OP.mult)
-    ts(X("sel", 8, 16), G8, WG, OP.mult, SIDEB, OP.mult)
-    ts(X("cj", 38, 39), X("ci", 0, 1), 15, OP.bitwise_and)
-    ts(QW, X("cj", 38, 39), 8.0, OP.add)
-    cp(X("nb16", 0, 256), X("nbi", 0, 256))
+    act(WG, col(M8 + 3), col(M8 + 2), 512.0)
+    act(WC, col(M8 + 1), col(M8), 128.0)
+    act(SIDEA, col(QM), col(QM + 1))
+    act(SIDEB, col(QM + 2), col(QM + 3))
+    act(WG, col(M8), WG, 4.0)
+    diagonal(IF, 1.0)
+    for K, bank in enumerate(("pc", "pd")):
+        tt(X("hrow", 384 * K, 384 * K + 384), IX("hlm", 128 * K + 128, "bk16", 0, 24, 128 * K), X("mb", 0, 384), OP.mult)
+        for b in range(16):
+            mm(X(bank, b, 128, 16, 0, 24), X("hrow", 384 * K + b, 384 * K + 384, 16), X("g8h", 0, 8), tag="border")
+        act(X("bq", 128 * K, 128 * K + 128, 1, 0, 24), X(bank, 0, 128, 1, 0, 24), MID)
+        if K == 0:
+            act(col(54), WC, 0.0, SIDEA)
+            act(col(55), MC(4), 0.0, 2.0 ** -20)
+            act(col(56), WC, 0.0, SIDEB)
+            act(col(57), MC(12), 0.0, 2.0)
+    for K, bank in enumerate(("pb", "pc")):
+        mm(X(bank, 0, 24), X("bq", 128 * K, 128 * K + 128, 1, 0, 24), X("iff", 0, 24, 1, 0, 24))
+    cp(X("hl16", 0, 256), X("hlf", 0, 256))
+    cp(X("hb16", 0, 24), X("pb", 0, 24))
+    iota(ONE, [[0, 128]], 1, 0)
     iota(X("own", 0, 128), [[0, 8], [1, 16]], V * r + OFFG, 16)
     iota(X("own", 128, 256), [[0, 8], [1, 16]], V * r, 16)
-    iota(X("one", 0, 144), [[0, 144]], 1, 0)
+    for c0, value in ((0, 2.0), (64, 1.0)):
+        where(X("wt", c0, c0 + 64), X("zero", 0, 64), [[-1, 64]], 0, 1, OP.not_equal, value)
+        where(X("wt", c0, c0 + 64), X("wt", c0, c0 + 64), [[-1, 64]], -64, 1, OP.not_equal, 8.0 * value)
     iota(X("e0", 256, 272), [[0, 16]], 0, 0)
-    iota(X("ar", 128, 144), [[0, 16]], 0, 0)
-    iota(X("ar", 272, 288), [[0, 16]], 0, 0)
-    for n in ("b0", "lt0", "q0", "zero"):
-        iota(X(n, 0, 144), [[0, 144]], 0, 0)
-    iota(X("wq", 0, 576), [[0, 576]], 0, 0)
+    HZ, ROW = (X("psw", 1408, 1536), X("psw", 1920, 2048)), X("one", 0, 128, 1, 0, 1)
+    for K in range(2):
+        mm(HZ[K], X("hlm", K * 128, K * 128 + 128), IF)
 
+    ts(X("bst", 0, 192), IX("nw", Z, "hb16", 0, 12), SA, OP.mult, BA, OP.add)
+    act(X("bst", 192, 384), IX("nw", Z, "hb16", 12, 24), BA, SA)
+    cp(X("hb16", 24, 48), X("pc", 0, 24))
+    tt(X("hst", 0, 384), IX("nw", Z, "hb16", 24, 48), X("bst", 0, 384), OP.max)
+    show("hl", "hst", "hl")
     a = 0
     for n in STEPS:
         act(X("hb", a, a + n), IX("nw", Z, "hl16", a // 16, (a + n) // 16), BA, SA)
         tt(X("hl", a, a + n), IX("nw", Z, "hl16", 128 + a // 16, 128 + (a + n) // 16), X("hb", a, a + n), OP.max)
         a += n
-    cp(X("hst", 0, 192), IX("hl", V, "bl16", 0, 12))
-    act(X("hst", 192, 384), IX("hl", V, "bl16", 12, 24))
-    show("hl", "hst", "hl")
     act(X("hl", mine, mine + C), X("hst", C * r, C * r + C))
-
+    act(col(52), WG, 0.0, SIDEA)
+    act(col(53), WG, 0.0, SIDEB)
+    for f in (2, 3, 4, 5, 0, 1):
+        act(X("sel", 8 * f, 8 * f + 8), G8, 0.0, col(52 + f))
     pick("pa", 0, "hl", 0, "sel", 16, 48, "own")
     pick("pb", 0, "hl", 0, "sel", 0, 16, "own")
-    ts(IF, X("dif", 0, 128), 0.0, OP.is_equal)
-    ts(IH, X("dif", 0, 128), 0.0, OP.is_equal)
-    ts(X("ti", 128, 256), X("dif", 0, 128), 0.0, OP.is_gt)
-    for K in range(2):
-        mm(X("pc", K * 128, K * 128 + 128), X("hlf", K * 128, K * 128 + 128), IF)
-    act(X("wt", 0, 64), X("ti", 64, 128), 0.0, 8.0)
-    act(F(0, 1, 0, 128), X("pa", 256, 384), float(OFFC))
-    act(F(1, 2, 0, 256), X("pa", 0, 256))
-    act(F(0, 1, 128, 256), X("pa", 384, 512))
-    tt(X("wt", 64, 128), X("wt", 0, 64), X("ti", 0, 64), OP.add)
-    ts(X("wt", 0, 64), X("wt", 64, 128), 2.0, OP.mult)
-    for K in range(2):
-        mm(X("pd", K * 128, K * 128 + 128), F(K, K + 1, 0, 128), IF)
-    ts(W64, MC(1), 64.0, OP.mult, MC(0), OP.add)
-    tt(X("less", 0, 256), X("pb", 0, 256), X("own", 0, 256), OP.is_lt)
-    ts(W64, MC(2), 64.0 ** 2, OP.mult, W64, OP.add)
-    ts(X("hz", 0, 256), X("pc", 0, 256), MID, OP.subtract)
-    ts(W64, MC(3), 64.0 ** 3, OP.mult, W64, OP.add)
-    ts(X("idx", 0, 256), X("pd", 0, 256), float(OFFC), OP.subtract)
-    ts(X("selw", 0, 8), G8, W64, OP.mult)
-    ONE, GRP = X("one", 0, 128), [[-16, 8], [0, 16]]
-    where(X("blk", 0, 128), ONE, GRP, 0, 1)
-    where(X("blk", 0, 128), X("blk", 0, 128), [[16, 8], [0, 16]], 15, -1)
+    LESS = 768
+    diagonal(X("i8", 0, 128), 8.0)
+    diagonal(X("i8", 128, 256), -8.0)
+    iota(X("cst", 0, 384, 1, 0, 1), [[1, 3], [0, 128]], 6, 0)
+    iota(X("ar", 128, 144), [[0, 16]], 0, 0)
+    iota(X("ar", 272, 288), [[0, 16]], 0, 0)
+    where(X("ti", 128, 256), ZERO, DIAG, 0, 1, OP.is_ge, 1.0)
 
     def pack(bank, parts, first=True, last=True):
         for c in range(4):
@@ -333,58 +348,63 @@ def rank_program(g, core, T, topo):
 
     share("gb", 0, "hl", Z, "hl16", 0, SHARE["nh"])
     pick("pc", 0, "gb", 0, "sel", 0, 32, "nh")
-    n = SHARE["nl"]
-    act(X("gb", V + n, 2 * V), IX("hl", Z, "hl16", 128 + n // 16, 256))
-    cp(X("gb", V, V + n // 2), IX("hl", Z, "hl16", 128, 128 + n // 32))
+    n1, n2 = SHARE["nl"]
+    act(F(0, 1, 0, 128), X("pa", 256, 384), float(OFFC))
+    act(F(1, 2, 0, 256), X("pa", 0, 256))
+    act(F(0, 1, 128, 256), X("pa", 384, 512))
+    act(X("gb", V + n2, 2 * V), IX("hl", Z, "hl16", 128 + n2 // 16, 256))
+    tt(X("psw", LESS, LESS + 256), X("pb", 0, 256), X("own", 0, 256), OP.is_lt)
+    cp(X("gb", V, V + n1), IX("hl", Z, "hl16", 128, 128 + n1 // 16))
     T1, VI = X("e0", 0, 128), X("e0", 128, 256)
     tt(X("e0", 0, 256), X("pc", 0, 256), X("own", 0, 256), OP.is_equal)
     pack("pd", [("e0", 0, 0), ("e0", 128, 64)])
-    cp(X("gb", V + n // 2, V + n), IX("hl", Z, "hl16", 128 + n // 32, 128 + n // 16))
+    for K in range(2):
+        mm(X("pb", K * 128, K * 128 + 128), F(K, K + 1, 0, 128), IF)
+    DM = 128
+    tt(X("psw", DM, DM + 256), X("pc", 256, 512), F(1, 2, 0, 256), OP.subtract)
     cp(X("ww", 256 * r, 256 * r + 256), X("pd", 0, 256))
     spread("w1", "ww")
+    cp(X("gb", V + n1, V + n2), IX("hl", Z, "hl16", 128 + n1 // 16, 128 + n2 // 16))
     pick("pa", 0, "gb", V, "sel", 0, 32, "nl")
+    ts(X("idx", 0, 256), X("pb", 0, 256), float(OFFC), OP.subtract)
     act(F(2, 3, 0, 256), X("pc", 256, 512))
     mm(X("pb", 0, 128), F(2, 3, 0, 128), IF)
-    UL, LL, LH = X("psw", 1024, 1152), X("psw", 1152, 1280), X("psw", 1280, 1408)
-    tt(X("tq", 0, 128), T1, VI, OP.is_ge)
-    tt(X("dm", 0, 256), X("pc", 256, 512), F(1, 2, 0, 256), OP.subtract)
-    act(LH, X("tq", 0, 128), 0.0, 4.0)
-    tt(X("e1", 0, 256), X("pa", 0, 256), X("own", 0, 256), OP.is_equal)
-    act(F(3, 4, 0, 256), X("pa", 256, 512))
-    mm(X("pb", 128, 256), F(3, 4, 0, 128), IF)
-    act(UL, X("e1", 0, 128), 6.0, -7.0)
-    tt(X("nth", 0, 128), X("e1", 0, 128), X("e1", 128, 256), OP.max)
-    tt(X("nth", 0, 128), X("nth", 0, 128), T1, OP.is_gt)
-    act(LL, X("nth", 0, 128), 4.0, -5.0)
+    act(W64, MC(1), MC(0), 64.0)
+    act(W64, MC(2), W64, 64.0 ** 2)
+    act(W64, MC(3), W64, 64.0 ** 3)
+    act(X("selw", 0, 8), G8, 0.0, W64)
     for K in range(2):
-        tt(X("dm", 128 * K, 128 * K + 128), X("dm", 128 * K, 128 * K + 128), VI, OP.mult)
-    ts(X("idx", 256, 512), X("pb", 0, 256), float(OFFC), OP.subtract)
+        tt(X("psw", DM + 128 * K, DM + 128 * K + 128), X("psw", DM + 128 * K, DM + 128 * K + 128), VI, OP.mult)
+    act(F(3, 4, 0, 256), X("pa", 256, 512))
+    tt(X("e1", 0, 256), X("pa", 0, 256), X("own", 0, 256), OP.is_equal)
+    mm(X("pb", 128, 256), F(3, 4, 0, 128), IF)
+    UL, LL, LH = X("psw", 1024, 1152), X("psw", 1152, 1280), X("psw", 1280, 1408)
+    P8, N8, EA, EB = X("i8", 0, 128), X("i8", 128, 256), X("e1", 0, 128), X("e1", 128, 256)
+    mm(X("psw", 1024, 1408), ROW, X("cst", 0, 384, 1, 0, 1), True, False, tag="bound")
+    terms = ((LH, P8, T1), (LH, N8, VI), (LL, P8, T1), (LL, P8, T1), (UL, N8, EA), (LL, N8, EA), (LL, N8, EB))
+    for i, (o, m, e) in enumerate(terms):
+        mm(o, m, e, False, i == len(terms) - 1, tag="bound")
 
     words = [("ww", 0, 128, 0, 1024)]
     dma("Y", "x", T.xw[:, 0:V], rg(X("xw", 0, V)), T.x[:, :], words)
     dma("Y", "xc", T.xc[:, :], rg(X("xc", 0, V)), T.x[:, :], [])
+    a = 512 * len(BOTH)
     for c in range(16):
-        dma("Y", "wr", T.wr[c:128:16, :], [("wr", 16 * k + c, 16 * k + c + 1, 0, V) for k in range(8)], T.w[:, 0:V], [])
-    BLK, QUAD = X("blk", 0, 128), [[-4, 32], [0, 4]]
-    where(X("lt", 0, 128), BLK, [[1, 128]], 0, -1, OP.is_gt)
-    where(X("lt", 0, 128), X("lt", 0, 128), [[1, 128]], 0, -1, OP.not_equal, -BIG)
-    where(X("ltq", 0, 128), ONE, QUAD, 0, 1)
-    where(X("ltq", 0, 128), X("ltq", 0, 128), [[1, 128]], 0, -1)
-    where(X("ltq", 0, 128), X("ltq", 0, 128), [[1, 128]], 0, -1, OP.not_equal, -8.0)
-    B0 = X("b0", 12, 140)
-    where(B0, BLK, [[0, 8], [-1, 16]], 3, 0)
-    where(X("lt0", 12, 140), B0, [[16, 8], [4, 16]], 0, -1, OP.is_gt)
-    where(X("q0", 12, 140), B0, [[-16, 8], [-4, 16]], 0, 1)
-    where(X("q0", 12, 140), X("q0", 12, 140), [[16, 8], [4, 16]], 3, -1)
-    SELR = X("selr", 0, 128, 1, 0, 16)
+        dma("Y", "wr", T.wr[c:128:16, a:V], [("wr", 16 * k + c, 16 * k + c + 1, 0, V) for k in range(8)], T.w[:, a:V], [])
+    diagonal(X("ibn", 0, 128), -MID)
+    diagonal(X("nti", 0, 128), -1.0)
+    where(X("nti", 128, 256), ZERO, DIAG, 0, 1, OP.is_ge, -1.0)
+    iota(X("wq", 0, 288), [[0, 288]], 0, 0)
+    iota(X("km", 0, 256), [[-1, 128], [0, 2]], 127, 0)
+    SELR, SELQ = X("selr", 0, 128, 1, 0, 16), X("selq", 0, 128, 1, 0, 16)
     where(SELR, X("one", 0, 128, 1, 0, 16), [[-16, 8], [0, 16]], -128, 16, OP.is_equal)
-    where(X("selq", 0, 128, 1, 0, 16), X("one", 0, 128, 1, 0, 16), [[-16, 8], [0, 16]], 0, 16, OP.is_equal)
-    iota(X("km", 0, 512), [[1, 128], [0, 4]], 0, 0)
-    iota(X("vl", 0, 32), [[16, 32]], V - int(BIG), 1)
+    where(SELQ, X("one", 0, 128, 1, 0, 16), [[-16, 8], [0, 16]], 0, 16, OP.is_equal)
     iota(X("xw", Z, Z + 16), [[0, 16]], 0, 0)
-    iota(X("sw", Z, Z + 16), [[0, 16]], 0, 0)
-    iota(X("sp", Z, Z + 16), [[0, 16]], int(BIG) // 16, 0)
-    iota(X("tw", 0, 8), [[0, 8]], 0, 0)
+    BLK = X("blk", 0, 128)
+    where(BLK, ONE, [[-16, 8], [0, 16]], 0, 1)
+    where(BLK, BLK, [[16, 8], [0, 16]], 15, -1)
+    where(X("lt", 0, 128), BLK, [[1, 128]], 0, -1, OP.is_gt)
+    where(X("lt", 0, 128), X("lt", 0, 128), [[1, 128]], 0, -1, OP.not_equal, BIG)
 
     def ask(L, win, n):
         share("gb", L * V, win, 1024, "idx", L * 128, n)
@@ -403,7 +423,9 @@ def rank_program(g, core, T, topo):
     for L in range(3):
         ask(L, "ww", n[L])
         answer(L, ("pc", "pc", "pd")[L], 128 * (L % 2))
-    mm(X("pa", 0, 256), X("zero", 0, 128), TI, True, False, tag="pack")
+        if L == 0:
+            ts(X("idx", 256, 512), X("pb", 0, 256), float(OFFC), OP.subtract)
+    mm(X("pa", 0, 256), ZERO, TI, True, False, tag="pack")
     pack("pa", [("e0", 0, 0)], False, False)
     tt(X("yi", 0, 256), X("pc", 0, 256), F(0, 2, 128, 256), OP.mult)
     ask(3, "ww", n[3])
@@ -419,110 +441,127 @@ def rank_program(g, core, T, topo):
     tt(ARL, X("zj", 128, 256), X("psw", TH + 256, TH + 384), OP.is_gt)
     pack("pa", [("ar", 0, 0)], False, False)
     pack("pa", [("ar", 144, 64)], False, True)
-    tt(X("tq", 0, 128), ARH, ARL, OP.add)
+    tt(F(2, 3, 0, 256), F(1, 2, 0, 256), X("psw", DM, DM + 256), OP.add)
     cp(X("wv", 256 * r, 256 * r + 256), X("pa", 0, 256))
     spread("w2", "wv")
 
-    tt(F(2, 3, 0, 256), F(1, 2, 0, 256), X("dm", 0, 256), OP.add)
     mm(X("pb", 0, 128), F(2, 3, 0, 128), IF)
+    NEG = X("nti", 0, 128)
+    mm(X("pd", 0, 128), ROW, ROW, True, False, tag="free")
+    mm(X("pd", 0, 128), NEG, ARH, False, False, tag="free")
+    mm(X("pd", 0, 128), NEG, ARL, False, True, tag="free")
     act(X("xst", 0, 384), IX("xc", V, "bl16", 0, 24))
     show("x", "xst", "xw")
     act(X("xw", mine, mine + C), X("xst", C * r, C * r + C))
-    act(X("nth", 0, 128), X("tq", 0, 128), -1.0, 5.0)
-    act(X("ibn", 0, 128), IB, 0.0, -MID)
-    act(X("nti", 0, 256), TI, 0.0, -1.0)
-    iota(X("inv", 0, 2688), [[0, 2688]], 0, 0)
-    for c in range(4):
-        act(col(64 + c), MC(4 + c), MC(c), 16.0)
-    act(col(76, 4), col(QM, 4), 0.0, QW)
-    act(col(72), col(QM + 1), 0.0, -1.0 / BIG)
-    act(col(73), B4, 0.0, -1.0 / BIG)
-    for c in range(4):
-        act(X("seli", c, 32, 4), G8, 0.0, col(64 + c), tag="wq")
-        act(X("wq", 144 * c + 8, 144 * c + 136, 16), G8, 0.0, col(QM + c), tag="wq")
-        act(X("wq", 144 * c + 4, 144 * c + 132, 16), G8, 0.0, col(76 + c), tag="wq")
-    act(X("km", 0, 512), X("km", 0, 512), col(73), col(72))
-    ts(X("idx", 256, 384), X("pb", 0, 128), float(OFFC), OP.subtract)
+    act(col(72), SIDEB, 0.0, -1.0 / BIG)
+    act(col(73), SIDEA, 0.0, -1.0 / BIG)
+    act(col(74), SIDEB, 1.0, 15.0)
+    act(X("km", 0, 256), X("km", 0, 256), col(73), col(72))
+    act(col(64, 8), col(M8, 8), 0.0, col(74))
+    cp(IH, IB)
     tt(X("m2", 0, 128), T1, ARH, OP.add)
-    tt(X("psw", 1152, 1280), X("psw", TH, TH + 128), X("nth", 0, 128), OP.max)
-    tt(X("psw", 1024, 1152), X("psw", TH + 128, TH + 256), X("nth", 0, 128), OP.max)
-
-    def mates(h, l, pz, first):
-        for K, m in enumerate((h, l)):
-            tt(X(pz, 128 * K, 128 * K + 128), m, X("hz", 128 * K, 128 * K + 128), OP.mult)
-            mm(X("psw", 0, 128), m, X("ibn", 0, 128), first and K == 0, False, tag="mate")
-            mm(X("psw", 0, 128), X(pz, 128 * K, 128 * K + 128), IH, False, not first and K == 1, tag="mate")
-
-    def lesser(h, l, nr, first):
-        for K, m in enumerate((h, l)):
-            tt(X(nr, 128 * K, 128 * K + 128), m, X("less", 128 * K, 128 * K + 128), OP.mult)
-            mm(X("psw", 512, 768), X(nr, 128 * K, 128 * K + 128), X("nti", 0, 256), False, not first and K == 1, tag="rep")
-
-    mates(X("m2", 0, 128), ARL, "pz2", True)
-
-    n = SHARE["r3"]
+    ts(X("idx", 256, 384), X("pb", 0, 128), float(OFFC), OP.subtract)
+    tt(F(2, 3, 128, 256), F(2, 3, 128, 256), X("pd", 0, 128), OP.mult)
+    for K, m in enumerate((X("m2", 0, 128), ARL)):
+        tt(X("pz2", 128 * K, 128 * K + 128), m, HZ[K], OP.mult)
+        mm(X("psw", 0, 128), m, X("ibn", 0, 128), K == 0, False, tag="mate")
+        mm(X("psw", 0, 128), X("pz2", 128 * K, 128 * K + 128), IH, False, False, tag="mate")
+    for K, m in enumerate((X("m2", 0, 128), ARL)):
+        tt(X("nr2", 128 * K, 128 * K + 128), m, X("psw", LESS + 128 * K, LESS + 128 * K + 128), OP.mult)
     mm(X("psw", 512, 768), ONE, TI, True, False, tag="rep")
-    lesser(X("m2", 0, 128), ARL, "nr2", True)
-    ask(2, "wv", n[0])
+    for K in range(2):
+        mm(X("psw", 512, 768), X("nr2", 128 * K, 128 * K + 128), X("nti", 0, 256), False, False, tag="rep")
+    ts(QW, X("cj", 32, 33), -1.0, OP.mult, 16.0, OP.add)
+    cp(X("nb16", 0, 256), X("nbi", 0, 256))
+    LTE = X("lte", 0, 128)
+    where(LTE, ONE, [[8, 16], [0, 8]], 7, -1)
+    where(LTE, LTE, [[-8, 16], [0, 8]], 0, 1)
+    where(LTE, LTE, [[1, 128]], 0, -1)
+    where(LTE, LTE, [[1, 128]], 0, -1, OP.not_equal, -16.0)
+    for name in ("b0", "lt0", "q0"):
+        iota(X(name, 0, 14), [[0, 14]], 0, 0)
+    B0 = X("b0", 14, 142)
+    where(B0, BLK, [[0, 8], [-1, 16]], 1, 0)
+    where(X("lt0", 14, 142), B0, [[16, 8], [8, 16]], 0, -1, OP.is_gt)
+    where(X("q0", 14, 142), B0, [[-16, 8], [-8, 16]], 0, 1)
+    where(X("q0", 14, 142), X("q0", 14, 142), [[16, 8], [8, 16]], 7, -1)
+    iota(X("vl", 0, 16), [[16, 16]], V - int(BIG), 1)
+    iota(X("sp", Z, Z + 16), [[0, 16]], 0, 0)
+    iota(X("inv", 0, 2448), [[0, 2448]], 0, 0)
+
+    n0, n1, n2 = SHARE["r3"]
+    ask(2, "wv", n0)
     answer(2, "pc", 0)
-    n1, n2 = n[1] // 2, n[1]
     act(X("gb", 3 * V + n2, 4 * V), IX("wv", 1024, "idx", 384 + n2 // 16, 512))
     cp(X("gb", 3 * V, 3 * V + n1), IX("wv", 1024, "idx", 384, 384 + n1 // 16))
     digit("zj", 0, "pc", 2, 6)
     cp(X("gb", 3 * V + n1, 3 * V + n2), IX("wv", 1024, "idx", 384 + n1 // 16, 384 + n2 // 16))
     answer(3, "pd", 0)
-    A3, L3 = X("ar3", 0, 128), X("ar3", 128, 256)
-    tt(A3, X("zj", 0, 128), X("psw", 1024, 1152), OP.is_gt)
+    A3, L3, TL = X("ar3", 0, 128), X("ar3", 128, 256), X("psw", TH, TH + 128)
+    tt(A3, X("zj", 0, 128), X("psw", TH + 128, TH + 256), OP.is_gt)
     ts(X("nth", 0, 128), X("zj", 0, 128), -2.5, OP.mult, 4.0, OP.add)
-    ts(X("tq", 0, 128), A3, 5.0, OP.mult, -1.0, OP.add)
-    tt(X("psw", 1152, 1280), X("psw", 1152, 1280), X("nth", 0, 128), OP.max)
-    tt(X("pz3", 0, 128), A3, X("hz", 0, 128), OP.mult)
-    tt(X("psw", 1152, 1280), X("psw", 1152, 1280), X("tq", 0, 128), OP.max)
+    act(X("tq", 0, 128), A3, -1.0, 5.0)
+    tt(X("pz3", 0, 128), A3, HZ[0], OP.mult)
+    tt(TL, TL, X("nth", 0, 128), OP.max)
     mm(X("psw", 0, 128), A3, X("ibn", 0, 128), False, False, tag="mate")
     mm(X("psw", 0, 128), X("pz3", 0, 128), IH, False, False, tag="mate")
-    digit("zj", 1, "pd", 3, 6)
-    tt(L3, X("zj", 128, 256), X("psw", 1152, 1280), OP.is_gt)
-    tt(X("pz3", 128, 256), L3, X("hz", 128, 256), OP.mult)
+    tt(X("yi", 128, 256), X("pd", 0, 128), F(3, 4, 128, 256), OP.mult)
+    tt(TL, TL, X("tq", 0, 128), OP.max)
+    ts(X("zj", 128, 256), X("yi", 128, 256), 6, OP.bitwise_and)
+    tt(L3, X("zj", 128, 256), TL, OP.is_gt)
+    tt(X("pz3", 128, 256), L3, HZ[1], OP.mult)
     mm(X("psw", 0, 128), L3, X("ibn", 0, 128), False, False, tag="mate")
     mm(X("psw", 0, 128), X("pz3", 128, 256), IH, False, True, tag="mate")
+    tt(X("nr3", 0, 256), X("ar3", 0, 256), X("psw", LESS, LESS + 256), OP.mult)
+    for c, side in enumerate((SIDEA, SIDEB)):
+        act(col(76 + c), side, 0.0, QW)
+        act(X("wq", 144 * c + 16, 144 * c + 144, 16), G8, 0.0, side, tag="wq")
+        act(X("wq", 144 * c + 8, 144 * c + 136, 16), G8, 0.0, col(76 + c), tag="wq")
+    for j in range(8):
+        act(X("seli", 8 * j, 8 * j + 8), col(64, 8), 0.0, X("g8", j, j + 1))
 
     ts(X("mate", 0, 128), X("psw", 0, 128), float(Z), OP.add)
-    def weights(j):
-        mm(X("psw", 512 * j, 512 * j + 512), SELR, X("wsb", 512 * j, 512 * j + 512, 1, 0, 16))
-
     nx = SHARE["x"]
     hx = (nx + V) // 2
-    tt(X("xf", 0, nx), IX("xw", Z + 16, "mate", 0, nx // 16), X("xc", 0, nx), OP.add)
     for bank, a, b in (("pa", nx, hx), ("pb", hx, V)):
         mm(X(bank, 0, b - a), IB, X("xc", a, b), True, False, tag="gx")
-    weights(2)
+    for K in range(2):
+        mm(X("psw", 512, 768), X("nr3", 128 * K, 128 * K + 128), X("nti", 0, 256), False, K == 1, tag="rep")
     for bank, a, b in (("pa", nx, hx), ("pb", hx, V)):
         act(X("gb", a - nx, b - nx), IX("xw", Z + 16, "mate", a // 16, b // 16))
         mm(X(bank, 0, b - a), IB, X("gb", a - nx, b - nx), False, True, tag="gx")
+    tt(X("xf", 0, nx), IX("xw", Z + 16, "mate", 0, nx // 16), X("xc", 0, nx), OP.add)
     for bank, a, b in (("pa", nx, hx), ("pb", hx, V)):
         act(X("xf", a, b), X(bank, 0, b - a))
-    weights(3)
-    weights(0)
-    lesser(A3, L3, "nr3", False)
-    act(X("xb", 0, 384), IX("xf", V, "bl16", 0, 24))
-    show("xs", "xb", "xf")
-    act(X("xf", mine, mine + C), X("xb", C * r, C * r + C))
-
+        if bank == "pa":
+            act(X("ru", 0, 256), X("psw", 512, 768))
     REP, UP = X("ru", 0, 128), X("ru", 128, 256)
-    cp(X("ru", 0, 256), X("psw", 512, 768))
+    cp(X("xb", 0, 192), IX("xf", V, "bl16", 0, 12))
+    act(X("xb", 192, 384), IX("xf", V, "bl16", 12, 24))
+    show("xs", "xb", "xf")
+    for b, a in zip(CUTS, CUTS[1:]):
+        iota(X("left", a // 16, b // 16), [[0, (b - a) // 16]], (V - a) // 128, 0)
+    iota(X("sw", Z, Z + 16), [[0, 16]], 0, 0)
+    iota(X("tw", V, V + 8), [[0, 8]], 0, 0)
+
+    act(X("xf", mine, mine + C), X("xb", C * r, C * r + C))
+    mm(X("pc", 0, 128), LTE, REP)
     mm(X("pd", 0, 128), BLK, UP, True, False, tag="num")
     mm(X("pd", 0, 128), X("lt", 0, 128), REP, False, True, tag="num")
-    mm(X("pc", 0, 128), X("ltq", 0, 128), REP)
-    act(X("cn", 0, 128), X("pd", 0, 128), BIG + V * r)
-    for i in range(4):
-        ts(X("mk", 128 * i, 128 * i + 128), X("pc", 0, 128), float(i - 8), OP.is_equal, -BIG, OP.mult)
-    for c in range(4):
-        for i in range(4):
-            mm(X("pa", c, 512, 4), X("wq", 144 * c + 4 - i, 144 * c + 132 - i), X("mk", 128 * i, 128 * i + 128), i == 0, i == 3, tag="four")
-    for m in range(4):
-        for i, (lhs, rhs, c0) in enumerate((("b0", "ru", 128), ("lt0", "ru", 0), ("q0", "mk", 0))):
-            mm(X("pb", 0, 32), X(lhs, 12 - 4 * m, 140 - 4 * m), X(rhs, c0 + m, c0 + 128, 4), m + i == 0, m + i == 5, tag="base")
-    weights(1)
+    act(X("cn", 0, 128), X("pd", 0, 128), V * r - BIG, func=AF.Relu)
+    mm(X("pa", 0, 256), ZERO, TI, True, False, tag="eight")
+    for m in range(8):
+        for k, (lhs, c0) in enumerate((("b0", 128), ("lt0", 0))):
+            mm(X("pb", 0, 16), X(lhs, 14 - 2 * m, 142 - 2 * m), X("ru", c0 + m, c0 + 128, 8), m + k == 0, False, tag="base")
+    for i in range(8):
+        MK = X("mk", 128 * i, 128 * i + 128)
+        ts(MK, X("pc", 0, 128), float(i - 16), OP.is_equal, -BIG, OP.mult)
+        for c in range(2):
+            mm(X("pa", c, 256, 2), X("wq", 144 * c + 8 - i, 144 * c + 136 - i), MK, False, c + i == 8, tag="eight")
+    for m in range(8):
+        mm(X("pb", 0, 16), X("q0", 14 - 2 * m, 142 - 2 * m), X("mk", m, 128, 8), False, m == 7, tag="base")
+    for j in (3, 2, 1, 0):
+        mm(X("psw", 512 * j, 512 * j + 512), SELR, X("wsb", 512 * j, 512 * j + 512, 1, 0, 16))
 
     def SP(c):
         return X("sp", c, V, 16)[0], [("sp%d" % c, 0, 128, 0, 128)]
@@ -536,17 +575,28 @@ def rank_program(g, core, T, topo):
             ts(SP(c), X("cn", 0, 128), MC(c), OP.mult)
         else:
             act(SP(c), X("cn", 0, 128), 0.0, MC(c))
+    tt(X("off", 0, 16), X("pb", 0, 16), X("vl", 0, 16), OP.min)
+    tt(X("rb", 0, 256), X("pa", 0, 256), X("km", 0, 256), OP.mult)
+    ts(X("off16", 0, 16), X("off", 0, 16), BIG + 16.0, OP.add)
+    o = IX("inv", 2448, "off16", 0, 16)
+    add("V", lambda e: e.tensor_copy(out=o[0], in_=T.rb[:, :]), rg(X("inv", 0, 2448)), rg(X("rb", 0, 256), X("off16", 0, 16)))
     act(X("sb", 0, 384), numbers("bl16", 0, 24, V))
     show("num", "sb", "sp")
 
-    for j in range(4):
+    for j in (3, 2, 1, 0):
         a, b = 512 * j, 512 * j + 512
         if j in BOTH:
-            mm(X(BOTH[j], 0, 512), X("selq", 0, 128, 1, 0, 16), X("wsb", a, b, 1, 0, 16))
+            mm(X(BOTH[j], 0, 512), SELQ, X("wsb", a, b, 1, 0, 16))
             act(X("p0", a, b), IX("xf", Z, "nb16", 32 * j, 32 * j + 32))
         act(X("g1", a, b), IX("xf", Z, "nb16", 128 + 32 * j, 160 + 32 * j))
-        if j == 0:
-            act(X("sp", mine, mine + C), X("sb", C * r, C * r + C))
+    act(X("sp", mine, mine + C), X("sb", C * r, C * r + C))
+    mm(X("pa", 0, 512), ZERO, X("ww", 0, 512), True, False, tag="inv")
+    for d in range(-7, 16):
+        o2 = T.pa[:, :, d + 7:d + 15], rg(X("pa", 0, 512))
+        mm(o2, X("inv", 16 + d, 16 + d + V - 15, 16), X("seli", 0, 64), False, d == 15, tag="inv")
+    act(X("ivt", 0, 128), (T.pa[:, :, 7:23], rg(X("pa", 0, 512))), 0.0, -1.0)
+    mm(X("pb", 0, 128), ONE, X("left", 0, 128), True, False, tag="iv")
+    mm(X("pb", 0, 128), X("ivt", 0, 128), IF, False, True, tag="iv")
 
     def first(j):
         a, b = 512 * j, 512 * j + 512
@@ -559,64 +609,47 @@ def rank_program(g, core, T, topo):
         a, b = 512 * j, 512 * j + 512
         tt(X("psw", a, b), X("g1", a, b), X("psw", a, b), OP.mult)
 
-    nc = SHARE["cm"]
-    first(0)
-    first(1)
-    second(0)
-    for j in range(4):
-        a, b = 512 * j, 512 * j + 512
-        if j < 3:
-            second(j + 1)
-        else:
-            tt(X("off", 0, 32), X("pb", 0, 32), X("vl", 0, 32), OP.min)
-        tt(X("sw", a, b), X("p0", a, b), X("psw", a, b), OP.add)
-        if j < 2:
-            first(j + 2)
-        if j == 1:
-            act(X("cmr", 0, nc), numbers("mate", 0, nc // 16, Z + 16))
-        if j == 3:
-            ts(X("off16", 0, 32), X("off", 0, 32), BIG + 16.0, OP.add)
-            cp(X("sst", 0, 192), IX("sw", V, "bl16", 0, 12))
-            act(X("sst", 192, 384), IX("sw", V, "bl16", 12, 24))
-            show("s", "sst", "sw")
-            act(X("sw", mine, mine + C), X("sst", C * r, C * r + C))
-        if j >= KEPT:
-            where(X("p0", a, b), X("sw", a, b), [[1, 512]], 0, 0)
-    if nc < V:
-        act(X("cmr", nc, V), numbers("mate", nc // 16, 128, Z + 16))
-    for j in range(KEPT):
-        act(X("psw", 512 * j, 512 * j + 512), X("sw", 512 * j, 512 * j + 512))
+    def keep(j):
+        where(X("p0", 512 * j, 512 * j + 512), X("sw", 512 * j, 512 * j + 512), [[1, 512]], 0, 0)
 
-    tt(X("rb", 0, 512), X("pa", 0, 512), X("km", 0, 512), OP.mult)
-    o = IX("inv", 2688, "off16", 0, 32)
-    add("V", lambda e: e.tensor_copy(out=o[0], in_=T.rb[:, :]), rg(X("inv", 0, 2688)), rg(X("rb", 0, 512), X("off16", 0, 32)))
-    mm(X("pa", 0, 512), X("zero", 0, 128), X("km", 0, 512), True, False, tag="inv")
-    for d in range(-3, 16):
-        o = T.pa[:, :, d + 3:d + 7], rg(X("pa", 0, 512))
-        mm(o, X("inv", 16 + d, 16 + d + V - 15, 16), X("seli", 0, 32), False, d == 15, tag="inv")
-    act(X("ivt", 0, 128), (T.pa[:, :, 3:19], rg(X("pa", 0, 512))))
-    mm(X("pb", 0, 128), X("ivt", 0, 128), IF)
-    pick("pc", 0, "cmr", 0, "g8", 0, 8, "cm")
-    for j in range(KEPT):
-        act(X("g1", 512 * j, 512 * j + 512), IX("sw", Z + 16, "mate", 32 * j, 32 * j + 32))
-    act(X("cmt", 0, 128), X("pc", 0, 128))
-    mm(X("pd", 0, 128), X("cmt", 0, 128), IF)
-    a = 512 * KEPT
-    tt(X("tw", 8 + a, 8 + V), IX("sw", Z + 16, "mate", a // 16, 128), X("p0", a, V), OP.add)
-    for j in range(KEPT):
+    nc = SHARE["cm"]
+    first(3)
+    first(2)
+    second(3)
+    for j in (3, 2, 1, 0):
         a, b = 512 * j, 512 * j + 512
-        if j == KEPT - 1:
-            cp(X("iv16", 0, 128), X("pb", 0, 128))
-        tt(X("tw", 8 + a, 8 + b), X("g1", a, b), X("psw", a, b), OP.add)
-    for j, (a, b) in enumerate(zip(CUTS, CUTS[1:])):
-        o, i = X("p0", a, b), IX("tw", V + 8, "iv16", a // 16, b // 16)
-        if j % 2 == 0:
+        tt(X("sw", a, b), X("p0", a, b), X("psw", a, b), OP.add)
+        if j > 0:
+            second(j - 1)
+        if j > 1:
+            first(j - 2)
+            keep(j)
+    act(X("cmr", 0, nc), numbers("mate", 0, nc // 16, Z + 16))
+    cp(X("sst", 0, 192), IX("sw", V, "bl16", 0, 12))
+    act(X("sst", 192, 384), IX("sw", V, "bl16", 12, 24))
+    show("s", "sst", "sw")
+    act(X("sw", mine, mine + C), X("sst", C * r, C * r + C))
+    keep(1)
+    keep(0)
+
+    cp(X("cmr", nc, V), numbers("mate", nc // 16, 128, Z + 16))
+    cp(X("iv16", 0, 128), X("pb", 0, 128))
+    pick("pc", 0, "cmr", 0, "g8", 0, 8, "cm")
+    mm(X("pd", 0, 128), IF, X("cn", 0, 128), True, False, tag="cm")
+    last = len(CUTS) - 2
+    for j, (b, a) in enumerate(zip(CUTS, CUTS[1:])):
+        tt(X("tw", a, b), IX("sw", Z + 16, "mate", a // 16, b // 16), X("p0", a, b), OP.add)
+        o, i = X("g1", a, b), IX("tw", V + 8, "iv16", a // 16, b // 16, a)
+        if j == last:
             cp(o, i)
         else:
             act(o, i)
         dma("Y", "y%d" % j, T.y[:, a:b], [], o[0], o[1])
-        if j == 0:
-            tt(X("cmv", 0, 128), X("pd", 0, 128), X("cn", 0, 128), OP.min)
+        if j == CM:
+            act(X("cmt", 0, 128), X("pc", 0, 128))
+            mm(X("pd", 0, 128), X("cmt", 0, 128), IF, False, True, tag="cm")
+        if j == CM + 1:
+            act(X("cmv", 0, 128), X("pd", 0, 128))
             dma("Y", "cm", T.cm[:, :], [], T.cmv[:, :], rg(X("cmv", 0, 128)))
     for s, v in total.items():
         if known["G"].get(s, 0) < v:

@@ -8,16 +8,17 @@ BIG, MID = 16384.0, 1216.0
 OFFG, OFFC = 128 * 517, 128 * 129
 F32, BF, F16, I32, U16 = "float32", "bfloat16", "float16", "int32", "uint16"
 WIDTHS = {
-    F32: dict(dn=128, hlf=256, hlm=256, mb=384, bq=256, col=128, ir=128, iff=128, own=256, nth=128, tq=128, xf=2432, cn=128,
-              vl=16, off=16, sp=2448, sb=384, g1=2048, p0=2048, sw=2448, sst=384, ivt=128, cmr=2048, cmt=128, cmv=128, tw=2056,
+    F32: dict(dn=128, nbm=256, hlm=256, mb=384, col=128, ir=128, iff=128, own=256, nth=128, tq=128, xf=2432, cn=128,
+              vl=16, off=16, g1=2048, p0=2048, sw=2448, sst=384, cmt=128, cmv=128, tw=2056,
               xb=384, g8=8),
     BF: dict(wsb=2048, xw=2448, xc=2048, nw=2432, bst=384, hb=2048, hl=2432, hst=384, xst=384, gb=8192, wr=2048, ti=256, nti=256,
              ibn=128, i8=256, cst=384, pm=8, sel=48, selw=8, seli=64, wt=128, e0=272, e1=256, ar=288, ar3=256, m2=128, nr2=256,
-             nr3=256, ww=1024, wv=1024, one=128, zero=128, ru=256, mk=1024, blk=128, lt=128, lte=128, b0=144, lt0=144, q0=144,
-             wq=288, km=256, rb=256, inv=2448, selr=128, selq=128, bt=128, irb=128, left=128),
-    F16: dict(pz2=256, pz3=256, ih=128, hrow=768, g8h=8),
-    I32: dict(bli=24, nbi=256, ci=64, cj=64, yi=256, zi=256, zj=256, bki=48),
-    U16: dict(bl16=24, hl16=256, idx=512, mate=128, off16=16, iv16=128, nb16=256, bk16=48, hb16=48),
+             nr3=256, ww=1024, wv=1024, one=128, zero=144, ru=256, mk=1024, blk=128, lt=128, lte=128, b0=144, lt0=144, q0=144,
+             wq=288, km=256, rb=256, inv=2448, selr=128, selq=128, bt=128, irb=128, left=128, sp=2448, sb=384, cmr=2048,
+             hilo=256, two=256, half=288, g8b=8),
+    F16: dict(pz2=256, pz3=256, ih=128, ivt=128, hrow=768, g8h=144),
+    I32: dict(bli=24, nbi=256, ci=64, cj=64, yi=256, yj=256, zi=256, zj=256, bki=48, gli=24),
+    U16: dict(gl16=24, bl16=24, hl16=256, idx=512, mate=128, off16=16, iv16=128, nb16=256, bk16=48, hb16=48),
 }
 PSUM = {"psw": 2048, "pa": 512, "pb": 512, "pc": 512, "pd": 512}
 SCRATCH = {"fld": ("sbuf", [128, 4, 256], F32)}
@@ -26,13 +27,13 @@ for _d in WIDTHS:
         SCRATCH[_n] = ("sbuf", [128, WIDTHS[_d][_n]], _d)
 for _n in PSUM:
     SCRATCH[_n] = ("psum", [128, 8, 64] if _n == "pa" else [128, PSUM[_n]], F32)
-SHARE = {"nh": 1024, "nl": (256, 768), "r2": (1024, 1024, 768, 768), "r3": (1024, 448, 832), "x": 1408, "sp": 3, "cm": 1024}
+SHARE = {"nh": 1024, "nl": (448, 896), "r2": (896, 1024, 896, 832), "r3": (1024, 896), "x": 1344, "sp": 10, "cm": (0, 1536)}
 STEPS = (384, 384, 416, 416, 448)
 BOTH = {1: "pd", 0: "pc"}
 CUTS = (2048, 1792, 1408, 1024, 640, 256, 0)
-CM = 2
+CM = 0
 EXCH = ["name", "hl", "w1", "w2", "x", "xs", "num", "s"]
-LOADS = ["bl", "nb", "w", "x", "xc", "wr", "cm"] + ["y%d" % _j for _j in range(len(CUTS) - 1)]
+LOADS = ["bl", "gl", "nb", "w", "x", "xc", "wr", "cm"] + ["y%d" % _j for _j in range(len(CUTS) - 1)]
 SEMAPHORES = ["cV", "cS", "cP", "cG"] + ["d_" + k for k in LOADS] + ["a_" + k for k in EXCH] + ["l_" + k for k in EXCH]
 
 
@@ -44,9 +45,9 @@ def engine_plan(topo, src, cores):
         for i, d in enumerate(group):
             free = [e for e in topo.engines(src, d) if e not in used]
             n = 1
-            while n * 2 <= len(free) // (len(group) - i) and n < 8:
+            while n * 2 <= len(free) // (len(group) - i) and n < 4:
                 n *= 2
-            out[d] = free[:n]
+            out[d] = free[:n] if group is away else free[::len(free) // n]
             used = used + out[d]
     return out
 
@@ -194,9 +195,12 @@ def rank_program(g, core, T, topo):
         for b in range(16):
             mm(X(bank, c0 + b, c0 + n, 16), X(src, s0 + b, s0 + V, 16), X(sel, w0, w1), tag=tag)
 
+    def gather(q, dst, a, win, w, offs, o, c0, c1):
+        (cp if q == "V" else act)(X(dst, a + c0, a + c1), IX(win, w, offs, o + c0 // 16, o + c1 // 16))
+
     def share(dst, a, win, w, offs, o, n):
-        cp(X(dst, a, a + n), IX(win, w, offs, o, o + n // 16))
-        act(X(dst, a + n, a + V), IX(win, w, offs, o + n // 16, o + 128))
+        gather("V", dst, a, win, w, offs, o, 0, n)
+        gather("S", dst, a, win, w, offs, o, n, V)
 
     IB, TI, IH, IF = X("ti", 0, 128), X("ti", 0, 256), X("ih", 0, 128), X("iff", 0, 128)
     ONE, ZERO, G8, DIAG = X("one", 0, 128), X("zero", 0, 128), X("g8", 0, 8), [[-1, 128]]
@@ -212,97 +216,94 @@ def rank_program(g, core, T, topo):
 
     dma("Y", "bl", T.bli[:, :], rg(X("bli", 0, 24)), T.bl[:, :], [])
     dma("S", "nb", T.nbi[:, :], rg(X("nbi", 0, 256)), T.nb[:, :], [])
+    dma("S", "gl", T.gli[:, 6 * r:6 * r + 6], rg(X("gli", 6 * r, 6 * r + 6)), T.bl[:, 6 * r:6 * r + 6], [])
     for d in range(2):
         dma("Y", "w", T.wsb[8 * d:8 * d + 8, :], rg(X("wsb", 0, V, 1, 8 * d, 8 * d + 8)), T.w[:, V * d:V * d + V], [])
 
     iota(X("ci", 0, 24), [[-1, 24]], 40, 1, True)
+    iota(X("zero", 0, 144), [[0, 144]], 0, 0)
     iota(X("ir", 0, 128), [[1, 128]], 0, 0)
-    iota(ZERO, [[0, 128]], 0, 0)
-    PM = X("pm", 0, 8, 1, 0, 16)
-    where(PM, X("zero", 0, 8, 1, 0, 16), [[-1, 8]], -8, 1, OP.not_equal, 1.0)
-    where(PM, PM, [[-1, 8]], 0, 1, OP.not_equal, -1.0)
     iota(X("ci", 24, 28), [[-4, 4]], 16, 1, True)
     diagonal(IB, 1.0)
     iota(X("ci", 32, 40), [[-16, 8]], 0, 1, True)
+    PM = X("pm", 0, 8, 1, 0, 16)
 
     def fill(x):
         add("V", lambda e: e.memset(T.col[:, PW + x:PW + x + 1], 64.0 ** -x), rg(col(PW + x)), [])
 
+    send("name", lambda d: X("bli", 6 * d, 6 * d + 6), X("gli", 6 * r, 6 * r + 6))
+    recv("name", [("gli", 0, 128, 6 * q, 6 * q + 6) for q in others])
     fill(0)
     fill(1)
     ts(X("cj", 0, 8), X("ci", 0, 8), 7, OP.bitwise_and)
+    ts(X("cj", 32, 48), X("ci", 8, 24), 15, OP.bitwise_and)
     fill(2)
     ts(col(M8, 8), X("cj", 0, 8), 0.0, OP.is_equal)
+    ts(col(30), X("cj", 1, 2), 0.0, OP.is_equal, 2.0 * r, OP.mult)
+    ts(col(31), X("cj", 3, 4), 0.0, OP.is_equal, 4.0 * r, OP.mult)
     fill(3)
+    cp(X("g8h", 0, 144), X("zero", 0, 144))
     act(X("irb", 0, 128), X("ir", 0, 128))
-    ts(K0, col(M8 + 3), 2.0, OP.mult, col(M8 + 1), OP.add)
-    ts(col(PW, 4), col(PW, 4), col(M8 + 4), OP.mult)
-    ts(K0, K0, 2.0 * r, OP.mult)
-    ts(col(TX, 4), X("ir", 0, 4), col(M8 + 2), OP.mult, K0, OP.add)
+    ts(col(TX, 4), X("ir", 0, 4), col(M8 + 2), OP.mult, col(30), OP.add)
+    ts(col(PW, 4), col(PW, 4), col(M8 + 4), OP.mult, col(31), OP.add)
+    ts(X("cj", 48, 52), X("ci", 24, 28), 2, OP.logical_shift_right, 3, OP.bitwise_and)
     tt(col(TX, 4), col(TX, 4), col(PW, 4), OP.add)
+    ts(col(32, 20), X("cj", 32, 52), 0.0, OP.is_equal)
     act(S8, col(M8 + 4), 1.0, -0.875)
+    act(col(DC + 1), col(M8 + 1), col(M8 + 3))
     act(col(DC + 2), col(M8 + 3), 0.0, 2.0)
     act(col(DC + 3), col(M8 + 3), col(M8 + 1), 3.0)
-    act(col(DC + 1), col(M8 + 1), col(M8 + 3))
+    act(K0, col(M8 + 3), col(M8 + 1), 2.0)
+    tt(PM, X("ti", 8, 16, 1, 0, 16), X("ti", 0, 8, 1, 0, 16), OP.subtract)
     for x in range(4):
-        if x < 3:
-            ts(X("nw", x, 512, 4), X("irb", 0, 128), col(M8), OP.mult, col(TX + x), OP.add, tag="nw")
-        else:
-            o = T.nw[:, x:512:4], [("nw3", 0, 128, 0, 512)]
-            act(o, X("irb", 0, 128), col(TX + x), col(M8))
-    NW = T.nw[:, 0:512], rg(X("nw", 0, 512), ("", [("nw3", 0, 128, 0, 512)]))
-    ts(X("nw", 1024, 1536), NW, S8, OP.mult, col(DC + 2), OP.add)
-    act(X("nw", 512, 768), (T.nw[:, 0:256], NW[1]), col(DC + 1))
-    ts(X("nw", 1536, 2048), NW, S8, OP.mult, col(DC + 3), OP.add)
-    ts(X("nw", 768, 1024), (T.nw[:, 256:512], NW[1]), col(DC + 1), OP.add)
-    cp(X("bl16", 0, 24), X("bli", 0, 24))
-    cp(X("bst", 0, 192), IX("nw", V, "bl16", 0, 12))
-    act(X("bst", 192, 384), IX("nw", V, "bl16", 12, 24))
-    show("name", "bst", "nw")
-    act(X("nw", mine, mine + C), X("bst", C * r, C * r + C))
+        ts(X("nw", x, 512, 4), X("irb", 0, 128), col(M8), OP.mult, col(TX + x), OP.add, tag="nw")
+    act(WG, col(M8 + 3), col(M8 + 2), 512.0)
+    act(WC, col(M8 + 1), col(M8), 128.0)
+    act(WG, col(M8), WG, 4.0)
+    act(SIDEA, col(QM), col(QM + 1))
+    act(SIDEB, col(QM + 2), col(QM + 3))
+    act(col(55), MC(4), 0.0, 2.0 ** -20)
+    act(col(57), MC(12), 0.0, 2.0)
+    act(X("nw", 512, 1024), X("nw", 0, 512), col(DC + 1))
 
     for b in range(16):
         mm(X("pa", b, 128, 16), X("wsb", b, V, 16, 0, 16), PM, tag="wt")
-    ts(X("bt", 0, 128), X("pa", 0, 128), 0.0, OP.is_gt)
-    mm(X("pb", 0, 128), X("bt", 0, 128), IB)
-    ts(X("cj", 32, 48), X("ci", 8, 24), 15, OP.bitwise_and)
-    ts(X("cj", 48, 52), X("ci", 24, 28), 2, OP.logical_shift_right, 3, OP.bitwise_and)
     ts(X("bki", 24, 48), X("bli", 0, 24), 15, OP.bitwise_and)
     ts(X("bki", 0, 24), X("bli", 0, 24), 4, OP.logical_shift_right)
-    ts(col(32, 20), X("cj", 32, 52), 0.0, OP.is_equal)
-    cp(X("bk16", 0, 48), X("bki", 0, 48))
     tt(X("dn", 0, 128), X("nbi", 128, 256), X("nbi", 0, 128), OP.subtract)
-    ts(X("cj", 56, 64), X("ci", 32, 40), 4, OP.arith_shift_right)
+    cp(X("bk16", 0, 48), X("bki", 0, 48))
+    ts(X("bt", 0, 128), X("pa", 0, 128), 0.0, OP.is_gt)
+    mm(X("pb", 0, 128), X("bt", 0, 128), IB)
+    ts(X("nbm", 0, 256), X("nbi", 0, 256), MID, OP.subtract)
     tt(X("pb", 0, 128), X("pb", 0, 128), X("dn", 0, 128), OP.mult)
-    ts(X("g8h", 0, 8), X("cj", 56, 64), 0.0, OP.is_equal)
-    tt(X("hlf", 0, 128), X("nbi", 0, 128), X("pb", 0, 128), OP.add)
-    tt(X("hlf", 128, 256), X("nbi", 128, 256), X("pb", 0, 128), OP.subtract)
+    ts(X("cj", 56, 64), X("ci", 32, 40), 4, OP.arith_shift_right)
+    tt(X("hlm", 0, 128), X("nbm", 0, 128), X("pb", 0, 128), OP.add)
+    tt(X("hlm", 128, 256), X("nbm", 128, 256), X("pb", 0, 128), OP.subtract)
+    ts(X("g8h", 16, 144, 16), X("cj", 56, 64), 0.0, OP.is_equal)
     ts(G8, X("cj", 56, 64), 0.0, OP.is_equal)
     act(X("mb", 0, 384), IX("col", 48, "bk16", 24, 48, 32))
-    for K in range(2):
-        act(X("hlm", 128 * K, 128 * K + 128), X("hlf", 128 * K, 128 * K + 128), -MID)
+    for j in (2, 3):
+        act(X("nw", 512 * j, 512 * j + 512), X("nw", 0, 512), col(DC + j), S8)
+    for q in range(4):
+        act(col(80 + q), K0, 0.0, 2.0 * (q - r))
+    for f, (w, side) in ((0, (WG, SIDEA)), (1, (WG, SIDEB)), (2, (WC, SIDEA)), (4, (WC, SIDEB))):
+        act(col(52 + f), w, 0.0, side)
+    diagonal(IF, 1.0)
     act(SA, MC(4), B4, 2.0 ** 21)
     act(BA, B4, 0.0, 128.0)
-    act(WG, col(M8 + 3), col(M8 + 2), 512.0)
-    act(WC, col(M8 + 1), col(M8), 128.0)
-    act(SIDEA, col(QM), col(QM + 1))
-    act(SIDEB, col(QM + 2), col(QM + 3))
-    act(WG, col(M8), WG, 4.0)
-    diagonal(IF, 1.0)
     for K, bank in enumerate(("pc", "pd")):
         tt(X("hrow", 384 * K, 384 * K + 384), IX("hlm", 128 * K + 128, "bk16", 0, 24, 128 * K), X("mb", 0, 384), OP.mult)
         for b in range(16):
-            mm(X(bank, b, 128, 16, 0, 24), X("hrow", 384 * K + b, 384 * K + 384, 16), X("g8h", 0, 8), tag="border")
-        act(X("bq", 128 * K, 128 * K + 128, 1, 0, 24), X(bank, 0, 128, 1, 0, 24), MID)
-        if K == 0:
-            act(col(54), WC, 0.0, SIDEA)
-            act(col(55), MC(4), 0.0, 2.0 ** -20)
-            act(col(56), WC, 0.0, SIDEB)
-            act(col(57), MC(12), 0.0, 2.0)
-    for K, bank in enumerate(("pb", "pc")):
-        mm(X(bank, 0, 24), X("bq", 128 * K, 128 * K + 128, 1, 0, 24), X("iff", 0, 24, 1, 0, 24))
-    cp(X("hl16", 0, 256), X("hlf", 0, 256))
-    cp(X("hb16", 0, 24), X("pb", 0, 24))
+            mm(X(bank, 0, 24), X("g8h", 16 - b, 144 - b), X("hrow", 384 * K + b, 384 * K + 384, 16), b == 0, b == 15, tag="border")
+    ts(X("hl16", 0, 256), X("hlm", 0, 256), MID, OP.add)
+    cp(X("gl16", 0, 24), X("gli", 0, 24))
+    for q in range(4):
+        o, i = X("nw", V + C * q, V + C * q + C), IX("nw", V, "gl16", 6 * q, 6 * q + 6)
+        if q < 2:
+            ts(o, i, col(80 + q), OP.add)
+        else:
+            act(o, i, col(80 + q))
+    ts(X("hb16", 0, 24), X("pc", 0, 24), MID, OP.add)
     iota(ONE, [[0, 128]], 1, 0)
     iota(X("own", 0, 128), [[0, 8], [1, 16]], V * r + OFFG, 16)
     iota(X("own", 128, 256), [[0, 8], [1, 16]], V * r, 16)
@@ -316,7 +317,7 @@ def rank_program(g, core, T, topo):
 
     ts(X("bst", 0, 192), IX("nw", Z, "hb16", 0, 12), SA, OP.mult, BA, OP.add)
     act(X("bst", 192, 384), IX("nw", Z, "hb16", 12, 24), BA, SA)
-    cp(X("hb16", 24, 48), X("pc", 0, 24))
+    ts(X("hb16", 24, 48), X("pd", 0, 24), MID, OP.add)
     tt(X("hst", 0, 384), IX("nw", Z, "hb16", 24, 48), X("bst", 0, 384), OP.max)
     show("hl", "hst", "hl")
     a = 0
@@ -325,12 +326,9 @@ def rank_program(g, core, T, topo):
         tt(X("hl", a, a + n), IX("nw", Z, "hl16", 128 + a // 16, 128 + (a + n) // 16), X("hb", a, a + n), OP.max)
         a += n
     act(X("hl", mine, mine + C), X("hst", C * r, C * r + C))
-    act(col(52), WG, 0.0, SIDEA)
-    act(col(53), WG, 0.0, SIDEB)
     for f in (2, 3, 4, 5, 0, 1):
         act(X("sel", 8 * f, 8 * f + 8), G8, 0.0, col(52 + f))
     pick("pa", 0, "hl", 0, "sel", 16, 48, "own")
-    pick("pb", 0, "hl", 0, "sel", 0, 16, "own")
     LESS = 768
     diagonal(X("i8", 0, 128), 8.0)
     diagonal(X("i8", 128, 256), -8.0)
@@ -353,26 +351,27 @@ def rank_program(g, core, T, topo):
     act(F(1, 2, 0, 256), X("pa", 0, 256))
     act(F(0, 1, 128, 256), X("pa", 384, 512))
     act(X("gb", V + n2, 2 * V), IX("hl", Z, "hl16", 128 + n2 // 16, 256))
-    tt(X("psw", LESS, LESS + 256), X("pb", 0, 256), X("own", 0, 256), OP.is_lt)
     cp(X("gb", V, V + n1), IX("hl", Z, "hl16", 128, 128 + n1 // 16))
     T1, VI = X("e0", 0, 128), X("e0", 128, 256)
     tt(X("e0", 0, 256), X("pc", 0, 256), X("own", 0, 256), OP.is_equal)
     pack("pd", [("e0", 0, 0), ("e0", 128, 64)])
+    TH, DM = 1536, 128
     for K in range(2):
-        mm(X("pb", K * 128, K * 128 + 128), F(K, K + 1, 0, 128), IF)
-    DM = 128
+        mm(X("psw", TH + K * 128, TH + K * 128 + 128), F(K, K + 1, 0, 128), IF)
     tt(X("psw", DM, DM + 256), X("pc", 256, 512), F(1, 2, 0, 256), OP.subtract)
     cp(X("ww", 256 * r, 256 * r + 256), X("pd", 0, 256))
     spread("w1", "ww")
     cp(X("gb", V + n1, V + n2), IX("hl", Z, "hl16", 128 + n1 // 16, 128 + n2 // 16))
     pick("pa", 0, "gb", V, "sel", 0, 32, "nl")
-    ts(X("idx", 0, 256), X("pb", 0, 256), float(OFFC), OP.subtract)
+    ts(X("idx", 0, 256), X("psw", TH, TH + 256), float(OFFC), OP.subtract)
     act(F(2, 3, 0, 256), X("pc", 256, 512))
     mm(X("pb", 0, 128), F(2, 3, 0, 128), IF)
     act(W64, MC(1), MC(0), 64.0)
     act(W64, MC(2), W64, 64.0 ** 2)
     act(W64, MC(3), W64, 64.0 ** 3)
     act(X("selw", 0, 8), G8, 0.0, W64)
+    cp(X("bl16", 0, 24), X("bli", 0, 24))
+    cp(IH, IB)
     for K in range(2):
         tt(X("psw", DM + 128 * K, DM + 128 * K + 128), X("psw", DM + 128 * K, DM + 128 * K + 128), VI, OP.mult)
     act(F(3, 4, 0, 256), X("pa", 256, 512))
@@ -395,6 +394,8 @@ def rank_program(g, core, T, topo):
     diagonal(X("nti", 0, 128), -1.0)
     where(X("nti", 128, 256), ZERO, DIAG, 0, 1, OP.is_ge, -1.0)
     iota(X("wq", 0, 288), [[0, 288]], 0, 0)
+    for a, b in ((0, 8), (136, 152), (280, 288)):
+        iota(X("half", a, b), [[0, b - a]], 0, 0)
     iota(X("km", 0, 256), [[-1, 128], [0, 2]], 127, 0)
     SELR, SELQ = X("selr", 0, 128, 1, 0, 16), X("selq", 0, 128, 1, 0, 16)
     where(SELR, X("one", 0, 128, 1, 0, 16), [[-16, 8], [0, 16]], -128, 16, OP.is_equal)
@@ -405,6 +406,10 @@ def rank_program(g, core, T, topo):
     where(BLK, BLK, [[16, 8], [0, 16]], 15, -1)
     where(X("lt", 0, 128), BLK, [[1, 128]], 0, -1, OP.is_gt)
     where(X("lt", 0, 128), X("lt", 0, 128), [[1, 128]], 0, -1, OP.not_equal, BIG)
+    LTE = X("lte", 0, 128)
+    where(LTE, ONE, [[-8, 16], [0, 8]], 0, 1)
+    where(LTE, LTE, [[1, 128]], 0, -1)
+    where(LTE, LTE, [[1, 128]], 0, -1, OP.not_equal, -16.0)
 
     def ask(L, win, n):
         share("gb", L * V, win, 1024, "idx", L * 128, n)
@@ -413,12 +418,13 @@ def rank_program(g, core, T, topo):
         pick(bank, c0, "gb", L * V, "selw", 0, 8, "word")
 
     n = SHARE["r2"]
-    TH = 1536
     ARH, ARL = X("ar", 0, 128), X("ar", 144, 272)
 
-    def digit(out, K, bank, f, mask):
-        tt(X("yi", 128 * K, 128 * K + 128), X(bank, 0, 128), F(f, f + 1, 128, 256), OP.mult)
-        ts(X(out, 128 * K, 128 * K + 128), X("yi", 128 * K, 128 * K + 128), mask, OP.bitwise_and)
+    def shift(K, bank, f):
+        tt(X("yj", 128 * K, 128 * K + 128), X(bank, 0, 128), F(f, f + 1, 128, 256), OP.mult)
+
+    def digit(K, mask):
+        ts(X("zj", 128 * K, 128 * K + 128), X("yj", 128 * K, 128 * K + 128), mask, OP.bitwise_and)
 
     for L in range(3):
         ask(L, "ww", n[L])
@@ -430,26 +436,32 @@ def rank_program(g, core, T, topo):
     tt(X("yi", 0, 256), X("pc", 0, 256), F(0, 2, 128, 256), OP.mult)
     ask(3, "ww", n[3])
     answer(3, "pb", 0)
+    shift(0, "pd", 2)
     ts(X("zi", 0, 256), X("yi", 0, 256), 6, OP.bitwise_and)
-    digit("zj", 0, "pd", 2, 4)
+    digit(0, 4)
     tt(X("zi", 0, 128), X("zi", 0, 128), UL, OP.min)
     ts(X("nth", 0, 128), X("zi", 128, 256), -2.5, OP.mult, 9.0, OP.add)
     tt(X("psw", TH, TH + 256), X("zi", 0, 256), X("psw", 1152, 1408), OP.max)
+    shift(1, "pb", 3)
     tt(X("psw", TH + 256, TH + 384), X("psw", TH, TH + 128), X("nth", 0, 128), OP.max)
+    digit(1, 4)
     tt(ARH, X("zj", 0, 128), X("psw", TH + 128, TH + 256), OP.is_gt)
-    digit("zj", 1, "pb", 3, 4)
     tt(ARL, X("zj", 128, 256), X("psw", TH + 256, TH + 384), OP.is_gt)
     pack("pa", [("ar", 0, 0)], False, False)
     pack("pa", [("ar", 144, 64)], False, True)
+    mm(X("pd", 128, 256), IB, T1, True, False, tag="m2")
+    mm(X("pd", 128, 256), IB, ARH, False, True, tag="m2")
     tt(F(2, 3, 0, 256), F(1, 2, 0, 256), X("psw", DM, DM + 256), OP.add)
     cp(X("wv", 256 * r, 256 * r + 256), X("pa", 0, 256))
     spread("w2", "wv")
 
     mm(X("pb", 0, 128), F(2, 3, 0, 128), IF)
     NEG = X("nti", 0, 128)
-    mm(X("pd", 0, 128), ROW, ROW, True, False, tag="free")
-    mm(X("pd", 0, 128), NEG, ARH, False, False, tag="free")
-    mm(X("pd", 0, 128), NEG, ARL, False, True, tag="free")
+    FREE = X("psw", 384, 512)
+    mm(FREE, ROW, ROW, True, False, tag="free")
+    mm(FREE, NEG, ARH, False, False, tag="free")
+    mm(FREE, NEG, ARL, False, True, tag="free")
+    pick("pc", 0, "hl", 0, "sel", 0, 16, "own")
     act(X("xst", 0, 384), IX("xc", V, "bl16", 0, 24))
     show("x", "xst", "xw")
     act(X("xw", mine, mine + C), X("xst", C * r, C * r + C))
@@ -458,26 +470,20 @@ def rank_program(g, core, T, topo):
     act(col(74), SIDEB, 1.0, 15.0)
     act(X("km", 0, 256), X("km", 0, 256), col(73), col(72))
     act(col(64, 8), col(M8, 8), 0.0, col(74))
-    cp(IH, IB)
-    tt(X("m2", 0, 128), T1, ARH, OP.add)
+    act(X("m2", 0, 128), X("pd", 128, 256))
     ts(X("idx", 256, 384), X("pb", 0, 128), float(OFFC), OP.subtract)
-    tt(F(2, 3, 128, 256), F(2, 3, 128, 256), X("pd", 0, 128), OP.mult)
-    for K, m in enumerate((X("m2", 0, 128), ARL)):
+    tt(F(2, 3, 128, 256), F(2, 3, 128, 256), FREE, OP.mult)
+    for K, m in ((1, ARL), (0, X("m2", 0, 128))):
         tt(X("pz2", 128 * K, 128 * K + 128), m, HZ[K], OP.mult)
-        mm(X("psw", 0, 128), m, X("ibn", 0, 128), K == 0, False, tag="mate")
+        mm(X("psw", 0, 128), m, X("ibn", 0, 128), K == 1, False, tag="mate")
         mm(X("psw", 0, 128), X("pz2", 128 * K, 128 * K + 128), IH, False, False, tag="mate")
+    tt(X("psw", LESS, LESS + 256), X("pc", 0, 256), X("own", 0, 256), OP.is_lt)
     for K, m in enumerate((X("m2", 0, 128), ARL)):
         tt(X("nr2", 128 * K, 128 * K + 128), m, X("psw", LESS + 128 * K, LESS + 128 * K + 128), OP.mult)
     mm(X("psw", 512, 768), ONE, TI, True, False, tag="rep")
     for K in range(2):
         mm(X("psw", 512, 768), X("nr2", 128 * K, 128 * K + 128), X("nti", 0, 256), False, False, tag="rep")
-    ts(QW, X("cj", 32, 33), -1.0, OP.mult, 16.0, OP.add)
-    cp(X("nb16", 0, 256), X("nbi", 0, 256))
-    LTE = X("lte", 0, 128)
-    where(LTE, ONE, [[8, 16], [0, 8]], 7, -1)
-    where(LTE, LTE, [[-8, 16], [0, 8]], 0, 1)
-    where(LTE, LTE, [[1, 128]], 0, -1)
-    where(LTE, LTE, [[1, 128]], 0, -1, OP.not_equal, -16.0)
+    cp(X("nb16", 128, 256), X("nbi", 128, 256))
     for name in ("b0", "lt0", "q0"):
         iota(X(name, 0, 14), [[0, 14]], 0, 0)
     B0 = X("b0", 14, 142)
@@ -489,13 +495,14 @@ def rank_program(g, core, T, topo):
     iota(X("sp", Z, Z + 16), [[0, 16]], 0, 0)
     iota(X("inv", 0, 2448), [[0, 2448]], 0, 0)
 
-    n0, n1, n2 = SHARE["r3"]
+    n0, n1 = SHARE["r3"]
     ask(2, "wv", n0)
     answer(2, "pc", 0)
-    act(X("gb", 3 * V + n2, 4 * V), IX("wv", 1024, "idx", 384 + n2 // 16, 512))
-    cp(X("gb", 3 * V, 3 * V + n1), IX("wv", 1024, "idx", 384, 384 + n1 // 16))
-    digit("zj", 0, "pc", 2, 6)
-    cp(X("gb", 3 * V + n1, 3 * V + n2), IX("wv", 1024, "idx", 384 + n1 // 16, 384 + n2 // 16))
+    ask(3, "wv", n1)
+    shift(0, "pc", 2)
+    ts(QW, X("cj", 32, 33), -1.0, OP.mult, 16.0, OP.add)
+    digit(0, 6)
+    cp(X("nb16", 0, 128), X("nbi", 0, 128))
     answer(3, "pd", 0)
     A3, L3, TL = X("ar3", 0, 128), X("ar3", 128, 256), X("psw", TH, TH + 128)
     tt(A3, X("zj", 0, 128), X("psw", TH + 128, TH + 256), OP.is_gt)
@@ -505,9 +512,9 @@ def rank_program(g, core, T, topo):
     tt(TL, TL, X("nth", 0, 128), OP.max)
     mm(X("psw", 0, 128), A3, X("ibn", 0, 128), False, False, tag="mate")
     mm(X("psw", 0, 128), X("pz3", 0, 128), IH, False, False, tag="mate")
-    tt(X("yi", 128, 256), X("pd", 0, 128), F(3, 4, 128, 256), OP.mult)
+    shift(1, "pd", 3)
     tt(TL, TL, X("tq", 0, 128), OP.max)
-    ts(X("zj", 128, 256), X("yi", 128, 256), 6, OP.bitwise_and)
+    digit(1, 6)
     tt(L3, X("zj", 128, 256), TL, OP.is_gt)
     tt(X("pz3", 128, 256), L3, HZ[1], OP.mult)
     mm(X("psw", 0, 128), L3, X("ibn", 0, 128), False, False, tag="mate")
@@ -517,12 +524,14 @@ def rank_program(g, core, T, topo):
         act(col(76 + c), side, 0.0, QW)
         act(X("wq", 144 * c + 16, 144 * c + 144, 16), G8, 0.0, side, tag="wq")
         act(X("wq", 144 * c + 8, 144 * c + 136, 16), G8, 0.0, col(76 + c), tag="wq")
+        act(X("half", 144 * c + 8, 144 * c + 136), IB, 0.0, side)
+    act(X("g8b", 0, 8), G8)
     for j in range(8):
         act(X("seli", 8 * j, 8 * j + 8), col(64, 8), 0.0, X("g8", j, j + 1))
 
     ts(X("mate", 0, 128), X("psw", 0, 128), float(Z), OP.add)
     nx = SHARE["x"]
-    hx = (nx + V) // 2
+    hx = nx + 384
     for bank, a, b in (("pa", nx, hx), ("pb", hx, V)):
         mm(X(bank, 0, b - a), IB, X("xc", a, b), True, False, tag="gx")
     for K in range(2):
@@ -533,9 +542,8 @@ def rank_program(g, core, T, topo):
     tt(X("xf", 0, nx), IX("xw", Z + 16, "mate", 0, nx // 16), X("xc", 0, nx), OP.add)
     for bank, a, b in (("pa", nx, hx), ("pb", hx, V)):
         act(X("xf", a, b), X(bank, 0, b - a))
-        if bank == "pa":
-            act(X("ru", 0, 256), X("psw", 512, 768))
     REP, UP = X("ru", 0, 128), X("ru", 128, 256)
+    cp(X("ru", 0, 256), X("psw", 512, 768))
     cp(X("xb", 0, 192), IX("xf", V, "bl16", 0, 12))
     act(X("xb", 192, 384), IX("xf", V, "bl16", 12, 24))
     show("xs", "xb", "xf")
@@ -544,22 +552,28 @@ def rank_program(g, core, T, topo):
     iota(X("sw", Z, Z + 16), [[0, 16]], 0, 0)
     iota(X("tw", V, V + 8), [[0, 8]], 0, 0)
 
-    act(X("xf", mine, mine + C), X("xb", C * r, C * r + C))
     mm(X("pc", 0, 128), LTE, REP)
     mm(X("pd", 0, 128), BLK, UP, True, False, tag="num")
     mm(X("pd", 0, 128), X("lt", 0, 128), REP, False, True, tag="num")
     act(X("cn", 0, 128), X("pd", 0, 128), V * r - BIG, func=AF.Relu)
+    HI, LO = X("hilo", 0, 128), X("hilo", 128, 256)
+    act(HI, X("pd", 0, 128), V * r - BIG, func=AF.Relu)
+    act(X("xf", mine, mine + C), X("xb", C * r, C * r + C))
     mm(X("pa", 0, 256), ZERO, TI, True, False, tag="eight")
-    for m in range(8):
-        for k, (lhs, c0) in enumerate((("b0", 128), ("lt0", 0))):
-            mm(X("pb", 0, 16), X(lhs, 14 - 2 * m, 142 - 2 * m), X("ru", c0 + m, c0 + 128, 8), m + k == 0, False, tag="base")
     for i in range(8):
         MK = X("mk", 128 * i, 128 * i + 128)
         ts(MK, X("pc", 0, 128), float(i - 16), OP.is_equal, -BIG, OP.mult)
         for c in range(2):
             mm(X("pa", c, 256, 2), X("wq", 144 * c + 8 - i, 144 * c + 136 - i), MK, False, c + i == 8, tag="eight")
+        if i == 2:
+            tt(LO, X("cn", 0, 128), HI, OP.subtract)
+            for c in range(2):
+                o = X("pd", 128 + 128 * c, 256 + 128 * c)
+                mm(o, X("half", 144 * c + 16 * c, 144 * c + 16 * c + 128), HI, True, False, tag="two")
+                mm(o, X("half", 144 * c + 8, 144 * c + 136), LO, False, True, tag="two")
     for m in range(8):
-        mm(X("pb", 0, 16), X("q0", 14 - 2 * m, 142 - 2 * m), X("mk", m, 128, 8), False, m == 7, tag="base")
+        for k, (lhs, rhs, c0) in enumerate((("b0", "ru", 128), ("lt0", "ru", 0), ("q0", "mk", 0))):
+            mm(X("pb", 0, 16), X(lhs, 14 - 2 * m, 142 - 2 * m), X(rhs, c0 + m, c0 + 128, 8), m + k == 0, m + k == 9, tag="base")
     for j in (3, 2, 1, 0):
         mm(X("psw", 512 * j, 512 * j + 512), SELR, X("wsb", 512 * j, 512 * j + 512, 1, 0, 16))
 
@@ -570,18 +584,13 @@ def rank_program(g, core, T, topo):
         ap, regs = IX("sp", b, offs, c, d)
         return ap, regs + [y for k in range(16) for y in SP(k)[1]]
 
+    act(X("two", 0, 256), X("pd", 128, 384))
     for c in range(16):
+        part = X("two", 128 * (c // 8), 128 * (c // 8) + 128)
         if c < SHARE["sp"]:
-            ts(SP(c), X("cn", 0, 128), MC(c), OP.mult)
+            ts(SP(c), part, col(M8 + c % 8), OP.mult)
         else:
-            act(SP(c), X("cn", 0, 128), 0.0, MC(c))
-    tt(X("off", 0, 16), X("pb", 0, 16), X("vl", 0, 16), OP.min)
-    tt(X("rb", 0, 256), X("pa", 0, 256), X("km", 0, 256), OP.mult)
-    ts(X("off16", 0, 16), X("off", 0, 16), BIG + 16.0, OP.add)
-    o = IX("inv", 2448, "off16", 0, 16)
-    add("V", lambda e: e.tensor_copy(out=o[0], in_=T.rb[:, :]), rg(X("inv", 0, 2448)), rg(X("rb", 0, 256), X("off16", 0, 16)))
-    act(X("sb", 0, 384), numbers("bl16", 0, 24, V))
-    show("num", "sb", "sp")
+            act(SP(c), part, 0.0, col(M8 + c % 8))
 
     for j in (3, 2, 1, 0):
         a, b = 512 * j, 512 * j + 512
@@ -589,14 +598,25 @@ def rank_program(g, core, T, topo):
             mm(X(BOTH[j], 0, 512), SELQ, X("wsb", a, b, 1, 0, 16))
             act(X("p0", a, b), IX("xf", Z, "nb16", 32 * j, 32 * j + 32))
         act(X("g1", a, b), IX("xf", Z, "nb16", 128 + 32 * j, 160 + 32 * j))
-    act(X("sp", mine, mine + C), X("sb", C * r, C * r + C))
-    mm(X("pa", 0, 512), ZERO, X("ww", 0, 512), True, False, tag="inv")
-    for d in range(-7, 16):
-        o2 = T.pa[:, :, d + 7:d + 15], rg(X("pa", 0, 512))
-        mm(o2, X("inv", 16 + d, 16 + d + V - 15, 16), X("seli", 0, 64), False, d == 15, tag="inv")
-    act(X("ivt", 0, 128), (T.pa[:, :, 7:23], rg(X("pa", 0, 512))), 0.0, -1.0)
-    mm(X("pb", 0, 128), ONE, X("left", 0, 128), True, False, tag="iv")
-    mm(X("pb", 0, 128), X("ivt", 0, 128), IF, False, True, tag="iv")
+
+
+    def columns():
+        tt(X("off", 0, 16), X("pb", 0, 16), X("vl", 0, 16), OP.min)
+        tt(X("rb", 0, 256), X("pa", 0, 256), X("km", 0, 256), OP.mult)
+        ts(X("off16", 0, 16), X("off", 0, 16), BIG + 16.0, OP.add)
+
+    def scatter():
+        o = IX("inv", 2448, "off16", 0, 16)
+        add("V", lambda e: e.tensor_copy(out=o[0], in_=T.rb[:, :]), rg(X("inv", 0, 2448)), rg(X("rb", 0, 256), X("off16", 0, 16)))
+        mm(X("pb", 0, 128), ONE, X("left", 0, 128), True, False, tag="iv")
+        mm(X("pa", 0, 512), ZERO, X("ww", 0, 512), True, False, tag="inv")
+        for d in range(-7, 16):
+            o2 = T.pa[:, :, d + 7:d + 15], rg(X("pa", 0, 512))
+            mm(o2, X("inv", 16 + d, 16 + d + V - 15, 16), X("seli", 0, 64), False, d == 15, tag="inv")
+
+    def inverse():
+        ts(X("ivt", 0, 128), (T.pa[:, :, 7:23], rg(X("pa", 0, 512))), -1.0, OP.mult)
+        mm(X("pb", 0, 128), X("ivt", 0, 128), IH, False, True, tag="iv")
 
     def first(j):
         a, b = 512 * j, 512 * j + 512
@@ -605,26 +625,36 @@ def rank_program(g, core, T, topo):
         else:
             tt(X("p0", a, b), IX("xf", Z, "nb16", a // 16, b // 16), X("wr", a, b), OP.mult)
 
-    def second(j):
-        a, b = 512 * j, 512 * j + 512
+    def second(a, b):
         tt(X("psw", a, b), X("g1", a, b), X("psw", a, b), OP.mult)
+
+    def both(a, b):
+        tt(X("sw", a, b), X("p0", a, b), X("psw", a, b), OP.add)
 
     def keep(j):
         where(X("p0", 512 * j, 512 * j + 512), X("sw", 512 * j, 512 * j + 512), [[1, 512]], 0, 0)
 
     nc = SHARE["cm"]
-    first(3)
-    first(2)
-    second(3)
-    for j in (3, 2, 1, 0):
-        a, b = 512 * j, 512 * j + 512
-        tt(X("sw", a, b), X("p0", a, b), X("psw", a, b), OP.add)
-        if j > 0:
-            second(j - 1)
-        if j > 1:
-            first(j - 2)
-            keep(j)
-    act(X("cmr", 0, nc), numbers("mate", 0, nc // 16, Z + 16))
+    nc, nd = nc
+    tt(X("p0", 1024, V), IX("xf", Z, "nb16", 64, 128), X("wr", 1024, V), OP.mult)
+    columns()
+    second(1536, V)
+    second(1024, 1536)
+    both(1536, V)
+    keep(3)
+    first(1)
+    both(1024, 1536)
+    keep(2)
+    act(X("sb", 0, 384), numbers("bl16", 0, 24, V))
+    show("num", "sb", "sp")
+    act(X("sp", mine, mine + C), X("sb", C * r, C * r + C))
+    second(512, 1024)
+    first(0)
+    second(0, 512)
+    both(512, 1024)
+    both(0, 512)
+    if nc:
+        act(X("cmr", 0, nc), numbers("mate", 0, nc // 16, Z + 16))
     cp(X("sst", 0, 192), IX("sw", V, "bl16", 0, 12))
     act(X("sst", 192, 384), IX("sw", V, "bl16", 12, 24))
     show("s", "sst", "sw")
@@ -632,13 +662,19 @@ def rank_program(g, core, T, topo):
     keep(1)
     keep(0)
 
-    cp(X("cmr", nc, V), numbers("mate", nc // 16, 128, Z + 16))
-    cp(X("iv16", 0, 128), X("pb", 0, 128))
-    pick("pc", 0, "cmr", 0, "g8", 0, 8, "cm")
     mm(X("pd", 0, 128), IF, X("cn", 0, 128), True, False, tag="cm")
+    scatter()
+    if nd > nc:
+        act(X("cmr", nc, nd), numbers("mate", nc // 16, nd // 16, Z + 16))
+    if nd < V:
+        cp(X("cmr", nd, V), numbers("mate", nd // 16, 128, Z + 16))
+    inverse()
+    pick("pc", 0, "cmr", 0, "g8b", 0, 8, "cm")
     last = len(CUTS) - 2
     for j, (b, a) in enumerate(zip(CUTS, CUTS[1:])):
         tt(X("tw", a, b), IX("sw", Z + 16, "mate", a // 16, b // 16), X("p0", a, b), OP.add)
+        if j == 0:
+            cp(X("iv16", 0, 128), X("pb", 0, 128))
         o, i = X("g1", a, b), IX("tw", V + 8, "iv16", a // 16, b // 16, a)
         if j == last:
             cp(o, i)
@@ -648,7 +684,7 @@ def rank_program(g, core, T, topo):
         if j == CM:
             act(X("cmt", 0, 128), X("pc", 0, 128))
             mm(X("pd", 0, 128), X("cmt", 0, 128), IF, False, True, tag="cm")
-        if j == CM + 1:
+        if j == CM + 2:
             act(X("cmv", 0, 128), X("pd", 0, 128))
             dma("Y", "cm", T.cm[:, :], [], T.cmv[:, :], rg(X("cmv", 0, 128)))
     for s, v in total.items():

@@ -1,39 +1,55 @@
 from concourse.bass import DstId, RemoteDMATransfer
-from concourse.mybir import AluOpType, ActivationFunctionType
+from concourse.mybir import AluOpType, ActivationFunctionType, AxisListType
 
 OP = AluOpType
 AF = ActivationFunctionType
 V, C, Z = 2048, 96, 2432
 BIG, MID = 16384.0, 1216.0
-OFFG, OFFC = 128 * 517, 128 * 129
+OFFN, OFFC = 8192 + 128, 1024 + 128
 F32, BF, F16, I32, U16 = "float32", "bfloat16", "float16", "int32", "uint16"
 WIDTHS = {
-    F32: dict(dn=128, nbm=256, hlm=256, mb=384, col=128, ir=128, iff=128, own=256, nth=128, tq=128, xf=2432, cn=128,
-              vl=16, off=16, g1=2048, p0=2048, sw=2448, sst=384, cmt=128, cmv=128, tw=2056,
-              xb=384, g8=8),
-    BF: dict(wsb=2048, xw=2448, xc=2048, nw=2432, bst=384, hb=2048, hl=2432, hst=384, xst=384, gb=8192, wr=2048, ti=256, nti=256,
-             ibn=128, i8=256, cst=384, pm=8, sel=48, selw=8, seli=64, wt=128, e0=272, e1=256, ar=288, ar3=256, m2=128, nr2=256,
-             nr3=256, ww=1024, wv=1024, one=128, zero=144, ru=256, mk=1024, blk=128, lt=128, lte=128, b0=144, lt0=144, q0=144,
-             wq=288, km=256, rb=256, inv=2448, selr=128, selq=128, bt=128, irb=128, left=128, sp=2448, sb=384, cmr=2048,
-             hilo=256, two=256, half=288, g8b=8),
-    F16: dict(pz2=256, pz3=256, ih=128, ivt=128, hrow=768, g8h=144),
-    I32: dict(bli=24, nbi=256, ci=64, cj=64, yi=256, yj=256, zi=256, zj=256, bki=48, gli=24),
-    U16: dict(gl16=24, bl16=24, hl16=256, idx=512, mate=128, off16=16, iv16=128, nb16=256, bk16=48, hb16=48),
+    F32: dict(dn=128, nbm=256, hlm=256, mb=384, col=128, ir=144, iff=128, xf=2432, cn=128, stm=72,
+              vl=16, off=16, g1=2048, p0=2048, sw=2448, sst=384, cmt=128, cmv=128, tw=2056, xb=384, fld=768),
+    BF: dict(wsb=2048, xw=2448, xc=2048, bst=384, hb=2048, hl=2432, hh=2432, hhh=2432, hst=384, cst=384, dst=384,
+             xst=384, gb=4096, wr=2048, ti=256, nti=256, ibn=128, dg=512, pm=8, selw=8, seli=64, e0=400, e1=272,
+             e2=512, ar=272, ar3=384, m2=128, nr2=256, nr3=256, wv=1024, one=128, zero=144, ru=256, mk=1024, blk=128, lt=128,
+             lte=128, b0=144, lt0=144, q0=144, wq=288, km=256, rb=256, inv=2448, selr=128, selq=128, bt=128, left=128,
+             nw=2432, sp=2448, sb=384, cmr=2048, hilo=256, two=256, half=288, g8b=8, g8h=144, pw=256),
+    F16: dict(pz2=256, pz3=256, ivt=128, hrow=768, c16=256),
+    I32: dict(bli=24, nbi=256, ci=24, cj=32, yj=256, zj=256, bki=48, gli=24),
+    U16: dict(gl16=24, bl16=24, hl16=256, idx=256, mate=128, off16=16, iv16=128, nb16=256, bk16=48, hb16=48),
 }
+SPD = 1
+SPW = ("sp", "nw", "hhh")[SPD]
+WIDTHS[BF]["hhh"] = 2448
+if SPD == 1:
+    for _n in ("nw", "sb", "cmr"):
+        WIDTHS[F32][_n] = WIDTHS[BF].pop(_n) + (16 if _n == "nw" else 0)
 PSUM = {"psw": 2048, "pa": 512, "pb": 512, "pc": 512, "pd": 512}
-SCRATCH = {"fld": ("sbuf", [128, 4, 256], F32)}
+SCRATCH = {"tg": ("sbuf", [128, 6, 128], F32), "sel": ("sbuf", [128, 4, 16], BF)}
 for _d in WIDTHS:
     for _n in WIDTHS[_d]:
         SCRATCH[_n] = ("sbuf", [128, WIDTHS[_d][_n]], _d)
 for _n in PSUM:
     SCRATCH[_n] = ("psum", [128, 8, 64] if _n == "pa" else [128, PSUM[_n]], F32)
-SHARE = {"nh": 1024, "nl": (448, 896), "r2": (896, 1024, 896, 832), "r3": (1024, 896), "x": 1344, "sp": 10, "cm": (0, 1536)}
-STEPS = (384, 384, 416, 416, 448)
+SHARE = {"ghost": 2, "bst": 24, "hh": 1024, "hhh": 960, "hhhh": 960, "l": 1024, "r3": (1024, 896), "x": 1344, "sp": 10, "cm": (0, 1536)}
+STEPS = (256, 384, 448, 480, 480)
 BOTH = {1: "pd", 0: "pc"}
 CUTS = (2048, 1792, 1408, 1024, 640, 256, 0)
-CM = 0
-EXCH = ["name", "hl", "w1", "w2", "x", "xs", "num", "s"]
-LOADS = ["bl", "gl", "nb", "w", "x", "xc", "wr", "cm"] + ["y%d" % _j for _j in range(len(CUTS) - 1)]
+CM = 3
+NUM = 1
+EARLY = 0
+BASE = 7
+NUMQ = "SSSS"
+INV = 768
+GL = 1
+RANK = 0
+RU = 0
+RUQ = "V"
+INVAT = 1
+LESSAT = 0
+EXCH = ["name", "hl", "hh", "hhh", "w2", "x", "xs", "num", "s"]
+LOADS = ["bl", "gl", "nb", "w", "m1", "m2", "m3", "x", "xc", "wr", "sp", "cm"] + ["y%d" % _j for _j in range(len(CUTS) - 1)]
 SEMAPHORES = ["cV", "cS", "cP", "cG"] + ["d_" + k for k in LOADS] + ["a_" + k for k in EXCH] + ["l_" + k for k in EXCH]
 
 
@@ -108,9 +124,9 @@ def rank_program(g, core, T, topo):
             ap = T[name][p0:p1, c0:c1] if step == 1 else T[name][p0:p1, c0:c1:step]
         return ap, [(name, p0, p1, c0, c1)]
 
-    def F(i0, i1, j0, j1):
-        ap = T.fld[:, i0:i1, j0:j1] if i1 - i0 > 1 else T.fld[:, i0, j0:j1]
-        return ap, [("fld", 0, 128, i * 256 + j0, i * 256 + j1) for i in range(i0, i1)]
+    def TG(i0, i1=None, step=1):
+        ap = T.tg[:, i0, :] if i1 is None else T.tg[:, i0:i1:step, :]
+        return ap, [("tg", 0, 128, 128 * i, 128 * i + 128) for i in range(i0, i1 or i0 + 1, step)]
 
     def IX(win, b, offs, c, d, a=0):
         return T[win][:, a:b].indirect(T[offs][:, c:d]), [(win, 0, 128, a, b), (offs, 0, 128, c, d)]
@@ -137,6 +153,12 @@ def rank_program(g, core, T, topo):
     def cp(out, a, tag=None):
         add("V", lambda e: e.tensor_copy(out=out[0], in_=a[0]), rg(out), rg(a), tag=tag)
 
+    def fill(out, value):
+        add("V", lambda e: e.memset(out[0], value), rg(out), [])
+
+    def scan(out, a, b, first, op0, op1):
+        add("V", lambda e: e.tensor_tensor_scan(out[0], a[0], b[0], first, op0, op1), rg(out), rg(a, b))
+
     def act(out, a, bias=0.0, scale=1.0, tag=None, func=AF.Identity):
         if isinstance(bias, float) and isinstance(scale, float) and bias == 0.0 and scale == 1.0:
             f = lambda e: e.activation(out=out[0], in_=a[0], func=func)
@@ -157,7 +179,10 @@ def rank_program(g, core, T, topo):
     def where(out, a, pattern, base, cm, op=OP.is_ge, fill=0.0):
         add("G", lambda e: e.affine_select(out[0], a[0], pattern, op, fill, base, cm), rg(out), rg(a))
 
-    def dma(q, key, out_ap, outs, in_ap, ins):
+    def dma(q, key, out_ap, outs, in_ap, ins, behind=None):
+        if behind and known[q].get("l_" + behind, 0) < total["l_" + behind]:
+            queue[q].wait_ge(T.sem["l_" + behind], total["l_" + behind])
+            known[q]["l_" + behind] = total["l_" + behind]
         add(q, lambda e: e.dma_start(out=out_ap, in_=in_ap), outs, ins, sem="d_" + key, inc=16)
 
     plans = {c: engine_plan(topo, c, cores) for c in cores}
@@ -185,31 +210,62 @@ def rank_program(g, core, T, topo):
         send(key, lambda d: X(stage, C * d, C * d + C), X(win, mine, mine + C))
         recv(key, [(win, 0, 128, V + C * q, V + C * q + C) for q in others])
 
+    def border(key, stage, win, make, engines="VVSS"):
+        runs = []
+        for q in others:
+            if runs and runs[-1][2] == q and engines[q] == runs[-1][0]:
+                runs[-1][2] = q + 1
+            else:
+                runs.append([engines[q], q, q + 1])
+        for e, q0, q1 in runs:
+            make(e, X(stage, C * q0, C * q1), q0, q1)
+        if key:
+            show(key, stage, win)
+        make(engines[r], X(win, mine, mine + C), r, r + 1)
+
     def spread(key, win):
         own = X(win, 256 * r, 256 * r + 256)
         send(key, lambda d: own, own)
         recv(key, [(win, 0, 128, 256 * q, 256 * q + 256) for q in others])
 
-    def pick(bank, c0, src, s0, sel, w0, w1, tag):
-        n = 16 * (w1 - w0)
+    def pick(bank, c0, src, s0, sel, n, tag, alone=True):
         for b in range(16):
-            mm(X(bank, c0 + b, c0 + n, 16), X(src, s0 + b, s0 + V, 16), X(sel, w0, w1), tag=tag)
+            mm(X(bank, c0 + b, c0 + 128 * n, 16), X(src, s0 + b, s0 + V, 16), sel, alone, alone or b == 15, tag=tag)
+
+    def move(q, out, a):
+        (cp if q == "V" else act)(out, a)
 
     def gather(q, dst, a, win, w, offs, o, c0, c1):
-        (cp if q == "V" else act)(X(dst, a + c0, a + c1), IX(win, w, offs, o + c0 // 16, o + c1 // 16))
+        move(q, X(dst, a + c0, a + c1), IX(win, w, offs, o + c0 // 16, o + c1 // 16))
 
     def share(dst, a, win, w, offs, o, n):
         gather("V", dst, a, win, w, offs, o, 0, n)
         gather("S", dst, a, win, w, offs, o, n, V)
 
-    IB, TI, IH, IF = X("ti", 0, 128), X("ti", 0, 256), X("ih", 0, 128), X("iff", 0, 128)
-    ONE, ZERO, G8, DIAG = X("one", 0, 128), X("zero", 0, 128), X("g8", 0, 8), [[-1, 128]]
-    M8, TX, PW, DC, QM = 0, 8, 12, 16, 48
-    K0, S8, SA, BA, SIDEA, SIDEB, WG, WC, W64, QW = (col(j) for j in range(20, 30))
-    B4 = col(QM)
+    def lister(win, w, offs, o=0):
+        return lambda e, out, q0, q1: move(e, out, IX(win, w, offs, o + 6 * q0, o + 6 * q1))
 
-    def MC(x):
-        return col(32 + x)
+    def merge(key, src, p0, p1, n=Z, a=0):
+        for i in range(2):
+            dma("Y", key, T.hl[p1 + i:128:16, a:n], [("hl", 16 * k + p1 + i, 16 * k + p1 + i + 1, a, n) for k in range(8)],
+                T[src][p0 + i:128:16, a:n], rg(X(src, a, n)))
+
+    IB, TI, IF = X("ti", 0, 128), X("ti", 0, 256), X("iff", 0, 128)
+    ONE, ZERO, G8, DIAG = X("one", 0, 128), X("zero", 0, 128), X("g8b", 0, 8), [[-1, 128]]
+    P2, P4, N4, PB = (X("dg", 128 * j, 128 * j + 128) for j in range(4))
+    M8 = 0
+    M81, M85, A04, A15, ST, N13 = (col(j) for j in range(8, 14))
+    FIRST, SA, BA, SIDEA, SIDEB, W8, QW, U0, U1 = (col(j) for j in range(18, 27))
+
+    def MC(x, n=1):
+        return col(32 + x, n)
+
+    def STM(i):
+        j = i if 0 < i < 8 else 20 + i // 8
+        return X("stm", j, j + 1)
+
+    def sum_of(out, a):
+        add("V", lambda e: e.tensor_reduce(out[0], a[0], AxisListType.X, OP.add), rg(out), rg(a))
 
     def diagonal(out, value):
         where(out, ZERO, DIAG, 0, 1, OP.not_equal, value)
@@ -220,385 +276,405 @@ def rank_program(g, core, T, topo):
     for d in range(2):
         dma("Y", "w", T.wsb[8 * d:8 * d + 8, :], rg(X("wsb", 0, V, 1, 8 * d, 8 * d + 8)), T.w[:, V * d:V * d + V], [])
 
-    iota(X("ci", 0, 24), [[-1, 24]], 40, 1, True)
-    iota(X("zero", 0, 144), [[0, 144]], 0, 0)
-    iota(X("ir", 0, 128), [[1, 128]], 0, 0)
-    iota(X("ci", 24, 28), [[-4, 4]], 16, 1, True)
-    diagonal(IB, 1.0)
-    iota(X("ci", 32, 40), [[-16, 8]], 0, 1, True)
     PM = X("pm", 0, 8, 1, 0, 16)
-
-    def fill(x):
-        add("V", lambda e: e.memset(T.col[:, PW + x:PW + x + 1], 64.0 ** -x), rg(col(PW + x)), [])
-
+    E1, E2, D0, D1 = (X("pw", 64 * j, 64 * j + 64) for j in range(4))
+    iota(X("ci", 0, 16), [[-1, 16]], 16, 1, True)
+    iota(X("ci", 16, 24), [[1, 8]], 9, 1, True)
+    for o, value in ((X("zero", 0, 144), 0.0), (X("ir", 40, 60), 0.0), (E1, 0.0), (E2, -0.875), (X("ir", 40, 41), 8192.0),
+                     (X("ir", 41, 42), 128.0)):
+        fill(o, value)
+    for o, value in ((X("ir", 58, 59), 2048.0 * r), (X("ir", 59, 60), -1.0), (X("pw", 0, 64, 8), 1.0), (X("pw", 64, 128, 8), -1.0),
+                     (ONE, 1.0), (X("g8h", 0, 144), 0.0)):
+        act(o, X("zero", 0, o[0].shape[1]), value)
+    iota(X("ir", 0, 8), [[64, 8]], 0, 0)
+    iota(X("ir", 8, 33), [[512, 25]], -6144, 0)
+    where(PM, X("zero", 0, 8, 1, 0, 16), [[-1, 8]], -8, 1, OP.not_equal, 1.0)
+    diagonal(IB, 1.0)
+    where(PM, PM, [[-1, 8]], 0, 1, OP.not_equal, -1.0)
     send("name", lambda d: X("bli", 6 * d, 6 * d + 6), X("gli", 6 * r, 6 * r + 6))
     recv("name", [("gli", 0, 128, 6 * q, 6 * q + 6) for q in others])
-    fill(0)
-    fill(1)
-    ts(X("cj", 0, 8), X("ci", 0, 8), 7, OP.bitwise_and)
-    ts(X("cj", 32, 48), X("ci", 8, 24), 15, OP.bitwise_and)
-    fill(2)
-    ts(col(M8, 8), X("cj", 0, 8), 0.0, OP.is_equal)
-    ts(col(30), X("cj", 1, 2), 0.0, OP.is_equal, 2.0 * r, OP.mult)
-    ts(col(31), X("cj", 3, 4), 0.0, OP.is_equal, 4.0 * r, OP.mult)
-    fill(3)
-    cp(X("g8h", 0, 144), X("zero", 0, 144))
-    act(X("irb", 0, 128), X("ir", 0, 128))
-    ts(col(TX, 4), X("ir", 0, 4), col(M8 + 2), OP.mult, col(30), OP.add)
-    ts(col(PW, 4), col(PW, 4), col(M8 + 4), OP.mult, col(31), OP.add)
-    ts(X("cj", 48, 52), X("ci", 24, 28), 2, OP.logical_shift_right, 3, OP.bitwise_and)
-    tt(col(TX, 4), col(TX, 4), col(PW, 4), OP.add)
-    ts(col(32, 20), X("cj", 32, 52), 0.0, OP.is_equal)
-    act(S8, col(M8 + 4), 1.0, -0.875)
-    act(col(DC + 1), col(M8 + 1), col(M8 + 3))
-    act(col(DC + 2), col(M8 + 3), 0.0, 2.0)
-    act(col(DC + 3), col(M8 + 3), col(M8 + 1), 3.0)
-    act(K0, col(M8 + 3), col(M8 + 1), 2.0)
-    tt(PM, X("ti", 8, 16, 1, 0, 16), X("ti", 0, 8, 1, 0, 16), OP.subtract)
-    for x in range(4):
-        ts(X("nw", x, 512, 4), X("irb", 0, 128), col(M8), OP.mult, col(TX + x), OP.add, tag="nw")
-    act(WG, col(M8 + 3), col(M8 + 2), 512.0)
-    act(WC, col(M8 + 1), col(M8), 128.0)
-    act(WG, col(M8), WG, 4.0)
-    act(SIDEA, col(QM), col(QM + 1))
-    act(SIDEB, col(QM + 2), col(QM + 3))
-    act(col(55), MC(4), 0.0, 2.0 ** -20)
-    act(col(57), MC(12), 0.0, 2.0)
-    act(X("nw", 512, 1024), X("nw", 0, 512), col(DC + 1))
+    ts(X("cj", 0, 24), X("ci", 0, 24), 15, OP.bitwise_and)
+    ts(X("cj", 24, 26), X("ci", 1, 6, 4), 7, OP.bitwise_and)
+    ts(X("cj", 26, 28), X("ci", 0, 2), 3, OP.bitwise_and)
+    ts(MC(0, 28), X("cj", 0, 28), 0.0, OP.is_equal)
+    tt(col(64, 20), MC(8, 20), X("ir", 40, 60), OP.mult)
+    ts(D1, E1, MC(25), OP.mult, MC(24), OP.add)
+    ts(D0, E2, MC(13), OP.mult, 1.0, OP.add)
+    ts(X("stm", 0, 33), X("ir", 0, 33), MC(26), OP.mult)
+    sum_of(FIRST, col(64, 20))
+    act(A04, MC(0), MC(4))
+    act(A15, MC(1), MC(5))
+    act(U0, A04, A15)
+    act(U1, A15, 0.0, 128.0)
+    act(SA, MC(13), U0, 2.0 ** 21)
+    act(BA, A04, U1, 8192.0)
+    add("V", lambda e: e.tensor_tensor_scan(T.nw[:, 0:64], D0[0], D1[0], FIRST[0], OP.mult, OP.add), rg(X("nw", 0, 64)), rg(D0, D1, FIRST))
+    ts(X("bki", 24, 48), X("bli", 0, 24), 15, OP.bitwise_and)
+    ts(X("bki", 0, 24), X("bli", 0, 24), 4, OP.logical_shift_right)
+    ts(X("nw", 64, 128), X("nw", 0, 64), STM(1), OP.add)
+    cp(X("bk16", 0, 48), X("bki", 0, 48))
+    ts(X("nw", 128, 192), X("nw", 0, 64), STM(2), OP.add)
+    ts(X("nw", 192, 256), X("nw", 0, 64), STM(3), OP.add)
+    tt(X("dn", 0, 128), X("nbi", 128, 256), X("nbi", 0, 128), OP.subtract)
+    ts(X("nw", 256, 512), X("nw", 0, 256), STM(4), OP.add)
+    G8H, SEL, PAIRS = X("g8h", 16, 144, 16), (T.sel[:, :, :], [("sel", 0, 128, 0, 64)]), [[-2, 4], [-8, 2], [-16, 8]]
+
+    def SF(a, b, step=1):
+        if step == 0:
+            return T.sel[:, a, 8 * b:8 * b + 8], [("sel", 0, 128, 16 * a + 8 * b, 16 * a + 8 * b + 8)]
+        return T.sel[:, a:b:step, :], [("sel", 0, 128, 16 * a, 16 * b)]
+
+    where(G8H, X("one", 0, 8), [[-16, 8]], 0, 1)
+    where(SEL, X("zero", 0, 64), PAIRS, 0, 1, OP.not_equal, 1.0)
+    where(G8H, G8H, [[16, 8]], 15, -1)
+    where(SEL, SEL, PAIRS, -1, 1, OP.not_equal, 1.0)
+    iota(TG(1, 3), [[0, 16], [1, 16]], V * r + OFFN, 16)
+    for (a, j), p, value in (((1, 1), 0, -1.0), ((2, 0), 4, 0.125), ((2, 1), 12, 0.0), ((1, 1), 1, -1.0)):
+        where(SF(a, j, 0), SF(a, j, 0), [[-16, 8]], -p, 1, OP.not_equal, value)
+    diagonal(IF, 1.0)
 
     for b in range(16):
         mm(X("pa", b, 128, 16), X("wsb", b, V, 16, 0, 16), PM, tag="wt")
-    ts(X("bki", 24, 48), X("bli", 0, 24), 15, OP.bitwise_and)
-    ts(X("bki", 0, 24), X("bli", 0, 24), 4, OP.logical_shift_right)
-    tt(X("dn", 0, 128), X("nbi", 128, 256), X("nbi", 0, 128), OP.subtract)
-    cp(X("bk16", 0, 48), X("bki", 0, 48))
+    act(X("mb", 0, 384), IX("col", 48, "bk16", 24, 48, 32))
     ts(X("bt", 0, 128), X("pa", 0, 128), 0.0, OP.is_gt)
     mm(X("pb", 0, 128), X("bt", 0, 128), IB)
     ts(X("nbm", 0, 256), X("nbi", 0, 256), MID, OP.subtract)
     tt(X("pb", 0, 128), X("pb", 0, 128), X("dn", 0, 128), OP.mult)
-    ts(X("cj", 56, 64), X("ci", 32, 40), 4, OP.arith_shift_right)
+    cp(X("bl16", 0, 24), X("bli", 0, 24))
     tt(X("hlm", 0, 128), X("nbm", 0, 128), X("pb", 0, 128), OP.add)
     tt(X("hlm", 128, 256), X("nbm", 128, 256), X("pb", 0, 128), OP.subtract)
-    ts(X("g8h", 16, 144, 16), X("cj", 56, 64), 0.0, OP.is_equal)
-    ts(G8, X("cj", 56, 64), 0.0, OP.is_equal)
-    act(X("mb", 0, 384), IX("col", 48, "bk16", 24, 48, 32))
-    for j in (2, 3):
-        act(X("nw", 512 * j, 512 * j + 512), X("nw", 0, 512), col(DC + j), S8)
-    for q in range(4):
-        act(col(80 + q), K0, 0.0, 2.0 * (q - r))
-    for f, (w, side) in ((0, (WG, SIDEA)), (1, (WG, SIDEB)), (2, (WC, SIDEA)), (4, (WC, SIDEB))):
-        act(col(52 + f), w, 0.0, side)
-    diagonal(IF, 1.0)
-    act(SA, MC(4), B4, 2.0 ** 21)
-    act(BA, B4, 0.0, 128.0)
+    for j in (1, 2, 3):
+        act(X("nw", 512 * j, 512 * j + 512), X("nw", 0, 512), STM(8 * j))
     for K, bank in enumerate(("pc", "pd")):
         tt(X("hrow", 384 * K, 384 * K + 384), IX("hlm", 128 * K + 128, "bk16", 0, 24, 128 * K), X("mb", 0, 384), OP.mult)
         for b in range(16):
             mm(X(bank, 0, 24), X("g8h", 16 - b, 144 - b), X("hrow", 384 * K + b, 384 * K + 384, 16), b == 0, b == 15, tag="border")
-    ts(X("hl16", 0, 256), X("hlm", 0, 256), MID, OP.add)
-    cp(X("gl16", 0, 24), X("gli", 0, 24))
+        if K == 0:
+            ts(X("hl16", 0, 256), X("hlm", 0, 256), MID, OP.add)
+        if K == GL:
+            cp(X("gl16", 0, 24), X("gli", 0, 24))
     for q in range(4):
         o, i = X("nw", V + C * q, V + C * q + C), IX("nw", V, "gl16", 6 * q, 6 * q + 6)
-        if q < 2:
-            ts(o, i, col(80 + q), OP.add)
+        if q < SHARE["ghost"]:
+            ts(o, i, STM(32 * (q - r)), OP.add)
         else:
-            act(o, i, col(80 + q))
+            act(o, i, STM(32 * (q - r)))
     ts(X("hb16", 0, 24), X("pc", 0, 24), MID, OP.add)
-    iota(ONE, [[0, 128]], 1, 0)
-    iota(X("own", 0, 128), [[0, 8], [1, 16]], V * r + OFFG, 16)
-    iota(X("own", 128, 256), [[0, 8], [1, 16]], V * r, 16)
-    for c0, value in ((0, 2.0), (64, 1.0)):
-        where(X("wt", c0, c0 + 64), X("zero", 0, 64), [[-1, 64]], 0, 1, OP.not_equal, value)
-        where(X("wt", c0, c0 + 64), X("wt", c0, c0 + 64), [[-1, 64]], -64, 1, OP.not_equal, 8.0 * value)
-    iota(X("e0", 256, 272), [[0, 16]], 0, 0)
-    HZ, ROW = (X("psw", 1408, 1536), X("psw", 1920, 2048)), X("one", 0, 128, 1, 0, 1)
+
+    def heavy(a, b):
+        act(X("hb", a, b), IX("nw", Z, "hl16", a // 16, b // 16), BA, SA)
+
+    def light(a, b):
+        tt(X("hl", a, b), IX("nw", Z, "hl16", 128 + a // 16, 128 + b // 16), X("hb", a, b), OP.max)
+
+    a, nb_ = STEPS[0], SHARE["bst"]
+    if nb_ < 24:
+        act(X("bst", 16 * nb_, 384), IX("nw", Z, "hb16", nb_, 24), BA, SA)
+    act(X("hl", 0, a), IX("nw", Z, "hl16", 0, a // 16), BA, SA)
+    act(X("hb", 0, a), IX("nw", Z, "hl16", 128, 128 + a // 16))
+    merge("m1", "hb", 8, 8, a)
+    ts(X("bst", 0, 16 * nb_), IX("nw", Z, "hb16", 0, nb_), SA, OP.mult, BA, OP.add)
+    ts(X("hb16", 24, 48), X("pd", 0, 24), MID, OP.add)
+    border("hl", "hst", "hl", lambda e, out, q0, q1: tt(out, IX("nw", Z, "hb16", 24 + 6 * q0, 24 + 6 * q1), X("bst", C * q0, C * q1), OP.max), "VVVV")
+    for n in STEPS[1:]:
+        heavy(a, a + n)
+        light(a, a + n)
+        a += n
+    for m, value in ((P4, 4.0), (PB, BIG), (N4, -4.0)):
+        diagonal(m, value)
+    iota(TG(4), [[0, 128]], 0, 0)
+    HZ, ROW = (X("psw", 1024, 1152), X("psw", 1152, 1280)), X("one", 0, 128, 1, 0, 1)
     for K in range(2):
         mm(HZ[K], X("hlm", K * 128, K * 128 + 128), IF)
 
-    ts(X("bst", 0, 192), IX("nw", Z, "hb16", 0, 12), SA, OP.mult, BA, OP.add)
-    act(X("bst", 192, 384), IX("nw", Z, "hb16", 12, 24), BA, SA)
-    ts(X("hb16", 24, 48), X("pd", 0, 24), MID, OP.add)
-    tt(X("hst", 0, 384), IX("nw", Z, "hb16", 24, 48), X("bst", 0, 384), OP.max)
-    show("hl", "hst", "hl")
-    a = 0
-    for n in STEPS:
-        act(X("hb", a, a + n), IX("nw", Z, "hl16", a // 16, (a + n) // 16), BA, SA)
-        tt(X("hl", a, a + n), IX("nw", Z, "hl16", 128 + a // 16, 128 + (a + n) // 16), X("hb", a, a + n), OP.max)
-        a += n
-    act(X("hl", mine, mine + C), X("hst", C * r, C * r + C))
-    for f in (2, 3, 4, 5, 0, 1):
-        act(X("sel", 8 * f, 8 * f + 8), G8, 0.0, col(52 + f))
-    pick("pa", 0, "hl", 0, "sel", 16, 48, "own")
+    pick("pa", 0, "hl", 0, SF(0, 4, 2), 4, "own")
+    border("hh", "cst", "hh", lister("hl", Z, "hb16"))
+    share("hh", 0, "hl", Z, "hl16", 0, SHARE["hh"])
+    pick("pc", 0, "hh", 0, SF(0, 4, 2), 4, "hh")
     LESS = 768
-    diagonal(X("i8", 0, 128), 8.0)
-    diagonal(X("i8", 128, 256), -8.0)
-    iota(X("cst", 0, 384, 1, 0, 1), [[1, 3], [0, 128]], 6, 0)
-    iota(X("ar", 128, 144), [[0, 16]], 0, 0)
-    iota(X("ar", 272, 288), [[0, 16]], 0, 0)
+    HN, OWN, LN, HH = TG(0), TG(1), TG(3), TG(5)
+    if LESSAT == 0:
+        act(TG(0, 4, 3), X("pa", 0, 256))
+    where(G8, X("one", 0, 8), [[-16, 8]], 0, 1)
+    iota(X("e0", 128, 136), [[0, 8]], 0, 0)
+    iota(X("ar", 128, 136), [[0, 8]], 0, 0)
+    iota(X("ar", 264, 272), [[0, 8]], 0, 0)
+    where(G8, G8, [[16, 8]], 15, -1)
     where(X("ti", 128, 256), ZERO, DIAG, 0, 1, OP.is_ge, 1.0)
+    T1, NHL, B, EH2 = X("e0", 0, 128), X("e0", 144, 272), X("e1", 0, 128), X("e1", 128, 256)
+    border("hhh", "dst", "hhh", lister("hh", Z, "hb16"))
+    merge("m2", "hh", 0, 2)
+    merge("m2", "hh", 8, 6)
+    share("hhh", 0, "hh", Z, "hl16", 0, SHARE["hhh"])
+    pick("pb", 0, "hhh", 0, SF(0, 1), 2, "hhh")
+    merge("m3", "hhh", 0, 10, V)
+    merge("m3", "hhh", 0, 10, Z, V)
+    tt(T1, X("pc", 0, 128), OWN, OP.is_equal)
+    tt(NHL, X("pc", 128, 256), OWN, OP.not_equal)
+    tt(X("psw", LESS, LESS + 256), X("pa", 0, 256), TG(1, 3), OP.is_lt)
+    if LESSAT == 1:
+        act(TG(0, 4, 3), X("pa", 0, 256))
+    act(X("fld", 0, 256), X("pc", 256, 512))
+    act(HH, X("pc", 0, 128))
+    act(X("fld", 256, 384), X("pc", 256, 384), -float(OFFC))
 
-    def pack(bank, parts, first=True, last=True):
-        for c in range(4):
-            for i, (name, c0, w0) in enumerate(parts):
-                digits = X(name, c0 + 4 * c, c0 + 4 * c + 128)
-                stop = i == len(parts) - 1 if first else last and c == 3
-                mm(X(bank, c, 256, 4), digits, X("wt", w0, w0 + 64), first and i == 0, stop, tag="pack")
-
-    share("gb", 0, "hl", Z, "hl16", 0, SHARE["nh"])
-    pick("pc", 0, "gb", 0, "sel", 0, 32, "nh")
-    n1, n2 = SHARE["nl"]
-    act(F(0, 1, 0, 128), X("pa", 256, 384), float(OFFC))
-    act(F(1, 2, 0, 256), X("pa", 0, 256))
-    act(F(0, 1, 128, 256), X("pa", 384, 512))
-    act(X("gb", V + n2, 2 * V), IX("hl", Z, "hl16", 128 + n2 // 16, 256))
-    cp(X("gb", V, V + n1), IX("hl", Z, "hl16", 128, 128 + n1 // 16))
-    T1, VI = X("e0", 0, 128), X("e0", 128, 256)
-    tt(X("e0", 0, 256), X("pc", 0, 256), X("own", 0, 256), OP.is_equal)
-    pack("pd", [("e0", 0, 0), ("e0", 128, 64)])
-    TH, DM = 1536, 128
-    for K in range(2):
-        mm(X("psw", TH + K * 128, TH + K * 128 + 128), F(K, K + 1, 0, 128), IF)
-    tt(X("psw", DM, DM + 256), X("pc", 256, 512), F(1, 2, 0, 256), OP.subtract)
-    cp(X("ww", 256 * r, 256 * r + 256), X("pd", 0, 256))
-    spread("w1", "ww")
-    cp(X("gb", V + n1, V + n2), IX("hl", Z, "hl16", 128 + n1 // 16, 128 + n2 // 16))
-    pick("pa", 0, "gb", V, "sel", 0, 32, "nl")
-    ts(X("idx", 0, 256), X("psw", TH, TH + 256), float(OFFC), OP.subtract)
-    act(F(2, 3, 0, 256), X("pc", 256, 512))
-    mm(X("pb", 0, 128), F(2, 3, 0, 128), IF)
-    act(W64, MC(1), MC(0), 64.0)
-    act(W64, MC(2), W64, 64.0 ** 2)
-    act(W64, MC(3), W64, 64.0 ** 3)
-    act(X("selw", 0, 8), G8, 0.0, W64)
-    cp(X("bl16", 0, 24), X("bli", 0, 24))
-    cp(IH, IB)
-    for K in range(2):
-        tt(X("psw", DM + 128 * K, DM + 128 * K + 128), X("psw", DM + 128 * K, DM + 128 * K + 128), VI, OP.mult)
-    act(F(3, 4, 0, 256), X("pa", 256, 512))
-    tt(X("e1", 0, 256), X("pa", 0, 256), X("own", 0, 256), OP.is_equal)
-    mm(X("pb", 128, 256), F(3, 4, 0, 128), IF)
-    UL, LL, LH = X("psw", 1024, 1152), X("psw", 1152, 1280), X("psw", 1280, 1408)
-    P8, N8, EA, EB = X("i8", 0, 128), X("i8", 128, 256), X("e1", 0, 128), X("e1", 128, 256)
-    mm(X("psw", 1024, 1408), ROW, X("cst", 0, 384, 1, 0, 1), True, False, tag="bound")
-    terms = ((LH, P8, T1), (LH, N8, VI), (LL, P8, T1), (LL, P8, T1), (UL, N8, EA), (LL, N8, EA), (LL, N8, EB))
-    for i, (o, m, e) in enumerate(terms):
-        mm(o, m, e, False, i == len(terms) - 1, tag="bound")
-
-    words = [("ww", 0, 128, 0, 1024)]
-    dma("Y", "x", T.xw[:, 0:V], rg(X("xw", 0, V)), T.x[:, :], words)
-    dma("Y", "xc", T.xc[:, :], rg(X("xc", 0, V)), T.x[:, :], [])
-    a = 512 * len(BOTH)
-    for c in range(16):
-        dma("Y", "wr", T.wr[c:128:16, a:V], [("wr", 16 * k + c, 16 * k + c + 1, 0, V) for k in range(8)], T.w[:, a:V], [])
+    dma("Y", "x", T.xw[:, 0:V], rg(X("xw", 0, V)), T.x[:, :], rg(X("hl", 0, Z)))
+    diagonal(P2, 2.0)
     diagonal(X("ibn", 0, 128), -MID)
     diagonal(X("nti", 0, 128), -1.0)
     where(X("nti", 128, 256), ZERO, DIAG, 0, 1, OP.is_ge, -1.0)
-    iota(X("wq", 0, 288), [[0, 288]], 0, 0)
-    for a, b in ((0, 8), (136, 152), (280, 288)):
-        iota(X("half", a, b), [[0, b - a]], 0, 0)
     iota(X("km", 0, 256), [[-1, 128], [0, 2]], 127, 0)
     SELR, SELQ = X("selr", 0, 128, 1, 0, 16), X("selq", 0, 128, 1, 0, 16)
     where(SELR, X("one", 0, 128, 1, 0, 16), [[-16, 8], [0, 16]], -128, 16, OP.is_equal)
     where(SELQ, X("one", 0, 128, 1, 0, 16), [[-16, 8], [0, 16]], 0, 16, OP.is_equal)
-    iota(X("xw", Z, Z + 16), [[0, 16]], 0, 0)
-    BLK = X("blk", 0, 128)
-    where(BLK, ONE, [[-16, 8], [0, 16]], 0, 1)
-    where(BLK, BLK, [[16, 8], [0, 16]], 15, -1)
-    where(X("lt", 0, 128), BLK, [[1, 128]], 0, -1, OP.is_gt)
-    where(X("lt", 0, 128), X("lt", 0, 128), [[1, 128]], 0, -1, OP.not_equal, BIG)
-    LTE = X("lte", 0, 128)
-    where(LTE, ONE, [[-8, 16], [0, 8]], 0, 1)
-    where(LTE, LTE, [[1, 128]], 0, -1)
-    where(LTE, LTE, [[1, 128]], 0, -1, OP.not_equal, -16.0)
+    iota(X("inv", INV, 2448), [[0, 2448 - INV]], 0, 0)
 
-    def ask(L, win, n):
-        share("gb", L * V, win, 1024, "idx", L * 128, n)
+    def pack(digits, weight, last=False):
+        name, c0 = digits[1][0][0], digits[1][0][3]
+        for c in range(2):
+            mm(X("pc", c, 256, 2), X(name, c0 + 8 * c, c0 + 8 * c + 128), weight, False, last and c == 1, tag="pack")
 
-    def answer(L, bank, c0):
-        pick(bank, c0, "gb", L * V, "selw", 0, 8, "word")
+    def total_of(out, terms, first=False, last=False, tag=None):
+        for i, (m, e) in enumerate(terms):
+            mm(out, m, e, first and i == 0, last and i == len(terms) - 1, tag=tag)
 
-    n = SHARE["r2"]
-    ARH, ARL = X("ar", 0, 128), X("ar", 144, 272)
-
-    def shift(K, bank, f):
-        tt(X("yj", 128 * K, 128 * K + 128), X(bank, 0, 128), F(f, f + 1, 128, 256), OP.mult)
-
-    def digit(K, mask):
-        ts(X("zj", 128 * K, 128 * K + 128), X("yj", 128 * K, 128 * K + 128), mask, OP.bitwise_and)
-
-    for L in range(3):
-        ask(L, "ww", n[L])
-        answer(L, ("pc", "pc", "pd")[L], 128 * (L % 2))
-        if L == 0:
-            ts(X("idx", 256, 512), X("pb", 0, 256), float(OFFC), OP.subtract)
-    mm(X("pa", 0, 256), ZERO, TI, True, False, tag="pack")
-    pack("pa", [("e0", 0, 0)], False, False)
-    tt(X("yi", 0, 256), X("pc", 0, 256), F(0, 2, 128, 256), OP.mult)
-    ask(3, "ww", n[3])
-    answer(3, "pb", 0)
-    shift(0, "pd", 2)
-    ts(X("zi", 0, 256), X("yi", 0, 256), 6, OP.bitwise_and)
-    digit(0, 4)
-    tt(X("zi", 0, 128), X("zi", 0, 128), UL, OP.min)
-    ts(X("nth", 0, 128), X("zi", 128, 256), -2.5, OP.mult, 9.0, OP.add)
-    tt(X("psw", TH, TH + 256), X("zi", 0, 256), X("psw", 1152, 1408), OP.max)
-    shift(1, "pb", 3)
-    tt(X("psw", TH + 256, TH + 384), X("psw", TH, TH + 128), X("nth", 0, 128), OP.max)
-    digit(1, 4)
-    tt(ARH, X("zj", 0, 128), X("psw", TH + 128, TH + 256), OP.is_gt)
-    tt(ARL, X("zj", 128, 256), X("psw", TH + 256, TH + 384), OP.is_gt)
-    pack("pa", [("ar", 0, 0)], False, False)
-    pack("pa", [("ar", 144, 64)], False, True)
-    mm(X("pd", 128, 256), IB, T1, True, False, tag="m2")
-    mm(X("pd", 128, 256), IB, ARH, False, True, tag="m2")
-    tt(F(2, 3, 0, 256), F(1, 2, 0, 256), X("psw", DM, DM + 256), OP.add)
-    cp(X("wv", 256 * r, 256 * r + 256), X("pa", 0, 256))
+    ARH, ARL = X("ar", 0, 128), X("ar", 136, 264)
+    THA, THL, S2, M2 = X("psw", 256, 384), X("psw", 1536, 1664), X("psw", 1664, 1792), X("m2", 0, 128)
+    E4 = X("pb", 256, 384)
+    share("gb", 0, "hhh", Z, "hl16", 0, SHARE["hhhh"])
+    tt(B, X("pb", 0, 128), HN, OP.is_equal)
+    tt(EH2, X("pb", 128, 256), HN, OP.is_equal)
+    mm(X("pc", 0, 256), ZERO, TI, True, False, tag="pack")
+    pack(T1, P4)
+    total_of(S2, ((N4, T1), (P4, B)), True, False, "s2")
+    total_of(E4, ((PB, NHL), (PB, B)), True, False, "hhhh")
+    pick("pb", 256, "gb", 0, SF(0, 0, 0), 1, "hhhh", False)
+    share("gb", V, "hl", Z, "hl16", 128, SHARE["l"])
+    pick("pd", 0, "gb", V, SF(0, 2), 4, "l")
+    tt(X("pa", 256, 512), X("pa", 256, 512), X("fld", 0, 256), OP.subtract)
+    tt(ARH, E4, HH, OP.is_equal)
+    ts(SIDEA, X("cj", 0, 1), 8.0, OP.is_lt)
+    for K in range(2):
+        tt(X("pa", 256 + 128 * K, 384 + 128 * K), X("pa", 256 + 128 * K, 384 + 128 * K), NHL, OP.mult)
+    ELH, ELL, TL1, THL1 = (X("e2", 128 * j, 128 * j + 128) for j in range(4))
+    tt(X("e2", 0, 512), X("pd", 0, 512), TG(1, 5), OP.is_equal)
+    pack(ARH, P4)
+    total_of(X("psw", 128, 256), ((IB, T1), (IB, ARH)), True, True, "m2")
+    border(None, "xst", "xw", lister("xw", V, "bl16"), "SSSS")
+    act(M2, X("psw", 128, 256))
+    total_of(S2, ((P2, ELH), (IB, ELL), (N4, TL1), (IB, THL1)), False, True, "s2")
+    tt(X("c16", 0, 128), X("pa", 256, 384), X("fld", 256, 384), OP.add)
+    tt(X("fld", 384, 512), X("pa", 384, 512), X("fld", 128, 256), OP.add)
+    ts(ARL, S2, 6.0, OP.is_ge)
+    mm(X("pb", 0, 128), X("c16", 0, 128), IB)
+    pack(ARL, P2, True)
+    cp(X("idx", 0, 128), X("pb", 0, 128))
+    cp(X("wv", 256 * r, 256 * r + 256), X("pc", 0, 256))
     spread("w2", "wv")
-
-    mm(X("pb", 0, 128), F(2, 3, 0, 128), IF)
-    NEG = X("nti", 0, 128)
-    FREE = X("psw", 384, 512)
-    mm(FREE, ROW, ROW, True, False, tag="free")
-    mm(FREE, NEG, ARH, False, False, tag="free")
-    mm(FREE, NEG, ARL, False, True, tag="free")
-    pick("pc", 0, "hl", 0, "sel", 0, 16, "own")
-    act(X("xst", 0, 384), IX("xc", V, "bl16", 0, 24))
-    show("x", "xst", "xw")
-    act(X("xw", mine, mine + C), X("xst", C * r, C * r + C))
-    act(col(72), SIDEB, 0.0, -1.0 / BIG)
+    pick("pa", 0, "gb", V, SF(2, 4), 4, "l2")
+    total_of(THA, ((P2, EH2), (P4, B), (P4, NHL), (P4, ARH)), True, True, "tha")
+    act(X("pw", 0, 8), X("zero", 0, 8), 0.125)
+    act(SIDEB, SIDEA, 1.0, -1.0)
     act(col(73), SIDEA, 0.0, -1.0 / BIG)
-    act(col(74), SIDEB, 1.0, 15.0)
+    act(col(72), SIDEA, -1.0 / BIG, 1.0 / BIG)
     act(X("km", 0, 256), X("km", 0, 256), col(73), col(72))
-    act(col(64, 8), col(M8, 8), 0.0, col(74))
-    act(X("m2", 0, 128), X("pd", 128, 256))
-    ts(X("idx", 256, 384), X("pb", 0, 128), float(OFFC), OP.subtract)
-    tt(F(2, 3, 128, 256), F(2, 3, 128, 256), FREE, OP.mult)
-    for K, m in ((1, ARL), (0, X("m2", 0, 128))):
+    scan(X("pw", 8, 16), X("pw", 0, 8), X("zero", 0, 8), 8.0, OP.mult, OP.add)
+    cp(X("nb16", 0, 256), X("nbi", 0, 256))
+    tt(col(64, 8), col(48, 8), X("pw", 8, 16), OP.mult)
+    ts(QW, X("cj", 0, 1), -1.0, OP.mult, 16.0, OP.add)
+    if not SPD:
+        tt(col(M8, 8), MC(0, 8), MC(8, 8), OP.add)
+
+    show("x", "xst", "xw")
+    dma("Y", "xc", T.xc[:, 0:SHARE["x"]], rg(X("xc", 0, SHARE["x"])), T.x[:, 0:SHARE["x"]], [], "x")
+    a = 512 * len(BOTH)
+    for c in range(16):
+        dma("Y", "wr", T.wr[c:128:16, a:V], [("wr", 16 * k + c, 16 * k + c + 1, 0, V) for k in range(8)], T.w[:, a:V], [])
+    EL2 = X("e0", 272, 400)
+    for K, m in ((1, ARL), (0, M2)):
         tt(X("pz2", 128 * K, 128 * K + 128), m, HZ[K], OP.mult)
-        mm(X("psw", 0, 128), m, X("ibn", 0, 128), K == 1, False, tag="mate")
-        mm(X("psw", 0, 128), X("pz2", 128 * K, 128 * K + 128), IH, False, False, tag="mate")
-    tt(X("psw", LESS, LESS + 256), X("pc", 0, 256), X("own", 0, 256), OP.is_lt)
-    for K, m in enumerate((X("m2", 0, 128), ARL)):
+    sum_of(W8, col(64, 8))
+    act(X("selw", 0, 8), G8, 0.0, W8)
+    ts(X("c16", 128, 256), X("pa", 0, 128), float(OFFC), OP.subtract)
+    mm(X("pd", 0, 128), X("c16", 128, 256), IB)
+    tt(EL2, X("pa", 256, 384), LN, OP.is_equal)
+    act(X("fld", 640, 768), X("pa", 128, 256))
+    for K, m in enumerate((M2, ARL)):
         tt(X("nr2", 128 * K, 128 * K + 128), m, X("psw", LESS + 128 * K, LESS + 128 * K + 128), OP.mult)
+    cp(X("idx", 128, 256), X("pd", 0, 128))
+    total_of(THL, ((ONE, P4), (N4, ELL), (P2, EL2), (P4, TL1), (N4, ELH), (N4, ELH), (PB, M2), (PB, ARL)), True, False, "thl")
+    for K, m in ((1, ARL), (0, M2)):
+        mm(X("psw", 0, 128), m, X("ibn", 0, 128), K == 1, False, tag="mate")
+        mm(X("psw", 0, 128), X("pz2", 128 * K, 128 * K + 128), IB, False, False, tag="mate")
     mm(X("psw", 512, 768), ONE, TI, True, False, tag="rep")
     for K in range(2):
         mm(X("psw", 512, 768), X("nr2", 128 * K, 128 * K + 128), X("nti", 0, 256), False, False, tag="rep")
-    cp(X("nb16", 128, 256), X("nbi", 128, 256))
+    LT, LTE, B0, Q0, SELI = X("lt", 0, 128), X("lte", 0, 128), X("b0", 14, 142), X("q0", 14, 142), X("seli", 0, 64)
+    BLK = X("blk", 0, 128)
+    where(BLK, ONE, [[-16, 8], [0, 16]], 0, 1)
+    iota(X("wq", 0, 288), [[0, 288]], 0, 0)
+    where(BLK, BLK, [[16, 8], [0, 16]], 15, -1)
+    iota(X("xw", Z, Z + 16), [[0, 16]], 0, 0)
+    where(LTE, ONE, [[-8, 16], [0, 8]], 0, 1)
+    where(LT, BLK, [[1, 128]], 0, -1, OP.is_gt)
+    where(LTE, LTE, [[1, 128]], 0, -1)
+    where(LT, LT, [[1, 128]], 0, -1, OP.not_equal, BIG)
+    where(LTE, LTE, [[1, 128]], 0, -1, OP.not_equal, -16.0)
+    where(B0, BLK, [[0, 8], [-1, 16]], 1, 0)
+    where(SELI, X("zero", 0, 64), [[-16, 8], [-1, 8]], 0, 1, OP.not_equal, 1.0)
+    where(Q0, B0, [[-16, 8], [-8, 16]], 0, 1)
+    where(X("lt0", 14, 142), B0, [[16, 8], [8, 16]], 0, -1, OP.is_gt)
+    where(Q0, Q0, [[16, 8], [8, 16]], 7, -1)
+    where(SELI, SELI, [[-16, 8], [-1, 8]], -8, 1, OP.not_equal, 16.0)
     for name in ("b0", "lt0", "q0"):
         iota(X(name, 0, 14), [[0, 14]], 0, 0)
-    B0 = X("b0", 14, 142)
-    where(B0, BLK, [[0, 8], [-1, 16]], 1, 0)
-    where(X("lt0", 14, 142), B0, [[16, 8], [8, 16]], 0, -1, OP.is_gt)
-    where(X("q0", 14, 142), B0, [[-16, 8], [-8, 16]], 0, 1)
-    where(X("q0", 14, 142), X("q0", 14, 142), [[16, 8], [8, 16]], 7, -1)
     iota(X("vl", 0, 16), [[16, 16]], V - int(BIG), 1)
-    iota(X("sp", Z, Z + 16), [[0, 16]], 0, 0)
-    iota(X("inv", 0, 2448), [[0, 2448]], 0, 0)
+    iota(X(SPW, Z, Z + 16), [[0, 16]], 0, 0)
+    for a, b in () if SPD else ((0, 8), (136, 152), (280, 288)):
+        iota(X("half", a, b), [[0, b - a]], 0, 0)
+    for c in range(0 if SPD else 2):
+        where(X("half", 144 * c + 8, 144 * c + 136), IB, [[0, 8], [1, 2], [0, 8]], -c, 0, OP.is_equal)
+
+    def ask(L, n):
+        share("gb", L * V, "wv", 1024, "idx", L * 128, n)
+
+    def answer(L, bank):
+        pick(bank, 0, "gb", L * V, X("selw", 0, 8), 1, "word")
+
+    def shift(K, bank):
+        tt(X("yj", 128 * K, 128 * K + 128), X(bank, 0, 128), X("fld", 384 + 256 * K, 512 + 256 * K), OP.mult)
+
+    def digit(K):
+        ts(X("zj", 128 * K, 128 * K + 128), X("yj", 128 * K, 128 * K + 128), 6, OP.bitwise_and)
 
     n0, n1 = SHARE["r3"]
-    ask(2, "wv", n0)
-    answer(2, "pc", 0)
-    ask(3, "wv", n1)
-    shift(0, "pc", 2)
-    ts(QW, X("cj", 32, 33), -1.0, OP.mult, 16.0, OP.add)
-    digit(0, 6)
-    cp(X("nb16", 0, 128), X("nbi", 0, 128))
-    answer(3, "pd", 0)
-    A3, L3, TL = X("ar3", 0, 128), X("ar3", 128, 256), X("psw", TH, TH + 128)
-    tt(A3, X("zj", 0, 128), X("psw", TH + 128, TH + 256), OP.is_gt)
-    ts(X("nth", 0, 128), X("zj", 0, 128), -2.5, OP.mult, 4.0, OP.add)
-    act(X("tq", 0, 128), A3, -1.0, 5.0)
+    ask(0, n0)
+    answer(0, "pc")
+    nx = SHARE["x"]
+    hx = nx + 384
+    for bank, a, b in (("pa", nx, hx), ("pb", hx, V)):
+        mm(X(bank, 0, b - a), IB, X("xw", a, b), True, False, tag="gx")
+    ask(1, n1)
+    shift(0, "pc")
+    digit(0)
+    answer(1, "pd")
+    A3, L3, Z0 = X("ar3", 0, 128), X("ar3", 128, 256), X("ar3", 256, 384)
+    tt(A3, X("zj", 0, 128), THA, OP.is_gt)
+    ts(Z0, X("zj", 0, 128), 0.0, OP.is_equal)
+    total_of(THL, ((PB, A3), (PB, Z0)), False, True, "thl")
     tt(X("pz3", 0, 128), A3, HZ[0], OP.mult)
-    tt(TL, TL, X("nth", 0, 128), OP.max)
     mm(X("psw", 0, 128), A3, X("ibn", 0, 128), False, False, tag="mate")
-    mm(X("psw", 0, 128), X("pz3", 0, 128), IH, False, False, tag="mate")
-    shift(1, "pd", 3)
-    tt(TL, TL, X("tq", 0, 128), OP.max)
-    digit(1, 6)
-    tt(L3, X("zj", 128, 256), TL, OP.is_gt)
+    mm(X("psw", 0, 128), X("pz3", 0, 128), IB, False, False, tag="mate")
+    shift(1, "pd")
+    digit(1)
+    tt(L3, X("zj", 128, 256), THL, OP.is_gt)
     tt(X("pz3", 128, 256), L3, HZ[1], OP.mult)
     mm(X("psw", 0, 128), L3, X("ibn", 0, 128), False, False, tag="mate")
-    mm(X("psw", 0, 128), X("pz3", 128, 256), IH, False, True, tag="mate")
+    mm(X("psw", 0, 128), X("pz3", 128, 256), IB, False, True, tag="mate")
     tt(X("nr3", 0, 256), X("ar3", 0, 256), X("psw", LESS, LESS + 256), OP.mult)
     for c, side in enumerate((SIDEA, SIDEB)):
         act(col(76 + c), side, 0.0, QW)
         act(X("wq", 144 * c + 16, 144 * c + 144, 16), G8, 0.0, side, tag="wq")
         act(X("wq", 144 * c + 8, 144 * c + 136, 16), G8, 0.0, col(76 + c), tag="wq")
-        act(X("half", 144 * c + 8, 144 * c + 136), IB, 0.0, side)
-    act(X("g8b", 0, 8), G8)
-    for j in range(8):
-        act(X("seli", 8 * j, 8 * j + 8), col(64, 8), 0.0, X("g8", j, j + 1))
+    if not INVAT:
+        act(X("inv", 0, INV), X("hh", 0, INV), 0.0, 0.0)
 
     ts(X("mate", 0, 128), X("psw", 0, 128), float(Z), OP.add)
     nx = SHARE["x"]
     hx = nx + 384
-    for bank, a, b in (("pa", nx, hx), ("pb", hx, V)):
-        mm(X(bank, 0, b - a), IB, X("xc", a, b), True, False, tag="gx")
     for K in range(2):
         mm(X("psw", 512, 768), X("nr3", 128 * K, 128 * K + 128), X("nti", 0, 256), False, K == 1, tag="rep")
+
+    def weights(j):
+        mm(X("psw", 512 * j, 512 * j + 512), SELR, X("wsb", 512 * j, 512 * j + 512, 1, 0, 16))
+
+    weights(3)
     for bank, a, b in (("pa", nx, hx), ("pb", hx, V)):
         act(X("gb", a - nx, b - nx), IX("xw", Z + 16, "mate", a // 16, b // 16))
         mm(X(bank, 0, b - a), IB, X("gb", a - nx, b - nx), False, True, tag="gx")
+    REP, UP, HI, LO = X("ru", 0, 128), X("ru", 128, 256), X("hilo", 0, 128), X("hilo", 128, 256)
+
+    def count():
+        move(RUQ, X("ru", 0, 256), X("psw", 512, 768))
+        mm(X("pc", 0, 128), LTE, REP)
+        if SPD:
+            mm(X("pd", 0, 128), UP, BLK, True, False, tag="num")
+            mm(X("pd", 0, 128), REP, X("lt", 0, 128), False, True, tag="num")
+        else:
+            mm(X("pd", 0, 128), BLK, UP, True, False, tag="num")
+            mm(X("pd", 0, 128), X("lt", 0, 128), REP, False, True, tag="num")
+
+    if RUQ == "S":
+        count()
+    weights(2)
     tt(X("xf", 0, nx), IX("xw", Z + 16, "mate", 0, nx // 16), X("xc", 0, nx), OP.add)
     for bank, a, b in (("pa", nx, hx), ("pb", hx, V)):
         act(X("xf", a, b), X(bank, 0, b - a))
-    REP, UP = X("ru", 0, 128), X("ru", 128, 256)
-    cp(X("ru", 0, 256), X("psw", 512, 768))
-    cp(X("xb", 0, 192), IX("xf", V, "bl16", 0, 12))
-    act(X("xb", 192, 384), IX("xf", V, "bl16", 12, 24))
-    show("xs", "xb", "xf")
+    if RUQ == "V":
+        count()
+    parts = (X("cn", 0, 128), HI)[:1 if SPD == 1 else 2]
+    for o in parts[:RU]:
+        ts(o, X("pd", 0, 128), V * r - BIG, OP.add, 0.0, OP.max)
+    border("xs", "xb", "xf", lister("xf", V, "bl16"))
+    if RANK:
+        act(X("bt", 0, 128), X("pc", 0, 128))
+    for o in parts[RU:]:
+        act(o, X("pd", 0, 128), V * r - BIG, func=AF.Relu)
     for b, a in zip(CUTS, CUTS[1:]):
         iota(X("left", a // 16, b // 16), [[0, (b - a) // 16]], (V - a) // 128, 0)
     iota(X("sw", Z, Z + 16), [[0, 16]], 0, 0)
     iota(X("tw", V, V + 8), [[0, 8]], 0, 0)
 
-    mm(X("pc", 0, 128), LTE, REP)
-    mm(X("pd", 0, 128), BLK, UP, True, False, tag="num")
-    mm(X("pd", 0, 128), X("lt", 0, 128), REP, False, True, tag="num")
-    act(X("cn", 0, 128), X("pd", 0, 128), V * r - BIG, func=AF.Relu)
-    HI, LO = X("hilo", 0, 128), X("hilo", 128, 256)
-    act(HI, X("pd", 0, 128), V * r - BIG, func=AF.Relu)
-    act(X("xf", mine, mine + C), X("xb", C * r, C * r + C))
+    if SPD != 1:
+        tt(LO, X("cn", 0, 128), HI, OP.subtract)
+    for c in range(0 if SPD else 2):
+        o = X("pd", 128 + 128 * c, 256 + 128 * c)
+        mm(o, X("half", 144 * c + 16 * c, 144 * c + 16 * c + 128), HI, True, False, tag="two")
+        mm(o, X("half", 144 * c + 8, 144 * c + 136), LO, False, True, tag="two")
+    for j in range(8 * SPD):
+        p, src, c = 16 * (j % 8) + j // 8, "cn" if SPD == 1 else "hilo", 16 * j
+        dma("Y", "sp", T[SPW][p:p + 1, 0:V], rg(X(SPW, 0, V, 1, p, p + 1)), T[src][:, c:c + 16], rg(X(src, c, c + 16)), "xs")
+    if INVAT:
+        act(X("inv", 0, INV), X("hh", 0, INV), 0.0, 0.0)
     mm(X("pa", 0, 256), ZERO, TI, True, False, tag="eight")
     for i in range(8):
         MK = X("mk", 128 * i, 128 * i + 128)
-        ts(MK, X("pc", 0, 128), float(i - 16), OP.is_equal, -BIG, OP.mult)
+        ts(MK, X("bt" if RANK else "pc", 0, 128), float(i - 16), OP.is_equal, -BIG, OP.mult)
         for c in range(2):
             mm(X("pa", c, 256, 2), X("wq", 144 * c + 8 - i, 144 * c + 136 - i), MK, False, c + i == 8, tag="eight")
-        if i == 2:
-            tt(LO, X("cn", 0, 128), HI, OP.subtract)
-            for c in range(2):
-                o = X("pd", 128 + 128 * c, 256 + 128 * c)
-                mm(o, X("half", 144 * c + 16 * c, 144 * c + 16 * c + 128), HI, True, False, tag="two")
-                mm(o, X("half", 144 * c + 8, 144 * c + 136), LO, False, True, tag="two")
-    for m in range(8):
-        for k, (lhs, rhs, c0) in enumerate((("b0", "ru", 128), ("lt0", "ru", 0), ("q0", "mk", 0))):
-            mm(X("pb", 0, 16), X(lhs, 14 - 2 * m, 142 - 2 * m), X(rhs, c0 + m, c0 + 128, 8), m + k == 0, m + k == 9, tag="base")
-    for j in (3, 2, 1, 0):
-        mm(X("psw", 512 * j, 512 * j + 512), SELR, X("wsb", 512 * j, 512 * j + 512, 1, 0, 16))
+        for m in range(8 if i == BASE else 0):
+            for k, (lhs, rhs, c0) in enumerate((("b0", "ru", 128), ("lt0", "ru", 0), ("q0", "mk", 0))):
+                mm(X("pb", 0, 16), X(lhs, 14 - 2 * m, 142 - 2 * m), X(rhs, c0 + m, c0 + 128, 8), m + k == 0, m + k == 9, tag="base")
 
     def SP(c):
         return X("sp", c, V, 16)[0], [("sp%d" % c, 0, 128, 0, 128)]
 
     def numbers(offs, c, d, b):
-        ap, regs = IX("sp", b, offs, c, d)
+        ap, regs = IX(SPW, b, offs, c, d)
         return ap, regs + [y for k in range(16) for y in SP(k)[1]]
 
-    act(X("two", 0, 256), X("pd", 128, 384))
-    for c in range(16):
+    if not SPD:
+        act(X("two", 0, 256), X("pd", 128, 384))
+    for c in range(0 if SPD else 16):
         part = X("two", 128 * (c // 8), 128 * (c // 8) + 128)
         if c < SHARE["sp"]:
             ts(SP(c), part, col(M8 + c % 8), OP.mult)
         else:
             act(SP(c), part, 0.0, col(M8 + c % 8))
 
-    for j in (3, 2, 1, 0):
+    for j in (4, 3, 2, 1, 0):
         a, b = 512 * j, 512 * j + 512
+        if j == 4:
+            if NUM == 4:
+                border("num", "sb", SPW, lambda e, out, q0, q1: move(e, out, numbers("bl16", 6 * q0, 6 * q1, V)), NUMQ)
+            continue
         if j in BOTH:
             mm(X(BOTH[j], 0, 512), SELQ, X("wsb", a, b, 1, 0, 16))
+            weights(j)
             act(X("p0", a, b), IX("xf", Z, "nb16", 32 * j, 32 * j + 32))
         act(X("g1", a, b), IX("xf", Z, "nb16", 128 + 32 * j, 160 + 32 * j))
-
+        if j == NUM:
+            border("num", "sb", SPW, lambda e, out, q0, q1: act(out, numbers("bl16", 6 * q0, 6 * q1, V)), "SSSS")
 
     def columns():
         tt(X("off", 0, 16), X("pb", 0, 16), X("vl", 0, 16), OP.min)
@@ -609,14 +685,14 @@ def rank_program(g, core, T, topo):
         o = IX("inv", 2448, "off16", 0, 16)
         add("V", lambda e: e.tensor_copy(out=o[0], in_=T.rb[:, :]), rg(X("inv", 0, 2448)), rg(X("rb", 0, 256), X("off16", 0, 16)))
         mm(X("pb", 0, 128), ONE, X("left", 0, 128), True, False, tag="iv")
-        mm(X("pa", 0, 512), ZERO, X("ww", 0, 512), True, False, tag="inv")
+        mm(X("pa", 0, 512), ZERO, X("wv", 0, 512), True, False, tag="inv")
         for d in range(-7, 16):
             o2 = T.pa[:, :, d + 7:d + 15], rg(X("pa", 0, 512))
             mm(o2, X("inv", 16 + d, 16 + d + V - 15, 16), X("seli", 0, 64), False, d == 15, tag="inv")
 
     def inverse():
         ts(X("ivt", 0, 128), (T.pa[:, :, 7:23], rg(X("pa", 0, 512))), -1.0, OP.mult)
-        mm(X("pb", 0, 128), X("ivt", 0, 128), IH, False, True, tag="iv")
+        mm(X("pb", 0, 128), X("ivt", 0, 128), IB, False, True, tag="iv")
 
     def first(j):
         a, b = 512 * j, 512 * j + 512
@@ -634,10 +710,14 @@ def rank_program(g, core, T, topo):
     def keep(j):
         where(X("p0", 512 * j, 512 * j + 512), X("sw", 512 * j, 512 * j + 512), [[1, 512]], 0, 0)
 
-    nc = SHARE["cm"]
-    nc, nd = nc
+    nc, nd = SHARE["cm"]
+    if EARLY > 0:
+        columns()
+    if EARLY > 1:
+        scatter()
     tt(X("p0", 1024, V), IX("xf", Z, "nb16", 64, 128), X("wr", 1024, V), OP.mult)
-    columns()
+    if EARLY < 1:
+        columns()
     second(1536, V)
     second(1024, 1536)
     both(1536, V)
@@ -645,9 +725,6 @@ def rank_program(g, core, T, topo):
     first(1)
     both(1024, 1536)
     keep(2)
-    act(X("sb", 0, 384), numbers("bl16", 0, 24, V))
-    show("num", "sb", "sp")
-    act(X("sp", mine, mine + C), X("sb", C * r, C * r + C))
     second(512, 1024)
     first(0)
     second(0, 512)
@@ -655,21 +732,26 @@ def rank_program(g, core, T, topo):
     both(0, 512)
     if nc:
         act(X("cmr", 0, nc), numbers("mate", 0, nc // 16, Z + 16))
-    cp(X("sst", 0, 192), IX("sw", V, "bl16", 0, 12))
-    act(X("sst", 192, 384), IX("sw", V, "bl16", 12, 24))
-    show("s", "sst", "sw")
-    act(X("sw", mine, mine + C), X("sst", C * r, C * r + C))
+    border("s", "sst", "sw", lister("sw", V, "bl16"))
     keep(1)
     keep(0)
 
-    mm(X("pd", 0, 128), IF, X("cn", 0, 128), True, False, tag="cm")
-    scatter()
+    if SPD:
+        mm(X("pd", 0, 128), X("cn", 0, 128), IF, True, False, tag="cm")
+    else:
+        mm(X("pd", 0, 128), IF, X("cn", 0, 128), True, False, tag="cm")
+    if EARLY < 2:
+        scatter()
     if nd > nc:
         act(X("cmr", nc, nd), numbers("mate", nc // 16, nd // 16, Z + 16))
     if nd < V:
         cp(X("cmr", nd, V), numbers("mate", nd // 16, 128, Z + 16))
     inverse()
-    pick("pc", 0, "cmr", 0, "g8b", 0, 8, "cm")
+    if SPD == 1:
+        for b in range(16):
+            mm(X("pc", b, 128, 16), X("cmr", b, V, 16), X("iff", 0, 128, 16), tag="cm")
+    else:
+        pick("pc", 0, "cmr", 0, SF(0, 0, 0) if SPD else G8, 1, "cm")
     last = len(CUTS) - 2
     for j, (b, a) in enumerate(zip(CUTS, CUTS[1:])):
         tt(X("tw", a, b), IX("sw", Z + 16, "mate", a // 16, b // 16), X("p0", a, b), OP.add)

@@ -5,41 +5,44 @@ OP = AluOpType
 AF = ActivationFunctionType
 V, C, Z = 2048, 96, 2432
 BIG, MID = 16384.0, 1216.0
-OFFN, OFFC = 8192 + 128, 1024 + 128
+OFFN, OFFC = 8192 + 128, 1016 + 7
 F32, BF, F16, I32, U16 = "float32", "bfloat16", "float16", "int32", "uint16"
 WIDTHS = {
     F32: dict(dn=128, nbm=256, hlm=256, mb=384, col=128, ir=144, iff=128, xf=2432, cn=128, stm=72,
               vl=16, off=16, g1=2048, p0=2048, sw=2448, sst=384, cmt=128, cmv=128, tw=2056, xb=384, fld=768),
     BF: dict(wsb=2048, xw=2448, xc=2048, bst=384, hb=2048, hl=2432, hh=2432, hhh=2432, hst=384, cst=384, dst=384,
-             xst=384, gb=4096, wr=2048, ti=256, nti=256, ibn=128, dg=512, pm=8, selw=8, seli=64, e0=400, e1=272,
-             e2=512, ar=272, ar3=384, m2=128, nr2=256, nr3=256, wv=1024, one=128, zero=144, ru=256, mk=1024, blk=128, lt=128,
+             xst=384, gb=4096, wr=2048, ti=256, nti=256, ibn=128, dg=768, pm=8, selw=8, seli=64, e0=400, e1=272,
+             e2=528, ar=128, ar3=384, m2=128, nr2=256, nr3=256, wv=1024, one=128, zero=144, ru=256, mk=1024, blk=128, lt=128,
              lte=128, b0=144, lt0=144, q0=144, wq=288, km=256, rb=256, inv=2448, selr=128, selq=128, bt=128, left=128,
-             nw=2432, sp=2448, sb=384, cmr=2048, hilo=256, two=256, half=288, g8b=8, g8h=144, pw=256),
+             nw=2432, sp=2448, sb=384, cmr=2048, hilo=256, two=256, half=288, g8b=8, g8h=144, g2h=144, pw=256),
     F16: dict(pz2=256, pz3=256, ivt=128, hrow=768, c16=256),
     I32: dict(bli=24, nbi=256, ci=24, cj=32, yj=256, zj=256, bki=48, gli=24),
     U16: dict(gl16=24, bl16=24, hl16=256, idx=256, mate=128, off16=16, iv16=128, nb16=256, bk16=48, hb16=48),
 }
-SPD = 1
+SPD = 2
 SPW = ("sp", "nw", "hhh")[SPD]
 WIDTHS[BF]["hhh"] = 2448
 if SPD == 1:
     for _n in ("nw", "sb", "cmr"):
         WIDTHS[F32][_n] = WIDTHS[BF].pop(_n) + (16 if _n == "nw" else 0)
 PSUM = {"psw": 2048, "pa": 512, "pb": 512, "pc": 512, "pd": 512}
-SCRATCH = {"tg": ("sbuf", [128, 6, 128], F32), "sel": ("sbuf", [128, 4, 16], BF)}
+SCRATCH = {"tg": ("sbuf", [128, 6, 128], F32), "sel": ("sbuf", [128, 4, 16], BF),
+           "t1": ("sbuf", [128, 8, 16], BF), "arh": ("sbuf", [128, 8, 16], BF),
+           "hhn": ("sbuf", [128, 8, 16], F32), "m8": ("sbuf", [128, 8, 8, 2], BF), "b16": ("sbuf", [128, 16], F32),
+           "t1p": ("sbuf", [128, 33, 8], BF), "arhp": ("sbuf", [128, 33, 8], BF)}
 for _d in WIDTHS:
     for _n in WIDTHS[_d]:
         SCRATCH[_n] = ("sbuf", [128, WIDTHS[_d][_n]], _d)
 for _n in PSUM:
-    SCRATCH[_n] = ("psum", [128, 8, 64] if _n == "pa" else [128, PSUM[_n]], F32)
-SHARE = {"ghost": 2, "bst": 24, "hh": 1024, "hhh": 960, "hhhh": 960, "l": 1024, "r3": (1024, 896), "x": 1344, "sp": 10, "cm": (0, 1536)}
-STEPS = (256, 384, 448, 480, 480)
+    SCRATCH[_n] = ("psum", {"pa": [128, 8, 64], "pb": [128, 32, 16]}.get(_n, [128, PSUM[_n]]), F32)
+SHARE = {"ghost": 2, "bst": 24, "hh": 1024, "hhh": 960, "q": (576, 896), "l": (512, 896), "r3": (1024, 960), "x": 1344, "hx": 384, "sp": 10, "cm": (0, 1280)}
+STEPS = (192, 448, 512, 512, 384)
 BOTH = {1: "pd", 0: "pc"}
-CUTS = (2048, 1792, 1408, 1024, 640, 256, 0)
-CM = 3
-NUM = 1
-EARLY = 0
-BASE = 7
+CUTS = (2048, 1792, 1408, 1024, 640, 384, 0)
+CM = 2
+NUM = 0
+EARLY = 1
+BASE = 6
 NUMQ = "SSSS"
 INV = 768
 GL = 1
@@ -48,8 +51,20 @@ RU = 0
 RUQ = "V"
 INVAT = 1
 LESSAT = 0
+RUAT = 384
+AHEAD = 1
+SUM = 512
+LEAD = 0
+SST = "SSSS"
+LOAT = 7
+BEHIND = None
+TAIL = 1
+LAST = 256
+FUSE = 960
+GHOST = None
+ORDER = ((1, 0), (1, 1), (0, 0), (1, 2), (0, 1), (1, 3), (0, 2), (1, 4), (0, 3), (0, 4))
 EXCH = ["name", "hl", "hh", "hhh", "w2", "x", "xs", "num", "s"]
-LOADS = ["bl", "gl", "nb", "w", "m1", "m2", "m3", "x", "xc", "wr", "sp", "cm"] + ["y%d" % _j for _j in range(len(CUTS) - 1)]
+LOADS = ["bl", "gl", "nb", "w", "m1", "m2", "x", "xc", "wr", "sp", "cm"] + ["y%d" % _j for _j in range(len(CUTS) - 1)]
 SEMAPHORES = ["cV", "cS", "cP", "cG"] + ["d_" + k for k in LOADS] + ["a_" + k for k in EXCH] + ["l_" + k for k in EXCH]
 
 
@@ -120,6 +135,8 @@ def rank_program(g, core, T, topo):
     def X(name, c0, c1, step=1, p0=0, p1=128):
         if name == "pa":
             ap = T.pa[p0:p1, c0 // 64:(c1 + 63) // 64, c0 % 64:64:step]
+        elif name == "pb":
+            ap = T.pb[p0:p1, c0 // 16:c1 // 16, :] if step == 1 else T.pb[p0:p1, c0 // 16:c1 // 16, c0 % 16]
         else:
             ap = T[name][p0:p1, c0:c1] if step == 1 else T[name][p0:p1, c0:c1:step]
         return ap, [(name, p0, p1, c0, c1)]
@@ -245,10 +262,10 @@ def rank_program(g, core, T, topo):
     def lister(win, w, offs, o=0):
         return lambda e, out, q0, q1: move(e, out, IX(win, w, offs, o + 6 * q0, o + 6 * q1))
 
-    def merge(key, src, p0, p1, n=Z, a=0):
+    def merge(key, src, p0, p1, n, step=16):
         for i in range(2):
-            dma("Y", key, T.hl[p1 + i:128:16, a:n], [("hl", 16 * k + p1 + i, 16 * k + p1 + i + 1, a, n) for k in range(8)],
-                T[src][p0 + i:128:16, a:n], rg(X(src, a, n)))
+            dma("Y", key, T.hl[p1 + i:128:step, 0:n], [("hl", p, p + 1, 0, n) for p in range(p1 + i, 128, step)],
+                T[src][p0 + i:128:step, 0:n], rg(X(src, 0, n)))
 
     IB, TI, IF = X("ti", 0, 128), X("ti", 0, 256), X("iff", 0, 128)
     ONE, ZERO, G8, DIAG = X("one", 0, 128), X("zero", 0, 128), X("g8b", 0, 8), [[-1, 128]]
@@ -293,8 +310,9 @@ def rank_program(g, core, T, topo):
     where(PM, PM, [[-1, 8]], 0, 1, OP.not_equal, -1.0)
     send("name", lambda d: X("bli", 6 * d, 6 * d + 6), X("gli", 6 * r, 6 * r + 6))
     recv("name", [("gli", 0, 128, 6 * q, 6 * q + 6) for q in others])
-    ts(X("cj", 0, 24), X("ci", 0, 24), 15, OP.bitwise_and)
+    ts(X("cj", 0, 16), X("ci", 0, 16), 15, OP.bitwise_and)
     ts(X("cj", 24, 26), X("ci", 1, 6, 4), 7, OP.bitwise_and)
+    ts(X("cj", 16, 24), X("ci", 16, 24), 7, OP.bitwise_and)
     ts(X("cj", 26, 28), X("ci", 0, 2), 3, OP.bitwise_and)
     ts(MC(0, 28), X("cj", 0, 28), 0.0, OP.is_equal)
     tt(col(64, 20), MC(8, 20), X("ir", 40, 60), OP.mult)
@@ -305,9 +323,12 @@ def rank_program(g, core, T, topo):
     act(A04, MC(0), MC(4))
     act(A15, MC(1), MC(5))
     act(U0, A04, A15)
-    act(U1, A15, 0.0, 128.0)
+    act(U1, MC(1), 0.0, 128.0)
+    act(BA, MC(0), 0.0, 8192.0)
     act(SA, MC(13), U0, 2.0 ** 21)
-    act(BA, A04, U1, 8192.0)
+    act(U1, MC(5), U1, 7.0)
+    act(BA, MC(4), BA, 8128.0)
+    act(BA, BA, U1)
     add("V", lambda e: e.tensor_tensor_scan(T.nw[:, 0:64], D0[0], D1[0], FIRST[0], OP.mult, OP.add), rg(X("nw", 0, 64)), rg(D0, D1, FIRST))
     ts(X("bki", 24, 48), X("bli", 0, 24), 15, OP.bitwise_and)
     ts(X("bki", 0, 24), X("bli", 0, 24), 4, OP.logical_shift_right)
@@ -317,7 +338,7 @@ def rank_program(g, core, T, topo):
     ts(X("nw", 192, 256), X("nw", 0, 64), STM(3), OP.add)
     tt(X("dn", 0, 128), X("nbi", 128, 256), X("nbi", 0, 128), OP.subtract)
     ts(X("nw", 256, 512), X("nw", 0, 256), STM(4), OP.add)
-    G8H, SEL, PAIRS = X("g8h", 16, 144, 16), (T.sel[:, :, :], [("sel", 0, 128, 0, 64)]), [[-2, 4], [-8, 2], [-16, 8]]
+    G8H, SEL, PAIRS = X("g8h", 16, 144, 16), (T.sel[:, 0:3, :], [("sel", 0, 128, 0, 48)]), [[-2, 3], [-8, 2], [-16, 8]]
 
     def SF(a, b, step=1):
         if step == 0:
@@ -325,13 +346,17 @@ def rank_program(g, core, T, topo):
         return T.sel[:, a:b:step, :], [("sel", 0, 128, 16 * a, 16 * b)]
 
     where(G8H, X("one", 0, 8), [[-16, 8]], 0, 1)
-    where(SEL, X("zero", 0, 64), PAIRS, 0, 1, OP.not_equal, 1.0)
+    where(SEL, X("zero", 0, 48), PAIRS, 0, 1, OP.not_equal, 1.0)
     where(G8H, G8H, [[16, 8]], 15, -1)
     where(SEL, SEL, PAIRS, -1, 1, OP.not_equal, 1.0)
+    where(SF(3, 4), X("zero", 0, 16), [[0, 2], [-16, 8]], 0, 1, OP.not_equal, 1.0)
     iota(TG(1, 3), [[0, 16], [1, 16]], V * r + OFFN, 16)
-    for (a, j), p, value in (((1, 1), 0, -1.0), ((2, 0), 4, 0.125), ((2, 1), 12, 0.0), ((1, 1), 1, -1.0)):
+    for (a, j), p, value in (((2, 0), 4, 0.125), ((2, 1), 12, 0.0)):
         where(SF(a, j, 0), SF(a, j, 0), [[-16, 8]], -p, 1, OP.not_equal, value)
+    where(SF(3, 4), SF(3, 4), [[0, 2], [-16, 8]], -1, 1, OP.not_equal, 1.0)
     diagonal(IF, 1.0)
+    NB = X("dg", 512, 640)
+    diagonal(NB, -BIG)
 
     for b in range(16):
         mm(X("pa", b, 128, 16), X("wsb", b, V, 16, 0, 16), PM, tag="wt")
@@ -370,11 +395,16 @@ def rank_program(g, core, T, topo):
     a, nb_ = STEPS[0], SHARE["bst"]
     if nb_ < 24:
         act(X("bst", 16 * nb_, 384), IX("nw", Z, "hb16", nb_, 24), BA, SA)
+    if LEAD:
+        heavy(a, a + LEAD)
     act(X("hl", 0, a), IX("nw", Z, "hl16", 0, a // 16), BA, SA)
     act(X("hb", 0, a), IX("nw", Z, "hl16", 128, 128 + a // 16))
     merge("m1", "hb", 8, 8, a)
     ts(X("bst", 0, 16 * nb_), IX("nw", Z, "hb16", 0, nb_), SA, OP.mult, BA, OP.add)
     ts(X("hb16", 24, 48), X("pd", 0, 24), MID, OP.add)
+    if LEAD:
+        light(a, a + LEAD)
+        a += LEAD
     border("hl", "hst", "hl", lambda e, out, q0, q1: tt(out, IX("nw", Z, "hb16", 24 + 6 * q0, 24 + 6 * q1), X("bst", C * q0, C * q1), OP.max), "VVVV")
     for n in STEPS[1:]:
         heavy(a, a + n)
@@ -382,7 +412,6 @@ def rank_program(g, core, T, topo):
         a += n
     for m, value in ((P4, 4.0), (PB, BIG), (N4, -4.0)):
         diagonal(m, value)
-    iota(TG(4), [[0, 128]], 0, 0)
     HZ, ROW = (X("psw", 1024, 1152), X("psw", 1152, 1280)), X("one", 0, 128, 1, 0, 1)
     for K in range(2):
         mm(HZ[K], X("hlm", K * 128, K * 128 + 128), IF)
@@ -390,35 +419,42 @@ def rank_program(g, core, T, topo):
     pick("pa", 0, "hl", 0, SF(0, 4, 2), 4, "own")
     border("hh", "cst", "hh", lister("hl", Z, "hb16"))
     share("hh", 0, "hl", Z, "hl16", 0, SHARE["hh"])
+    tt(X("dn", 0, 128), X("hlm", 128, 256), X("hlm", 0, 128), OP.subtract)
+    DZ, QL = X("psw", 1280, 1408), X("psw", 384, 512)
+    mm(DZ, X("dn", 0, 128), IF)
+    mm(QL, IF, X("hlm", 0, 128), True, False, tag="q")
     pick("pc", 0, "hh", 0, SF(0, 4, 2), 4, "hh")
     LESS = 768
-    HN, OWN, LN, HH = TG(0), TG(1), TG(3), TG(5)
-    if LESSAT == 0:
-        act(TG(0, 4, 3), X("pa", 0, 256))
+    HN, OWN, LN, HL, HH = TG(0), TG(1), TG(3), TG(4), (T.hhn[:, :, :], [("hhn", 0, 128, 0, 128)])
+    act(TG(0, 4, 3), X("pa", 0, 256))
     where(G8, X("one", 0, 8), [[-16, 8]], 0, 1)
-    iota(X("e0", 128, 136), [[0, 8]], 0, 0)
-    iota(X("ar", 128, 136), [[0, 8]], 0, 0)
-    iota(X("ar", 264, 272), [[0, 8]], 0, 0)
+    for name in ("t1p", "arhp"):
+        iota((T[name][:, 0:33:2, :], [(name, 0, 128, 0, 264)]), [[0, 136]], 0, 0)
     where(G8, G8, [[16, 8]], 15, -1)
+    iota(X("e2", 512, 528), [[0, 16]], 0, 0)
     where(X("ti", 128, 256), ZERO, DIAG, 0, 1, OP.is_ge, 1.0)
-    T1, NHL, B, EH2 = X("e0", 0, 128), X("e0", 144, 272), X("e1", 0, 128), X("e1", 128, 256)
+    NHL, B, EH2 = X("e0", 144, 272), X("e1", 0, 128), X("e1", 128, 256)
+    T1, ARH = ((T[name][:, :, :], [(name, 0, 128, 0, 128)]) for name in ("t1", "arh"))
+
+    def pad(name):
+        for c in range(2):
+            o = T[name + "p"][:, 16 * c + 1:16 * c + 16:2, :], [(name + "p", 0, 128, 128 * c, 128 * c + 128)]
+            i = T[name][:, :, 8 * c:8 * c + 8], [(name, 0, 128, 0, 128)]
+            if name == "t1":
+                where(o, i, [[0, 64]], 0, 0)
+            else:
+                act(o, i)
+
     border("hhh", "dst", "hhh", lister("hh", Z, "hb16"))
-    merge("m2", "hh", 0, 2)
-    merge("m2", "hh", 8, 6)
+    merge("m2", "hh", 0, 2, Z, 8)
     share("hhh", 0, "hh", Z, "hl16", 0, SHARE["hhh"])
     pick("pb", 0, "hhh", 0, SF(0, 1), 2, "hhh")
-    merge("m3", "hhh", 0, 10, V)
-    merge("m3", "hhh", 0, 10, Z, V)
-    tt(T1, X("pc", 0, 128), OWN, OP.is_equal)
-    tt(NHL, X("pc", 128, 256), OWN, OP.not_equal)
-    tt(X("psw", LESS, LESS + 256), X("pa", 0, 256), TG(1, 3), OP.is_lt)
-    if LESSAT == 1:
-        act(TG(0, 4, 3), X("pa", 0, 256))
     act(X("fld", 0, 256), X("pc", 256, 512))
     act(HH, X("pc", 0, 128))
-    act(X("fld", 256, 384), X("pc", 256, 384), -float(OFFC))
+    tt(X("psw", LESS, LESS + 256), X("pa", 0, 256), TG(1, 3), OP.is_lt)
+    ts(SIDEA, X("cj", 0, 1), 8.0, OP.is_lt)
 
-    dma("Y", "x", T.xw[:, 0:V], rg(X("xw", 0, V)), T.x[:, :], rg(X("hl", 0, Z)))
+    dma("Y", "x", T.xw[:, 0:V], rg(X("xw", 0, V)), T.x[:, :], [], "hhh")
     diagonal(P2, 2.0)
     diagonal(X("ibn", 0, 128), -MID)
     diagonal(X("nti", 0, 128), -1.0)
@@ -427,89 +463,117 @@ def rank_program(g, core, T, topo):
     SELR, SELQ = X("selr", 0, 128, 1, 0, 16), X("selq", 0, 128, 1, 0, 16)
     where(SELR, X("one", 0, 128, 1, 0, 16), [[-16, 8], [0, 16]], -128, 16, OP.is_equal)
     where(SELQ, X("one", 0, 128, 1, 0, 16), [[-16, 8], [0, 16]], 0, 16, OP.is_equal)
-    iota(X("inv", INV, 2448), [[0, 2448 - INV]], 0, 0)
 
-    def pack(digits, weight, last=False):
-        name, c0 = digits[1][0][0], digits[1][0][3]
+    WORDS = 1792
+
+    def pack(flags, weight, last=False):
+        name, c0 = flags[1][0][0], flags[1][0][3]
         for c in range(2):
-            mm(X("pc", c, 256, 2), X(name, c0 + 8 * c, c0 + 8 * c + 128), weight, False, last and c == 1, tag="pack")
+            if name in ("t1", "arh"):
+                for j in (16 * c, 16 * c + 1):
+                    mm(X("psw", WORDS + c, WORDS + 256, 2), (T[name + "p"][:, j:j + 16, :], [(name + "p", 0, 128, 0, 264)]), weight, False, False, tag="pack")
+            else:
+                mm(X("psw", WORDS + c, WORDS + 256, 2), X(name, c0 + 8 * c, c0 + 8 * c + 128), weight, False, last and c == 1, tag="pack")
 
     def total_of(out, terms, first=False, last=False, tag=None):
         for i, (m, e) in enumerate(terms):
             mm(out, m, e, first and i == 0, last and i == len(terms) - 1, tag=tag)
 
-    ARH, ARL = X("ar", 0, 128), X("ar", 136, 264)
-    THA, THL, S2, M2 = X("psw", 256, 384), X("psw", 1536, 1664), X("psw", 1664, 1792), X("m2", 0, 128)
-    E4 = X("pb", 256, 384)
-    share("gb", 0, "hhh", Z, "hl16", 0, SHARE["hhhh"])
+    ARL = X("ar", 0, 128)
+    THA, THL, S2, M2 = X("psw", 256, 384), X("psw", 1536, 1664), X("pc", 0, 128), X("m2", 0, 128)
+    EH, EL = X("pb", 256, 384), X("pb", 384, 512)
+    ELH, ELL, TL1, QB = (X("e2", 128 * j, 128 * j + 128) for j in range(4))
+    n0, n2 = SHARE["l"]
+    gather("S", "gb", V, "hl", Z, "hl16", 128, n2, V)
+    gather("V", "gb", V, "hl", Z, "hl16", 128, 0, n0)
+    mm(X("psw", WORDS, WORDS + 256), ZERO, TI, True, False, tag="pack")
     tt(B, X("pb", 0, 128), HN, OP.is_equal)
     tt(EH2, X("pb", 128, 256), HN, OP.is_equal)
-    mm(X("pc", 0, 256), ZERO, TI, True, False, tag="pack")
-    pack(T1, P4)
-    total_of(S2, ((N4, T1), (P4, B)), True, False, "s2")
-    total_of(E4, ((PB, NHL), (PB, B)), True, False, "hhhh")
-    pick("pb", 256, "gb", 0, SF(0, 0, 0), 1, "hhhh", False)
-    share("gb", V, "hl", Z, "hl16", 128, SHARE["l"])
+    tt(T1, X("pc", 0, 128), OWN, OP.is_equal)
+    pack(B, P4)
+    tt(X("dn", 0, 128), DZ, B, OP.mult)
+    mm(QL, X("dn", 0, 128), IF, False, True, tag="q")
+    tt(NHL, X("pc", 128, 256), OWN, OP.not_equal)
+    pad("t1")
+    iota(X("inv", INV, 1664), [[0, 1664 - INV]], 0, 0)
+    gather("V", "gb", V, "hl", Z, "hl16", 128, n0, n2)
+    ts(X("mate", 0, 128), QL, MID, OP.add)
+    act(U0, SIDEA, 100.0, -94.0)
+    mm(X("pb", 256, 512), ZERO, TI, True, False, tag="q2")
+    total_of(EH, ((PB, NHL), (PB, B)), False, False, "q2")
     pick("pd", 0, "gb", V, SF(0, 2), 4, "l")
+    n0, n1 = SHARE["q"]
+    gather("S", "gb", 0, "hhh", Z, "mate", 0, n1, V)
+    gather("V", "gb", 0, "hhh", Z, "mate", 0, 0, n0)
+    tt(X("e2", 0, 384), X("pd", 0, 384), TG(1, 4), OP.is_equal)
+    gather("V", "gb", 0, "hhh", Z, "mate", 0, n0, n1)
+    act(HL, X("pd", 0, 128), -2.0 * BIG)
+    pack(T1, PB)
+    total_of(EL, ((NB, B), (NB, ELL), (PB, TL1)), False, False, "q2")
+    pick("pb", 256, "gb", 0, SF(3, 4), 2, "q2", False)
+    pack(ELH, P2)
     tt(X("pa", 256, 512), X("pa", 256, 512), X("fld", 0, 256), OP.subtract)
-    tt(ARH, E4, HH, OP.is_equal)
-    ts(SIDEA, X("cj", 0, 1), 8.0, OP.is_lt)
+    EL2 = X("e0", 272, 400)
+    tt(EL2, X("pd", 384, 512), LN, OP.is_equal)
     for K in range(2):
         tt(X("pa", 256 + 128 * K, 384 + 128 * K), X("pa", 256 + 128 * K, 384 + 128 * K), NHL, OP.mult)
-    ELH, ELL, TL1, THL1 = (X("e2", 128 * j, 128 * j + 128) for j in range(4))
-    tt(X("e2", 0, 512), X("pd", 0, 512), TG(1, 5), OP.is_equal)
-    pack(ARH, P4)
-    total_of(X("psw", 128, 256), ((IB, T1), (IB, ARH)), True, True, "m2")
-    border(None, "xst", "xw", lister("xw", V, "bl16"), "SSSS")
-    act(M2, X("psw", 128, 256))
-    total_of(S2, ((P2, ELH), (IB, ELL), (N4, TL1), (IB, THL1)), False, True, "s2")
-    tt(X("c16", 0, 128), X("pa", 256, 384), X("fld", 256, 384), OP.add)
-    tt(X("fld", 384, 512), X("pa", 384, 512), X("fld", 128, 256), OP.add)
-    ts(ARL, S2, 6.0, OP.is_ge)
-    mm(X("pb", 0, 128), X("c16", 0, 128), IB)
-    pack(ARL, P2, True)
-    cp(X("idx", 0, 128), X("pb", 0, 128))
-    cp(X("wv", 256 * r, 256 * r + 256), X("pc", 0, 256))
-    spread("w2", "wv")
-    pick("pa", 0, "gb", V, SF(2, 4), 4, "l2")
-    total_of(THA, ((P2, EH2), (P4, B), (P4, NHL), (P4, ARH)), True, True, "tha")
     act(X("pw", 0, 8), X("zero", 0, 8), 0.125)
     act(SIDEB, SIDEA, 1.0, -1.0)
     act(col(73), SIDEA, 0.0, -1.0 / BIG)
     act(col(72), SIDEA, -1.0 / BIG, 1.0 / BIG)
     act(X("km", 0, 256), X("km", 0, 256), col(73), col(72))
-    scan(X("pw", 8, 16), X("pw", 0, 8), X("zero", 0, 8), 8.0, OP.mult, OP.add)
-    cp(X("nb16", 0, 256), X("nbi", 0, 256))
+    border(None, "xst", "xw", lister("xw", V, "bl16"), "SSSS")
+    for c in range(2):
+        tt((T.arhp[:, 16 * c + 1:16 * c + 16:2, :], [("arhp", 0, 128, 128 * c, 128 * c + 128)]),
+           (T.pb[:, 16:24, 8 * c:8 * c + 8], EH[1]), (T.hhn[:, :, 8 * c:8 * c + 8], HH[1]), OP.is_equal)
+    tt(QB, EL, HL, OP.is_equal)
+    pack(ARH, PB)
+    pack(QB, P2, True)
+    tt(ARH, EH, HH, OP.is_equal)
+    tt(X("c16", 0, 128), X("pa", 256, 384), X("fld", 0, 128), OP.add)
+    tt(X("fld", 384, 512), X("pa", 384, 512), X("fld", 128, 256), OP.add)
+    ts(X("wv", 256 * r, 256 * r + 256), X("psw", WORDS, WORDS + 256), U0, OP.is_ge)
+    spread("w2", "wv")
+    total_of(X("psw", 128, 256), ((IB, T1), (IB, ARH)), True, True, "m2")
+    act(M2, X("psw", 128, 256))
+    mm(X("pb", 0, 128), X("c16", 0, 128), IB)
+    total_of(S2, ((N4, T1), (P4, B), (P2, ELH), (P2, QB)), True, True, "s2")
+    pick("pa", 0, "gb", V, SF(2, 3), 2, "l2")
+    scan(X("pw", 8, 16), X("pw", 0, 8), X("zero", 0, 8), 16.0, OP.mult, OP.add)
+    ts(X("idx", 0, 128), X("pb", 0, 128), float(OFFC), OP.subtract)
+    ts(ARL, S2, 6.0, OP.is_ge)
     tt(col(64, 8), col(48, 8), X("pw", 8, 16), OP.mult)
-    ts(QW, X("cj", 0, 1), -1.0, OP.mult, 16.0, OP.add)
-    if not SPD:
-        tt(col(M8, 8), MC(0, 8), MC(8, 8), OP.add)
+    cp(X("nb16", 0, 256), X("nbi", 0, 256))
+    total_of(THA, ((P2, EH2), (P4, B), (P4, NHL), (P4, ARH)), True, True, "tha")
 
     show("x", "xst", "xw")
     dma("Y", "xc", T.xc[:, 0:SHARE["x"]], rg(X("xc", 0, SHARE["x"])), T.x[:, 0:SHARE["x"]], [], "x")
-    a = 512 * len(BOTH)
+    a = FUSE
     for c in range(16):
         dma("Y", "wr", T.wr[c:128:16, a:V], [("wr", 16 * k + c, 16 * k + c + 1, 0, V) for k in range(8)], T.w[:, a:V], [])
-    EL2 = X("e0", 272, 400)
-    for K, m in ((1, ARL), (0, M2)):
-        tt(X("pz2", 128 * K, 128 * K + 128), m, HZ[K], OP.mult)
     sum_of(W8, col(64, 8))
     act(X("selw", 0, 8), G8, 0.0, W8)
     ts(X("c16", 128, 256), X("pa", 0, 128), float(OFFC), OP.subtract)
     mm(X("pd", 0, 128), X("c16", 128, 256), IB)
-    tt(EL2, X("pa", 256, 384), LN, OP.is_equal)
     act(X("fld", 640, 768), X("pa", 128, 256))
     for K, m in enumerate((M2, ARL)):
-        tt(X("nr2", 128 * K, 128 * K + 128), m, X("psw", LESS + 128 * K, LESS + 128 * K + 128), OP.mult)
+        tt(X("pz2", 128 * K, 128 * K + 128), m, HZ[K], OP.mult)
     cp(X("idx", 128, 256), X("pd", 0, 128))
+    for K, m in enumerate((M2, ARL)):
+        tt(X("nr2", 128 * K, 128 * K + 128), m, X("psw", LESS + 128 * K, LESS + 128 * K + 128), OP.mult)
+    ts(QW, X("cj", 0, 1), -1.0, OP.mult, 16.0, OP.add)
     total_of(THL, ((ONE, P4), (N4, ELL), (P2, EL2), (P4, TL1), (N4, ELH), (N4, ELH), (PB, M2), (PB, ARL)), True, False, "thl")
-    for K, m in ((1, ARL), (0, M2)):
-        mm(X("psw", 0, 128), m, X("ibn", 0, 128), K == 1, False, tag="mate")
-        mm(X("psw", 0, 128), X("pz2", 128 * K, 128 * K + 128), IB, False, False, tag="mate")
+
+    def mates(flags, numbers, first=False, last=False):
+        mm(X("psw", 0, 128), flags, X("ibn", 0, 128), first, False, tag="mate")
+        mm(X("psw", 0, 128), numbers, IB, False, last, tag="mate")
+
+    mates(ARL, X("pz2", 128, 256), True)
+    mates(M2, X("pz2", 0, 128))
     mm(X("psw", 512, 768), ONE, TI, True, False, tag="rep")
     for K in range(2):
         mm(X("psw", 512, 768), X("nr2", 128 * K, 128 * K + 128), X("nti", 0, 256), False, False, tag="rep")
-    LT, LTE, B0, Q0, SELI = X("lt", 0, 128), X("lte", 0, 128), X("b0", 14, 142), X("q0", 14, 142), X("seli", 0, 64)
+    LT, LTE, LT8, Q8, B16, SELI = X("lt", 0, 128), X("lte", 0, 128), X("lt0", 0, 128), X("q0", 0, 128), X("b16", 0, 16), X("seli", 0, 64)
     BLK = X("blk", 0, 128)
     where(BLK, ONE, [[-16, 8], [0, 16]], 0, 1)
     iota(X("wq", 0, 288), [[0, 288]], 0, 0)
@@ -520,16 +584,17 @@ def rank_program(g, core, T, topo):
     where(LTE, LTE, [[1, 128]], 0, -1)
     where(LT, LT, [[1, 128]], 0, -1, OP.not_equal, BIG)
     where(LTE, LTE, [[1, 128]], 0, -1, OP.not_equal, -16.0)
-    where(B0, BLK, [[0, 8], [-1, 16]], 1, 0)
+    iota(B16, [[0, 16]], 1, 0)
+    where(Q8, ONE, [[-16, 8], [0, 8], [-8, 2]], 0, 1)
+    where(B16, B16, [[-8, 16]], 0, 1)
     where(SELI, X("zero", 0, 64), [[-16, 8], [-1, 8]], 0, 1, OP.not_equal, 1.0)
-    where(Q0, B0, [[-16, 8], [-8, 16]], 0, 1)
-    where(X("lt0", 14, 142), B0, [[16, 8], [8, 16]], 0, -1, OP.is_gt)
-    where(Q0, Q0, [[16, 8], [8, 16]], 7, -1)
+    where(B16, B16, [[8, 16]], 7, -1)
+    where(Q8, Q8, [[16, 8], [0, 8], [8, 2]], 7, -1)
     where(SELI, SELI, [[-16, 8], [-1, 8]], -8, 1, OP.not_equal, 16.0)
-    for name in ("b0", "lt0", "q0"):
-        iota(X(name, 0, 14), [[0, 14]], 0, 0)
+    where(LT8, BLK, [[16, 8], [0, 8], [8, 2]], 0, -1, OP.is_gt)
     iota(X("vl", 0, 16), [[16, 16]], V - int(BIG), 1)
     iota(X(SPW, Z, Z + 16), [[0, 16]], 0, 0)
+    iota(X("inv", 1664, 2448), [[0, 784]], 0, 0)
     for a, b in () if SPD else ((0, 8), (136, 152), (280, 288)):
         iota(X("half", a, b), [[0, b - a]], 0, 0)
     for c in range(0 if SPD else 2):
@@ -551,8 +616,9 @@ def rank_program(g, core, T, topo):
     ask(0, n0)
     answer(0, "pc")
     nx = SHARE["x"]
-    hx = nx + 384
-    for bank, a, b in (("pa", nx, hx), ("pb", hx, V)):
+    hx = nx + SHARE["hx"]
+    halves = (("pa", nx, hx), ("pb", hx, V))
+    for bank, a, b in halves:
         mm(X(bank, 0, b - a), IB, X("xw", a, b), True, False, tag="gx")
     ask(1, n1)
     shift(0, "pc")
@@ -563,25 +629,23 @@ def rank_program(g, core, T, topo):
     ts(Z0, X("zj", 0, 128), 0.0, OP.is_equal)
     total_of(THL, ((PB, A3), (PB, Z0)), False, True, "thl")
     tt(X("pz3", 0, 128), A3, HZ[0], OP.mult)
-    mm(X("psw", 0, 128), A3, X("ibn", 0, 128), False, False, tag="mate")
-    mm(X("psw", 0, 128), X("pz3", 0, 128), IB, False, False, tag="mate")
+    mates(A3, X("pz3", 0, 128))
     shift(1, "pd")
     digit(1)
     tt(L3, X("zj", 128, 256), THL, OP.is_gt)
     tt(X("pz3", 128, 256), L3, HZ[1], OP.mult)
-    mm(X("psw", 0, 128), L3, X("ibn", 0, 128), False, False, tag="mate")
-    mm(X("psw", 0, 128), X("pz3", 128, 256), IB, False, True, tag="mate")
+    mates(L3, X("pz3", 128, 256), False, True)
     tt(X("nr3", 0, 256), X("ar3", 0, 256), X("psw", LESS, LESS + 256), OP.mult)
+    ts(X("mate", 0, 128), X("psw", 0, 128), float(Z), OP.add)
     for c, side in enumerate((SIDEA, SIDEB)):
         act(col(76 + c), side, 0.0, QW)
         act(X("wq", 144 * c + 16, 144 * c + 144, 16), G8, 0.0, side, tag="wq")
         act(X("wq", 144 * c + 8, 144 * c + 136, 16), G8, 0.0, col(76 + c), tag="wq")
+    for i in range(8):
+        act((T.m8[:, :, i, :], [("m8", 0, 128, 0, 128)]), X("one", 0, 16), 0.0, col(55 - i), tag="m8")
     if not INVAT:
         act(X("inv", 0, INV), X("hh", 0, INV), 0.0, 0.0)
 
-    ts(X("mate", 0, 128), X("psw", 0, 128), float(Z), OP.add)
-    nx = SHARE["x"]
-    hx = nx + 384
     for K in range(2):
         mm(X("psw", 512, 768), X("nr3", 128 * K, 128 * K + 128), X("nti", 0, 256), False, K == 1, tag="rep")
 
@@ -589,7 +653,7 @@ def rank_program(g, core, T, topo):
         mm(X("psw", 512 * j, 512 * j + 512), SELR, X("wsb", 512 * j, 512 * j + 512, 1, 0, 16))
 
     weights(3)
-    for bank, a, b in (("pa", nx, hx), ("pb", hx, V)):
+    for bank, a, b in halves:
         act(X("gb", a - nx, b - nx), IX("xw", Z + 16, "mate", a // 16, b // 16))
         mm(X(bank, 0, b - a), IB, X("gb", a - nx, b - nx), False, True, tag="gx")
     REP, UP, HI, LO = X("ru", 0, 128), X("ru", 128, 256), X("hilo", 0, 128), X("hilo", 128, 256)
@@ -604,17 +668,24 @@ def rank_program(g, core, T, topo):
             mm(X("pd", 0, 128), BLK, UP, True, False, tag="num")
             mm(X("pd", 0, 128), X("lt", 0, 128), REP, False, True, tag="num")
 
-    if RUQ == "S":
+        mm(X("psw", 128, 256), UP, BLK, True, False, tag="base")
+        mm(X("psw", 128, 256), REP, LT8, False, False, tag="base")
+
+    def mask(i):
+        ts(X("mk", 128 * i, 128 * i + 128), X("pc", 0, 128), float(i - 16), OP.is_equal, -BIG, OP.mult)
+
+    if RUAT:
+        tt(X("xf", 0, RUAT), IX("xw", Z + 16, "mate", 0, RUAT // 16), X("xc", 0, RUAT), OP.add)
         count()
     weights(2)
-    tt(X("xf", 0, nx), IX("xw", Z + 16, "mate", 0, nx // 16), X("xc", 0, nx), OP.add)
-    for bank, a, b in (("pa", nx, hx), ("pb", hx, V)):
+    tt(X("xf", RUAT, nx), IX("xw", Z + 16, "mate", RUAT // 16, nx // 16), X("xc", RUAT, nx), OP.add)
+    for bank, a, b in halves:
         act(X("xf", a, b), X(bank, 0, b - a))
-    if RUQ == "V":
+    if not RUAT:
         count()
-    parts = (X("cn", 0, 128), HI)[:1 if SPD == 1 else 2]
-    for o in parts[:RU]:
-        ts(o, X("pd", 0, 128), V * r - BIG, OP.add, 0.0, OP.max)
+    for i in range(AHEAD):
+        mask(i)
+    parts = (X("cn", 0, 128), HI)
     border("xs", "xb", "xf", lister("xf", V, "bl16"))
     if RANK:
         act(X("bt", 0, 128), X("pc", 0, 128))
@@ -622,29 +693,33 @@ def rank_program(g, core, T, topo):
         act(o, X("pd", 0, 128), V * r - BIG, func=AF.Relu)
     for b, a in zip(CUTS, CUTS[1:]):
         iota(X("left", a // 16, b // 16), [[0, (b - a) // 16]], (V - a) // 128, 0)
+    where(X("g2h", 0, 144), X("g8h", 0, 144), [[16, 9], [0, 16]], -15, -1)
     iota(X("sw", Z, Z + 16), [[0, 16]], 0, 0)
     iota(X("tw", V, V + 8), [[0, 8]], 0, 0)
 
-    if SPD != 1:
-        tt(LO, X("cn", 0, 128), HI, OP.subtract)
-    for c in range(0 if SPD else 2):
-        o = X("pd", 128 + 128 * c, 256 + 128 * c)
-        mm(o, X("half", 144 * c + 16 * c, 144 * c + 16 * c + 128), HI, True, False, tag="two")
-        mm(o, X("half", 144 * c + 8, 144 * c + 136), LO, False, True, tag="two")
-    for j in range(8 * SPD):
-        p, src, c = 16 * (j % 8) + j // 8, "cn" if SPD == 1 else "hilo", 16 * j
-        dma("Y", "sp", T[SPW][p:p + 1, 0:V], rg(X(SPW, 0, V, 1, p, p + 1)), T[src][:, c:c + 16], rg(X(src, c, c + 16)), "xs")
+    def rows():
+        if SPD != 1:
+            tt(LO, X("cn", 0, 128), HI, OP.subtract)
+        for j in range(8 * SPD):
+            p, src, c = 16 * (j % 8) + j // 8, "cn" if SPD == 1 else "hilo", 16 * j
+            dma("Y", "sp", T[SPW][p:p + 1, 0:V], rg(X(SPW, 0, V, 1, p, p + 1)), T[src][:, c:c + 16], rg(X(src, c, c + 16)), BEHIND)
+
     if INVAT:
         act(X("inv", 0, INV), X("hh", 0, INV), 0.0, 0.0)
     mm(X("pa", 0, 256), ZERO, TI, True, False, tag="eight")
     for i in range(8):
         MK = X("mk", 128 * i, 128 * i + 128)
-        ts(MK, X("bt" if RANK else "pc", 0, 128), float(i - 16), OP.is_equal, -BIG, OP.mult)
+        if i >= AHEAD:
+            mask(i)
         for c in range(2):
             mm(X("pa", c, 256, 2), X("wq", 144 * c + 8 - i, 144 * c + 136 - i), MK, False, c + i == 8, tag="eight")
-        for m in range(8 if i == BASE else 0):
-            for k, (lhs, rhs, c0) in enumerate((("b0", "ru", 128), ("lt0", "ru", 0), ("q0", "mk", 0))):
-                mm(X("pb", 0, 16), X(lhs, 14 - 2 * m, 142 - 2 * m), X(rhs, c0 + m, c0 + 128, 8), m + k == 0, m + k == 9, tag="base")
+        if i == 0:
+            mm(X("psw", 128, 256), MK, Q8, False, True, tag="base")
+        if i == BASE:
+            tt(X("dn", 0, 128), X("psw", 128, 256), (T.m8[:, :, :, :], [("m8", 0, 128, 0, 128)]), OP.mult)
+            mm(X("psw", 0, 16), X("dn", 0, 128), B16)
+        if i == LOAT:
+            rows()
 
     def SP(c):
         return X("sp", c, V, 16)[0], [("sp%d" % c, 0, 128, 0, 128)]
@@ -669,21 +744,21 @@ def rank_program(g, core, T, topo):
                 border("num", "sb", SPW, lambda e, out, q0, q1: move(e, out, numbers("bl16", 6 * q0, 6 * q1, V)), NUMQ)
             continue
         if j in BOTH:
-            mm(X(BOTH[j], 0, 512), SELQ, X("wsb", a, b, 1, 0, 16))
-            weights(j)
-            act(X("p0", a, b), IX("xf", Z, "nb16", 32 * j, 32 * j + 32))
+            act(X("p0", a, min(b, FUSE)), IX("xf", Z, "nb16", 32 * j, min(b, FUSE) // 16))
         act(X("g1", a, b), IX("xf", Z, "nb16", 128 + 32 * j, 160 + 32 * j))
         if j == NUM:
             border("num", "sb", SPW, lambda e, out, q0, q1: act(out, numbers("bl16", 6 * q0, 6 * q1, V)), "SSSS")
 
     def columns():
-        tt(X("off", 0, 16), X("pb", 0, 16), X("vl", 0, 16), OP.min)
+        tt(X("off", 0, 16), X("psw", 0, 16), X("vl", 0, 16), OP.min)
         tt(X("rb", 0, 256), X("pa", 0, 256), X("km", 0, 256), OP.mult)
         ts(X("off16", 0, 16), X("off", 0, 16), BIG + 16.0, OP.add)
 
     def scatter():
         o = IX("inv", 2448, "off16", 0, 16)
         add("V", lambda e: e.tensor_copy(out=o[0], in_=T.rb[:, :]), rg(X("inv", 0, 2448)), rg(X("rb", 0, 256), X("off16", 0, 16)))
+
+    def shifted():
         mm(X("pb", 0, 128), ONE, X("left", 0, 128), True, False, tag="iv")
         mm(X("pa", 0, 512), ZERO, X("wv", 0, 512), True, False, tag="inv")
         for d in range(-7, 16):
@@ -695,11 +770,8 @@ def rank_program(g, core, T, topo):
         mm(X("pb", 0, 128), X("ivt", 0, 128), IB, False, True, tag="iv")
 
     def first(j):
-        a, b = 512 * j, 512 * j + 512
-        if j in BOTH:
-            tt(X("p0", a, b), X("p0", a, b), X(BOTH[j], 0, 512), OP.mult)
-        else:
-            tt(X("p0", a, b), IX("xf", Z, "nb16", a // 16, b // 16), X("wr", a, b), OP.mult)
+        a, b = 512 * j, min(512 * j + 512, FUSE)
+        tt(X("p0", a, b), X("p0", a, b), X(BOTH[j], 0, b - a), OP.mult)
 
     def second(a, b):
         tt(X("psw", a, b), X("g1", a, b), X("psw", a, b), OP.mult)
@@ -715,43 +787,63 @@ def rank_program(g, core, T, topo):
         columns()
     if EARLY > 1:
         scatter()
-    tt(X("p0", 1024, V), IX("xf", Z, "nb16", 64, 128), X("wr", 1024, V), OP.mult)
+    tt(X("p0", FUSE, V), IX("xf", Z, "nb16", FUSE // 16, 128), X("wr", FUSE, V), OP.mult)
     if EARLY < 1:
         columns()
-    second(1536, V)
+    for j in BOTH:
+        b = min(512 * j + 512, FUSE)
+        mm(X(BOTH[j], 0, b - 512 * j), SELQ, X("wsb", 512 * j, b, 1, 0, 16))
+        weights(j)
+    if SUM:
+        a = V - SUM
+        mm(X("pb", 0, SUM), IF, X("p0", a, V), True, False, tag="sum")
+        tt(X("g1", a, V), X("g1", a, V), X("psw", a, V), OP.mult)
+        mm(X("pb", 0, SUM), IF, X("g1", a, V), False, True, tag="sum")
+        act(X("sw", a, V), X("pb", 0, SUM))
+    if SUM < 512:
+        second(1536, V - SUM)
     second(1024, 1536)
-    both(1536, V)
-    keep(3)
+    if SUM < 512:
+        both(1536, V - SUM)
+    if not SUM:
+        keep(3)
     first(1)
     both(1024, 1536)
     keep(2)
     second(512, 1024)
     first(0)
-    second(0, 512)
-    both(512, 1024)
-    both(0, 512)
+    if TAIL:
+        both(512, 1024)
+        second(0, 256)
+        second(256, 512)
+        both(0, 256)
+        both(256, 512)
+    else:
+        second(0, 512)
+        both(512, 1024)
+        both(0, 512)
+    if NUM == -1:
+        border("num", "sb", SPW, lambda e, out, q0, q1: act(out, numbers("bl16", 6 * q0, 6 * q1, V)), "SSSS")
     if nc:
         act(X("cmr", 0, nc), numbers("mate", 0, nc // 16, Z + 16))
-    border("s", "sst", "sw", lister("sw", V, "bl16"))
+    border("s", "sst", "sw", lister("sw", V, "bl16"), SST)
+    if SUM:
+        keep(3)
     keep(1)
     keep(0)
 
-    if SPD:
-        mm(X("pd", 0, 128), X("cn", 0, 128), IF, True, False, tag="cm")
-    else:
-        mm(X("pd", 0, 128), IF, X("cn", 0, 128), True, False, tag="cm")
+    mm(X("pd", 0, 128), HI, IB, True, False, tag="cm")
+    mm(X("pd", 0, 128), LO, IB, False, False, tag="cm")
     if EARLY < 2:
         scatter()
+    shifted()
     if nd > nc:
         act(X("cmr", nc, nd), numbers("mate", nc // 16, nd // 16, Z + 16))
     if nd < V:
         cp(X("cmr", nd, V), numbers("mate", nd // 16, 128, Z + 16))
     inverse()
-    if SPD == 1:
-        for b in range(16):
-            mm(X("pc", b, 128, 16), X("cmr", b, V, 16), X("iff", 0, 128, 16), tag="cm")
-    else:
-        pick("pc", 0, "cmr", 0, SF(0, 0, 0) if SPD else G8, 1, "cm")
+    for b in range(16):
+        mm(X("pd", 0, 128), X("g2h", 16 - b, 144 - b), X("cmr", b, V, 16), False, b == 15, tag="cm")
     last = len(CUTS) - 2
     for j, (b, a) in enumerate(zip(CUTS, CUTS[1:])):
         tt(X("tw", a, b), IX("sw", Z + 16, "mate", a // 16, b // 16), X("p0", a, b), OP.add)
@@ -759,14 +851,13 @@ def rank_program(g, core, T, topo):
             cp(X("iv16", 0, 128), X("pb", 0, 128))
         o, i = X("g1", a, b), IX("tw", V + 8, "iv16", a // 16, b // 16, a)
         if j == last:
-            cp(o, i)
+            cp(X("g1", 0, LAST), IX("tw", V + 8, "iv16", 0, LAST // 16))
+            if LAST < b:
+                act(X("g1", LAST, b), IX("tw", V + 8, "iv16", LAST // 16, b // 16))
         else:
             act(o, i)
         dma("Y", "y%d" % j, T.y[:, a:b], [], o[0], o[1])
         if j == CM:
-            act(X("cmt", 0, 128), X("pc", 0, 128))
-            mm(X("pd", 0, 128), X("cmt", 0, 128), IF, False, True, tag="cm")
-        if j == CM + 2:
             act(X("cmv", 0, 128), X("pd", 0, 128))
             dma("Y", "cm", T.cm[:, :], [], T.cmv[:, :], rg(X("cmv", 0, 128)))
     for s, v in total.items():

from concourse.bass import DstId, RemoteDMATransfer
from concourse.mybir import AluOpType, ActivationFunctionType, AxisListType

OP = AluOpType
AF = ActivationFunctionType
V, C, Z = 2048, 96, 2432
BIG, MID = 16384.0, 1216.0
OFFN, OFFC = 8192 + 128, 1016 + 7
F32, BF, F16, I32, U16 = "float32", "bfloat16", "float16", "int32", "uint16"
WIDTHS = {
    F32: dict(dn=128, nbm=256, hlm=256, mb=384, col=128, ir=144, iff=128, xf=2432, cn=128, stm=72,
              vl=16, off=16, g1=2048, p0=2048, sw=2448, sst=384, cmt=128, cmv=128, tw=2056, xb=384, fld=768),
    BF: dict(wsb=2048, xw=2448, xc=2048, bst=384, hb=2048, hl=2432, hh=2432, hhh=2432, hst=384, cst=384, dst=384,
             xst=384, gb=4096, wr=2048, ti=256, nti=256, ibn=128, dg=768, pm=8, selw=8, seli=64, e0=400, e1=272,
             e2=528, ar=128, ar3=384, m2=128, nr2=256, nr3=256, wv=1024, one=128, zero=144, ru=256, mk=1024, blk=128, lt=128,
             lte=128, b0=144, lt0=144, q0=144, wq=288, km=256, rb=256, inv=2448, selr=128, selq=128, bt=128, left=128,
             nw=2432, sp=2448, sb=384, cmr=2048, hilo=256, two=256, half=288, g8b=8, g8h=144, g2h=144, pw=256),
    F16: dict(pz2=256, pz3=256, ivt=128, hrow=768, c16=256),
    I32: dict(bli=24, nbi=256, ci=24, cj=32, yj=256, zj=256, bki=48, gli=24),
    U16: dict(gl16=24, bl16=24, hl16=256, idx=256, mate=128, off16=16, iv16=128, nb16=256, bk16=48, hb16=48),
}
SPD = 2
SPW = ("sp", "nw", "hhh")[SPD]
WIDTHS[BF]["hhh"] = 2448
if SPD == 1:
    for _n in ("nw", "sb", "cmr"):
        WIDTHS[F32][_n] = WIDTHS[BF].pop(_n) + (16 if _n == "nw" else 0)
PSUM = {"psw": 2048, "pa": 512, "pb": 512, "pc": 512, "pd": 512}
SCRATCH = {"tg": ("sbuf", [128, 6, 128], F32), "sel": ("sbuf", [128, 4, 16], BF),
           "t1": ("sbuf", [128, 8, 16], BF), "arh": ("sbuf", [128, 8, 16], BF),
           "hhn": ("sbuf", [128, 8, 16], F32), "m8": ("sbuf", [128, 8, 8, 2], BF), "b16": ("sbuf", [128, 16], F32),
           "t1p": ("sbuf", [128, 33, 8], BF), "arhp": ("sbuf", [128, 33, 8], BF)}
for _d in WIDTHS:
    for _n in WIDTHS[_d]:
        SCRATCH[_n] = ("sbuf", [128, WIDTHS[_d][_n]], _d)
for _n in PSUM:
    SCRATCH[_n] = ("psum", {"pa": [128, 8, 64], "pb": [128, 32, 16]}.get(_n, [128, PSUM[_n]]), F32)
SHARE = {"ghost": 2, "bst": 24, "hh": 1024, "hhh": 960, "q": (576, 896), "l": (512, 896), "r3": (1024, 960), "x": 1344, "hx": 384, "sp": 10, "cm": (0, 1280)}
STEPS = (192, 448, 512, 512, 384)
BOTH = {1: "pd", 0: "pc"}
CUTS = (2048, 1792, 1408, 1024, 640, 384, 0)
CM = 2
NUM = 0
EARLY = 1
BASE = 6
NUMQ = "SSSS"
INV = 768
GL = 1
RANK = 0
RU = 0
RUQ = "V"
INVAT = 1
LESSAT = 0
RUAT = 384
AHEAD = 1
SUM = 512
LEAD = 0
SST = "SSSS"
LOAT = 7
BEHIND = None
TAIL = 1
LAST = 256
FUSE = 960
GHOST = None
ORDER = ((1, 0), (1, 1), (0, 0), (1, 2), (0, 1), (1, 3), (0, 2), (1, 4), (0, 3), (0, 4))
EXCH = ["name", "hl", "hh", "hhh", "w2", "x", "xs", "num", "s"]
LOADS = ["bl", "gl", "nb", "w", "m1", "m2", "x", "xc", "wr", "sp", "cm"] + ["y%d" % _j for _j in range(len(CUTS) - 1)]
SEMAPHORES = ["cV", "cS", "cP", "cG"] + ["d_" + k for k in LOADS] + ["a_" + k for k in EXCH] + ["l_" + k for k in EXCH]


def engine_plan(topo, src, cores):
    away = [d for d in cores if d != src and topo.chip(d) != topo.chip(src)]
    near = [d for d in cores if d != src and topo.chip(d) == topo.chip(src)]
    used, out = [], {}
    for group in (away, near):
        for i, d in enumerate(group):
            free = [e for e in topo.engines(src, d) if e not in used]
            n = 1
            while n * 2 <= len(free) // (len(group) - i) and n < 4:
                n *= 2
            out[d] = free[:n] if group is away else free[::len(free) // n]
            used = used + out[d]
    return out


def rank_program(g, core, T, topo):
    r = T.rank_of(core)
    if r is None:
        return
    cores = [int(c) for c in T.cores]
    others = [d for d in range(len(cores)) if d != r]
    queue = {"V": g.vector, "S": g.scalar, "P": g.tensor, "G": g, "Y": g.sync}
    total, known, hist = {}, {q: {} for q in queue}, {}

    def deps(q, tag, regs, kind, need):
        for name, p0, p1, c0, c1 in regs:
            ps = name in PSUM
            for o, k, a0, a1, b0, b1 in hist.get(name, ()):
                cross = ps and o["q"] != q
                if kind == "r" and k == "r" and not cross:
                    continue
                if tag is not None and o["tag"] == tag and o["q"] == q:
                    continue
                if cross:
                    hit = c0 // 512 <= (b1 - 1) // 512 and b0 // 512 <= (c1 - 1) // 512
                else:
                    hit = c0 < b1 and b0 < c1 and p0 < a1 and a0 < p1
                if hit and (o["sem"] not in need or need[o["sem"]]["val"] < o["val"]):
                    need[o["sem"]] = o

    def note(o, outs, ins):
        for kind, regs in (("w", outs), ("r", ins)):
            for name, p0, p1, c0, c1 in regs:
                hist.setdefault(name, []).append((o, kind, p0, p1, c0, c1))

    def add(q, fn, outs, ins, sem=None, inc=1, tag=None, chain=True):
        need, kq = {}, known[q]
        deps(q, tag, ins, "r", need)
        deps(q, tag, outs, "w", need)
        for s, o in need.items():
            if kq.get(s, 0) >= o["val"] or any(p is not o and p["know"].get(s, 0) >= o["val"] for p in need.values()):
                continue
            queue[q].wait_ge(T.sem[s], o["val"])
            for k, v in o["know"].items():
                kq[k] = max(kq.get(k, 0), v)
        sem = sem or "c" + q
        total[sem] = total.get(sem, 0) + inc
        o = {"q": q if sem == "c" + q else q + sem, "tag": tag, "sem": sem, "val": total[sem], "know": dict(kq)}
        o["know"][sem] = total[sem]
        made = fn(queue[q])
        if chain:
            made.then_inc(T.sem[sem], inc)
        note(o, outs, ins)

    def X(name, c0, c1, step=1, p0=0, p1=128):
        if name == "pa":
            ap = T.pa[p0:p1, c0 // 64:(c1 + 63) // 64, c0 % 64:64:step]
        elif name == "pb":
            ap = T.pb[p0:p1, c0 // 16:c1 // 16, :] if step == 1 else T.pb[p0:p1, c0 // 16:c1 // 16, c0 % 16]
        else:
            ap = T[name][p0:p1, c0:c1] if step == 1 else T[name][p0:p1, c0:c1:step]
        return ap, [(name, p0, p1, c0, c1)]

    def TG(i0, i1=None, step=1):
        ap = T.tg[:, i0, :] if i1 is None else T.tg[:, i0:i1:step, :]
        return ap, [("tg", 0, 128, 128 * i, 128 * i + 128) for i in range(i0, i1 or i0 + 1, step)]

    def IX(win, b, offs, c, d, a=0):
        return T[win][:, a:b].indirect(T[offs][:, c:d]), [(win, 0, 128, a, b), (offs, 0, 128, c, d)]

    def col(j, n=1):
        return X("col", j, j + n)

    def sc(s):
        return s[0] if isinstance(s, tuple) else s

    def rg(*xs):
        return [y for x in xs if isinstance(x, tuple) for y in x[1]]

    def tt(out, a, b, op, tag=None):
        add("V", lambda e: e.tensor_tensor(out=out[0], in0=a[0], in1=b[0], op=op), rg(out), rg(a, b), tag=tag)

    def ts(out, a, s1, op0, s2=None, op1=None, tag=None):
        if op1 is None:
            f = lambda e: e.tensor_scalar(out=out[0], in0=a[0], scalar1=sc(s1), scalar2=None, op0=op0)
        else:
            f = lambda e: e.tensor_scalar(out=out[0], in0=a[0], scalar1=sc(s1), scalar2=sc(s2), op0=op0, op1=op1)
        add("V", f, rg(out), rg(a, s1, s2), tag=tag)

    def cp(out, a, tag=None):
        add("V", lambda e: e.tensor_copy(out=out[0], in_=a[0]), rg(out), rg(a), tag=tag)

    def fill(out, value):
        add("V", lambda e: e.memset(out[0], value), rg(out), [])

    def scan(out, a, b, first, op0, op1):
        add("V", lambda e: e.tensor_tensor_scan(out[0], a[0], b[0], first, op0, op1), rg(out), rg(a, b))

    def act(out, a, bias=0.0, scale=1.0, tag=None, func=AF.Identity):
        if isinstance(bias, float) and isinstance(scale, float) and bias == 0.0 and scale == 1.0:
            f = lambda e: e.activation(out=out[0], in_=a[0], func=func)
        else:
            f = lambda e: e.activation(out=out[0], in_=a[0], func=func, bias=sc(bias), scale=sc(scale))
        add("S", f, rg(out), rg(a, bias, scale), tag=tag)

    def mm(out, lhsT, rhs, start=True, stop=True, tag=None):
        add("P", lambda e: e.matmul(out=out[0], lhsT=lhsT[0], rhs=rhs[0], start=start, stop=stop), rg(out), rg(lhsT, rhs), tag=tag)

    def iota(out, pattern, base, cm, whole=False):
        if whole:
            f = lambda e: e.iota(out[0], pattern, base, cm)
        else:
            f = lambda e: e.iota(out[0], pattern, base, cm, allow_small_or_imprecise_dtypes=True)
        add("G", f, rg(out), [])

    def where(out, a, pattern, base, cm, op=OP.is_ge, fill=0.0):
        add("G", lambda e: e.affine_select(out[0], a[0], pattern, op, fill, base, cm), rg(out), rg(a))

    def dma(q, key, out_ap, outs, in_ap, ins, behind=None):
        if behind and known[q].get("l_" + behind, 0) < total["l_" + behind]:
            queue[q].wait_ge(T.sem["l_" + behind], total["l_" + behind])
            known[q]["l_" + behind] = total["l_" + behind]
        add(q, lambda e: e.dma_start(out=out_ap, in_=in_ap), outs, ins, sem="d_" + key, inc=16)

    plans = {c: engine_plan(topo, c, cores) for c in cores}

    def send(key, src, dst):
        parts, regs, n = [], [], 0
        for d in others:
            eng = plans[core][cores[d]]
            n += len(eng)
            a = topo.addr(cores[d])
            s = src(d)
            regs += s[1]
            parts.append(RemoteDMATransfer(dst_ids=[DstId(rid=a[0], pnc=a[1])], dma_engine_mask=sum(1 << e for e in eng),
                                           remote_sem=T.sem["a_" + key], srcs=[s[0]], dsts=[dst[0]]))
        add("G", lambda e: e.remote_dma_fused(parts, local_sem=T.sem["l_" + key]), [], regs, sem="l_" + key, inc=n, chain=False)

    def recv(key, regs):
        n = sum(len(plans[cores[q]][core]) for q in others)
        total["a_" + key] = n
        note({"q": "R", "tag": None, "sem": "a_" + key, "val": n, "know": {"a_" + key: n}}, regs, [])

    mine = V + C * r

    def show(key, stage, win):
        send(key, lambda d: X(stage, C * d, C * d + C), X(win, mine, mine + C))
        recv(key, [(win, 0, 128, V + C * q, V + C * q + C) for q in others])

    def border(key, stage, win, make, engines="VVSS"):
        runs = []
        for q in others:
            if runs and runs[-1][2] == q and engines[q] == runs[-1][0]:
                runs[-1][2] = q + 1
            else:
                runs.append([engines[q], q, q + 1])
        for e, q0, q1 in runs:
            make(e, X(stage, C * q0, C * q1), q0, q1)
        if key:
            show(key, stage, win)
        make(engines[r], X(win, mine, mine + C), r, r + 1)

    def spread(key, win):
        own = X(win, 256 * r, 256 * r + 256)
        send(key, lambda d: own, own)
        recv(key, [(win, 0, 128, 256 * q, 256 * q + 256) for q in others])

    def pick(bank, c0, src, s0, sel, n, tag, alone=True):
        for b in range(16):
            mm(X(bank, c0 + b, c0 + 128 * n, 16), X(src, s0 + b, s0 + V, 16), sel, alone, alone or b == 15, tag=tag)

    def move(q, out, a):
        (cp if q == "V" else act)(out, a)

    def gather(q, dst, a, win, w, offs, o, c0, c1):
        move(q, X(dst, a + c0, a + c1), IX(win, w, offs, o + c0 // 16, o + c1 // 16))

    def share(dst, a, win, w, offs, o, n):
        gather("V", dst, a, win, w, offs, o, 0, n)
        gather("S", dst, a, win, w, offs, o, n, V)

    def lister(win, w, offs, o=0):
        return lambda e, out, q0, q1: move(e, out, IX(win, w, offs, o + 6 * q0, o + 6 * q1))

    def merge(key, src, p0, p1, n, step=16):
        for i in range(2):
            dma("Y", key, T.hl[p1 + i:128:step, 0:n], [("hl", p, p + 1, 0, n) for p in range(p1 + i, 128, step)],
                T[src][p0 + i:128:step, 0:n], rg(X(src, 0, n)))

    IB, TI, IF = X("ti", 0, 128), X("ti", 0, 256), X("iff", 0, 128)
    ONE, ZERO, G8, DIAG = X("one", 0, 128), X("zero", 0, 128), X("g8b", 0, 8), [[-1, 128]]
    P2, P4, N4, PB = (X("dg", 128 * j, 128 * j + 128) for j in range(4))
    M8 = 0
    M81, M85, A04, A15, ST, N13 = (col(j) for j in range(8, 14))
    FIRST, SA, BA, SIDEA, SIDEB, W8, QW, U0, U1 = (col(j) for j in range(18, 27))

    def MC(x, n=1):
        return col(32 + x, n)

    def STM(i):
        j = i if 0 < i < 8 else 20 + i // 8
        return X("stm", j, j + 1)

    def sum_of(out, a):
        add("V", lambda e: e.tensor_reduce(out[0], a[0], AxisListType.X, OP.add), rg(out), rg(a))

    def diagonal(out, value):
        where(out, ZERO, DIAG, 0, 1, OP.not_equal, value)

    dma("Y", "bl", T.bli[:, :], rg(X("bli", 0, 24)), T.bl[:, :], [])
    dma("S", "nb", T.nbi[:, :], rg(X("nbi", 0, 256)), T.nb[:, :], [])
    dma("S", "gl", T.gli[:, 6 * r:6 * r + 6], rg(X("gli", 6 * r, 6 * r + 6)), T.bl[:, 6 * r:6 * r + 6], [])
    for d in range(2):
        dma("Y", "w", T.wsb[8 * d:8 * d + 8, :], rg(X("wsb", 0, V, 1, 8 * d, 8 * d + 8)), T.w[:, V * d:V * d + V], [])

    PM = X("pm", 0, 8, 1, 0, 16)
    E1, E2, D0, D1 = (X("pw", 64 * j, 64 * j + 64) for j in range(4))
    iota(X("ci", 0, 16), [[-1, 16]], 16, 1, True)
    iota(X("ci", 16, 24), [[1, 8]], 9, 1, True)
    for o, value in ((X("zero", 0, 144), 0.0), (X("ir", 40, 60), 0.0), (E1, 0.0), (E2, -0.875), (X("ir", 40, 41), 8192.0),
                     (X("ir", 41, 42), 128.0)):
        fill(o, value)
    for o, value in ((X("ir", 58, 59), 2048.0 * r), (X("ir", 59, 60), -1.0), (X("pw", 0, 64, 8), 1.0), (X("pw", 64, 128, 8), -1.0),
                     (ONE, 1.0), (X("g8h", 0, 144), 0.0)):
        act(o, X("zero", 0, o[0].shape[1]), value)
    iota(X("ir", 0, 8), [[64, 8]], 0, 0)
    iota(X("ir", 8, 33), [[512, 25]], -6144, 0)
    where(PM, X("zero", 0, 8, 1, 0, 16), [[-1, 8]], -8, 1, OP.not_equal, 1.0)
    diagonal(IB, 1.0)
    where(PM, PM, [[-1, 8]], 0, 1, OP.not_equal, -1.0)
    send("name", lambda d: X("bli", 6 * d, 6 * d + 6), X("gli", 6 * r, 6 * r + 6))
    recv("name", [("gli", 0, 128, 6 * q, 6 * q + 6) for q in others])
    ts(X("cj", 0, 16), X("ci", 0, 16), 15, OP.bitwise_and)
    ts(X("cj", 24, 26), X("ci", 1, 6, 4), 7, OP.bitwise_and)
    ts(X("cj", 16, 24), X("ci", 16, 24), 7, OP.bitwise_and)
    ts(X("cj", 26, 28), X("ci", 0, 2), 3, OP.bitwise_and)
    ts(MC(0, 28), X("cj", 0, 28), 0.0, OP.is_equal)
    tt(col(64, 20), MC(8, 20), X("ir", 40, 60), OP.mult)
    ts(D1, E1, MC(25), OP.mult, MC(24), OP.add)
    ts(D0, E2, MC(13), OP.mult, 1.0, OP.add)
    ts(X("stm", 0, 33), X("ir", 0, 33), MC(26), OP.mult)
    sum_of(FIRST, col(64, 20))
    act(A04, MC(0), MC(4))
    act(A15, MC(1), MC(5))
    act(U0, A04, A15)
    act(U1, MC(1), 0.0, 128.0)
    act(BA, MC(0), 0.0, 8192.0)
    act(SA, MC(13), U0, 2.0 ** 21)
    act(U1, MC(5), U1, 7.0)
    act(BA, MC(4), BA, 8128.0)
    act(BA, BA, U1)
    add("V", lambda e: e.tensor_tensor_scan(T.nw[:, 0:64], D0[0], D1[0], FIRST[0], OP.mult, OP.add), rg(X("nw", 0, 64)), rg(D0, D1, FIRST))
    ts(X("bki", 24, 48), X("bli", 0, 24), 15, OP.bitwise_and)
    ts(X("bki", 0, 24), X("bli", 0, 24), 4, OP.logical_shift_right)
    ts(X("nw", 64, 128), X("nw", 0, 64), STM(1), OP.add)
    cp(X("bk16", 0, 48), X("bki", 0, 48))
    ts(X("nw", 128, 192), X("nw", 0, 64), STM(2), OP.add)
    ts(X("nw", 192, 256), X("nw", 0, 64), STM(3), OP.add)
    tt(X("dn", 0, 128), X("nbi", 128, 256), X("nbi", 0, 128), OP.subtract)
    ts(X("nw", 256, 512), X("nw", 0, 256), STM(4), OP.add)
    G8H, SEL, PAIRS = X("g8h", 16, 144, 16), (T.sel[:, 0:3, :], [("sel", 0, 128, 0, 48)]), [[-2, 3], [-8, 2], [-16, 8]]

    def SF(a, b, step=1):
        if step == 0:
            return T.sel[:, a, 8 * b:8 * b + 8], [("sel", 0, 128, 16 * a + 8 * b, 16 * a + 8 * b + 8)]
        return T.sel[:, a:b:step, :], [("sel", 0, 128, 16 * a, 16 * b)]

    where(G8H, X("one", 0, 8), [[-16, 8]], 0, 1)
    where(SEL, X("zero", 0, 48), PAIRS, 0, 1, OP.not_equal, 1.0)
    where(G8H, G8H, [[16, 8]], 15, -1)
    where(SEL, SEL, PAIRS, -1, 1, OP.not_equal, 1.0)
    where(SF(3, 4), X("zero", 0, 16), [[0, 2], [-16, 8]], 0, 1, OP.not_equal, 1.0)
    iota(TG(1, 3), [[0, 16], [1, 16]], V * r + OFFN, 16)
    for (a, j), p, value in (((2, 0), 4, 0.125), ((2, 1), 12, 0.0)):
        where(SF(a, j, 0), SF(a, j, 0), [[-16, 8]], -p, 1, OP.not_equal, value)
    where(SF(3, 4), SF(3, 4), [[0, 2], [-16, 8]], -1, 1, OP.not_equal, 1.0)
    diagonal(IF, 1.0)
    NB = X("dg", 512, 640)
    diagonal(NB, -BIG)

    for b in range(16):
        mm(X("pa", b, 128, 16), X("wsb", b, V, 16, 0, 16), PM, tag="wt")
    act(X("mb", 0, 384), IX("col", 48, "bk16", 24, 48, 32))
    ts(X("bt", 0, 128), X("pa", 0, 128), 0.0, OP.is_gt)
    mm(X("pb", 0, 128), X("bt", 0, 128), IB)
    ts(X("nbm", 0, 256), X("nbi", 0, 256), MID, OP.subtract)
    tt(X("pb", 0, 128), X("pb", 0, 128), X("dn", 0, 128), OP.mult)
    cp(X("bl16", 0, 24), X("bli", 0, 24))
    tt(X("hlm", 0, 128), X("nbm", 0, 128), X("pb", 0, 128), OP.add)
    tt(X("hlm", 128, 256), X("nbm", 128, 256), X("pb", 0, 128), OP.subtract)
    for j in (1, 2, 3):
        act(X("nw", 512 * j, 512 * j + 512), X("nw", 0, 512), STM(8 * j))
    for K, bank in enumerate(("pc", "pd")):
        tt(X("hrow", 384 * K, 384 * K + 384), IX("hlm", 128 * K + 128, "bk16", 0, 24, 128 * K), X("mb", 0, 384), OP.mult)
        for b in range(16):
            mm(X(bank, 0, 24), X("g8h", 16 - b, 144 - b), X("hrow", 384 * K + b, 384 * K + 384, 16), b == 0, b == 15, tag="border")
        if K == 0:
            ts(X("hl16", 0, 256), X("hlm", 0, 256), MID, OP.add)
        if K == GL:
            cp(X("gl16", 0, 24), X("gli", 0, 24))
    for q in range(4):
        o, i = X("nw", V + C * q, V + C * q + C), IX("nw", V, "gl16", 6 * q, 6 * q + 6)
        if q < SHARE["ghost"]:
            ts(o, i, STM(32 * (q - r)), OP.add)
        else:
            act(o, i, STM(32 * (q - r)))
    ts(X("hb16", 0, 24), X("pc", 0, 24), MID, OP.add)

    def heavy(a, b):
        act(X("hb", a, b), IX("nw", Z, "hl16", a // 16, b // 16), BA, SA)

    def light(a, b):
        tt(X("hl", a, b), IX("nw", Z, "hl16", 128 + a // 16, 128 + b // 16), X("hb", a, b), OP.max)

    a, nb_ = STEPS[0], SHARE["bst"]
    if nb_ < 24:
        act(X("bst", 16 * nb_, 384), IX("nw", Z, "hb16", nb_, 24), BA, SA)
    if LEAD:
        heavy(a, a + LEAD)
    act(X("hl", 0, a), IX("nw", Z, "hl16", 0, a // 16), BA, SA)
    act(X("hb", 0, a), IX("nw", Z, "hl16", 128, 128 + a // 16))
    merge("m1", "hb", 8, 8, a)
    ts(X("bst", 0, 16 * nb_), IX("nw", Z, "hb16", 0, nb_), SA, OP.mult, BA, OP.add)
    ts(X("hb16", 24, 48), X("pd", 0, 24), MID, OP.add)
    if LEAD:
        light(a, a + LEAD)
        a += LEAD
    border("hl", "hst", "hl", lambda e, out, q0, q1: tt(out, IX("nw", Z, "hb16", 24 + 6 * q0, 24 + 6 * q1), X("bst", C * q0, C * q1), OP.max), "VVVV")
    for n in STEPS[1:]:
        heavy(a, a + n)
        light(a, a + n)
        a += n
    for m, value in ((P4, 4.0), (PB, BIG), (N4, -4.0)):
        diagonal(m, value)
    HZ, ROW = (X("psw", 1024, 1152), X("psw", 1152, 1280)), X("one", 0, 128, 1, 0, 1)
    for K in range(2):
        mm(HZ[K], X("hlm", K * 128, K * 128 + 128), IF)

    pick("pa", 0, "hl", 0, SF(0, 4, 2), 4, "own")
    border("hh", "cst", "hh", lister("hl", Z, "hb16"))
    share("hh", 0, "hl", Z, "hl16", 0, SHARE["hh"])
    tt(X("dn", 0, 128), X("hlm", 128, 256), X("hlm", 0, 128), OP.subtract)
    DZ, QL = X("psw", 1280, 1408), X("psw", 384, 512)
    mm(DZ, X("dn", 0, 128), IF)
    mm(QL, IF, X("hlm", 0, 128), True, False, tag="q")
    pick("pc", 0, "hh", 0, SF(0, 4, 2), 4, "hh")
    LESS = 768
    HN, OWN, LN, HL, HH = TG(0), TG(1), TG(3), TG(4), (T.hhn[:, :, :], [("hhn", 0, 128, 0, 128)])
    act(TG(0, 4, 3), X("pa", 0, 256))
    where(G8, X("one", 0, 8), [[-16, 8]], 0, 1)
    for name in ("t1p", "arhp"):
        iota((T[name][:, 0:33:2, :], [(name, 0, 128, 0, 264)]), [[0, 136]], 0, 0)
    where(G8, G8, [[16, 8]], 15, -1)
    iota(X("e2", 512, 528), [[0, 16]], 0, 0)
    where(X("ti", 128, 256), ZERO, DIAG, 0, 1, OP.is_ge, 1.0)
    NHL, B, EH2 = X("e0", 144, 272), X("e1", 0, 128), X("e1", 128, 256)
    T1, ARH = ((T[name][:, :, :], [(name, 0, 128, 0, 128)]) for name in ("t1", "arh"))

    def pad(name):
        for c in range(2):
            o = T[name + "p"][:, 16 * c + 1:16 * c + 16:2, :], [(name + "p", 0, 128, 128 * c, 128 * c + 128)]
            i = T[name][:, :, 8 * c:8 * c + 8], [(name, 0, 128, 0, 128)]
            if name == "t1":
                where(o, i, [[0, 64]], 0, 0)
            else:
                act(o, i)

    border("hhh", "dst", "hhh", lister("hh", Z, "hb16"))
    merge("m2", "hh", 0, 2, Z, 8)
    share("hhh", 0, "hh", Z, "hl16", 0, SHARE["hhh"])
    pick("pb", 0, "hhh", 0, SF(0, 1), 2, "hhh")
    act(X("fld", 0, 256), X("pc", 256, 512))
    act(HH, X("pc", 0, 128))
    tt(X("psw", LESS, LESS + 256), X("pa", 0, 256), TG(1, 3), OP.is_lt)
    ts(SIDEA, X("cj", 0, 1), 8.0, OP.is_lt)

    dma("Y", "x", T.xw[:, 0:V], rg(X("xw", 0, V)), T.x[:, :], [], "hhh")
    diagonal(P2, 2.0)
    diagonal(X("ibn", 0, 128), -MID)
    diagonal(X("nti", 0, 128), -1.0)
    where(X("nti", 128, 256), ZERO, DIAG, 0, 1, OP.is_ge, -1.0)
    iota(X("km", 0, 256), [[-1, 128], [0, 2]], 127, 0)
    SELR, SELQ = X("selr", 0, 128, 1, 0, 16), X("selq", 0, 128, 1, 0, 16)
    where(SELR, X("one", 0, 128, 1, 0, 16), [[-16, 8], [0, 16]], -128, 16, OP.is_equal)
    where(SELQ, X("one", 0, 128, 1, 0, 16), [[-16, 8], [0, 16]], 0, 16, OP.is_equal)

    WORDS = 1792

    def pack(flags, weight, last=False):
        name, c0 = flags[1][0][0], flags[1][0][3]
        for c in range(2):
            if name in ("t1", "arh"):
                for j in (16 * c, 16 * c + 1):
                    mm(X("psw", WORDS + c, WORDS + 256, 2), (T[name + "p"][:, j:j + 16, :], [(name + "p", 0, 128, 0, 264)]), weight, False, False, tag="pack")
            else:
                mm(X("psw", WORDS + c, WORDS + 256, 2), X(name, c0 + 8 * c, c0 + 8 * c + 128), weight, False, last and c == 1, tag="pack")

    def total_of(out, terms, first=False, last=False, tag=None):
        for i, (m, e) in enumerate(terms):
            mm(out, m, e, first and i == 0, last and i == len(terms) - 1, tag=tag)

    ARL = X("ar", 0, 128)
    THA, THL, S2, M2 = X("psw", 256, 384), X("psw", 1536, 1664), X("pc", 0, 128), X("m2", 0, 128)
    EH, EL = X("pb", 256, 384), X("pb", 384, 512)
    ELH, ELL, TL1, QB = (X("e2", 128 * j, 128 * j + 128) for j in range(4))
    n0, n2 = SHARE["l"]
    gather("S", "gb", V, "hl", Z, "hl16", 128, n2, V)
    gather("V", "gb", V, "hl", Z, "hl16", 128, 0, n0)
    mm(X("psw", WORDS, WORDS + 256), ZERO, TI, True, False, tag="pack")
    tt(B, X("pb", 0, 128), HN, OP.is_equal)
    tt(EH2, X("pb", 128, 256), HN, OP.is_equal)
    tt(T1, X("pc", 0, 128), OWN, OP.is_equal)
    pack(B, P4)
    tt(X("dn", 0, 128), DZ, B, OP.mult)
    mm(QL, X("dn", 0, 128), IF, False, True, tag="q")
    tt(NHL, X("pc", 128, 256), OWN, OP.not_equal)
    pad("t1")
    iota(X("inv", INV, 1664), [[0, 1664 - INV]], 0, 0)
    gather("V", "gb", V, "hl", Z, "hl16", 128, n0, n2)
    ts(X("mate", 0, 128), QL, MID, OP.add)
    act(U0, SIDEA, 100.0, -94.0)
    mm(X("pb", 256, 512), ZERO, TI, True, False, tag="q2")
    total_of(EH, ((PB, NHL), (PB, B)), False, False, "q2")
    pick("pd", 0, "gb", V, SF(0, 2), 4, "l")
    n0, n1 = SHARE["q"]
    gather("S", "gb", 0, "hhh", Z, "mate", 0, n1, V)
    gather("V", "gb", 0, "hhh", Z, "mate", 0, 0, n0)
    tt(X("e2", 0, 384), X("pd", 0, 384), TG(1, 4), OP.is_equal)
    gather("V", "gb", 0, "hhh", Z, "mate", 0, n0, n1)
    act(HL, X("pd", 0, 128), -2.0 * BIG)
    pack(T1, PB)
    total_of(EL, ((NB, B), (NB, ELL), (PB, TL1)), False, False, "q2")
    pick("pb", 256, "gb", 0, SF(3, 4), 2, "q2", False)
    pack(ELH, P2)
    tt(X("pa", 256, 512), X("pa", 256, 512), X("fld", 0, 256), OP.subtract)
    EL2 = X("e0", 272, 400)
    tt(EL2, X("pd", 384, 512), LN, OP.is_equal)
    for K in range(2):
        tt(X("pa", 256 + 128 * K, 384 + 128 * K), X("pa", 256 + 128 * K, 384 + 128 * K), NHL, OP.mult)
    act(X("pw", 0, 8), X("zero", 0, 8), 0.125)
    act(SIDEB, SIDEA, 1.0, -1.0)
    act(col(73), SIDEA, 0.0, -1.0 / BIG)
    act(col(72), SIDEA, -1.0 / BIG, 1.0 / BIG)
    act(X("km", 0, 256), X("km", 0, 256), col(73), col(72))
    border(None, "xst", "xw", lister("xw", V, "bl16"), "SSSS")
    for c in range(2):
        tt((T.arhp[:, 16 * c + 1:16 * c + 16:2, :], [("arhp", 0, 128, 128 * c, 128 * c + 128)]),
           (T.pb[:, 16:24, 8 * c:8 * c + 8], EH[1]), (T.hhn[:, :, 8 * c:8 * c + 8], HH[1]), OP.is_equal)
    tt(QB, EL, HL, OP.is_equal)
    pack(ARH, PB)
    pack(QB, P2, True)
    tt(ARH, EH, HH, OP.is_equal)
    tt(X("c16", 0, 128), X("pa", 256, 384), X("fld", 0, 128), OP.add)
    tt(X("fld", 384, 512), X("pa", 384, 512), X("fld", 128, 256), OP.add)
    ts(X("wv", 256 * r, 256 * r + 256), X("psw", WORDS, WORDS + 256), U0, OP.is_ge)
    spread("w2", "wv")
    total_of(X("psw", 128, 256), ((IB, T1), (IB, ARH)), True, True, "m2")
    act(M2, X("psw", 128, 256))
    mm(X("pb", 0, 128), X("c16", 0, 128), IB)
    total_of(S2, ((N4, T1), (P4, B), (P2, ELH), (P2, QB)), True, True, "s2")
    pick("pa", 0, "gb", V, SF(2, 3), 2, "l2")
    scan(X("pw", 8, 16), X("pw", 0, 8), X("zero", 0, 8), 16.0, OP.mult, OP.add)
    ts(X("idx", 0, 128), X("pb", 0, 128), float(OFFC), OP.subtract)
    ts(ARL, S2, 6.0, OP.is_ge)
    tt(col(64, 8), col(48, 8), X("pw", 8, 16), OP.mult)
    cp(X("nb16", 0, 256), X("nbi", 0, 256))
    total_of(THA, ((P2, EH2), (P4, B), (P4, NHL), (P4, ARH)), True, True, "tha")

    show("x", "xst", "xw")
    dma("Y", "xc", T.xc[:, 0:SHARE["x"]], rg(X("xc", 0, SHARE["x"])), T.x[:, 0:SHARE["x"]], [], "x")
    a = FUSE
    for c in range(16):
        dma("Y", "wr", T.wr[c:128:16, a:V], [("wr", 16 * k + c, 16 * k + c + 1, 0, V) for k in range(8)], T.w[:, a:V], [])
    sum_of(W8, col(64, 8))
    act(X("selw", 0, 8), G8, 0.0, W8)
    ts(X("c16", 128, 256), X("pa", 0, 128), float(OFFC), OP.subtract)
    mm(X("pd", 0, 128), X("c16", 128, 256), IB)
    act(X("fld", 640, 768), X("pa", 128, 256))
    for K, m in enumerate((M2, ARL)):
        tt(X("pz2", 128 * K, 128 * K + 128), m, HZ[K], OP.mult)
    cp(X("idx", 128, 256), X("pd", 0, 128))
    for K, m in enumerate((M2, ARL)):
        tt(X("nr2", 128 * K, 128 * K + 128), m, X("psw", LESS + 128 * K, LESS + 128 * K + 128), OP.mult)
    ts(QW, X("cj", 0, 1), -1.0, OP.mult, 16.0, OP.add)
    total_of(THL, ((ONE, P4), (N4, ELL), (P2, EL2), (P4, TL1), (N4, ELH), (N4, ELH), (PB, M2), (PB, ARL)), True, False, "thl")

    def mates(flags, numbers, first=False, last=False):
        mm(X("psw", 0, 128), flags, X("ibn", 0, 128), first, False, tag="mate")
        mm(X("psw", 0, 128), numbers, IB, False, last, tag="mate")

    mates(ARL, X("pz2", 128, 256), True)
    mates(M2, X("pz2", 0, 128))
    mm(X("psw", 512, 768), ONE, TI, True, False, tag="rep")
    for K in range(2):
        mm(X("psw", 512, 768), X("nr2", 128 * K, 128 * K + 128), X("nti", 0, 256), False, False, tag="rep")
    LT, LTE, LT8, Q8, B16, SELI = X("lt", 0, 128), X("lte", 0, 128), X("lt0", 0, 128), X("q0", 0, 128), X("b16", 0, 16), X("seli", 0, 64)
    BLK = X("blk", 0, 128)
    where(BLK, ONE, [[-16, 8], [0, 16]], 0, 1)
    iota(X("wq", 0, 288), [[0, 288]], 0, 0)
    where(BLK, BLK, [[16, 8], [0, 16]], 15, -1)
    iota(X("xw", Z, Z + 16), [[0, 16]], 0, 0)
    where(LTE, ONE, [[-8, 16], [0, 8]], 0, 1)
    where(LT, BLK, [[1, 128]], 0, -1, OP.is_gt)
    where(LTE, LTE, [[1, 128]], 0, -1)
    where(LT, LT, [[1, 128]], 0, -1, OP.not_equal, BIG)
    where(LTE, LTE, [[1, 128]], 0, -1, OP.not_equal, -16.0)
    iota(B16, [[0, 16]], 1, 0)
    where(Q8, ONE, [[-16, 8], [0, 8], [-8, 2]], 0, 1)
    where(B16, B16, [[-8, 16]], 0, 1)
    where(SELI, X("zero", 0, 64), [[-16, 8], [-1, 8]], 0, 1, OP.not_equal, 1.0)
    where(B16, B16, [[8, 16]], 7, -1)
    where(Q8, Q8, [[16, 8], [0, 8], [8, 2]], 7, -1)
    where(SELI, SELI, [[-16, 8], [-1, 8]], -8, 1, OP.not_equal, 16.0)
    where(LT8, BLK, [[16, 8], [0, 8], [8, 2]], 0, -1, OP.is_gt)
    iota(X("vl", 0, 16), [[16, 16]], V - int(BIG), 1)
    iota(X(SPW, Z, Z + 16), [[0, 16]], 0, 0)
    iota(X("inv", 1664, 2448), [[0, 784]], 0, 0)
    for a, b in () if SPD else ((0, 8), (136, 152), (280, 288)):
        iota(X("half", a, b), [[0, b - a]], 0, 0)
    for c in range(0 if SPD else 2):
        where(X("half", 144 * c + 8, 144 * c + 136), IB, [[0, 8], [1, 2], [0, 8]], -c, 0, OP.is_equal)

    def ask(L, n):
        share("gb", L * V, "wv", 1024, "idx", L * 128, n)

    def answer(L, bank):
        pick(bank, 0, "gb", L * V, X("selw", 0, 8), 1, "word")

    def shift(K, bank):
        tt(X("yj", 128 * K, 128 * K + 128), X(bank, 0, 128), X("fld", 384 + 256 * K, 512 + 256 * K), OP.mult)

    def digit(K):
        ts(X("zj", 128 * K, 128 * K + 128), X("yj", 128 * K, 128 * K + 128), 6, OP.bitwise_and)

    n0, n1 = SHARE["r3"]
    ask(0, n0)
    answer(0, "pc")
    nx = SHARE["x"]
    hx = nx + SHARE["hx"]
    halves = (("pa", nx, hx), ("pb", hx, V))
    for bank, a, b in halves:
        mm(X(bank, 0, b - a), IB, X("xw", a, b), True, False, tag="gx")
    ask(1, n1)
    shift(0, "pc")
    digit(0)
    answer(1, "pd")
    A3, L3, Z0 = X("ar3", 0, 128), X("ar3", 128, 256), X("ar3", 256, 384)
    tt(A3, X("zj", 0, 128), THA, OP.is_gt)
    ts(Z0, X("zj", 0, 128), 0.0, OP.is_equal)
    total_of(THL, ((PB, A3), (PB, Z0)), False, True, "thl")
    tt(X("pz3", 0, 128), A3, HZ[0], OP.mult)
    mates(A3, X("pz3", 0, 128))
    shift(1, "pd")
    digit(1)
    tt(L3, X("zj", 128, 256), THL, OP.is_gt)
    tt(X("pz3", 128, 256), L3, HZ[1], OP.mult)
    mates(L3, X("pz3", 128, 256), False, True)
    tt(X("nr3", 0, 256), X("ar3", 0, 256), X("psw", LESS, LESS + 256), OP.mult)
    ts(X("mate", 0, 128), X("psw", 0, 128), float(Z), OP.add)
    for c, side in enumerate((SIDEA, SIDEB)):
        act(col(76 + c), side, 0.0, QW)
        act(X("wq", 144 * c + 16, 144 * c + 144, 16), G8, 0.0, side, tag="wq")
        act(X("wq", 144 * c + 8, 144 * c + 136, 16), G8, 0.0, col(76 + c), tag="wq")
    for i in range(8):
        act((T.m8[:, :, i, :], [("m8", 0, 128, 0, 128)]), X("one", 0, 16), 0.0, col(55 - i), tag="m8")
    if not INVAT:
        act(X("inv", 0, INV), X("hh", 0, INV), 0.0, 0.0)

    for K in range(2):
        mm(X("psw", 512, 768), X("nr3", 128 * K, 128 * K + 128), X("nti", 0, 256), False, K == 1, tag="rep")

    def weights(j):
        mm(X("psw", 512 * j, 512 * j + 512), SELR, X("wsb", 512 * j, 512 * j + 512, 1, 0, 16))

    weights(3)
    for bank, a, b in halves:
        act(X("gb", a - nx, b - nx), IX("xw", Z + 16, "mate", a // 16, b // 16))
        mm(X(bank, 0, b - a), IB, X("gb", a - nx, b - nx), False, True, tag="gx")
    REP, UP, HI, LO = X("ru", 0, 128), X("ru", 128, 256), X("hilo", 0, 128), X("hilo", 128, 256)

    def count():
        move(RUQ, X("ru", 0, 256), X("psw", 512, 768))
        mm(X("pc", 0, 128), LTE, REP)
        if SPD:
            mm(X("pd", 0, 128), UP, BLK, True, False, tag="num")
            mm(X("pd", 0, 128), REP, X("lt", 0, 128), False, True, tag="num")
        else:
            mm(X("pd", 0, 128), BLK, UP, True, False, tag="num")
            mm(X("pd", 0, 128), X("lt", 0, 128), REP, False, True, tag="num")

        mm(X("psw", 128, 256), UP, BLK, True, False, tag="base")
        mm(X("psw", 128, 256), REP, LT8, False, False, tag="base")

    def mask(i):
        ts(X("mk", 128 * i, 128 * i + 128), X("pc", 0, 128), float(i - 16), OP.is_equal, -BIG, OP.mult)

    if RUAT:
        tt(X("xf", 0, RUAT), IX("xw", Z + 16, "mate", 0, RUAT // 16), X("xc", 0, RUAT), OP.add)
        count()
    weights(2)
    tt(X("xf", RUAT, nx), IX("xw", Z + 16, "mate", RUAT // 16, nx // 16), X("xc", RUAT, nx), OP.add)
    for bank, a, b in halves:
        act(X("xf", a, b), X(bank, 0, b - a))
    if not RUAT:
        count()
    for i in range(AHEAD):
        mask(i)
    parts = (X("cn", 0, 128), HI)
    border("xs", "xb", "xf", lister("xf", V, "bl16"))
    if RANK:
        act(X("bt", 0, 128), X("pc", 0, 128))
    for o in parts[RU:]:
        act(o, X("pd", 0, 128), V * r - BIG, func=AF.Relu)
    for b, a in zip(CUTS, CUTS[1:]):
        iota(X("left", a // 16, b // 16), [[0, (b - a) // 16]], (V - a) // 128, 0)
    where(X("g2h", 0, 144), X("g8h", 0, 144), [[16, 9], [0, 16]], -15, -1)
    iota(X("sw", Z, Z + 16), [[0, 16]], 0, 0)
    iota(X("tw", V, V + 8), [[0, 8]], 0, 0)

    def rows():
        if SPD != 1:
            tt(LO, X("cn", 0, 128), HI, OP.subtract)
        for j in range(8 * SPD):
            p, src, c = 16 * (j % 8) + j // 8, "cn" if SPD == 1 else "hilo", 16 * j
            dma("Y", "sp", T[SPW][p:p + 1, 0:V], rg(X(SPW, 0, V, 1, p, p + 1)), T[src][:, c:c + 16], rg(X(src, c, c + 16)), BEHIND)

    if INVAT:
        act(X("inv", 0, INV), X("hh", 0, INV), 0.0, 0.0)
    mm(X("pa", 0, 256), ZERO, TI, True, False, tag="eight")
    for i in range(8):
        MK = X("mk", 128 * i, 128 * i + 128)
        if i >= AHEAD:
            mask(i)
        for c in range(2):
            mm(X("pa", c, 256, 2), X("wq", 144 * c + 8 - i, 144 * c + 136 - i), MK, False, c + i == 8, tag="eight")
        if i == 0:
            mm(X("psw", 128, 256), MK, Q8, False, True, tag="base")
        if i == BASE:
            tt(X("dn", 0, 128), X("psw", 128, 256), (T.m8[:, :, :, :], [("m8", 0, 128, 0, 128)]), OP.mult)
            mm(X("psw", 0, 16), X("dn", 0, 128), B16)
        if i == LOAT:
            rows()

    def SP(c):
        return X("sp", c, V, 16)[0], [("sp%d" % c, 0, 128, 0, 128)]

    def numbers(offs, c, d, b):
        ap, regs = IX(SPW, b, offs, c, d)
        return ap, regs + [y for k in range(16) for y in SP(k)[1]]

    if not SPD:
        act(X("two", 0, 256), X("pd", 128, 384))
    for c in range(0 if SPD else 16):
        part = X("two", 128 * (c // 8), 128 * (c // 8) + 128)
        if c < SHARE["sp"]:
            ts(SP(c), part, col(M8 + c % 8), OP.mult)
        else:
            act(SP(c), part, 0.0, col(M8 + c % 8))

    for j in (4, 3, 2, 1, 0):
        a, b = 512 * j, 512 * j + 512
        if j == 4:
            if NUM == 4:
                border("num", "sb", SPW, lambda e, out, q0, q1: move(e, out, numbers("bl16", 6 * q0, 6 * q1, V)), NUMQ)
            continue
        if j in BOTH:
            act(X("p0", a, min(b, FUSE)), IX("xf", Z, "nb16", 32 * j, min(b, FUSE) // 16))
        act(X("g1", a, b), IX("xf", Z, "nb16", 128 + 32 * j, 160 + 32 * j))
        if j == NUM:
            border("num", "sb", SPW, lambda e, out, q0, q1: act(out, numbers("bl16", 6 * q0, 6 * q1, V)), "SSSS")

    def columns():
        tt(X("off", 0, 16), X("psw", 0, 16), X("vl", 0, 16), OP.min)
        tt(X("rb", 0, 256), X("pa", 0, 256), X("km", 0, 256), OP.mult)
        ts(X("off16", 0, 16), X("off", 0, 16), BIG + 16.0, OP.add)

    def scatter():
        o = IX("inv", 2448, "off16", 0, 16)
        add("V", lambda e: e.tensor_copy(out=o[0], in_=T.rb[:, :]), rg(X("inv", 0, 2448)), rg(X("rb", 0, 256), X("off16", 0, 16)))

    def shifted():
        mm(X("pb", 0, 128), ONE, X("left", 0, 128), True, False, tag="iv")
        mm(X("pa", 0, 512), ZERO, X("wv", 0, 512), True, False, tag="inv")
        for d in range(-7, 16):
            o2 = T.pa[:, :, d + 7:d + 15], rg(X("pa", 0, 512))
            mm(o2, X("inv", 16 + d, 16 + d + V - 15, 16), X("seli", 0, 64), False, d == 15, tag="inv")

    def inverse():
        ts(X("ivt", 0, 128), (T.pa[:, :, 7:23], rg(X("pa", 0, 512))), -1.0, OP.mult)
        mm(X("pb", 0, 128), X("ivt", 0, 128), IB, False, True, tag="iv")

    def first(j):
        a, b = 512 * j, min(512 * j + 512, FUSE)
        tt(X("p0", a, b), X("p0", a, b), X(BOTH[j], 0, b - a), OP.mult)

    def second(a, b):
        tt(X("psw", a, b), X("g1", a, b), X("psw", a, b), OP.mult)

    def both(a, b):
        tt(X("sw", a, b), X("p0", a, b), X("psw", a, b), OP.add)

    def keep(j):
        where(X("p0", 512 * j, 512 * j + 512), X("sw", 512 * j, 512 * j + 512), [[1, 512]], 0, 0)

    nc, nd = SHARE["cm"]
    if EARLY > 0:
        columns()
    if EARLY > 1:
        scatter()
    tt(X("p0", FUSE, V), IX("xf", Z, "nb16", FUSE // 16, 128), X("wr", FUSE, V), OP.mult)
    if EARLY < 1:
        columns()
    for j in BOTH:
        b = min(512 * j + 512, FUSE)
        mm(X(BOTH[j], 0, b - 512 * j), SELQ, X("wsb", 512 * j, b, 1, 0, 16))
        weights(j)
    if SUM:
        a = V - SUM
        mm(X("pb", 0, SUM), IF, X("p0", a, V), True, False, tag="sum")
        tt(X("g1", a, V), X("g1", a, V), X("psw", a, V), OP.mult)
        mm(X("pb", 0, SUM), IF, X("g1", a, V), False, True, tag="sum")
        act(X("sw", a, V), X("pb", 0, SUM))
    if SUM < 512:
        second(1536, V - SUM)
    second(1024, 1536)
    if SUM < 512:
        both(1536, V - SUM)
    if not SUM:
        keep(3)
    first(1)
    both(1024, 1536)
    keep(2)
    second(512, 1024)
    first(0)
    if TAIL:
        both(512, 1024)
        second(0, 256)
        second(256, 512)
        both(0, 256)
        both(256, 512)
    else:
        second(0, 512)
        both(512, 1024)
        both(0, 512)
    if NUM == -1:
        border("num", "sb", SPW, lambda e, out, q0, q1: act(out, numbers("bl16", 6 * q0, 6 * q1, V)), "SSSS")
    if nc:
        act(X("cmr", 0, nc), numbers("mate", 0, nc // 16, Z + 16))
    border("s", "sst", "sw", lister("sw", V, "bl16"), SST)
    if SUM:
        keep(3)
    keep(1)
    keep(0)

    mm(X("pd", 0, 128), HI, IB, True, False, tag="cm")
    mm(X("pd", 0, 128), LO, IB, False, False, tag="cm")
    if EARLY < 2:
        scatter()
    shifted()
    if nd > nc:
        act(X("cmr", nc, nd), numbers("mate", nc // 16, nd // 16, Z + 16))
    if nd < V:
        cp(X("cmr", nd, V), numbers("mate", nd // 16, 128, Z + 16))
    inverse()
    for b in range(16):
        mm(X("pd", 0, 128), X("g2h", 16 - b, 144 - b), X("cmr", b, V, 16), False, b == 15, tag="cm")
    last = len(CUTS) - 2
    for j, (b, a) in enumerate(zip(CUTS, CUTS[1:])):
        tt(X("tw", a, b), IX("sw", Z + 16, "mate", a // 16, b // 16), X("p0", a, b), OP.add)
        if j == 0:
            cp(X("iv16", 0, 128), X("pb", 0, 128))
        o, i = X("g1", a, b), IX("tw", V + 8, "iv16", a // 16, b // 16, a)
        if j == last:
            cp(X("g1", 0, LAST), IX("tw", V + 8, "iv16", 0, LAST // 16))
            if LAST < b:
                act(X("g1", LAST, b), IX("tw", V + 8, "iv16", LAST // 16, b // 16))
        else:
            act(o, i)
        dma("Y", "y%d" % j, T.y[:, a:b], [], o[0], o[1])
        if j == CM:
            act(X("cmv", 0, 128), X("pd", 0, 128))
            dma("Y", "cm", T.cm[:, :], [], T.cmv[:, :], rg(X("cmv", 0, 128)))
    for s, v in total.items():
        if known["G"].get(s, 0) < v:
            g.wait_ge(T.sem[s], v)
